import numpy as np, ml_dtypes
CORES = [48,51,52,55]
N = 4
BF = ml_dtypes.bfloat16
W, A, T, M, RO, EPS, TH = 4096, 1024, 256, 3, 4, 48, 720
WT = 15 * np.arange(16) + 7
RI, GI = np.arange(N)[:, None, None], np.arange(8)[None, :, None]
def clue(d):
    return np.add.reduce(d * WT, axis=-1)
def side(v):
    return (5 * v + (v >> 2)) & (A - 1)
def apart(cand, used):
    v = clue(cand); p, c = v & (A - 1), side(v)
    return cand[np.argmax((p != c) & ~np.isin(p, used) & ~np.isin(c, used))]
def rows128(a):
    return np.ascontiguousarray(np.swapaxes(a, 2, 3)).reshape(N, 128, -1)
def pack(X, S, K, z, l):
    return {"x0": rows128(X).astype(np.float32).astype(BF), "asc": rows128(S).astype(np.int32), "kw": rows128(K).astype(np.int32), "z0": rows128(z).astype(np.float32).astype(BF), "l0": np.ascontiguousarray(l).astype(np.int32)}
def parts(rng):
    mid = rng.integers(0, 256, (8, 32, 16)); order = np.argsort(rng.random((N, 8, W)), axis=-1); h = W >> 1
    X = rng.integers(0, 256, (N, 8, W, 16))
    X[RI, GI, order[:, :, :h]] = np.clip(mid[None, :, np.arange(h) % 32] + rng.integers(-20, 21, (N, 8, h, 16)), 0, 255)
    c = rng.integers(0, 32, (N, 8, T)); m = rng.random((N, 8, T, 1))
    z = np.clip(mid[GI, c] + rng.integers(-20, 21, (N, 8, T, 16)), 0, 255)
    z = np.where(m < 0.5, z, np.where(m < 0.8, rng.integers(0, 256, z.shape), rng.integers(96, 160, z.shape)))
    own = order[RI[..., None], GI[..., None], c[..., None] + 32 * rng.integers(0, W >> 6, (N, 8, T, 16))]
    share = rng.choice(np.array([0.0, 0.15, 0.5]), (N, 8, T, 1))
    K = np.where(rng.random((N, 8, T, 16)) < share, own, rng.integers(0, W, (N, 8, T, 16)))
    S = rng.integers(0, W, (N, 8, A, 16)); l = rng.choice(np.array([0, 0, 1, 1, 2, 3, 5, 8, 14, 15]), (N, 8, T))
    return X, S, K, z, l
def setup_inputs(rng):
    return pack(*parts(rng))
def setup_inputs_corners(rng):
    X, S, K, z, l = parts(rng)
    X[:, 6, 0] = 0; X[:, 6, W - 1] = 255
    S[:, 1] = (W - 1) * rng.integers(0, 2, (N, A, 16)); S[:, 3] = S[:, 3, :, :1].copy(); S[:, 5] = np.arange(A)[:, None]; S[:, 7] = rng.choice(np.array([0, 1, W - 2, W - 1]), (N, A, 16))
    mode = rng.integers(0, 8, (N, 8, T)); mo = mode[..., None]
    K = np.where((mo == 0) | (mo == 3), K[..., :1], np.where(mo == 1, (W - 1) * rng.integers(0, 2, K.shape), K))
    own = np.take_along_axis(K, rng.integers(0, 16, (N, 8, T, 1)), 3)[..., 0]
    z = np.where((mo == 2) | (mo == 3), X[RI, GI, own], np.where(mo == 7, 255 * rng.integers(0, 2, z.shape), z))
    l = np.where((mode == 4) | (mode == 7), 15, np.where(mode == 5, 14, np.where(mode == 6, 0, l)))
    zc = rng.integers(0, 256, 16); X[:, 2, W - 1] = zc; S[:, 2, 0] = rng.integers(0, W - 1, (N, 16)); S[::2, 2, 0, 15] = W - 1
    for t, n in ((0, 15), (T - 1, 14)):
        z[:, 2, t] = zc; K[:, 2, t] = W - 1; l[:, 2, t] = n
    lane = np.arange(T); bq = (np.arange(N)[:, None] + 1 + lane % M) % N; even = np.arange(N) % 2 == 0
    dl = rng.integers(1, 60, 16); z[:, 0] = rng.integers(64, 192, (N, T, 16)); z[:, 0, :, 0] = 0
    X[:, 0, :T] = z[:, 0] + dl * (2 * rng.integers(0, 2, (N, T, 16)) - 1); X[:, 0, :T, 0] = rng.permutation(T); K[:, 0] = lane[:, None]
    pat = rng.integers(0, 256, (16, 16))
    for m in range(4): X[:, 0, W - 64 + 16 * m:W - 48 + 16 * m] = pat
    S[:, 0] = W - 64 + 16 * (np.arange(N) % 4)[:, None, None] + np.argsort(rng.random((N, A, 16)), axis=-1)
    dl = rng.integers(0, 11, 16); z[:, 4] = np.where(bq % 2 == 0, 120, 135)[:, :, None] + rng.integers(-3, 4, (N, T, 16)); z[:, 4, :, 0] = 0
    X[:, 4] = np.where(even, 40, 215)[:, None, None] + rng.integers(-3, 4, (N, W, 16)); X[:, 4, :, 0] = 0
    X[:, 4, :T] = z[:, 4] + dl; X[:, 4, :T, 0] = rng.permutation(T); K[:, 4] = lane[:, None]
    S[:, 4] = T + np.argsort(rng.random((N, A, 1)), axis=1)
    lev = np.where(even, 100, 150); X[:, 5, :W - T] = lev[:, None, None] + rng.integers(-3, 4, (N, W - T, 16))
    z[:, 5] = lev[bq][:, :, None] + rng.integers(-3, 4, (N, T, 16)); X[:, 5, W - T:] = z[:, 5] + rng.integers(0, 11, (N, T, 16)); K[:, 5] = W - T + lane[:, None]
    return pack(X, S, K, z, l)
def setup_inputs_crowd(rng):
    X, S, K, z, l = parts(rng); lane = np.arange(T); bq = (np.arange(N)[:, None] + 1 + lane % M) % N
    for g in (0, 4):
        pat = rng.integers(40, 200, (16, 16)); pat[15] = rng.integers(0, 20, 16)
        if (clue(pat[15]) & (A - 1)) == side(clue(pat[15])): pat[15, 0] += 1
        X[:, g] = pat[np.arange(W) & 15]
        S[:, g] = np.argsort(rng.random((N, A, 16)), axis=-1) + 16 * rng.integers(0, W >> 4, (N, A, 16))
        z[:, g] = 0; l[:, g] = 0; K[:, g] = rng.integers(0, W, (N, T, 16)); K[:, g, :, 0] = (K[:, g, :, 0] >> 4) << 4
        if g == 4:
            K[:, g, 5] = 15 + 16 * rng.integers(0, W >> 4, (N, 16)); c = int(side(clue(pat[15])))
            S[:, g, c] = np.where((S[:, g, c] & 15) == 15, S[:, g, c] - 15, S[:, g, c])
    for g in (1, 5):
        dl = rng.integers(1, 60, 16)
        if (clue(dl) & (A - 1)) == 0: dl[0] += 1
        z[:, g] = rng.integers(64, 192, (N, T, 16)); X[:, g, :T] = z[:, g] + dl * (2 * rng.integers(0, 2, (N, T, 16)) - 1); K[:, g] = lane[:, None]
        pat = rng.integers(0, 256, (16, 16))
        for m in range(4): X[:, g, W - 64 + 16 * m:W - 48 + 16 * m] = pat
        S[:, g] = W - 64 + 16 * (np.arange(N) % 4)[:, None, None] + np.argsort(rng.random((N, 1, 16)), axis=-1)
        if g == 5: X[:, g, T] = z[:, g, 7]; K[:, g, 7] = T
    for g in (2, 6):
        X[:, g, W - 1] = np.where(np.arange(N) % 2 == 0, 40, 215)[:, None] + rng.integers(-3, 4, (N, 16)); S[:, g] = W - 1
        z[:, g] = np.where(bq % 2 == 0, 120, 135)[:, :, None] + rng.integers(-3, 4, (N, T, 16))
        X[:, g, :T] = z[:, g] + rng.integers(0, 21, (N, T, 16)); K[:, g] = lane[:, None]
        if g == 6: z[:, g, 9] = X[bq[:, 9], g, W - 1]; X[:, g, 9] = z[:, g, 9]
    for g in (3, 7):
        pat = rng.integers(0, 31, (16, 16)); pat[4] = rng.integers(185, 221, 16); pat[7] = 255; pat[8] = 0
        for q in range(3):
            e = rng.permutation(64); s = clue(pat[q]) + 7 * (e - pat[q, 0])
            pat[q, 0] = e[np.argmax(((s >> 2) & 15) == ((1 - 4 * q) & 15))]
        v = clue(pat[:3]); pat[3] = apart(rng.integers(0, 31, (64, 16)), np.concatenate([v & (A - 1), side(v)]))
        v = clue(pat[:4]); pat[6] = apart(rng.integers(0, 31, (64, 16)), np.concatenate([v & (A - 1), side(v)]))
        v3, v6 = int(clue(pat[3])), int(clue(pat[6])); a = ((RO - 1) * (T - (1 if g == 7 else 0))) & 31
        if g == 3: dl = np.concatenate([np.array([1, 2, 31]), rng.integers(1, 32, N - 3)])
        else: dl = np.concatenate([np.array([a - 1, a, a + 1]), a + rng.integers(-1, 3, N - 3)])
        dl = rng.permutation(dl)
        X[:, g] = pat[np.arange(W) & 15]; X[:, g, 5::16] = pat[4]; X[:, g, 5::16, 15] += dl[:, None]
        S[:, g] = 4 + 16 * rng.integers(0, W >> 4, (N, A, 16))
        S[:, g, side(v3)] += 1; S[:, g, v6 & (A - 1)] += 4; S[:, g, side(v6)] += 3
        z[:, g] = 0; K[:, g] = 4 - RO + 16 * rng.integers(0, W >> 4, (N, T, 16))
        if g == 7: K[:, g, T - 1] = 6 + 16 * rng.integers(0, W >> 4, (N, 16))
    return pack(X, S, K, z, l)
def setup_inputs_ends(rng):
    X = 255 * rng.integers(0, 2, (N, 8, W, 16)); pal = 255 * rng.integers(0, 2, (8, 8, 16)); pal[:, 0] = 0; pal[:, 1] = 255
    X = np.where(rng.random((N, 8, W, 1)) < 0.5, pal[GI, rng.integers(0, 8, (N, 8, W))], X)
    z = np.where(rng.random((N, 8, T, 1)) < 0.6, pal[GI, rng.integers(0, 8, (N, 8, T))], 255 * rng.integers(0, 2, (N, 8, T, 16)))
    S = np.where((np.arange(A) % 4 == 3)[:, None], rng.integers(0, W, (N, 8, A, 16)), (W - 1) * rng.integers(0, 2, (N, 8, A, 16)))
    K = np.where((np.arange(T) % 4 == 3)[:, None], rng.integers(0, W, (N, 8, T, 16)), (W - 1) * rng.integers(0, 2, (N, 8, T, 16)))
    l = 15 * rng.integers(0, 2, (N, 8, T)); top = int(clue(np.full(16, 255))); c1, c2 = top & (A - 1), int(side(top))
    for g in (0, 7):
        X[:, g, 0] = 0; X[:, g, W - 1] = 255
        for t in (0, T - 1): z[:, g, t] = 0; l[:, g, t] = 0; K[:, g, t] = 0; K[:, g, t, 1] = W - 1; K[:, g, t, 15] = W - 1
        for t in (1, T - 2): z[:, g, t] = 0; l[:, g, t] = 15; K[:, g, t] = 0; K[:, g, t, ::2] = W - 1
        for t in (2, T - 3): z[:, g, t] = 255; l[:, g, t] = 15; K[:, g, t] = 0
        for q in range(N):
            S[q, g, c1] = 0; S[q, g, c2] = 0; S[q, g, 0] = W - 1
            if q % 2 == 1: S[q, g, c1, 1] = W - 1; S[q, g, c1, 15] = W - 1
            if q % 3 == 1: S[q, g, c2, 2] = W - 1; S[q, g, c2, 15] = W - 1
            if q % 2 == 0: S[q, g, 0, 3] = 0; S[q, g, 0, 14] = 0
    return pack(X, S, K, z, l)
def setup_inputs_spread(rng):
    X = (np.exp2(8 * rng.random((N, 8, W, 1))) * rng.random((N, 8, W, 16))).astype(np.int64) * (rng.random((N, 8, W, 1)) > 0.0625)
    z = (np.exp2(8 * rng.random((N, 8, T, 1))) * rng.random((N, 8, T, 16))).astype(np.int64)
    X = np.where(rng.random((N, 8, W, 1)) < 0.3, 255 - X, X); z = np.where(rng.random((N, 8, T, 1)) < 0.5, 255 - z, z)
    S = (W * rng.random((N, 8, A, 16)) ** 3).astype(np.int64); K = (W * rng.random((N, 8, T, 16)) ** 4).astype(np.int64); l = (16 * rng.random((N, 8, T)) ** 3).astype(np.int64)
    return pack(X, S, K, z, l)
def setup_inputs_ties(rng):
    X, S, K, z, l = parts(rng); few = np.array([0, EPS, EPS + 1, 2 * EPS, 255])
    for g in (0, 2, 4, 6):
        s = few[:3] if g < 4 else few
        X[:, g] = rng.choice(s, (N, W, 16)); z[:, g] = rng.choice(s, (N, T, 16))
    for g, e in ((1, 1), (3, 31), (7, 32)):
        y = np.full((N, 16), 100); y[1::2, 15] += e; X[:, g, W - 1] = y; S[:, g] = W - 1
        dev = np.full((N, T, 16), TH >> 4); dev[..., 0] += rng.integers(-2, 3, (N, T))
        z[:, g] = 100 + (2 * rng.integers(0, 2, (N, T, 1)) - 1) * dev; X[:, g, :T] = z[:, g]; K[:, g] = np.arange(T)[:, None]
    lane = np.arange(T); bq = (np.arange(N)[:, None] + 1 + lane % M) % N; cq = (bq[:, 0] + 1) % N
    own = rng.integers(0, 251, (N, 16)); own[:, 0] = 30 * np.arange(N)
    order = rng.permutation(N); dl = rng.integers(1, 5, N); dl[order[:4]] = np.array([1, 2, 3, 1])
    near = np.roll(own, 1, axis=0); near[:, 15] += dl
    X[:, 5, W - 1] = own; X[:, 5, W - 2] = near
    S[:, 5, 0] = W - 1 - (np.argsort(rng.random((N, 16)), axis=-1) & 1)
    z[:, 5] = own[bq]; z[:, 5, 0] = np.where((cq != order[3])[:, None], near[cq], own[bq[:, 0]])
    X[:, 5, :T] = z[:, 5]; K[:, 5] = lane[:, None]
    return pack(X, S, K, z, l)
def check_inputs(d):
    bad = []
    for k, lo, hi in (("x0", 0, 255), ("asc", 0, W - 1), ("kw", 0, W - 1), ("z0", 0, 255), ("l0", 0, 15)):
        v = np.asarray(d[k]).astype(np.float64)
        if not (np.min(v) >= lo and np.max(v) <= hi): bad.append("range of " + k)
        elif np.any(v != np.floor(v)): bad.append("whole numbers of " + k)
    return bad
def reference(x0, asc, kw, z0, l0):
    def turn(a):
        return np.ascontiguousarray(np.swapaxes(a.astype(np.float32).astype(np.int32).reshape(N, 8, 16, -1), 2, 3))
    X, S, K, z, l = turn(x0), turn(asc), turn(kw), turn(z0), l0.astype(np.int32)
    ri, gi = np.arange(N)[:, None, None], np.arange(8)[None, :, None]; i16 = np.arange(16); wt = (15 * np.arange(16) + 7).astype(np.int32)
    b = (np.arange(N)[:, None] + 1 + np.arange(T)[None, :] % M) % N; c = (b + 1) % N
    al = np.zeros((N, 8), np.int32)
    def look(q, col, aim, dl):
        p = S[q[:, None, :], gi, col]; y = X[q[:, None, :, None], gi[..., None], p]
        e = np.add.reduce(np.abs(np.abs(y - aim[:, :, :, None]) - dl[:, :, :, None]), axis=-1); j = np.argmin(e, axis=-1)
        return p, j, np.take_along_axis(e, j[..., None], 3)[..., 0], np.take_along_axis(y, j[..., None, None], 3)[:, :, :, 0]
    for rnd in range(RO):
        x = X[ri[..., None], gi[..., None], K]; dx = np.abs(x - z[:, :, :, None])
        fit = ~np.any((dx > EPS) & (i16 < l[..., None])[:, :, :, None], axis=-1)
        may = fit | ~np.any(fit, axis=-1, keepdims=True)
        k = np.argmax(np.where(may, np.add.reduce(dx, axis=-1), -1), axis=-1)[..., None, None]
        de = np.take_along_axis(dx, k, 3)[:, :, :, 0]; xs = np.take_along_axis(x, k, 3)[:, :, :, 0]
        v = np.add.reduce(de * wt, axis=-1); cb = v & (A - 1); cc = (5 * v + (v >> 2)) & (A - 1)
        p, j, eb, y = look(b, cb, z, de); pg, g, ec, yg = look(c, cc, z, de)
        hit = ec <= eb + (al[c[:, None, :], gi] & 31); con = ~hit & (eb < TH); nei = ~hit & ~con
        zn = np.where(con[..., None], y, np.where(nei[..., None], (z + xs) >> 1, z)); ln = np.where(con, (l + 1) & 15, l)
        off = np.any((np.abs(x - zn[:, :, :, None]) > EPS) & (i16 < ln[..., None])[:, :, :, None], axis=-1)
        K = np.where(hit[..., None], (5 * K + (v >> 2)[..., None]) & (W - 1), np.where(con[..., None] & off, p, K))
        word = np.take_along_axis(p, j[..., None], 3)[..., 0]; new = (y + de) >> 1
        column = np.where(i16 == j[..., None], np.take_along_axis(pg, g[..., None], 3), p)
        for t in range(T):
            r, h = np.nonzero(nei[:, :, t]); X[b[r, t], h, word[r, h, t]] = new[r, h, t]
            r, h = np.nonzero(hit[:, :, t]); S[b[r, t], h, cb[r, h, t]] = column[r, h, t]
            al[c[:, t]] += hit[:, :, t]
        z, l = zn, ln
    def back(a):
        return np.ascontiguousarray(np.swapaxes(a, 2, 3)).reshape(N, 128, -1).astype(np.float32)
    return {"yx": back(X).astype(BF), "ya": back(S), "yk": back(K), "yz": back(z).astype(BF), "yl": l.astype(np.float32)}

@@ -1,0 +1,837 @@
+from concourse.bass import DstId, RemoteDMATransfer
+from concourse.mybir import AluOpType as OP, AxisListType, ActivationFunctionType as AF
+
+N, W, A, TL, RO, EPS, TH = 4, 4096, 1024, 256, 4, 48, 720
+WX = 5248
+NRING = 5
+BIAS = [8000, -3000, 12000, 3000, 1000, 3000, 1000, 2000, 0, 2000, 2000, 8000]
+NV = [2, 2]
+WIN, VPEN = 40.0, 150.0
+
+SCRATCH = {
+    "X": ("sbuf", [128, WX], "bfloat16"), "S": ("sbuf", [128, WX], "float32"),
+    "Si": ("sbuf", [128, A], "int32"), "Ki": ("sbuf", [128, TL], "int32"), "Li": ("sbuf", [128, TL], "int32"),
+    "Lb": ("sbuf", [128, TL], "bfloat16"), "Lo": ("sbuf", [128, TL], "float32"),
+    "Ku": ("sbuf", [128, TL], "uint16"), "Kf": ("sbuf", [128, TL], "float32"),
+    "z": ("sbuf", [128, TL], "bfloat16"), "Lh": ("sbuf", [128, TL], "bfloat16"),
+    "at": ("sbuf", [128, 32], "float32"), "ai": ("sbuf", [128, 16], "int32"),
+    "CB": ("sbuf", [128, 5632], "bfloat16"), "CF": ("sbuf", [128, 2560], "float32"),
+    "CI": ("sbuf", [128, 16], "int32"), "TF": ("sbuf", [128, 1680], "float32"),
+    "sx": ("dram", [4, 128, 1024], "bfloat16"), "lx": ("dram", [4, 128, 1024], "bfloat16"), "mx": ("dram", [4, 128, 1024], "bfloat16"),
+    "sz": ("dram", [4, 128, 64], "bfloat16"), "lz": ("dram", [4, 128, 64], "bfloat16"), "mz": ("dram", [4, 128, 64], "bfloat16"),
+    "sk": ("dram", [4, 128, 64], "int32"), "lk": ("dram", [4, 128, 64], "int32"),
+    "sl": ("dram", [4, 128, 4], "int32"), "ll": ("dram", [4, 128, 4], "int32"),
+    "ol": ("dram", [4, 128, 4], "float32"), "ml": ("dram", [4, 128, 4], "float32"),
+    "ss": ("dram", [4, 128, 256], "int32"), "ls": ("dram", [4, 128, 256], "int32"),
+    "oa": ("dram", [4, 128, 256], "float32"), "ma": ("dram", [4, 128, 256], "float32"),
+    "ok": ("dram", [4, 128, 64], "float32"), "mk": ("dram", [4, 128, 64], "float32"),
+    "ox": ("dram", [4, 128, 1024], "bfloat16"), "oz": ("dram", [4, 128, 64], "bfloat16"),
+}
+for _h in range(2):
+    SCRATCH.update({
+        "xg%d" % _h: ("sbuf", [128, 2048], "bfloat16"), "yg%d" % _h: ("sbuf", [128, 4096], "bfloat16"),
+        "ur%d" % _h: ("sbuf", [128, 512 * NRING], "bfloat16"), "vr%d" % _h: ("sbuf", [128, 512 * NRING], "bfloat16"),
+        "wb%d" % _h: ("sbuf", [128, 4608], "bfloat16"), "wf%d" % _h: ("sbuf", [128, 3200], "float32"),
+        "wi%d" % _h: ("sbuf", [128, 1024], "int32"), "wu%d" % _h: ("sbuf", [128, 320], "uint16"),
+    })
+for _b in range(8):
+    SCRATCH["ps%d" % _b] = ("psum", [128, 512], "float32")
+
+SEMAPHORES = ["P", "V", "A", "G", "stx0", "stx1", "stx2", "stx3", "stk", "sts", "snd",
+              "ax0", "ax1", "ax2", "ax3", "ak", "as_", "inx", "ink", "ins",
+              "ox0", "ox1", "ox2", "ox3", "oa", "ok",
+              "bx0", "bx1", "bx2", "bx3", "ba", "bk", "fin", "fin2"]
+
+CYC, PCYC, LAT, FIX = 0.83, 0.42, 60.0, 55.0
+
+
+def build_ops(T):
+    ops = []
+
+    def add(alts, reads, writes, banks=()):
+        ops.append({"alts": alts, "r": list(reads), "w": list(writes), "b": list(banks), "bias": bias[0]})
+
+    bias = [0.0]
+
+    def vc(n, rate=1.0):
+        return FIX + max(64, n * rate) * CYC
+
+    nsess = [0]
+
+    def session(h):
+        nsess[0] += 1
+        return {"bank": None, "id": nsess[0], "h": h, "left": 0}
+
+    def sap(s, a=0, b=512):
+        return ("slot", s, a, b)
+
+    def R(ap):
+        return T["ps%d" % ap[1]["bank"]][:, ap[2]:ap[3]] if isinstance(ap, tuple) else ap
+
+    def pe(mms, reads, writes, banks):
+        cost = 30.0
+        for (o, l, r, st, sp, n, m, f) in mms:
+            cost += max(min(64, m), n) * (4 if f else 1) * PCYC
+
+        def run(g):
+            last = None
+            for (o, l, r, st, sp, n, m, f) in mms:
+                last = g.tensor.matmul(R(o), l, r, st, sp)
+            return last
+        add({"P": (cost, run)}, reads, writes, banks)
+
+    def ts(out, in0, s1, s2, op0, op1, n, reads, writes, banks=(), rate=1.0, act=None):
+        if op1 is None:
+            alts = {"V": (vc(n, rate), lambda g: g.vector.tensor_scalar(out, R(in0), s1, None, op0))}
+        else:
+            alts = {"V": (vc(n, rate), lambda g: g.vector.tensor_scalar(out, R(in0), s1, s2, op0, op1))}
+        if act is not None:
+            alts["A"] = (vc(n) + 15, lambda g: g.scalar.activation(out, R(in0), act[0], bias=act[1], scale=act[2]))
+        add(alts, reads, writes, banks)
+
+    def tt(out, a, b, op, n, reads, writes, banks=(), rate=None):
+        if rate is None:
+            rate = 1.0 if banks else 2.0
+        add({"V": (vc(n, rate), lambda g: g.vector.tensor_tensor(out, R(a), R(b), op))}, reads, writes, banks)
+
+    def cp(out, in_, n, reads, writes, banks=(), rate=1.0, flex=False):
+        alts = {"V": (vc(n, rate), lambda g: g.vector.tensor_copy(out, R(in_)))}
+        if flex:
+            alts["A"] = (vc(n, max(rate, 1.0)) + 15, lambda g: g.scalar.activation(out, R(in_), AF.Copy))
+        add(alts, reads, writes, banks)
+
+    def act(out, in_, func, n, reads, writes, banks=(), bias=0.0):
+        add({"A": (vc(n) + 15, lambda g: g.scalar.activation(R(out), R(in_), func, bias=bias))}, reads, writes, banks)
+
+    def scan(out, d0, d1, op0, op1, n, reads, writes, banks=()):
+        add({"V": (vc(n), lambda g: g.vector.tensor_tensor_scan(out, d0, d1, 0.0, op0, op1))}, reads, writes, banks)
+
+    def iota(out, pat, base, cm, n, writes, isint=False):
+        if isint:
+            add({"G": (130 + 2 * n * CYC, lambda g: g.iota(out, pat, base, cm))}, [], writes)
+        else:
+            add({"G": (130 + 2 * n * CYC, lambda g: g.iota(out, pat, base, cm, allow_small_or_imprecise_dtypes=True))}, [], writes)
+
+    def mset(ap, v, n, writes):
+        add({"V": (vc(n), lambda g: g.vector.memset(ap, v))}, [], writes)
+
+    pos = {"CB": 0, "CF": 0, "TF": 0}
+    C = {}
+
+    def alloc(buf, name, n):
+        C[name] = (T[buf], pos[buf], n)
+        pos[buf] += (n + 15) // 16 * 16
+
+    def c(name, a=0, b=None, p0=0, p1=128):
+        t, o, n = C[name]
+        return t[p0:p1, o + a:o + (n if b is None else b)]
+
+    for nm, n in (("II", 256), ("nII", 256), ("I22", 128), ("ONES", 128), ("B8", 8), ("Wd", 8), ("Ww", 8), ("W32", 16),
+                  ("CH", 256), ("CR", 256), ("MM16", 128), ("WV", 128), ("W4", 128), ("W21h", 256), ("W21l", 256),
+                  ("MK", 256), ("MKp", 128), ("WV8", 8), ("EX0", 256), ("MKt", 128), ("W32n", 8), ("W64", 8), ("TRI", 512),
+                  ("Z8", 240), ("Zw", 144), ("THN", 128), ("LS", 128), ("LW", 8), ("EXb", 128)):
+        alloc("CB", nm, n)
+    for nm, n in (("IIf", 256), ("I20", 128), ("B8f", 16), ("BBf", 256), ("MM", 256), ("hold", 256), ("holdr", 256),
+                  ("TR", 128), ("KX0", 128), ("KX1", 128), ("EXf", 128), ("col", 32)):
+        alloc("CF", nm, n)
+    for nm, n in (("t0", 256), ("t1", 256), ("t2", 256), ("t3", 256), ("t4", 256), ("t5", 256), ("t6", 144)):
+        alloc("TF", nm, n)
+    colnames = ["p", "pm", "pb", "w", "pw", "th", "thn", "w21", "w21h", "w21l", "n1024", "n5120", "trash", "p16",
+                "e0", "e1", "b0", "b1", "b2", "bc", "w4", "m15"]
+
+    def col(nm, p0=0, p1=128):
+        k = colnames.index(nm)
+        return c("col", k, k + 1, p0, p1)
+
+    CI = T.CI
+    iota(CI[:, 0:1], [[0, 1]], 0, 1, 1, ["ci0"], True)
+    cp(col("p"), CI[:, 0:1], 1, ["ci0"], ["c.p"])
+    ts(CI[:, 1:2], CI[:, 0:1], 15, None, OP.bitwise_and, None, 1, ["ci0"], ["ci1"])
+    ts(CI[:, 2:3], CI[:, 0:1], 4, None, OP.arith_shift_right, None, 1, ["ci0"], ["ci2"])
+    cp(col("pm"), CI[:, 1:2], 1, ["ci1"], ["c.pm"])
+    cp(col("pb"), CI[:, 2:3], 1, ["ci2"], ["c.pb"])
+
+    def cts(nm, src, s1, s2, o0, o1):
+        ts(col(nm), col(src), s1, s2, o0, o1, 1, ["c." + src], ["c." + nm])
+    iota(c("t0"), [[0, 2], [1, 128]], 0, 0, 256, ["t0"])
+    iota(c("t1"), [[0, 2], [1, 8], [0, 16]], 0, 0, 256, ["t1"])
+    iota(c("t2"), [[0, 16], [1, 16]], 0, 0, 256, ["t2"])
+    iota(c("t3", 0, 16), [[0, 2], [1, 8]], 0, 0, 16, ["t3"])
+
+    def eq(dst, src, cn, mul, n, a=0):
+        if mul is None:
+            ts(c(dst, a, a + n), c(src, 0, n), col(cn), None, OP.is_equal, None, n, [src, "c." + cn], [dst])
+        else:
+            rd = [src, "c." + cn] + (["c." + mul] if isinstance(mul, str) else [])
+            ts(c(dst, a, a + n), c(src, 0, n), col(cn), col(mul) if isinstance(mul, str) else mul, OP.is_equal, OP.mult, n, rd, [dst])
+    eq("II", "t0", "p", None, 256)
+    eq("nII", "t0", "p", -1.0, 256)
+    eq("MM", "t2", "pm", None, 256)
+    eq("B8f", "t3", "pb", None, 16)
+    eq("B8", "t3", "pb", None, 8)
+    eq("Wd", "t3", "pb", -2048.0, 8)
+    mset(c("t4", 0, 16), 0.5, 16, ["t4"])
+    mset(c("t4", 16, 32), 0.0, 16, ["t4"])
+    add({"V": (vc(16), lambda g: g.vector.tensor_tensor_scan(c("t4", 32, 48), c("t4", 0, 16), c("t4", 16, 32), 65536.0, OP.mult, OP.add))}, ["t4"], ["t4b"])
+    tt(c("t4", 48, 64), c("t4", 32, 48), c("MM", 0, 16), OP.mult, 16, ["t4b", "MM"], ["t4c"])
+    add({"V": (vc(16), lambda g: g.vector.tensor_reduce(col("th"), c("t4", 48, 64), AxisListType.X, OP.add))}, ["t4c"], ["c.th"])
+    cts("m15", "pm", 15.0, None, OP.is_lt, None)
+    ts(col("pw"), col("th"), 0.5, col("m15"), OP.mult, OP.mult, 1, ["c.th", "c.m15"], ["c.pw"])
+    eq("Ww", "t3", "pb", "pw", 8)
+    cts("e0", "pm", 15.0, -32768.0, OP.is_equal, OP.mult)
+    tt(col("thn"), col("e0"), col("pw"), OP.subtract, 1, ["c.e0", "c.pw"], ["c.thn"])
+    cts("e1", "th", -1.0, None, OP.mult, None)
+    eq("CH", "t1", "pb", "e1", 128, 128)
+    cts("b0", "pb", 0.0, None, OP.is_equal, None)
+    cts("b1", "pb", 1.0, -2048.0, OP.is_equal, OP.mult)
+    cts("b2", "pb", 2.0, -4194304.0, OP.is_equal, OP.mult)
+    tt(col("bc"), col("b1"), col("b2"), OP.add, 1, ["c.b1", "c.b2"], ["c.bc"])
+    ts(c("CH", 0, 128), c("t2", 0, 128), col("b0"), col("bc"), OP.mult, OP.add, 128, ["t2", "c.b0", "c.bc"], ["CH"])
+    eq("I22", "t0", "p", 4194304.0, 128)
+    cts("p16", "p", 16.0, None, OP.mult, None)
+    eq("MM16", "t2", "pm", "p16", 128)
+    ts(c("hold"), c("t2"), 0.0, None, OP.not_equal, None, 256, ["t2"], ["hold"])
+    ts(c("holdr"), c("t2"), 15.0, None, OP.not_equal, None, 256, ["t2"], ["holdr"])
+    eq("IIf", "t0", "p", None, 256)
+    eq("I20", "t0", "p", 20.0, 128)
+    eq("BBf", "t1", "pb", None, 256)
+    cts("w", "pm", 15.0, 7.0, OP.mult, OP.add)
+    cts("w4", "w", 4.0, None, OP.mult, None)
+    cts("w21", "w", 21.0, None, OP.mult, None)
+    eq("WV", "t1", "pb", "w", 128)
+    eq("W4", "t1", "pb", "w4", 128)
+    eq("WV8", "t3", "pb", "w", 8)
+    eq("W21h", "t1", "pb", "w21", 256)
+    ts(c("t5"), c("BBf"), col("w21"), None, OP.mult, None, 256, ["BBf", "c.w21"], ["t5"])
+    tt(c("W21l"), c("t5"), c("W21h"), OP.subtract, 256, ["t5", "W21h"], ["W21l"])
+    ts(c("MK"), c("MM"), -1.0, 16777216.0, OP.add, OP.mult, 256, ["MM"], ["MK"])
+    ts(c("t5", 0, 128), c("MM", 0, 128), -0.5, None, OP.mult, None, 128, ["MM"], ["t5"])
+    tt(c("MKp"), c("t5", 0, 128), c("MK", 0, 128), OP.subtract, 128, ["t5", "MK"], ["MKp"])
+    mset(c("ONES"), 1.0, 128, ["ONES"])
+    eq("W32", "t3", "pb", 32.0, 16)
+    cts("b0", "p", 0.0, None, OP.is_equal, None)
+    cts("b1", "p", 1.0, -262144.0, OP.is_equal, OP.mult)
+    ts(c("CR"), c("t2"), col("b0"), col("b1"), OP.mult, OP.add, 256, ["t2", "c.b0", "c.b1"], ["CR"])
+    ts(CI[:, 3:4], CI[:, 0:1], 7, None, OP.bitwise_and, None, 1, ["ci0"], ["ci3"])
+    cp(col("b2"), CI[:, 3:4], 1, ["ci3"], ["c.b2"])
+    cts("b0", "p", 8.0, 128.0, OP.is_ge, OP.mult)
+    cts("b1", "b0", 128.0, None, OP.add, None)
+    eq("EX0", "t1", "b2", "b1", 256)
+    eq("EXf", "t1", "p", None, 128)
+    eq("EXb", "t1", "p", None, 128)
+    for q in range(2):
+        ts(c("TRI", 256 * q, 256 * q + 256), c("t0"), col("p"), -64.0, OP.is_ge, OP.mult, 256, ["t0", "c.p"], ["TRI"])
+    mset(c("Z8"), 0.0, 240, ["Z8"])
+    mset(c("Z8", 112, 128), 8192.0, 16, ["Z8"])
+    iota(c("t6", 0, 144), [[1, 144]], -16, 0, 144, ["t6"])
+    cts("b2", "pb", 16.0, None, OP.mult, None)
+    eq("Zw", "t6", "b2", "pw", 144)
+    eq("THN", "t1", "pb", "thn", 128)
+    cts("e0", "pm", 15.0, -16.0, OP.is_equal, OP.mult)
+    ts(col("e1"), col("p"), 1.0, col("e0"), OP.add, OP.add, 1, ["c.p", "c.e0"], ["c.e1"])
+    eq("LS", "t0", "e1", None, 128)
+    eq("W32n", "t3", "pb", -32.0, 8)
+    eq("W64", "t3", "pb", 64.0, 8)
+    tt(c("t5", 0, 128), c("t0", 0, 128), c("MM", 0, 128), OP.mult, 128, ["t0", "MM"], ["t5"])
+    tt(c("MKt"), c("t5", 0, 128), c("MK", 0, 128), OP.add, 128, ["t5", "MK"], ["MKt"])
+    eq("LW", "t3", "pb", "pm", 8)
+    cts("n1024", "p", -1.0, -1024.0, OP.mult, OP.add)
+    cts("n5120", "p", -1.0, -5120.0, OP.mult, OP.add)
+    cts("trash", "p", 5120.5, None, OP.add, None)
+    ts(c("t5", 0, 128), c("t0", 0, 128), col("pm"), 5120.0, OP.add, OP.add, 128, ["t0", "c.pm"], ["t5"])
+    ts(c("TR"), c("hold", 0, 128), -1.0, 1.0, OP.mult, OP.add, 128, ["hold"], ["TR"])
+    tt(c("TR"), c("TR"), c("t5", 0, 128), OP.mult, 128, ["TR", "t5"], ["TR"])
+    for q in range(8):
+        ts(c("t5", 16 * q, 16 * q + 16), c("t4", 32, 48), (1.0 if q % 2 == 0 else -1.0) / 65536.0, None, OP.mult, None, 16, ["t4b"], ["t5"])
+    iota(c("t3", 128, 256), [[1, 4], [0, 32]], 0, 0, 128, ["t3b"])
+    for q in range(2):
+        cts("b2", "p", -4.0 * q, None, OP.add, None)
+        ts(c("KX%d" % q), c("t3", 128, 256), col("b2"), None, OP.is_equal, None, 128, ["t3b", "c.b2"], ["KX%d" % q])
+        tt(c("KX%d" % q), c("KX%d" % q), c("t5", 0, 128), OP.mult, 128, ["KX%d" % q, "t5"], ["KX%d" % q])
+
+    X, S, Ku, Kf, z, Lh, at, ai = T.X, T.S, T.Ku, T.Kf, T.z, T.Lh, T.at, T.ai
+    mset(at[:, 0:8], 0.0, 8, ["atot"])
+    mset(at[:, 8:16], 16.0, 8, ["athr"])
+
+    def zwin(h, rnd, j, n=1):
+        o = 3072 + 384 * (rnd % 2) + 128 * j
+        return T["wb%d" % h][:, o:o + 128 * n]
+
+    def lwin(h, rnd, j, n=1):
+        o = 3840 + 384 * (rnd % 2) + 128 * j
+        return T["wb%d" % h][:, o:o + 128 * n]
+
+    def kwin(h, rnd, j, n=1):
+        o = 2432 + 384 * (rnd % 2) + 128 * j
+        return T["wf%d" % h][:, o:o + 128 * n]
+
+    def skeys(h, rnd):
+        return ["%s%d%d" % (s, rnd % 2, h) for s in ("zw", "lw", "kw")]
+
+    for h in range(2):
+        L = slice(128 * h, 128 * h + 128)
+        zk, lk, kk_ = skeys(h, 0)
+        cp(Ku[:, L], T.Ki[:, L], 128, ["in0"], ["Ku%d" % h])
+        cp(kwin(h, 0, 1), T.Ki[:, L], 128, ["in0"], [kk_])
+        cp(zwin(h, 0, 0), z[:, L], 128, ["in0", "z%d" % h], [zk], rate=0.5)
+        cp(T.Lb[0:8, L], T.Li[0:8, L], 128, ["in0"], ["Lb%d" % h])
+        m = T["ps%d" % (6 + h)]
+        pe([(m[:, 0:128], c("EXb", 0, 128, 0, 8), T.Lb[0:8, L], True, True, 128, 128, 0)], ["EXb", "Lb%d" % h], ["m0%d" % h], [6 + h])
+        ts(lwin(h, 0, 0), m[:, 0:128], col("pm"), None, OP.is_equal, None, 128, ["m0%d" % h, "c.pm"], [lk], [6 + h])
+        cp(lwin(h, 0, 1), lwin(h, 0, 0), 128, [lk], [lk + "b"], rate=0.5)
+    cp(S[:, W:W + A], T.Si[:, :], A, ["in2", "Spad"], ["S"])
+
+    ring = [0, 0]
+
+    def names(h):
+        return lambda s: "%s%d" % (s, h)
+
+    def bufs(h):
+        wb, wf, wi, wu = T["wb%d" % h], T["wf%d" % h], T["wi%d" % h], T["wu%d" % h]
+        return wb, wf, wi, wu
+
+    def sub_chunk(h, src, skeys, base, ch, lz, rz, zkeys):
+        s = session(h)
+        mms = []
+        for kk in range(4):
+            mms.append((sap(s, 128 * kk, 128 * kk + 128), c("II", 0, 128), src[:, base + 4 * ch + kk:base + 2048:16], True, False, 128, 128, 0))
+            mms.append((sap(s, 128 * kk, 128 * kk + 128), lz, rz, False, True, 128, 128, 0))
+        pe(mms, ["II", "nII"] + skeys + zkeys, ["sl%d" % s["id"]], [s])
+        return s, "sl%d" % s["id"]
+
+    def ringbuf(h):
+        r = ring[h]
+        ring[h] = (r + 1) % NRING
+        return r
+
+    def gather(out, win, off, n, reads, writes, flex=True):
+        cp(out, win.indirect(off), n, reads, writes, rate=1.5, flex=flex)
+
+    def perm(h, out, wide, src, back, f):
+        mms = []
+        for cl in range(3):
+            o = (cl - 128 * h) % 3
+            s = 32 * (cl + 1) if back else 128 - 32 * (cl + 1)
+            mms.append((out(o), wide(s), src(o), True, True, 43, 128, f))
+        return mms
+
+    def stage_a(h, rnd):
+        bias[0] = BIAS[0] * (1 - h)
+        k = names(h)
+        wb, wf, wi, wu = bufs(h)
+        xg, acc, m = T["xg%d" % h], T["ps%d" % (4 + h)], T["ps%d" % (6 + h)]
+        ab, mb = [4 + h], [6 + h]
+        L = slice(128 * h, 128 * h + 128)
+        l0 = 128 * h
+        for q in range(2):
+            gather(xg[:, 1024 * q:1024 * q + 1024], X[:, 0:W], Ku[:, l0 + 64 * q:l0 + 64 * q + 64], 1024, ["X", "in1", k("Ku")], [k("xg%d" % q)])
+        allm = [k("m0"), k("m1"), k("m2"), k("m3")]
+        zk, lk, kk_ = skeys(h, rnd)
+        zc, lc = zwin(h, rnd, 0), lwin(h, rnd, 0)
+        pe([(m[:, 256:384], c("LS"), lc, True, True, 128, 128, 0)], [lk, "LS"], [k("m2")], mb)
+        cp(lwin(h, rnd, 2), m[:, 256:384], 128, [k("m2")], [k("dL")], mb, flex=True)
+        pe([(acc[:, 0:128], lc, c("CH", 0, 128), True, False, 128, 128, 0),
+            (m[:, 0:128], lc, c("CH", 128, 256), True, False, 128, 128, 0)], [lk, "CH"], [k("acc")] + allm, ab + mb)
+        for ch in range(4):
+            s, sl = sub_chunk(h, xg, [k("xg0"), k("xg1")], 0, ch, c("nII", 0, 128), zc, [zk])
+            r = ringbuf(h)
+            u, v = T["ur%d" % h][:, 512 * r:512 * r + 512], T["vr%d" % h][:, 512 * r:512 * r + 512]
+            act(u, sap(s), AF.Abs, 512, [sl], [k("u%d" % r)], [s])
+            ts(v, u, 48.0, None, OP.is_gt, None, 512, [k("u%d" % r)], [k("v%d" % r)], rate=0.5)
+            mu, mv = [], []
+            for kk in range(4):
+                kq = 4 * ch + kk
+                mu.append((acc[:, kq:128:16], T["ur%d" % h][:, 512 * r + 128 * kk:512 * r + 128 * kk + 128], c("Wd"), False, False, 8, 128, 0))
+                mv.append((m[:, kq:128:16], T["vr%d" % h][:, 512 * r + 128 * kk:512 * r + 128 * kk + 128], c("Ww"), False, kq == 15, 8, 128, 0))
+            pe(mu + mv, [k("u%d" % r), k("v%d" % r), "Wd", "Ww", k("acc")], [k("acc")] + allm, ab + mb)
+        bias[0] = BIAS[1] * (1 - h) + BIAS[11]
+        act(wb[:, 0:128], m[:, 0:128], AF.Sign, 128, [k("m0")], [k("sg")], mb, bias=0.5)
+        pe([(acc[:, 0:128], c("I22"), wb[:, 0:128], False, True, 128, 128, 0)], [k("sg"), "I22", k("acc")], [k("acc")], ab)
+        scan(wf[:, 0:128], c("hold", 0, 128), acc[:, 0:128], OP.mult, OP.min, 128, [k("acc"), "hold"], [k("s1")], ab)
+        o = C["holdr"][1]
+        scan(acc[:, 383:255:-1], T.CF[:, o + 127:o - 1:-1], wf[:, 127::-1], OP.mult, OP.min, 128, [k("s1"), "holdr"], [k("acc")], ab)
+        tt(wf[:, 512:640], acc[:, 256:384], c("MM", 0, 128), OP.mult, 128, [k("acc"), "MM"], [k("s3")], ab)
+        pe([(m[:, 0:8], wf[:, 512:640], c("B8f", 0, 8), True, False, 8, 128, 1),
+            (m[:, 0:8], c("MM16"), c("B8"), False, True, 8, 128, 0)], [k("s3"), "B8f", "B8", "MM16"], [k("m0")], mb)
+        cp(wi[:, 0:8], m[:, 0:8], 8, [k("m0")], [k("i0")], mb)
+        ts(wi[:, 8:16], wi[:, 0:8], 2047, None, OP.bitwise_and, None, 8, [k("i0")], [k("i1")])
+        cp(wu[:, 0:8], wi[:, 8:16], 8, [k("i1")], [k("ou")])
+        tt(wb[:, 128:256], xg[:, 0:2048].indirect(wu[:, 0:8]), zc, OP.subtract, 128, [k("xg0"), k("xg1"), k("ou"), zk], [k("as")], rate=1.5)
+        act(wb[:, 256:384], wb[:, 128:256], AF.Abs, 128, [k("as")], [k("D")])
+        z0 = 3072 + 384 * (rnd % 2)
+        pe(perm(h, lambda o: m[:, o:128:3], lambda s: c("II", s, s + 128), lambda o: wb[:, z0 + o:z0 + 128:3], False, 0)
+           + perm(h, lambda o: m[:, 128 + o:256:3], lambda s: c("II", s, s + 128), lambda o: wb[:, 256 + o:384:3], False, 0),
+           ["II", zk, k("D")], [k("m0"), k("m1")], mb)
+        cp(wb[:, 384:640], m[:, 0:256], 256, [k("m0"), k("m1")], [k("zD")], mb, flex=True)
+        DB = wb[:, 512:640]
+        pe([(m[:, 0:256], c("II", 0, 128), c("MK"), True, False, 256, 128, 0),
+            (m[:, 0:128], c("W4"), DB, False, False, 128, 128, 0),
+            (m[:, 128:256], c("W21h", 96, 224), DB, False, False, 128, 128, 0),
+            (m[:, 128:256], c("W21l", 96, 224), DB, False, True, 128, 128, 0)],
+           ["II", "MK", "W4", "W21h", "W21l", k("zD")], [k("m0"), k("m1")], mb)
+        scan(wf[:, 640:896], c("hold"), m[:, 0:256], OP.mult, OP.max, 256, [k("m0"), k("m1"), "hold"], [k("sc")], mb)
+        cp(wi[:, 16:32], wf[:, 655:896:16], 16, [k("sc")], [k("i2")])
+        ts(wi[:, 32:48], wi[:, 16:32], 2, 1023, OP.arith_shift_right, OP.bitwise_and, 16, [k("i2")], [k("i3")])
+        cp(wu[:, 8:24], wi[:, 32:48], 16, [k("i3")], [k("cu")])
+        gather(wu[:, 64:320], S[:, W:W + A], wu[:, 8:24], 256, ["S", k("cu")], [k("Pu")], flex=False)
+        gather(wf[:, 896:1152], S[:, W:W + A], wu[:, 8:24], 256, ["S", k("cu")], [k("Pf")])
+        pe([(m[:, 256:264], DB, c("WV8"), True, True, 8, 128, 0),
+            (m[:, 384:512], c("WV"), wb[:, 256:384], True, False, 128, 128, 0),
+            (m[:, 384:512], c("I20"), kwin(h, rnd, 1), False, True, 128, 128, 1)],
+           ["WV8", "WV", "I20", k("zD"), k("D"), kk_], [k("m2"), k("m3")], mb)
+        cp(wi[:, 48:56], m[:, 256:264], 8, [k("m2")], [k("i4")], mb)
+        ts(wi[:, 56:64], wi[:, 48:56], 1023, None, OP.bitwise_and, None, 8, [k("i4")], [k("i5")])
+        ts(wf[:, 1152:1160], wi[:, 56:64], col("n1024"), None, OP.add, None, 8, [k("i5"), "c.n1024"], [k("kc")])
+        cp(wi[:, 128:256], m[:, 384:512], 128, [k("m3")], [k("k1")], mb)
+        ts(wi[:, 256:384], wi[:, 128:256], 2, 4095, OP.arith_shift_right, OP.bitwise_and, 128, [k("k1")], [k("k2")])
+        cp(kwin(h, rnd, 0), wi[:, 256:384], 128, [k("k2")], [k("K5")])
+        ts(wi[:, 384:512], wb[:, 128:256], 0.5, -0.25, OP.mult, OP.add, 128, [k("as")], [k("hfi")])
+        tt(zwin(h, rnd, 1), wi[:, 384:512], zc, OP.add, 128, [k("hfi"), zk], [k("zf")])
+        pe(perm(h, lambda o: m[:, 384 + o:512:3], lambda s: c("IIf", s, s + 128), lambda o: wf[:, 896 + o:1024:3], True, 1),
+           ["IIf", k("Pf")], [k("m3")], mb)
+        tt(wf[:, 1664:1792], m[:, 384:512], kwin(h, rnd, 1), OP.subtract, 128, [k("m3"), kk_], [k("d2")], mb)
+        if NV[h]:
+            cp(wb[:, 1536:1664], DB, 128, [k("zD")], [k("D4")], rate=0.5)
+            cp(wb[:, 1664:1792], DB, 128, [k("zD")], [k("D4")], rate=0.5)
+            cp(wb[:, 1792:2048], wb[:, 1536:1792], 256, [k("D4")], [k("D4")], rate=0.5)
+
+    def stage_c(h, rnd):
+        bias[0] = BIAS[2] * (1 - h)
+        k = names(h)
+        wb, wf, wi, wu = bufs(h)
+        yg, acc, m = T["yg%d" % h], T["ps%d" % (4 + h)], T["ps%d" % (6 + h)]
+        ab, mb = [4 + h], [6 + h]
+        L = slice(128 * h, 128 * h + 128)
+        l0 = 128 * h
+        zB, DB = wb[:, 384:512], wb[:, 512:640]
+        for q in range(4):
+            gather(yg[:, 1024 * q:1024 * q + 1024], X[:, 0:W], wu[:, 64 + 64 * q:128 + 64 * q], 1024, ["X", k("Pu")], [k("yg%d" % q)])
+        pe([(acc[:, 0:256], c("ONES"), c("CR"), True, False, 256, 128, 0)], ["ONES", "CR"], [k("acc")], ab)
+        for role in range(2):
+            lz = c("nII", 96 * role, 96 * role + 128)
+            for ch in range(4):
+                s, sl = sub_chunk(h, yg, [k("yg%d" % (2 * role)), k("yg%d" % (2 * role + 1))], 2048 * role, ch, lz, zB, [k("zD")])
+                r = ringbuf(h)
+                u, v = T["ur%d" % h][:, 512 * r:512 * r + 512], T["vr%d" % h][:, 512 * r:512 * r + 512]
+                if role == 0 and ch >= 4 - NV[h]:
+                    act(sap(s), sap(s), AF.Abs, 512, [sl], [sl], [s])
+                    tt(u, sap(s), wb[:, 1536:2048], OP.subtract, 512, [sl, k("D4")], [k("u%d" % r)], [s])
+                    ts(v, u, 0.0, None, OP.max, None, 512, [k("u%d" % r)], [k("v%d" % r)], rate=0.5)
+                    mv = []
+                    for kk in range(4):
+                        kq = 4 * ch + kk
+                        for buf, wt in (("ur", "W32n"), ("vr", "W64")):
+                            mv.append((acc[:, kq:128:16], T["%s%d" % (buf, h)][:, 512 * r + 128 * kk:512 * r + 128 * kk + 128],
+                                       c(wt), False, False, 8, 128, 0))
+                    pe(mv, [k("u%d" % r), k("v%d" % r), "W32n", "W64", k("acc")], [k("acc")], ab)
+                    continue
+                act(u, sap(s), AF.Abs, 512, [sl], [k("u%d" % r)], [s])
+                mms = [(sap(s), c("II", 0, 128), u, True, False, 512, 128, 0)]
+                for kk in range(4):
+                    mms.append((sap(s, 128 * kk, 128 * kk + 128), lz, DB, False, kk == 3, 128, 128, 0))
+                pe(mms, ["II", "nII", k("zD"), sl, k("u%d" % r)], [sl], [s])
+                act(v, sap(s), AF.Abs, 512, [sl], [k("v%d" % r)], [s])
+                mv = []
+                for kk in range(4):
+                    kq = 4 * ch + kk
+                    mv.append((acc[:, 128 * role + kq:128 * role + 128:16], T["vr%d" % h][:, 512 * r + 128 * kk:512 * r + 128 * kk + 128],
+                               c("W32", 2 * role, 2 * role + 8), False, role == 1 and kq == 15, 8, 128, 0))
+                pe(mv, [k("v%d" % r), "W32", k("acc")], [k("acc")], ab)
+        bias[0] = BIAS[3] * (1 - h) + BIAS[10]
+        scan(wf[:, 0:256], c("hold"), acc[:, 0:256], OP.mult, OP.min, 256, [k("acc"), "hold"], [k("s1")], ab)
+        o = C["holdr"][1]
+        scan(wf[:, 511:255:-1], T.CF[:, o + 255:o - 1:-1], wf[:, 255::-1], OP.mult, OP.min, 256, [k("s1"), "holdr"], [k("s2")])
+        tt(wb[:, 640:896], acc[:, 0:256], wf[:, 256:512], OP.is_equal, 256, [k("acc"), k("s2")], [k("oh")], ab)
+        I = c("II", 0, 128)
+        pe([(m[:, 0:128], wb[:, 640:768], I, True, True, 128, 128, 0),
+            (m[32:64, 128:256], wb[:, 768:800], I, True, True, 128, 32, 0),
+            (m[64:128, 128:256], wb[:, 800:864], I, True, True, 128, 64, 0),
+            (m[0:32, 128:256], wb[:, 864:896], I, True, True, 128, 32, 0)], ["II", k("oh")], [k("m0"), k("m1")], mb)
+        tt(wf[:, 1792:2048], m[:, 0:256], wf[:, 896:1152], OP.mult, 256, [k("m0"), k("m1"), k("Pf")], [k("pay")], mb)
+        pe([(m[:, 256:384], I, c("MK", 0, 128), True, False, 128, 128, 0),
+            (m[:, 256:384], c("BBf", 0, 128), wf[:, 1792:1920], False, True, 128, 128, 1)], ["II", "MK", "BBf", k("pay")], [k("m2")], mb)
+        scan(wf[:, 640:768], c("hold", 0, 128), m[:, 256:384], OP.mult, OP.max, 128, [k("m2"), "hold"], [k("sc")], mb)
+        cp(wu[:, 24:32], wf[:, 655:768:16], 8, [k("sc")], [k("ju")])
+        gather(wb[:, 896:1024], X[:, 0:W], wu[:, 24:32], 128, ["X", k("ju")], [k("yj")])
+        pe([(m[:, 128:136], wf[:, 1792:1920], c("B8f", 0, 8), True, True, 8, 128, 1),
+            (m[:, 384:512], c("BBf", 32, 160), wf[:, 1920:2048], True, True, 128, 128, 1)], ["B8f", "BBf", k("pay")], [k("m1"), k("m3")], mb)
+        ts(wf[:, 1160:1168], m[:, 128:136], col("n5120"), None, OP.add, None, 8, [k("m1"), "c.n5120"], [k("kw")], mb)
+        tt(wf[:, 2048:2176], m[:, 384:512], wf[:, 896:1024], OP.subtract, 128, [k("m3"), k("Pf")], [k("c1")], mb)
+        tt(wf[:, 2176:2304], m[:, 0:128], wf[:, 2048:2176], OP.mult, 128, [k("m0"), k("c1")], [k("c2")], mb)
+        pe(perm(h, lambda o: m[:, 256 + o:384:3], lambda s: c("II", s, s + 128), lambda o: wb[:, 896 + o:1024:3], True, 0),
+           ["II", k("yj")], [k("m2")], mb)
+        cp(zwin(h, rnd, 2), m[:, 256:384], 128, [k("m2")], [k("yh")], mb, flex=True)
+        pe([(m[:, 384:512], I, wb[:, 896:1024], True, False, 128, 128, 0),
+            (m[:, 384:512], I, DB, False, True, 128, 128, 0)], ["II", k("yj"), k("zD")], [k("m3")], mb)
+        ts(wi[:, 512:640], m[:, 384:512], 0.5, -0.25, OP.mult, OP.add, 128, [k("m3")], [k("nw")], mb)
+        ME, MF = wf[:, 15:128:16], wf[:, 143:256:16]
+        thr = float(32 * TH - 262144)
+        tt(wf[:, 1168:1176], MF, ME, OP.subtract, 8, [k("s1")], [k("dt")])
+        tt(wb[:, 1152:1160], wf[:, 1168:1176], at[:, 8:16], OP.is_le, 8, [k("dt"), "athr"], [k("hit")])
+        ts(wb[:, 1184:1192], ME, thr, None, OP.is_ge, None, 8, [k("s1")], [k("ge")])
+        ts(wb[:, 1192:1200], ME, thr, None, OP.is_lt, None, 8, [k("s1")], [k("lt")])
+        tt(wb[:, 1160:1168], wb[:, 1184:1192], wb[:, 1152:1160], OP.is_gt, 8, [k("ge"), k("hit")], [k("nei")])
+        tt(wb[:, 1168:1176], wb[:, 1192:1200], wb[:, 1152:1160], OP.is_gt, 8, [k("lt"), k("hit")], [k("con")])
+        tt(wf[:, 1176:1192], wb[:, 1152:1168], wf[:, 1152:1168], OP.mult, 16, [k("hit"), k("nei"), k("kc"), k("kw")], [k("km")])
+        tt(wf[:, 1192:1200], wf[:, 1176:1184], wf[:, 1184:1192], OP.add, 8, [k("km")], [k("ks")])
+        ts(wf[:, 1200:1208], wf[:, 1192:1200], col("trash"), None, OP.add, None, 8, [k("ks"), "c.trash"], [k("key")])
+
+    def stage_e(h, rnd):
+        last = rnd == RO - 1
+        zk, lk, kk_ = skeys(h, rnd)
+        zn, ln, kn = skeys(h, rnd + 1)
+        bias[0] = BIAS[4] * (1 - h) + BIAS[9]
+        k = names(h)
+        wb, wf, wi, wu = bufs(h)
+        xg, acc, m = T["xg%d" % h], T["ps%d" % (4 + h)], T["ps%d" % (6 + h)]
+        ab, mb = [4 + h], [6 + h]
+        L = slice(128 * h, 128 * h + 128)
+        I = c("II", 0, 128)
+        pe([(m[0:8, 128:256], wf[:, 1200:1208], c("IIf", 0, 128), True, True, 128, 8, 1)], ["IIf", k("key")], [k("m1")], mb)
+        cp(wf[0:8, 2304:2432], m[0:8, 128:256], 128, [k("m1")], [k("Rf")], mb, flex=True)
+        s = session(2 + h)
+        sl = "sl%d" % s["id"]
+        pe([(sap(s, 128 * q, 128 * q + 128), c("KX%d" % q, 0, 128, 0, 8), wf[0:8, 2304:2432], True, True, 128, 128, 1) for q in range(2)],
+           ["KX0", "KX1", k("Rf")], [sl], [s])
+        cp(wi[:, 640:896], sap(s, 0, 256), 256, [sl], [k("r1")], [s])
+        tt(wb[:, 1280:1536], wi[:, 640:896], sap(s, 0, 256), OP.is_gt, 256, [sl, k("r1")], [k("bits")], [s])
+        for q in range(2):
+            s = session(2 + h)
+            sl = "sl%d" % s["id"]
+            mms = [(sap(s), I, c("TRI"), True, False, 512, 128, 0)]
+            for a in range(4):
+                bt = wb[32 * a:32 * a + 32, 1280 + 128 * q:1408 + 128 * q]
+                mms.append((sap(s, 128 * a, 128 * a + 128), bt, bt, False, a == 3, 128, 128, 0))
+                pe(mms, ["II", "TRI", k("bits"), sl], [sl], [s])
+                ops[-1]["fence"] = 1
+                mms = []
+            ts(wb[:, 2048 + 512 * q:2560 + 512 * q], sap(s), -15.0, 0.0, OP.add, OP.max, 512, [sl], [k("e%d" % q)], [s],
+               act=(AF.Relu, -15.0, 1.0))
+        mms = [(m[:, 128:256], I, c("MKp"), True, False, 128, 128, 0),
+               (m[:, 128:256], c("EXf", 0, 128, 0, 8), wf[0:8, 2304:2432], False, False, 128, 128, 1)]
+        for b in range(8):
+            mms.append((m[:, 128:256], c("Z8", 112 - 16 * b, 240 - 16 * b), wb[:, 2048 + 128 * b:2176 + 128 * b], False, b == 7, 128, 128, 0))
+        pe(mms, ["II", "MKp", "EXf", "Z8", k("Rf"), k("e0"), k("e1")], [k("m1")], mb)
+        scan(wf[:, 640:768], c("TR"), m[:, 128:256], OP.max, OP.min, 128, [k("m1"), "TR"], [k("sc")], mb)
+        cp(wu[:, 32:40], wf[:, 655:768:16], 8, [k("sc")], [k("ku")])
+        bias[0] = BIAS[5] * (1 - h) + BIAS[6]
+        mms = [(m[0:16, 0:128], wb[:, 1160:1176], I, True, True, 128, 16, 0)]
+        if not last:
+            mms.append((m[:, 256:264], c("ONES"), wb[:, 1152:1160], True, True, 8, 128, 0))
+        pe(mms, ["II", "ONES", k("hit"), k("nei"), k("con")], [k("m0"), k("m2")], mb)
+        cp(wb[0:16, 1024:1152], m[0:16, 0:128], 128, [k("m0")], [k("Rb")], mb, flex=True)
+        if not last:
+            tt(wf[:, 1208:1216], m[:, 256:264], at[:, 0:8] if h == 0 else T.wf0[:, 1208:1216], OP.add, 8,
+               [k("m2"), "atot", "cnt0"], [k("cnt")], mb)
+        mms = [(m[:, 384:512], I, c("MKt"), True, False, 128, 128, 0)]
+        for j, mm in enumerate(perm(h, lambda o: m[:, 384 + o:512:3], lambda s: c("EX0", s, s + 128, 0, 16), lambda o: wb[0:16, 1024 + o:1152:3], True, 0)):
+            mms.append(mm[:3] + (False, j == 2) + mm[5:])
+        pe(mms, ["II", "MKt", "EX0", k("Rb")], [k("m3")], mb)
+        scan(wf[:, 768:896], c("hold", 0, 128), m[:, 384:512], OP.mult, OP.max, 128, [k("m3"), "hold"], [k("sc2"), k("sc")], mb)
+        cp(wu[:, 40:48], wf[:, 783:896:16], 8, [k("sc2")], [k("su")])
+        su = wu[:, 40:48]
+        gather(z[:, L] if last else zwin(h, rnd + 1, 0), zwin(h, rnd, 0, 3), su, 128, [k("su"), zk, k("zf"), k("yh")], [k("z") if last else zn])
+        gather(lwin(h, rnd + 1, 0), lwin(h, rnd, 0, 3), su, 128, [k("su"), lk, lk + "b", k("dL")], [ln])
+        if not last:
+            cp(lwin(h, rnd + 1, 1), lwin(h, rnd + 1, 0), 128, [ln], [ln + "b"], rate=0.5)
+        bias[0] = BIAS[7] * (1 - h) + BIAS[8]
+        pe([(acc[:, 0:128], c("THN"), lwin(h, rnd, 0), True, False, 128, 128, 0)], ["THN", lk], [k("acc")], ab)
+        for ch in range(4):
+            s, sl = sub_chunk(h, xg, [k("xg0"), k("xg1")], 0, ch, c("nII", 0, 128), zwin(h, rnd, 2), [k("yh")])
+            r = ringbuf(h)
+            u, v = T["ur%d" % h][:, 512 * r:512 * r + 512], T["vr%d" % h][:, 512 * r:512 * r + 512]
+            act(u, sap(s), AF.Abs, 512, [sl], [k("u%d" % r)], [s])
+            ts(v, u, 48.0, None, OP.is_gt, None, 512, [k("u%d" % r)], [k("v%d" % r)], rate=0.5)
+            mv = []
+            for kk in range(4):
+                kq = 4 * ch + kk
+                mv.append((acc[:, 0:128], c("Zw", 16 - kq, 144 - kq), T["vr%d" % h][:, 512 * r + 128 * kk:512 * r + 128 * kk + 128], False, kq == 15, 128, 128, 0))
+            pe(mv, [k("v%d" % r), "Zw", k("acc")], [k("acc")], ab)
+        ts(acc[:, 0:128], acc[:, 0:128], -0.5, None, OP.is_gt, None, 128, [k("acc")], [k("acc")], ab)
+        tt(acc[:, 0:128], acc[:, 0:128], wf[:, 1664:1792], OP.mult, 128, [k("acc"), k("d2")], [k("acc")], ab)
+        tt(kwin(h, rnd, 2), acc[:, 0:128], kwin(h, rnd, 1), OP.add, 128, [k("acc"), kk_], [k("Kc")], ab)
+        if not last:
+            gather(Ku[:, L], kwin(h, rnd, 0, 3), su, 128, [k("su"), kk_, k("K5"), k("Kc")], [k("Ku")], flex=False)
+        gather(Kf[:, L] if last else kwin(h, rnd + 1, 1), kwin(h, rnd, 0, 3), su, 128, [k("su"), kk_, k("K5"), k("Kc")], [k("Kf") if last else kn])
+        if last:
+            pe([(m[0:8, 0:128], c("LW"), lwin(h, rnd + 1, 0), True, True, 128, 8, 0)], ["LW", ln], [k("m0")], mb)
+            cp(T.Lo[0:8, L], m[0:8, 0:128], 128, [k("m0")], [k("Lo")], mb, flex=True)
+
+    def writes(h):
+        k = names(h)
+        wb, wf, wi, wu = bufs(h)
+        cp(X[:, 0:WX].indirect(wu[:, 32:40]), wi[:, 512:640], 128, [k("ku"), k("nw"), "Xpad", "X"], ["X"], rate=3.8)
+        tt(S[:, 0:WX].indirect(wu[:, 32:40]), wf[:, 2176:2304], wf[:, 896:1024], OP.add, 128, [k("ku"), k("c2"), k("Pf"), "S"], ["S"], rate=3.8)
+
+    for rnd in range(RO):
+        last = rnd == RO - 1
+        for stage in (stage_a, stage_c, stage_e):
+            for h in range(2):
+                stage(h, rnd)
+        bias[0] = 0.0
+        writes(0); writes(1)
+        if not last:
+            cp(at[:, 0:8], T.wf1[:, 1208:1216], 8, ["cnt1"], ["atot"])
+            cp(ai[:, 0:8], T.wf1[:, 1208:1216], 8, ["cnt1"], ["ai0"])
+            ts(ai[:, 8:16], ai[:, 0:8], 31, None, OP.bitwise_and, None, 8, ["ai0"], ["ai1"])
+            ts(at[:, 8:16], ai[:, 8:16], 32.0, 16.0, OP.mult, OP.add, 8, ["ai1"], ["athr"])
+    return ops
+
+
+READY = {"in0": 10000.0, "in1": 13000.0, "in2": 16000.0}
+
+
+def schedule(ops):
+    n = len(ops)
+    deps = [set() for _ in range(n)]
+    lastw, readers = {}, {}
+    for i, o in enumerate(ops):
+        for key in o["r"]:
+            if key in lastw:
+                deps[i].add(lastw[key])
+        for key in o["w"]:
+            if key in lastw:
+                deps[i].add(lastw[key])
+            deps[i].update(readers.get(key, ()))
+        for key in o["r"]:
+            readers.setdefault(key, []).append(i)
+        for key in o["w"]:
+            lastw[key] = i
+            readers[key] = []
+        deps[i].discard(i)
+    first, order_only = {}, [set() for _ in range(n)]
+    for i, o in enumerate(ops):
+        for b in o["b"]:
+            if isinstance(b, dict):
+                if b["left"] == 0:
+                    if b["h"] in first and first[b["h"]] not in deps[i]:
+                        deps[i].add(first[b["h"]])
+                    first[b["h"]] = i
+                b["left"] += 1
+    succ = [[] for _ in range(n)]
+    for i in range(n):
+        for d in deps[i]:
+            succ[d].append(i)
+    prio = [0.0] * n
+    for i in range(n - 1, -1, -1):
+        prio[i] = min(a[0] for a in ops[i]["alts"].values()) + LAT + max([prio[s] for s in succ[i]], default=0.0)
+    left = [len(deps[i]) for i in range(n)]
+    ready = [i for i in range(n) if left[i] == 0]
+    dready = [max([READY.get(key, 0.0) for key in ops[i]["r"]], default=0.0) for i in range(n)]
+    efree = {"P": 0.0, "V": 0.0, "A": 0.0, "G": 0.0}
+    bfree, blast = [0.0] * 8, [None] * 8
+    eng, end, order = [None] * n, [0.0] * n, []
+    held = [False] * 4
+    for i in range(n):
+        prio[i] += ops[i]["bias"]
+    while ready:
+        best = None
+        cand = []
+        free = sorted([b for b in range(4) if not held[b]], key=lambda b: bfree[b])
+        for i in ready:
+            o = ops[i]
+            banks = []
+            for b in o["b"]:
+                if isinstance(b, dict):
+                    b = b["bank"] if b["bank"] is not None else (free[0] if free else None)
+                banks.append(b)
+            if None in banks:
+                continue
+            pick = None
+            for e, (cost, _) in o["alts"].items():
+                st = max(efree[e], dready[i])
+                for b in banks:
+                    if blast[b] is not None:
+                        st = max(st, bfree[b] + (LAT if eng[blast[b]] != e else 0.0))
+                val = st + cost + (VPEN if e == "V" else 0.0)
+                if pick is None or val < pick[3]:
+                    pick = (st, e, cost, val)
+            cand.append((pick[0], i, pick[1], pick[2], banks))
+        t0 = min(x[0] for x in cand)
+        for x in cand:
+            if x[0] <= t0 + WIN and (best is None or prio[x[1]] > prio[best[1]]):
+                best = x
+        st, i, e, cost, banks = best
+        ready.remove(i)
+        eng[i], end[i] = e, st + cost
+        efree[e] = end[i]
+        for b0, b in zip(ops[i]["b"], banks):
+            if isinstance(b0, dict):
+                b0["bank"] = b
+                b0["left"] -= 1
+                held[b] = b0["left"] > 0
+            if blast[b] is not None:
+                deps[i].add(blast[b])
+            blast[b], bfree[b] = i, end[i]
+        order.append(i)
+        for s in succ[i]:
+            left[s] -= 1
+            dready[s] = max(dready[s], end[i] + LAT)
+            if left[s] == 0:
+                ready.append(s)
+    return order, eng, deps, end, lastw
+
+
+def rank_program(g, core, T, topo):
+    q = T.rank_of(core)
+    if q is None:
+        return
+    sem = T.sem
+    others = [(q + d) % N for d in (1, 2, 3)]
+    rows = lambda r: slice(32 * r, 32 * r + 32)
+
+    def dst(r):
+        rid, pid, _ = topo.addr(T.cores[r])
+        return DstId(rid=rid, pnc=pid)
+
+    def send(src, land, r, rsem):
+        rid, pid, _ = topo.addr(T.cores[r])
+        g.remote_dma(land, src, rsem, sem.snd, pid, rid, topo.mask(core, T.cores[r]))
+        return len(topo.engines(core, T.cores[r]))
+
+    def fused(src, land, rsem):
+        trs, tot = [], 0
+        for j, r in enumerate(others):
+            en = topo.engines(core, T.cores[r])
+            w = len(en) // 4
+            mk = sum(1 << e for e in en[w * j:w * j + w])
+            trs.append(RemoteDMATransfer(dst_ids=[dst(r)], dma_engine_mask=mk, remote_sem=rsem, src=src[r], dst=land[q]))
+            tot += w
+        g.remote_dma_fused(trs, local_sem=sem.snd)
+        return tot
+
+    def quarter(r):
+        return len(topo.engines(T.cores[r], core)) // 4
+
+    def full(r):
+        return len(topo.engines(T.cores[r], core))
+
+    ops = build_ops(T)
+    order, eng, deps, end, lastw = schedule(ops)
+    Q = {"P": g.tensor, "V": g.vector, "A": g.scalar, "G": g}
+    idx, cnt = {}, {"P": 0, "V": 0, "A": 0, "G": 0}
+    for i in order:
+        cnt[eng[i]] += 1
+        idx[i] = cnt[eng[i]]
+
+    for r in others:
+        g.sync.dma_start(T.sx[r], T.x0[rows(r), :]).then_inc(sem["stx%d" % r], 16)
+    g.scalar.dma_start(T.sk[:, :, :], T.kw[:]).then_inc(sem.stk, 16)
+    g.scalar.dma_start(T.sl[:, :, :], T.l0[:]).then_inc(sem.stk, 16)
+    g.scalar.dma_start(T.sz[:, :, :], T.z0[:]).then_inc(sem.stk, 16)
+    g.scalar.dma_start(T.z[rows(q), :], T.z0[rows(q), :]).then_inc(sem.ink, 16)
+    g.scalar.dma_start(T.Ki[rows(q), :], T.kw[rows(q), :]).then_inc(sem.ink, 16)
+    g.scalar.dma_start(T.Li[2 * q:2 * q + 2, :], T.l0[2 * q:2 * q + 2, :]).then_inc(sem.ink, 16)
+    g.sync.dma_start(T.X[rows(q), 0:W], T.x0[rows(q), :]).then_inc(sem.inx, 16)
+    g.sync.dma_start(T.ss[:, :, :], T.asc[:]).then_inc(sem.sts, 16)
+    g.scalar.dma_start(T.Si[rows(q), :], T.asc[rows(q), :]).then_inc(sem.ins, 16)
+    nin, nink, nins = 16 * N, 48 * N, 16 * N
+
+    known = {e: {"P": 0, "V": 0, "A": 0, "G": 0, "in0": 0, "in1": 0, "in2": 0} for e in Q}
+    clock = {}
+
+    def emit(i):
+        e = eng[i]
+        kn = known[e]
+        need = {}
+        for d in deps[i]:
+            if e == "P" and eng[d] == "P" and not ("fence" in ops[i] and "fence" in ops[d]):
+                continue
+            if idx[d] > kn[eng[d]] and idx[d] > need.get(eng[d], (0, None))[0]:
+                need[eng[d]] = (idx[d], d)
+        for f, (v, d) in sorted(need.items(), key=lambda x: -end[x[1][1]]):
+            if v > kn[f]:
+                Q[e].wait_ge(sem[f], v)
+                kn[f] = v
+                for f2, v2 in clock[d].items():
+                    kn[f2] = max(kn[f2], v2)
+        for key, s, v in (("in0", sem.ink, nink), ("in1", sem.inx, nin), ("in2", sem.ins, nins)):
+            if key in ops[i]["r"] and not kn[key]:
+                Q[e].wait_ge(s, v)
+                kn[key] = 1
+        ops[i]["alts"][e][1](g).then_inc(sem[e], 1)
+        clock[i] = dict(kn)
+
+    gfirst = [i for i in order if eng[i] == "G" and not deps[i]]
+    for i in gfirst:
+        emit(i)
+    sent = 0
+    for j, r in enumerate(others):
+        g.wait_ge(sem["stx%d" % r], 16)
+        sent += send(T.sx[r], T.lx[q], r, sem["ax%d" % q])
+        if j == 1:
+            g.wait_ge(sem.stk, 48)
+            sent += fused(T.sl, T.ll, sem.ak)
+            sent += fused(T.sk, T.lk, sem.ak)
+            sent += fused(T.sz, T.lz, sem.ak)
+    g.wait_ge(sem.sts, 16)
+    sent += fused(T.ss, T.ls, sem.as_)
+    back = [(q - d) % N for d in (1, 2, 3)]
+    g.scalar.wait_ge(sem.ak, 3 * sum(quarter(r2) for r2 in others))
+    for r2 in back:
+        g.scalar.dma_start(T.Ki[rows(r2), :], T.lk[r2]).then_inc(sem.ink, 16)
+        g.scalar.dma_start(T.Li[2 * r2:2 * r2 + 2, :], T.ll[r2]).then_inc(sem.ink, 16)
+        g.scalar.dma_start(T.z[rows(r2), :], T.lz[r2]).then_inc(sem.ink, 16)
+    for j, r in enumerate(back):
+        g.sync.wait_ge(sem["ax%d" % r], full(r))
+        g.sync.dma_start(T.X[rows(r), 0:W], T.lx[r]).then_inc(sem.inx, 16)
+    g.sync.wait_ge(sem.as_, sum(quarter(r) for r in others))
+    for r in back:
+        g.sync.dma_start(T.Si[rows(r), :], T.ls[r]).then_inc(sem.ins, 16)
+
+    for i in order:
+        if i not in gfirst:
+            emit(i)
+
+    def after(queue, keys):
+        need = {}
+        for key in keys:
+            d = lastw[key]
+            need[eng[d]] = max(need.get(eng[d], 0), idx[d])
+        for f, v in need.items():
+            queue.wait_ge(sem[f], v)
+
+    SA = slice(W, W + A)
+    after(g.sync, ["X"])
+    for r in others:
+        g.sync.dma_start(T.ox[r], T.X[rows(r), 0:W]).then_inc(sem["ox%d" % r], 16)
+    after(g.sync, ["S"])
+    g.sync.dma_start(T.oa[:, :, :], T.S[:, SA]).then_inc(sem.oa, 16)
+    g.sync.dma_start(T.yx[rows(q), :], T.X[rows(q), 0:W]).then_inc(sem.fin, 16)
+    g.sync.dma_start(T.ya[rows(q), :], T.S[rows(q), SA]).then_inc(sem.fin, 16)
+    after(g.scalar, ["Kf0", "Kf1", "Lo0", "Lo1", "z0", "z1"])
+    g.scalar.dma_start(T.ok[:, :, :], T.Kf[:, :]).then_inc(sem.ok, 16)
+    g.scalar.dma_start(T.ol[:, :, :], T.Lo[0:8, :]).then_inc(sem.ok, 16)
+    g.scalar.dma_start(T.oz[:, :, :], T.z[:, :]).then_inc(sem.ok, 16)
+    g.scalar.dma_start(T.yz[rows(q), :], T.z[rows(q), :]).then_inc(sem.fin2, 16)
+    g.scalar.dma_start(T.yk[rows(q), :], T.Kf[rows(q), :]).then_inc(sem.fin2, 16)
+    g.scalar.dma_start(T.yl[2 * q:2 * q + 2, :], T.Lo[2 * q:2 * q + 2, :]).then_inc(sem.fin2, 16)
+    for r in others:
+        g.wait_ge(sem["ox%d" % r], 16)
+        sent += send(T.ox[r], T.mx[q], r, sem["bx%d" % q])
+    g.wait_ge(sem.oa, 16)
+    sent += fused(T.oa, T.ma, sem.ba)
+    g.wait_ge(sem.ok, 48)
+    sent += fused(T.ok, T.mk, sem.bk)
+    sent += fused(T.oz, T.mz, sem.bk)
+    sent += fused(T.ol, T.ml, sem.bk)
+    for r in back:
+        g.sync.wait_ge(sem["bx%d" % r], full(r))
+        g.sync.dma_start(T.yx[rows(r), :], T.mx[r]).then_inc(sem.fin, 16)
+    g.scalar.wait_ge(sem.ba, sum(quarter(r) for r in others))
+    for r in back:
+        g.scalar.dma_start(T.ya[rows(r), :], T.ma[r]).then_inc(sem.fin2, 16)
+    g.sync.wait_ge(sem.bk, 3 * sum(quarter(r) for r in others))
+    g.scalar.wait_ge(sem.bk, 3 * sum(quarter(r) for r in others))
+    for j, r in enumerate(back):
+        g.sync.dma_start(T.yk[rows(r), :], T.mk[r]).then_inc(sem.fin, 16)
+        g.scalar.dma_start(T.yz[rows(r), :], T.mz[r]).then_inc(sem.fin2, 16)
+        if j % 2:
+            g.scalar.dma_start(T.yl[2 * r:2 * r + 2, :], T.ml[r]).then_inc(sem.fin2, 16)
+        else:
+            g.sync.dma_start(T.yl[2 * r:2 * r + 2, :], T.ml[r]).then_inc(sem.fin, 16)
+    g.sync.wait_ge(sem.fin, 32 + 32 * (N - 1) + 32)
+    g.scalar.wait_ge(sem.fin2, 48 + 32 * (N - 1) + 16)
+    g.wait_ge(sem.snd, sent)
+    for f in Q:
+        g.wait_ge(sem[f], cnt[f])

@@ -1,12 +1,18 @@
+import numpy as np
 from concourse.bass import DstId, RemoteDMATransfer
 from concourse.mybir import AluOpType as OP, AxisListType, ActivationFunctionType as AF
 
 N, W, A, TL, RO, EPS, TH = 4, 4096, 1024, 256, 4, 48, 720
 WX = 5248
 NRING = 5
-BIAS = [8000, -3000, 12000, 3000, 1000, 3000, 1000, 2000, 0, 2000, 2000, 8000]
-NV = [2, 2]
-WIN, VPEN = 40.0, 150.0
+BIAS = [8000, -3000, 12000, 8000, -1000, 3000, 3000, 2000, 0, 3000, 1000, 8000, 4000, 5000, 0]
+NV = [3, 4]
+NE = [0, 1]
+STEPS = 2200
+WIN, VPEN = 40.0, 300.0
+NUDGE = {}
+LEAN = {}
+GAM, SCA = 1.5, 3.8
 
 SCRATCH = {
     "X": ("sbuf", [128, WX], "bfloat16"), "S": ("sbuf", [128, WX], "float32"),
@@ -14,8 +20,9 @@ SCRATCH = {
     "Lb": ("sbuf", [128, TL], "bfloat16"), "Lo": ("sbuf", [128, TL], "float32"),
     "Ku": ("sbuf", [128, TL], "uint16"), "Kf": ("sbuf", [128, TL], "float32"),
     "z": ("sbuf", [128, TL], "bfloat16"), "Lh": ("sbuf", [128, TL], "bfloat16"),
+    "OX": ("sbuf", [128, W], "bfloat16"), "OS": ("sbuf", [128, A], "float32"),
     "at": ("sbuf", [128, 32], "float32"), "ai": ("sbuf", [128, 16], "int32"),
-    "CB": ("sbuf", [128, 5632], "bfloat16"), "CF": ("sbuf", [128, 2560], "float32"),
+    "CB": ("sbuf", [128, 6144], "bfloat16"), "CF": ("sbuf", [128, 2560], "float32"),
     "CI": ("sbuf", [128, 16], "int32"), "TF": ("sbuf", [128, 1680], "float32"),
     "sx": ("dram", [4, 128, 1024], "bfloat16"), "lx": ("dram", [4, 128, 1024], "bfloat16"), "mx": ("dram", [4, 128, 1024], "bfloat16"),
     "sz": ("dram", [4, 128, 64], "bfloat16"), "lz": ("dram", [4, 128, 64], "bfloat16"), "mz": ("dram", [4, 128, 64], "bfloat16"),
@@ -30,8 +37,9 @@ SCRATCH = {
 for _h in range(2):
     SCRATCH.update({
         "xg%d" % _h: ("sbuf", [128, 2048], "bfloat16"), "yg%d" % _h: ("sbuf", [128, 4096], "bfloat16"),
+        "ov%d" % _h: ("sbuf", [128, 2048], "bfloat16"),
         "ur%d" % _h: ("sbuf", [128, 512 * NRING], "bfloat16"), "vr%d" % _h: ("sbuf", [128, 512 * NRING], "bfloat16"),
-        "wb%d" % _h: ("sbuf", [128, 4608], "bfloat16"), "wf%d" % _h: ("sbuf", [128, 3200], "float32"),
+        "wb%d" % _h: ("sbuf", [128, 4864], "bfloat16"), "wf%d" % _h: ("sbuf", [128, 3200], "float32"),
         "wi%d" % _h: ("sbuf", [128, 1024], "int32"), "wu%d" % _h: ("sbuf", [128, 320], "uint16"),
     })
 for _b in range(8):
@@ -40,18 +48,19 @@ for _b in range(8):
 SEMAPHORES = ["P", "V", "A", "G", "stx0", "stx1", "stx2", "stx3", "stk", "sts", "snd",
               "ax0", "ax1", "ax2", "ax3", "ak", "as_", "inx", "ink", "ins",
               "ox0", "ox1", "ox2", "ox3", "oa", "ok",
-              "bx0", "bx1", "bx2", "bx3", "ba", "bk", "fin", "fin2"]
+              "bx0", "bx1", "bx2", "bx3", "ba0", "ba1", "ba2", "ba3", "bk", "fin", "fin2"]
 
 CYC, PCYC, LAT, FIX = 0.83, 0.42, 60.0, 55.0
 
 
-def build_ops(T):
+def build_ops(T, others=(1, 2, 3)):
     ops = []
 
     def add(alts, reads, writes, banks=()):
-        ops.append({"alts": alts, "r": list(reads), "w": list(writes), "b": list(banks), "bias": bias[0]})
+        ops.append({"alts": alts, "r": list(reads), "w": list(writes), "b": list(banks), "bias": bias[0],
+                    "pos": len(ops) - base[0] if base[0] >= 0 else -1})
 
-    bias = [0.0]
+    bias, base = [0.0], [-1]
 
     def vc(n, rate=1.0):
         return FIX + max(64, n * rate) * CYC
@@ -127,12 +136,12 @@ def build_ops(T):
         return t[p0:p1, o + a:o + (n if b is None else b)]
 
     for nm, n in (("II", 256), ("nII", 256), ("I22", 128), ("ONES", 128), ("B8", 8), ("Wd", 8), ("Ww", 8), ("W32", 16),
-                  ("CH", 256), ("CR", 256), ("MM16", 128), ("WV", 128), ("W4", 128), ("W21h", 256), ("W21l", 256),
+                  ("CH", 256), ("CR", 256), ("MM16", 128), ("WV", 128), ("W4", 256), ("TK", 128), ("KX0", 128), ("KX1", 128), ("TRT", 512), ("W21h", 256), ("W21l", 256),
                   ("MK", 256), ("MKp", 128), ("WV8", 8), ("EX0", 256), ("MKt", 128), ("W32n", 8), ("W64", 8), ("TRI", 512),
                   ("Z8", 240), ("Zw", 144), ("THN", 128), ("LS", 128), ("LW", 8), ("EXb", 128)):
         alloc("CB", nm, n)
     for nm, n in (("IIf", 256), ("I20", 128), ("B8f", 16), ("BBf", 256), ("MM", 256), ("hold", 256), ("holdr", 256),
-                  ("TR", 128), ("KX0", 128), ("KX1", 128), ("EXf", 128), ("col", 32)):
+                  ("TR", 128), ("col", 32)):
         alloc("CF", nm, n)
     for nm, n in (("t0", 256), ("t1", 256), ("t2", 256), ("t3", 256), ("t4", 256), ("t5", 256), ("t6", 144)):
         alloc("TF", nm, n)
@@ -199,7 +208,7 @@ def build_ops(T):
     cts("w4", "w", 4.0, None, OP.mult, None)
     cts("w21", "w", 21.0, None, OP.mult, None)
     eq("WV", "t1", "pb", "w", 128)
-    eq("W4", "t1", "pb", "w4", 128)
+    eq("W4", "t1", "pb", "w4", 256)
     eq("WV8", "t3", "pb", "w", 8)
     eq("W21h", "t1", "pb", "w21", 256)
     ts(c("t5"), c("BBf"), col("w21"), None, OP.mult, None, 256, ["BBf", "c.w21"], ["t5"])
@@ -214,13 +223,13 @@ def build_ops(T):
     ts(c("CR"), c("t2"), col("b0"), col("b1"), OP.mult, OP.add, 256, ["t2", "c.b0", "c.b1"], ["CR"])
     ts(CI[:, 3:4], CI[:, 0:1], 7, None, OP.bitwise_and, None, 1, ["ci0"], ["ci3"])
     cp(col("b2"), CI[:, 3:4], 1, ["ci3"], ["c.b2"])
-    cts("b0", "p", 8.0, 128.0, OP.is_ge, OP.mult)
+    cts("b0", "p", 8.0, 128.0, OP.is_lt, OP.mult)
     cts("b1", "b0", 128.0, None, OP.add, None)
     eq("EX0", "t1", "b2", "b1", 256)
-    eq("EXf", "t1", "p", None, 128)
     eq("EXb", "t1", "p", None, 128)
     for q in range(2):
         ts(c("TRI", 256 * q, 256 * q + 256), c("t0"), col("p"), -64.0, OP.is_ge, OP.mult, 256, ["t0", "c.p"], ["TRI"])
+    ts(c("TRT"), c("TRI"), -1.0, 15.5, OP.mult, OP.add, 512, ["TRI"], ["TRT"], rate=0.5)
     mset(c("Z8"), 0.0, 240, ["Z8"])
     mset(c("Z8", 112, 128), 8192.0, 16, ["Z8"])
     iota(c("t6", 0, 144), [[1, 144]], -16, 0, 144, ["t6"])
@@ -237,7 +246,11 @@ def build_ops(T):
     eq("LW", "t3", "pb", "pm", 8)
     cts("n1024", "p", -1.0, -1024.0, OP.mult, OP.add)
     cts("n5120", "p", -1.0, -5120.0, OP.mult, OP.add)
-    cts("trash", "p", 5120.5, None, OP.add, None)
+    cts("b0", "p", 0.0, None, OP.is_equal, None)
+    cts("b1", "p", 1.0, 5120.0, OP.is_equal, OP.mult)
+    cts("b2", "p", 2.0, 0.5, OP.is_equal, OP.mult)
+    tt(col("trash"), col("b1"), col("b2"), OP.add, 1, ["c.b1", "c.b2"], ["c.trash"])
+    ts(c("TK"), c("t0", 0, 128), col("b0"), col("trash"), OP.mult, OP.add, 128, ["t0", "c.b0", "c.trash"], ["TK"])
     ts(c("t5", 0, 128), c("t0", 0, 128), col("pm"), 5120.0, OP.add, OP.add, 128, ["t0", "c.pm"], ["t5"])
     ts(c("TR"), c("hold", 0, 128), -1.0, 1.0, OP.mult, OP.add, 128, ["hold"], ["TR"])
     tt(c("TR"), c("TR"), c("t5", 0, 128), OP.mult, 128, ["TR", "t5"], ["TR"])
@@ -254,15 +267,15 @@ def build_ops(T):
     mset(at[:, 8:16], 16.0, 8, ["athr"])
 
     def zwin(h, rnd, j, n=1):
-        o = 3072 + 384 * (rnd % 2) + 128 * j
+        o = 3072 + 384 * (rnd % 2) + 128 * (3 - n - j)
         return T["wb%d" % h][:, o:o + 128 * n]
 
     def lwin(h, rnd, j, n=1):
-        o = 3840 + 384 * (rnd % 2) + 128 * j
+        o = 3840 + 384 * (rnd % 2) + 128 * (3 - n - j)
         return T["wb%d" % h][:, o:o + 128 * n]
 
     def kwin(h, rnd, j, n=1):
-        o = 2432 + 384 * (rnd % 2) + 128 * j
+        o = 2432 + 384 * (rnd % 2) + 128 * (3 - n - j)
         return T["wf%d" % h][:, o:o + 128 * n]
 
     def skeys(h, rnd):
@@ -305,7 +318,8 @@ def build_ops(T):
         return r
 
     def gather(out, win, off, n, reads, writes, flex=True):
-        cp(out, win.indirect(off), n, reads, writes, rate=1.5, flex=flex)
+        cp(out, win.indirect(off), n, reads, writes, rate=GAM, flex=flex)
+        ops[-1]["ng"] = n * CYC
 
     def perm(h, out, wide, src, back, f):
         mms = []
@@ -356,25 +370,27 @@ def build_ops(T):
         cp(wi[:, 0:8], m[:, 0:8], 8, [k("m0")], [k("i0")], mb)
         ts(wi[:, 8:16], wi[:, 0:8], 2047, None, OP.bitwise_and, None, 8, [k("i0")], [k("i1")])
         cp(wu[:, 0:8], wi[:, 8:16], 8, [k("i1")], [k("ou")])
-        tt(wb[:, 128:256], xg[:, 0:2048].indirect(wu[:, 0:8]), zc, OP.subtract, 128, [k("xg0"), k("xg1"), k("ou"), zk], [k("as")], rate=1.5)
+        tt(wb[:, 128:256], xg[:, 0:2048].indirect(wu[:, 0:8]), zc, OP.subtract, 128, [k("xg0"), k("xg1"), k("ou"), zk], [k("as")], rate=GAM)
         act(wb[:, 256:384], wb[:, 128:256], AF.Abs, 128, [k("as")], [k("D")])
-        z0 = 3072 + 384 * (rnd % 2)
-        pe(perm(h, lambda o: m[:, o:128:3], lambda s: c("II", s, s + 128), lambda o: wb[:, z0 + o:z0 + 128:3], False, 0)
-           + perm(h, lambda o: m[:, 128 + o:256:3], lambda s: c("II", s, s + 128), lambda o: wb[:, 256 + o:384:3], False, 0),
-           ["II", zk, k("D")], [k("m0"), k("m1")], mb)
-        cp(wb[:, 384:640], m[:, 0:256], 256, [k("m0"), k("m1")], [k("zD")], mb, flex=True)
+        z0 = 3072 + 384 * (rnd % 2) + 256
+        mms = [(m[:, 0:256], c("II", 0, 128), c("MK"), True, False, 256, 128, 0)]
+        for wt, o0, sh in (("W4", 0, 0), ("W21h", 128, 96), ("W21l", 128, 96)):
+            for mm in perm(h, lambda o: m[:, o0 + o:o0 + 128:3], lambda s: c(wt, (s + sh) % 128, (s + sh) % 128 + 128),
+                           lambda o: wb[:, 256 + o:384:3], False, 0):
+                mms.append(mm[:3] + (False, len(mms) == 9) + mm[5:])
+        pe(mms, ["II", "MK", "W4", "W21h", "W21l", k("D")], [k("m0"), k("m1")], mb)
+        pe(perm(h, lambda o: acc[:, 256 + o:384:3], lambda s: c("II", s, s + 128), lambda o: wb[:, z0 + o:z0 + 128:3], False, 0)
+           + perm(h, lambda o: acc[:, 384 + o:512:3], lambda s: c("II", s, s + 128), lambda o: wb[:, 256 + o:384:3], False, 0),
+           ["II", zk, k("D")], [k("acc")], ab)
+        cp(wb[:, 384:640], acc[:, 256:512], 256, [k("acc")], [k("zD")], ab, flex=True)
         DB = wb[:, 512:640]
-        pe([(m[:, 0:256], c("II", 0, 128), c("MK"), True, False, 256, 128, 0),
-            (m[:, 0:128], c("W4"), DB, False, False, 128, 128, 0),
-            (m[:, 128:256], c("W21h", 96, 224), DB, False, False, 128, 128, 0),
-            (m[:, 128:256], c("W21l", 96, 224), DB, False, True, 128, 128, 0)],
-           ["II", "MK", "W4", "W21h", "W21l", k("zD")], [k("m0"), k("m1")], mb)
-        scan(wf[:, 640:896], c("hold"), m[:, 0:256], OP.mult, OP.max, 256, [k("m0"), k("m1"), "hold"], [k("sc")], mb)
-        cp(wi[:, 16:32], wf[:, 655:896:16], 16, [k("sc")], [k("i2")])
-        ts(wi[:, 32:48], wi[:, 16:32], 2, 1023, OP.arith_shift_right, OP.bitwise_and, 16, [k("i2")], [k("i3")])
+        scan(wi[:, 640:896], c("hold"), m[:, 0:256], OP.mult, OP.max, 256, [k("m0"), k("m1"), "hold"], [k("r1")], mb)
+        ts(wi[:, 32:48], wi[:, 655:896:16], 2, 1023, OP.arith_shift_right, OP.bitwise_and, 16, [k("r1")], [k("i3")])
         cp(wu[:, 8:24], wi[:, 32:48], 16, [k("i3")], [k("cu")])
         gather(wu[:, 64:320], S[:, W:W + A], wu[:, 8:24], 256, ["S", k("cu")], [k("Pu")], flex=False)
-        gather(wf[:, 896:1152], S[:, W:W + A], wu[:, 8:24], 256, ["S", k("cu")], [k("Pf")])
+        gather(wf[:, 896:1152], S[:, W:W + A], wu[:, 8:24], 256, ["S", k("cu"), k("Pu")], [k("Pf")])
+        ops[-1]["alts"]["V"] = (vc(256), lambda g: g.vector.tensor_copy(wf[:, 896:1152], wu[:, 64:320]))
+        ops[-1]["ng"] = 0.0
         pe([(m[:, 256:264], DB, c("WV8"), True, True, 8, 128, 0),
             (m[:, 384:512], c("WV"), wb[:, 256:384], True, False, 128, 128, 0),
             (m[:, 384:512], c("I20"), kwin(h, rnd, 1), False, True, 128, 128, 1)],
@@ -391,9 +407,9 @@ def build_ops(T):
            ["IIf", k("Pf")], [k("m3")], mb)
         tt(wf[:, 1664:1792], m[:, 384:512], kwin(h, rnd, 1), OP.subtract, 128, [k("m3"), kk_], [k("d2")], mb)
         if NV[h]:
-            cp(wb[:, 1536:1664], DB, 128, [k("zD")], [k("D4")], rate=0.5)
-            cp(wb[:, 1664:1792], DB, 128, [k("zD")], [k("D4")], rate=0.5)
-            cp(wb[:, 1792:2048], wb[:, 1536:1792], 256, [k("D4")], [k("D4")], rate=0.5)
+            cp(wb[:, 1536:1664], DB, 128, [k("zD")], [k("D4")], rate=0.5, flex=True)
+            cp(wb[:, 1664:1792], DB, 128, [k("zD")], [k("D4")], rate=0.5, flex=True)
+            cp(wb[:, 1792:2048], wb[:, 1536:1792], 256, [k("D4")], [k("D4")], rate=0.5, flex=True)
 
     def stage_c(h, rnd):
         bias[0] = BIAS[2] * (1 - h)
@@ -406,8 +422,41 @@ def build_ops(T):
         zB, DB = wb[:, 384:512], wb[:, 512:640]
         for q in range(4):
             gather(yg[:, 1024 * q:1024 * q + 1024], X[:, 0:W], wu[:, 64 + 64 * q:128 + 64 * q], 1024, ["X", k("Pu")], [k("yg%d" % q)])
-        pe([(acc[:, 0:256], c("ONES"), c("CR"), True, False, 256, 128, 0)], ["ONES", "CR"], [k("acc")], ab)
+        I = c("II", 0, 128)
+        ho = C["holdr"][1]
+
+        def best(role):
+            a, n = 128 * role, "BC"[role]
+            scan(wf[:, a:a + 128], c("hold", 0, 128), acc[:, a:a + 128], OP.mult, OP.min, 128, [k("acc"), "hold"], [k("s1" + n[:role])], ab)
+            src = wf[:, 127::-1] if role == 0 else wf[:, 255:127:-1]
+            scan(wf[:, 383 + a:255 + a:-1], T.CF[:, ho + 127:ho - 1:-1], src, OP.mult, OP.min, 128, [k("s1" + n[:role]), "holdr"], [k("s2" + n)])
+            tt(wb[:, 640 + a:768 + a], acc[:, a:a + 128], wf[:, 256 + a:384 + a], OP.is_equal, 128, [k("acc"), k("s2" + n)], [k("oh" + n)], ab)
+
+        def partner():
+            best(0)
+            pe([(m[:, 0:128], wb[:, 640:768], I, True, True, 128, 128, 0)], ["II", k("ohB")], [k("m0")], mb)
+            tt(wf[:, 1792:1920], m[:, 0:128], wf[:, 896:1024], OP.mult, 128, [k("m0"), k("Pf")], [k("pay")], mb)
+            pe([(m[:, 256:384], I, c("MK", 0, 128), True, False, 128, 128, 0),
+                (m[:, 256:384], c("BBf", 0, 128), wf[:, 1792:1920], False, True, 128, 128, 1),
+                (m[:, 128:136], wf[:, 1792:1920], c("B8f", 0, 8), True, True, 8, 128, 1)], ["II", "MK", "BBf", "B8f", k("pay")], [k("m1"), k("m2")], mb)
+            scan(wf[:, 640:768], c("hold", 0, 128), m[:, 256:384], OP.mult, OP.max, 128, [k("m2"), "hold"], [k("sc")], mb)
+            cp(wu[:, 24:32], wf[:, 655:768:16], 8, [k("sc")], [k("ju")])
+            gather(wb[:, 896:1024], X[:, 0:W], wu[:, 24:32], 128, ["X", k("ju")], [k("yj")])
+            ts(wf[:, 1160:1168], m[:, 128:136], col("n5120"), None, OP.add, None, 8, [k("m1"), "c.n5120"], [k("kw")], mb,
+               act=(AF.Identity, col("n5120"), 1.0))
+            pe(perm(h, lambda o: m[:, 256 + o:384:3], lambda s: c("II", s, s + 128), lambda o: wb[:, 896 + o:1024:3], True, 0)
+               + [(m[:, 384:512], I, wb[:, 896:1024], True, False, 128, 128, 0), (m[:, 384:512], I, DB, False, True, 128, 128, 0)],
+               ["II", k("yj"), k("zD")], [k("m2"), k("m3")], mb)
+            cp(zwin(h, rnd, 2), m[:, 256:384], 128, [k("m2")], [k("yh")], mb, flex=True)
+            ts(wi[:, 512:640], m[:, 384:512], 0.5, -0.25, OP.mult, OP.add, 128, [k("m3")], [k("nw")], mb)
+            ts(wb[:, 1184:1192], wf[:, 15:128:16], float(32 * TH - 262144), None, OP.is_ge, None, 8, [k("s1")], [k("ge")])
+
         for role in range(2):
+            if role == 1:
+                bias[0] = BIAS[12] * (1 - h) + BIAS[13]
+                partner()
+                bias[0] = BIAS[2] * (1 - h)
+            pe([(acc[:, 128 * role:128 * role + 128], c("ONES"), c("CR", 0, 128), True, False, 128, 128, 0)], ["ONES", "CR"], [k("acc")], ab)
             lz = c("nII", 96 * role, 96 * role + 128)
             for ch in range(4):
                 s, sl = sub_chunk(h, yg, [k("yg%d" % (2 * role)), k("yg%d" % (2 * role + 1))], 2048 * role, ch, lz, zB, [k("zD")])
@@ -416,13 +465,13 @@ def build_ops(T):
                 if role == 0 and ch >= 4 - NV[h]:
                     act(sap(s), sap(s), AF.Abs, 512, [sl], [sl], [s])
                     tt(u, sap(s), wb[:, 1536:2048], OP.subtract, 512, [sl, k("D4")], [k("u%d" % r)], [s])
-                    ts(v, u, 0.0, None, OP.max, None, 512, [k("u%d" % r)], [k("v%d" % r)], rate=0.5)
+                    ts(v, u, 0.0, None, OP.max, None, 512, [k("u%d" % r)], [k("v%d" % r)], rate=0.5, act=(AF.Relu, 0.0, 1.0))
                     mv = []
                     for kk in range(4):
                         kq = 4 * ch + kk
                         for buf, wt in (("ur", "W32n"), ("vr", "W64")):
                             mv.append((acc[:, kq:128:16], T["%s%d" % (buf, h)][:, 512 * r + 128 * kk:512 * r + 128 * kk + 128],
-                                       c(wt), False, False, 8, 128, 0))
+                                       c(wt), False, kq == 15 and buf == "vr", 8, 128, 0))
                     pe(mv, [k("u%d" % r), k("v%d" % r), "W32n", "W64", k("acc")], [k("acc")], ab)
                     continue
                 act(u, sap(s), AF.Abs, 512, [sl], [k("u%d" % r)], [s])
@@ -435,46 +484,24 @@ def build_ops(T):
                 for kk in range(4):
                     kq = 4 * ch + kk
                     mv.append((acc[:, 128 * role + kq:128 * role + 128:16], T["vr%d" % h][:, 512 * r + 128 * kk:512 * r + 128 * kk + 128],
-                               c("W32", 2 * role, 2 * role + 8), False, role == 1 and kq == 15, 8, 128, 0))
+                               c("W32", 2 * role, 2 * role + 8), False, kq == 15, 8, 128, 0))
                 pe(mv, [k("v%d" % r), "W32", k("acc")], [k("acc")], ab)
         bias[0] = BIAS[3] * (1 - h) + BIAS[10]
-        scan(wf[:, 0:256], c("hold"), acc[:, 0:256], OP.mult, OP.min, 256, [k("acc"), "hold"], [k("s1")], ab)
-        o = C["holdr"][1]
-        scan(wf[:, 511:255:-1], T.CF[:, o + 255:o - 1:-1], wf[:, 255::-1], OP.mult, OP.min, 256, [k("s1"), "holdr"], [k("s2")])
-        tt(wb[:, 640:896], acc[:, 0:256], wf[:, 256:512], OP.is_equal, 256, [k("acc"), k("s2")], [k("oh")], ab)
-        I = c("II", 0, 128)
-        pe([(m[:, 0:128], wb[:, 640:768], I, True, True, 128, 128, 0),
-            (m[32:64, 128:256], wb[:, 768:800], I, True, True, 128, 32, 0),
-            (m[64:128, 128:256], wb[:, 800:864], I, True, True, 128, 64, 0),
-            (m[0:32, 128:256], wb[:, 864:896], I, True, True, 128, 32, 0)], ["II", k("oh")], [k("m0"), k("m1")], mb)
-        tt(wf[:, 1792:2048], m[:, 0:256], wf[:, 896:1152], OP.mult, 256, [k("m0"), k("m1"), k("Pf")], [k("pay")], mb)
-        pe([(m[:, 256:384], I, c("MK", 0, 128), True, False, 128, 128, 0),
-            (m[:, 256:384], c("BBf", 0, 128), wf[:, 1792:1920], False, True, 128, 128, 1)], ["II", "MK", "BBf", k("pay")], [k("m2")], mb)
-        scan(wf[:, 640:768], c("hold", 0, 128), m[:, 256:384], OP.mult, OP.max, 128, [k("m2"), "hold"], [k("sc")], mb)
-        cp(wu[:, 24:32], wf[:, 655:768:16], 8, [k("sc")], [k("ju")])
-        gather(wb[:, 896:1024], X[:, 0:W], wu[:, 24:32], 128, ["X", k("ju")], [k("yj")])
-        pe([(m[:, 128:136], wf[:, 1792:1920], c("B8f", 0, 8), True, True, 8, 128, 1),
-            (m[:, 384:512], c("BBf", 32, 160), wf[:, 1920:2048], True, True, 128, 128, 1)], ["B8f", "BBf", k("pay")], [k("m1"), k("m3")], mb)
-        ts(wf[:, 1160:1168], m[:, 128:136], col("n5120"), None, OP.add, None, 8, [k("m1"), "c.n5120"], [k("kw")], mb)
+        tt(wf[:, 1168:1176], wf[:, 15:128:16], at[:, 8:16], OP.add, 8, [k("s1"), "athr"], [k("dt")])
+        best(1)
+        tt(wb[:, 1152:1160], wf[:, 143:256:16], wf[:, 1168:1176], OP.is_le, 8, [k("dt"), k("s1C")], [k("hit")])
+        bias[0] = BIAS[14]
+        pe([(m[32:64, 384:512], wb[:, 768:800], I, True, True, 128, 32, 0),
+            (m[64:128, 384:512], wb[:, 800:864], I, True, True, 128, 64, 0),
+            (m[0:32, 384:512], wb[:, 864:896], I, True, True, 128, 32, 0)], ["II", k("ohC")], [k("m3")], mb)
+        tt(wf[:, 1920:2048], m[:, 384:512], wf[:, 1024:1152], OP.mult, 128, [k("m3"), k("Pf")], [k("payC")], mb)
+        pe([(m[:, 384:512], c("BBf", 32, 160), wf[:, 1920:2048], True, True, 128, 128, 1)], ["BBf", k("payC")], [k("m3")], mb)
         tt(wf[:, 2048:2176], m[:, 384:512], wf[:, 896:1024], OP.subtract, 128, [k("m3"), k("Pf")], [k("c1")], mb)
         tt(wf[:, 2176:2304], m[:, 0:128], wf[:, 2048:2176], OP.mult, 128, [k("m0"), k("c1")], [k("c2")], mb)
-        pe(perm(h, lambda o: m[:, 256 + o:384:3], lambda s: c("II", s, s + 128), lambda o: wb[:, 896 + o:1024:3], True, 0),
-           ["II", k("yj")], [k("m2")], mb)
-        cp(zwin(h, rnd, 2), m[:, 256:384], 128, [k("m2")], [k("yh")], mb, flex=True)
-        pe([(m[:, 384:512], I, wb[:, 896:1024], True, False, 128, 128, 0),
-            (m[:, 384:512], I, DB, False, True, 128, 128, 0)], ["II", k("yj"), k("zD")], [k("m3")], mb)
-        ts(wi[:, 512:640], m[:, 384:512], 0.5, -0.25, OP.mult, OP.add, 128, [k("m3")], [k("nw")], mb)
-        ME, MF = wf[:, 15:128:16], wf[:, 143:256:16]
-        thr = float(32 * TH - 262144)
-        tt(wf[:, 1168:1176], MF, ME, OP.subtract, 8, [k("s1")], [k("dt")])
-        tt(wb[:, 1152:1160], wf[:, 1168:1176], at[:, 8:16], OP.is_le, 8, [k("dt"), "athr"], [k("hit")])
-        ts(wb[:, 1184:1192], ME, thr, None, OP.is_ge, None, 8, [k("s1")], [k("ge")])
-        ts(wb[:, 1192:1200], ME, thr, None, OP.is_lt, None, 8, [k("s1")], [k("lt")])
+        bias[0] = BIAS[3] * (1 - h) + BIAS[10]
         tt(wb[:, 1160:1168], wb[:, 1184:1192], wb[:, 1152:1160], OP.is_gt, 8, [k("ge"), k("hit")], [k("nei")])
-        tt(wb[:, 1168:1176], wb[:, 1192:1200], wb[:, 1152:1160], OP.is_gt, 8, [k("lt"), k("hit")], [k("con")])
         tt(wf[:, 1176:1192], wb[:, 1152:1168], wf[:, 1152:1168], OP.mult, 16, [k("hit"), k("nei"), k("kc"), k("kw")], [k("km")])
-        tt(wf[:, 1192:1200], wf[:, 1176:1184], wf[:, 1184:1192], OP.add, 8, [k("km")], [k("ks")])
-        ts(wf[:, 1200:1208], wf[:, 1192:1200], col("trash"), None, OP.add, None, 8, [k("ks"), "c.trash"], [k("key")])
+        tt(wf[:, 1200:1208], wf[:, 1176:1184], wf[:, 1184:1192], OP.add, 8, [k("km")], [k("key")])
 
     def stage_e(h, rnd):
         last = rnd == RO - 1
@@ -487,66 +514,70 @@ def build_ops(T):
         ab, mb = [4 + h], [6 + h]
         L = slice(128 * h, 128 * h + 128)
         I = c("II", 0, 128)
-        pe([(m[0:8, 128:256], wf[:, 1200:1208], c("IIf", 0, 128), True, True, 128, 8, 1)], ["IIf", k("key")], [k("m1")], mb)
-        cp(wf[0:8, 2304:2432], m[0:8, 128:256], 128, [k("m1")], [k("Rf")], mb, flex=True)
+        pe([(m[0:8, 128:256], c("ONES", 0, 8), c("TK"), True, False, 128, 8, 0),
+            (m[0:8, 128:256], wf[:, 1200:1208], c("IIf", 0, 128), False, True, 128, 8, 1)], ["IIf", "ONES", "TK", k("key")], [k("m1")], mb)
+        Rh, Rl = wb[0:8, 4608:4736], wb[0:8, 4736:4864]
+        cp(Rh, m[0:8, 128:256], 128, [k("m1")], [k("Rf")], mb, flex=True)
+        tt(Rl, m[0:8, 128:256], Rh, OP.subtract, 128, [k("m1"), k("Rf")], [k("Rl")], mb)
         s = session(2 + h)
         sl = "sl%d" % s["id"]
-        pe([(sap(s, 128 * q, 128 * q + 128), c("KX%d" % q, 0, 128, 0, 8), wf[0:8, 2304:2432], True, True, 128, 128, 1) for q in range(2)],
-           ["KX0", "KX1", k("Rf")], [sl], [s])
+        pe([(sap(s, 128 * q, 128 * q + 128), c("KX%d" % q, 0, 128, 0, 8), (Rh, Rl)[j], j == 0, j == 1, 128, 128, 0) for q in range(2) for j in range(2)],
+           ["KX0", "KX1", k("Rf"), k("Rl")], [sl], [s])
         cp(wi[:, 640:896], sap(s, 0, 256), 256, [sl], [k("r1")], [s])
         tt(wb[:, 1280:1536], wi[:, 640:896], sap(s, 0, 256), OP.is_gt, 256, [sl, k("r1")], [k("bits")], [s])
         for q in range(2):
             s = session(2 + h)
             sl = "sl%d" % s["id"]
-            mms = [(sap(s), I, c("TRI"), True, False, 512, 128, 0)]
+            onv = q < NE[h]
+            mms = [] if onv else [(sap(s), I, c("TRI"), True, False, 512, 128, 0)]
             for a in range(4):
                 bt = wb[32 * a:32 * a + 32, 1280 + 128 * q:1408 + 128 * q]
-                mms.append((sap(s, 128 * a, 128 * a + 128), bt, bt, False, a == 3, 128, 128, 0))
+                mms.append((sap(s, 128 * a, 128 * a + 128), bt, bt, onv, onv or a == 3, 128, 128, 0))
                 pe(mms, ["II", "TRI", k("bits"), sl], [sl], [s])
                 ops[-1]["fence"] = 1
                 mms = []
-            ts(wb[:, 2048 + 512 * q:2560 + 512 * q], sap(s), -15.0, 0.0, OP.add, OP.max, 512, [sl], [k("e%d" % q)], [s],
-               act=(AF.Relu, -15.0, 1.0))
+            if onv:
+                tt(wb[:, 2048 + 512 * q:2560 + 512 * q], sap(s), c("TRT"), OP.is_gt, 512, [sl, "TRT"], [k("e%d" % q)], [s])
+            else:
+                ts(wb[:, 2048 + 512 * q:2560 + 512 * q], sap(s), -15.0, 0.0, OP.add, OP.max, 512, [sl], [k("e%d" % q)], [s],
+                   act=(AF.Relu, -15.0, 1.0))
         mms = [(m[:, 128:256], I, c("MKp"), True, False, 128, 128, 0),
-               (m[:, 128:256], c("EXf", 0, 128, 0, 8), wf[0:8, 2304:2432], False, False, 128, 128, 1)]
+               (m[:, 128:256], c("EXb", 0, 128, 0, 8), Rh, False, False, 128, 128, 0),
+               (m[:, 128:256], c("EXb", 0, 128, 0, 8), Rl, False, False, 128, 128, 0)]
         for b in range(8):
             mms.append((m[:, 128:256], c("Z8", 112 - 16 * b, 240 - 16 * b), wb[:, 2048 + 128 * b:2176 + 128 * b], False, b == 7, 128, 128, 0))
-        pe(mms, ["II", "MKp", "EXf", "Z8", k("Rf"), k("e0"), k("e1")], [k("m1")], mb)
+        pe(mms, ["II", "MKp", "EXb", "Z8", k("Rf"), k("Rl"), k("e0"), k("e1")], [k("m1")], mb)
         scan(wf[:, 640:768], c("TR"), m[:, 128:256], OP.max, OP.min, 128, [k("m1"), "TR"], [k("sc")], mb)
         cp(wu[:, 32:40], wf[:, 655:768:16], 8, [k("sc")], [k("ku")])
         bias[0] = BIAS[5] * (1 - h) + BIAS[6]
-        mms = [(m[0:16, 0:128], wb[:, 1160:1176], I, True, True, 128, 16, 0)]
+        pe([(m[0:16, 256:384], wb[:, 1152:1168], I, True, True, 128, 16, 0)], ["II", k("hit"), k("nei")], [k("m2")], mb)
+        cp(wb[0:16, 1024:1152], m[0:16, 256:384], 128, [k("m2")], [k("Rb")], mb, flex=True)
         if not last:
-            mms.append((m[:, 256:264], c("ONES"), wb[:, 1152:1160], True, True, 8, 128, 0))
-        pe(mms, ["II", "ONES", k("hit"), k("nei"), k("con")], [k("m0"), k("m2")], mb)
-        cp(wb[0:16, 1024:1152], m[0:16, 0:128], 128, [k("m0")], [k("Rb")], mb, flex=True)
-        if not last:
-            tt(wf[:, 1208:1216], m[:, 256:264], at[:, 0:8] if h == 0 else T.wf0[:, 1208:1216], OP.add, 8,
-               [k("m2"), "atot", "cnt0"], [k("cnt")], mb)
-        mms = [(m[:, 384:512], I, c("MKt"), True, False, 128, 128, 0)]
-        for j, mm in enumerate(perm(h, lambda o: m[:, 384 + o:512:3], lambda s: c("EX0", s, s + 128, 0, 16), lambda o: wb[0:16, 1024 + o:1152:3], True, 0)):
+            pe([(m[:, 384:392], c("ONES"), wb[:, 1152:1160], True, True, 8, 128, 0)], ["ONES", k("hit")], [k("m3")], mb)
+            tt(at[:, 0:8], m[:, 384:392], at[:, 0:8], OP.add, 8, [k("m3"), "atot"], ["atot"], mb)
+        mms = [(m[:, 256:384], I, c("MKt"), True, False, 128, 128, 0)]
+        for j, mm in enumerate(perm(h, lambda o: m[:, 256 + o:384:3], lambda s: c("EX0", s, s + 128, 0, 16), lambda o: wb[0:16, 1024 + o:1152:3], True, 0)):
             mms.append(mm[:3] + (False, j == 2) + mm[5:])
-        pe(mms, ["II", "MKt", "EX0", k("Rb")], [k("m3")], mb)
-        scan(wf[:, 768:896], c("hold", 0, 128), m[:, 384:512], OP.mult, OP.max, 128, [k("m3"), "hold"], [k("sc2"), k("sc")], mb)
+        pe(mms, ["II", "MKt", "EX0", k("Rb")], [k("m2")], mb)
+        scan(wf[:, 768:896], c("hold", 0, 128), m[:, 256:384], OP.mult, OP.max, 128, [k("m2"), "hold"], [k("sc2")], mb)
         cp(wu[:, 40:48], wf[:, 783:896:16], 8, [k("sc2")], [k("su")])
         su = wu[:, 40:48]
         gather(z[:, L] if last else zwin(h, rnd + 1, 0), zwin(h, rnd, 0, 3), su, 128, [k("su"), zk, k("zf"), k("yh")], [k("z") if last else zn])
         gather(lwin(h, rnd + 1, 0), lwin(h, rnd, 0, 3), su, 128, [k("su"), lk, lk + "b", k("dL")], [ln])
         if not last:
-            cp(lwin(h, rnd + 1, 1), lwin(h, rnd + 1, 0), 128, [ln], [ln + "b"], rate=0.5)
+            cp(lwin(h, rnd + 1, 1), lwin(h, rnd + 1, 0), 128, [ln], [ln + "b"], rate=0.5, flex=True)
         bias[0] = BIAS[7] * (1 - h) + BIAS[8]
-        pe([(acc[:, 0:128], c("THN"), lwin(h, rnd, 0), True, False, 128, 128, 0)], ["THN", lk], [k("acc")], ab)
+        ov = T["ov%d" % h]
         for ch in range(4):
-            s, sl = sub_chunk(h, xg, [k("xg0"), k("xg1")], 0, ch, c("nII", 0, 128), zwin(h, rnd, 2), [k("yh")])
-            r = ringbuf(h)
-            u, v = T["ur%d" % h][:, 512 * r:512 * r + 512], T["vr%d" % h][:, 512 * r:512 * r + 512]
-            act(u, sap(s), AF.Abs, 512, [sl], [k("u%d" % r)], [s])
-            ts(v, u, 48.0, None, OP.is_gt, None, 512, [k("u%d" % r)], [k("v%d" % r)], rate=0.5)
-            mv = []
-            for kk in range(4):
-                kq = 4 * ch + kk
-                mv.append((acc[:, 0:128], c("Zw", 16 - kq, 144 - kq), T["vr%d" % h][:, 512 * r + 128 * kk:512 * r + 128 * kk + 128], False, kq == 15, 128, 128, 0))
-            pe(mv, [k("v%d" % r), "Zw", k("acc")], [k("acc")], ab)
+            s, sl = sub_chunk(4 + h, xg, [k("xg0"), k("xg1")], 0, ch, c("nII", 0, 128), zwin(h, rnd, 2), [k("yh")])
+            act(ov[:, 512 * ch:512 * ch + 512], sap(s), AF.Abs, 512, [sl], [k("ov%d" % ch)], [s])
+            if ch % 2:
+                u = ov[:, 512 * ch - 512:512 * ch + 512]
+                ts(u, u, 48.0, None, OP.is_gt, None, 1024, [k("ov%d" % (ch - 1)), k("ov%d" % ch)], [k("ov%d" % (ch - 1)), k("ov%d" % ch)], rate=0.5)
+                mv = [(acc[:, 0:128], c("THN"), lwin(h, rnd, 0), True, False, 128, 128, 0)] if ch == 1 else []
+                for kq in range(4 * ch - 4, 4 * ch + 4):
+                    mv.append((acc[:, 0:128], c("Zw", 16 - kq, 144 - kq), ov[:, 128 * kq:128 * kq + 128], False, kq == 15, 128, 128, 0))
+                pe(mv, [k("ov%d" % (ch - 1)), k("ov%d" % ch), "Zw", "THN", lk, k("acc")], [k("acc")], ab)
         ts(acc[:, 0:128], acc[:, 0:128], -0.5, None, OP.is_gt, None, 128, [k("acc")], [k("acc")], ab)
         tt(acc[:, 0:128], acc[:, 0:128], wf[:, 1664:1792], OP.mult, 128, [k("acc"), k("d2")], [k("acc")], ab)
         tt(kwin(h, rnd, 2), acc[:, 0:128], kwin(h, rnd, 1), OP.add, 128, [k("acc"), kk_], [k("Kc")], ab)
@@ -560,21 +591,31 @@ def build_ops(T):
     def writes(h):
         k = names(h)
         wb, wf, wi, wu = bufs(h)
-        cp(X[:, 0:WX].indirect(wu[:, 32:40]), wi[:, 512:640], 128, [k("ku"), k("nw"), "Xpad", "X"], ["X"], rate=3.8)
-        tt(S[:, 0:WX].indirect(wu[:, 32:40]), wf[:, 2176:2304], wf[:, 896:1024], OP.add, 128, [k("ku"), k("c2"), k("Pf"), "S"], ["S"], rate=3.8)
+        cp(X[:, 0:WX].indirect(wu[:, 32:40]), wi[:, 512:640], 128, [k("ku"), k("nw"), "Xpad", "X"], ["X"], rate=SCA)
+        tt(S[:, 0:WX].indirect(wu[:, 32:40]), wf[:, 2176:2304], wf[:, 896:1024], OP.add, 128, [k("ku"), k("c2"), k("Pf"), "S"], ["S"], rate=SCA)
+        ops[-1]["ns"] = ops[-2]["ns"] = 128 * CYC
 
     for rnd in range(RO):
         last = rnd == RO - 1
-        for stage in (stage_a, stage_c, stage_e):
+        for j, stage in enumerate((stage_a, stage_c, stage_e)):
             for h in range(2):
+                base[0] = len(ops) - 100 * (2 * j + h)
                 stage(h, rnd)
+        base[0] = len(ops) - 600
         bias[0] = 0.0
         writes(0); writes(1)
         if not last:
-            cp(at[:, 0:8], T.wf1[:, 1208:1216], 8, ["cnt1"], ["atot"])
-            cp(ai[:, 0:8], T.wf1[:, 1208:1216], 8, ["cnt1"], ["ai0"])
+            cp(ai[:, 0:8], at[:, 0:8], 8, ["atot"], ["ai0"])
             ts(ai[:, 8:16], ai[:, 0:8], 31, None, OP.bitwise_and, None, 8, ["ai0"], ["ai1"])
             ts(at[:, 8:16], ai[:, 8:16], 32.0, 16.0, OP.mult, OP.add, 8, ["ai1"], ["athr"])
+    for r in others:
+        bias[0] = -3000.0 * others.index(r)
+        for cq in range(4):
+            cp(T.OX[32 * cq:32 * cq + 32, 1024 * r:1024 * r + 1024], X[32 * r:32 * r + 32, 1024 * cq:1024 * cq + 1024], 1024,
+               ["X"], ["OX%d%d" % (r, cq)], rate=0.5, flex=True)
+        for cq in range(4):
+            cp(T.OS[32 * cq:32 * cq + 32, 256 * r:256 * r + 256], S[32 * r:32 * r + 32, W + 256 * cq:W + 256 * cq + 256], 256,
+               ["S"], ["OS%d%d" % (r, cq)], flex=True)
     return ops
 
 
@@ -599,7 +640,11 @@ def schedule(ops):
             lastw[key] = i
             readers[key] = []
         deps[i].discard(i)
-    first, order_only = {}, [set() for _ in range(n)]
+    first = {}
+    for o in ops:
+        for b in o["b"]:
+            if isinstance(b, dict):
+                b["bank"], b["left"] = None, 0
     for i, o in enumerate(ops):
         for b in o["b"]:
             if isinstance(b, dict):
@@ -623,7 +668,7 @@ def schedule(ops):
     eng, end, order = [None] * n, [0.0] * n, []
     held = [False] * 4
     for i in range(n):
-        prio[i] += ops[i]["bias"]
+        prio[i] += ops[i]["bias"] + 500.0 * NUDGE.get(ops[i]["pos"], 0)
     while ready:
         best = None
         cand = []
@@ -643,7 +688,7 @@ def schedule(ops):
                 for b in banks:
                     if blast[b] is not None:
                         st = max(st, bfree[b] + (LAT if eng[blast[b]] != e else 0.0))
-                val = st + cost + (VPEN if e == "V" else 0.0)
+                val = st + cost + (VPEN + 400.0 * LEAN.get(o["pos"], 0) if e == "V" else 0.0)
                 if pick is None or val < pick[3]:
                     pick = (st, e, cost, val)
             cand.append((pick[0], i, pick[1], pick[2], banks))
@@ -670,6 +715,52 @@ def schedule(ops):
             if left[s] == 0:
                 ready.append(s)
     return order, eng, deps, end, lastw
+
+
+SPREAD = [(1.5, 3.8, 60.0, 1.0), (1.04, 1.6, 40.0, 1.0), (2.08, 6.0, 60.0, 1.0), (1.9, 5.0, 120.0, 1.0)]
+TUNED = []
+
+
+def span(ops):
+    order, eng, deps, end, lastw = schedule(ops)
+    tot = 0.0
+    for gam, sca, lat, f in SPREAD:
+        fin, free = [0.0] * len(ops), {"P": 0.0, "V": 0.0, "A": 0.0, "G": 0.0}
+        for i in order:
+            o, e = ops[i], eng[i]
+            st = free[e]
+            if o["in"] > st:
+                st = o["in"]
+            for d in deps[i]:
+                t = fin[d] + (0.0 if e == "P" and eng[d] == "P" and "fence" not in o else lat)
+                if t > st:
+                    st = t
+            fin[i] = free[e] = st + f * (o["alts"][e][0] + o.get("ng", 0) * (gam - GAM) + o.get("ns", 0) * (sca - SCA))
+        tot += max(fin) / f
+    return tot / len(SPREAD)
+
+
+def tune(ops, steps):
+    rng = np.random.RandomState(7)
+    for o in ops:
+        o["in"] = max([READY.get(key, 0.0) for key in o["r"]], default=0.0)
+    poss = sorted({o["pos"] for o in ops if o["pos"] >= 0})
+    flex = sorted({o["pos"] for o in ops if o["pos"] >= 0 and len(o["alts"]) > 1})
+    best = span(ops)
+    for _ in range(steps):
+        keep = (dict(NUDGE), dict(LEAN))
+        if rng.rand() < 0.65:
+            p, w, d = poss[rng.randint(len(poss))], (1, 1, 3, 6, 15)[rng.randint(5)], (-8, -4, -2, -1, 1, 2, 4, 8)[rng.randint(8)]
+            for j in range(p, p + w):
+                NUDGE[j] = NUDGE.get(j, 0) + d
+        else:
+            LEAN[flex[rng.randint(len(flex))]] = (-4, -2, 0, 2, 4)[rng.randint(5)]
+        s = span(ops)
+        if s <= best:
+            best = s
+        else:
+            NUDGE.clear(); NUDGE.update(keep[0]); LEAN.clear(); LEAN.update(keep[1])
+    return best
 
 
 def rank_program(g, core, T, topo):
@@ -706,7 +797,9 @@ def rank_program(g, core, T, topo):
     def full(r):
         return len(topo.engines(T.cores[r], core))
 
-    ops = build_ops(T)
+    ops = build_ops(T, others)
+    if not TUNED:
+        TUNED.append(tune(ops, STEPS))
     order, eng, deps, end, lastw = schedule(ops)
     Q = {"P": g.tensor, "V": g.vector, "A": g.scalar, "G": g}
     idx, cnt = {}, {"P": 0, "V": 0, "A": 0, "G": 0}
@@ -723,8 +816,9 @@ def rank_program(g, core, T, topo):
     g.scalar.dma_start(T.Ki[rows(q), :], T.kw[rows(q), :]).then_inc(sem.ink, 16)
     g.scalar.dma_start(T.Li[2 * q:2 * q + 2, :], T.l0[2 * q:2 * q + 2, :]).then_inc(sem.ink, 16)
     g.sync.dma_start(T.X[rows(q), 0:W], T.x0[rows(q), :]).then_inc(sem.inx, 16)
-    g.sync.dma_start(T.ss[:, :, :], T.asc[:]).then_inc(sem.sts, 16)
-    g.scalar.dma_start(T.Si[rows(q), :], T.asc[rows(q), :]).then_inc(sem.ins, 16)
+    g.sync.wait_ge(sem["stx%d" % others[2]], 16)
+    for r in others:
+        g.sync.dma_start(T.ss[r], T.asc[rows(r), :]).then_inc(sem.sts, 16)
     nin, nink, nins = 16 * N, 48 * N, 16 * N
 
     known = {e: {"P": 0, "V": 0, "A": 0, "G": 0, "in0": 0, "in1": 0, "in2": 0} for e in Q}
@@ -756,15 +850,14 @@ def rank_program(g, core, T, topo):
     for i in gfirst:
         emit(i)
     sent = 0
+    g.wait_ge(sem.stk, 48)
+    sent += fused(T.sl, T.ll, sem.ak)
+    sent += fused(T.sk, T.lk, sem.ak)
+    sent += fused(T.sz, T.lz, sem.ak)
     for j, r in enumerate(others):
         g.wait_ge(sem["stx%d" % r], 16)
         sent += send(T.sx[r], T.lx[q], r, sem["ax%d" % q])
-        if j == 1:
-            g.wait_ge(sem.stk, 48)
-            sent += fused(T.sl, T.ll, sem.ak)
-            sent += fused(T.sk, T.lk, sem.ak)
-            sent += fused(T.sz, T.lz, sem.ak)
-    g.wait_ge(sem.sts, 16)
+    g.wait_ge(sem.sts, 48)
     sent += fused(T.ss, T.ls, sem.as_)
     back = [(q - d) % N for d in (1, 2, 3)]
     g.scalar.wait_ge(sem.ak, 3 * sum(quarter(r2) for r2 in others))
@@ -775,6 +868,8 @@ def rank_program(g, core, T, topo):
     for j, r in enumerate(back):
         g.sync.wait_ge(sem["ax%d" % r], full(r))
         g.sync.dma_start(T.X[rows(r), 0:W], T.lx[r]).then_inc(sem.inx, 16)
+        if j == 0:
+            g.sync.dma_start(T.Si[rows(q), :], T.asc[rows(q), :]).then_inc(sem.ins, 16)
     g.sync.wait_ge(sem.as_, sum(quarter(r) for r in others))
     for r in back:
         g.sync.dma_start(T.Si[rows(r), :], T.ls[r]).then_inc(sem.ins, 16)
@@ -793,45 +888,49 @@ def rank_program(g, core, T, topo):
 
     SA = slice(W, W + A)
     after(g.sync, ["X"])
-    for r in others:
-        g.sync.dma_start(T.ox[r], T.X[rows(r), 0:W]).then_inc(sem["ox%d" % r], 16)
-    after(g.sync, ["S"])
-    g.sync.dma_start(T.oa[:, :, :], T.S[:, SA]).then_inc(sem.oa, 16)
     g.sync.dma_start(T.yx[rows(q), :], T.X[rows(q), 0:W]).then_inc(sem.fin, 16)
+    after(g.sync, ["S"])
     g.sync.dma_start(T.ya[rows(q), :], T.S[rows(q), SA]).then_inc(sem.fin, 16)
+    after(g.sync, ["Lo0", "Lo1", "z0", "z1"])
+    g.sync.dma_start(T.ol[:, :, :], T.Lo[0:8, :]).then_inc(sem.ok, 16)
+    g.sync.dma_start(T.oz[:, :, :], T.z[:, :]).then_inc(sem.ok, 16)
+    after(g.sync, ["Kf0", "Kf1"])
+    g.sync.dma_start(T.ok[:, :, :], T.Kf[:, :]).then_inc(sem.ok, 16)
     after(g.scalar, ["Kf0", "Kf1", "Lo0", "Lo1", "z0", "z1"])
-    g.scalar.dma_start(T.ok[:, :, :], T.Kf[:, :]).then_inc(sem.ok, 16)
-    g.scalar.dma_start(T.ol[:, :, :], T.Lo[0:8, :]).then_inc(sem.ok, 16)
-    g.scalar.dma_start(T.oz[:, :, :], T.z[:, :]).then_inc(sem.ok, 16)
     g.scalar.dma_start(T.yz[rows(q), :], T.z[rows(q), :]).then_inc(sem.fin2, 16)
     g.scalar.dma_start(T.yk[rows(q), :], T.Kf[rows(q), :]).then_inc(sem.fin2, 16)
     g.scalar.dma_start(T.yl[2 * q:2 * q + 2, :], T.Lo[2 * q:2 * q + 2, :]).then_inc(sem.fin2, 16)
     for r in others:
-        g.wait_ge(sem["ox%d" % r], 16)
-        sent += send(T.ox[r], T.mx[q], r, sem["bx%d" % q])
-    g.wait_ge(sem.oa, 16)
-    sent += fused(T.oa, T.ma, sem.ba)
-    g.wait_ge(sem.ok, 48)
-    sent += fused(T.ok, T.mk, sem.bk)
-    sent += fused(T.oz, T.mz, sem.bk)
-    sent += fused(T.ol, T.ml, sem.bk)
+        after(g, ["OX%d%d" % (r, cq) for cq in range(4)])
+        sent += send(T.OX[:, 1024 * r:1024 * r + 1024], T.mx[q], r, sem["bx%d" % q])
+        after(g, ["OS%d%d" % (r, cq) for cq in range(4)])
+        sent += send(T.OS[:, 256 * r:256 * r + 256], T.ma[q], r, sem["ba%d" % q])
+        if r == others[1]:
+            g.wait_ge(sem.ok, 48)
+            sent += fused(T.ok, T.mk, sem.bk)
+            sent += fused(T.oz, T.mz, sem.bk)
+            sent += fused(T.ol, T.ml, sem.bk)
     for r in back:
+        if r == back[2]:
+            g.sync.wait_ge(sem.bk, 3 * sum(quarter(r2) for r2 in others))
+            g.scalar.wait_ge(sem.bk, 3 * sum(quarter(r2) for r2 in others))
+            for j, r2 in enumerate(back):
+                g.sync.dma_start(T.yk[rows(r2), :], T.mk[r2]).then_inc(sem.fin, 16)
+                g.scalar.dma_start(T.yz[rows(r2), :], T.mz[r2]).then_inc(sem.fin2, 16)
+                if j % 2:
+                    g.scalar.dma_start(T.yl[2 * r2:2 * r2 + 2, :], T.ml[r2]).then_inc(sem.fin2, 16)
+                else:
+                    g.sync.dma_start(T.yl[2 * r2:2 * r2 + 2, :], T.ml[r2]).then_inc(sem.fin, 16)
         g.sync.wait_ge(sem["bx%d" % r], full(r))
-        g.sync.dma_start(T.yx[rows(r), :], T.mx[r]).then_inc(sem.fin, 16)
-    g.scalar.wait_ge(sem.ba, sum(quarter(r) for r in others))
-    for r in back:
-        g.scalar.dma_start(T.ya[rows(r), :], T.ma[r]).then_inc(sem.fin2, 16)
-    g.sync.wait_ge(sem.bk, 3 * sum(quarter(r) for r in others))
-    g.scalar.wait_ge(sem.bk, 3 * sum(quarter(r) for r in others))
-    for j, r in enumerate(back):
-        g.sync.dma_start(T.yk[rows(r), :], T.mk[r]).then_inc(sem.fin, 16)
-        g.scalar.dma_start(T.yz[rows(r), :], T.mz[r]).then_inc(sem.fin2, 16)
-        if j % 2:
-            g.scalar.dma_start(T.yl[2 * r:2 * r + 2, :], T.ml[r]).then_inc(sem.fin2, 16)
-        else:
-            g.sync.dma_start(T.yl[2 * r:2 * r + 2, :], T.ml[r]).then_inc(sem.fin, 16)
-    g.sync.wait_ge(sem.fin, 32 + 32 * (N - 1) + 32)
-    g.scalar.wait_ge(sem.fin2, 48 + 32 * (N - 1) + 16)
+        g.scalar.wait_ge(sem["bx%d" % r], full(r))
+        for cq in range(4):
+            (g.sync, g.scalar)[cq % 2].dma_start(T.yx[rows(r), 1024 * cq:1024 * cq + 1024], T.mx[r, rows(cq), :]).then_inc((sem.fin, sem.fin2)[cq % 2], 16)
+        g.sync.wait_ge(sem["ba%d" % r], full(r))
+        g.scalar.wait_ge(sem["ba%d" % r], full(r))
+        for cq in range(4):
+            (g.sync, g.scalar)[cq % 2].dma_start(T.ya[rows(r), 256 * cq:256 * cq + 256], T.ma[r, rows(cq), :]).then_inc((sem.fin, sem.fin2)[cq % 2], 16)
+    g.sync.wait_ge(sem.fin, 32 + 80 * (N - 1) + 32)
+    g.scalar.wait_ge(sem.fin2, 48 + 80 * (N - 1) + 16)
     g.wait_ge(sem.snd, sent)
     for f in Q:
         g.wait_ge(sem[f], cnt[f])

@@ -6,55 +6,63 @@ N, W, A, TL, RO, EPS, TH = 4, 4096, 1024, 256, 4, 48, 720
 WX = 5248
 NRING = 5
 BIAS = [8000, -3000, 12000, 8000, -1000, 3000, 3000, 2000, 0, 3000, 1000, 8000, 4000, 5000, 0]
-NV = [3, 4]
-NE = [0, 1]
-STEPS = 2200
+NE = [4, 4]
+STEPS = 3000
 WIN, VPEN = 40.0, 300.0
 NUDGE = {}
 LEAN = {}
 GAM, SCA = 1.5, 3.8
+MAGIC = 12582912.0
+S97 = 169.0 / 16384
+U = 2.0 ** -13
 
 SCRATCH = {
     "X": ("sbuf", [128, WX], "bfloat16"), "S": ("sbuf", [128, WX], "float32"),
+    "NX": ("sbuf", [128, WX], "bfloat16"), "NS": ("sbuf", [128, WX], "float32"),
     "Si": ("sbuf", [128, A], "int32"), "Ki": ("sbuf", [128, TL], "int32"), "Li": ("sbuf", [128, TL], "int32"),
-    "Lb": ("sbuf", [128, TL], "bfloat16"), "Lo": ("sbuf", [128, TL], "float32"),
+    "Lb": ("sbuf", [128, TL], "bfloat16"), "Lo": ("sbuf", [128, 128], "float32"),
     "Ku": ("sbuf", [128, TL], "uint16"), "Kf": ("sbuf", [128, TL], "float32"),
-    "z": ("sbuf", [128, TL], "bfloat16"), "Lh": ("sbuf", [128, TL], "bfloat16"),
-    "OX": ("sbuf", [128, W], "bfloat16"), "OS": ("sbuf", [128, A], "float32"),
-    "at": ("sbuf", [128, 32], "float32"), "ai": ("sbuf", [128, 16], "int32"),
-    "CB": ("sbuf", [128, 6144], "bfloat16"), "CF": ("sbuf", [128, 2560], "float32"),
-    "CI": ("sbuf", [128, 16], "int32"), "TF": ("sbuf", [128, 1680], "float32"),
+    "z": ("sbuf", [128, TL], "bfloat16"), "AR": ("sbuf", [128, 128], "bfloat16"),
+    "LK": ("sbuf", [128, 64], "uint16"), "KU": ("sbuf", [128, 16], "uint16"),
+    "at": ("sbuf", [128, 16], "float32"), "ai": ("sbuf", [128, 16], "int32"),
+    "CB": ("sbuf", [128, 9344], "bfloat16"), "CF": ("sbuf", [128, 512], "float32"), "C16": ("sbuf", [128, 528], "float16"),
+    "CI": ("sbuf", [128, 16], "int32"), "TB": ("sbuf", [128, 2048], "bfloat16"),
     "sx": ("dram", [4, 128, 1024], "bfloat16"), "lx": ("dram", [4, 128, 1024], "bfloat16"), "mx": ("dram", [4, 128, 1024], "bfloat16"),
-    "sz": ("dram", [4, 128, 64], "bfloat16"), "lz": ("dram", [4, 128, 64], "bfloat16"), "mz": ("dram", [4, 128, 64], "bfloat16"),
+    "sz": ("dram", [4, 128, 64], "bfloat16"), "lz": ("dram", [4, 128, 64], "bfloat16"),
     "sk": ("dram", [4, 128, 64], "int32"), "lk": ("dram", [4, 128, 64], "int32"),
     "sl": ("dram", [4, 128, 4], "int32"), "ll": ("dram", [4, 128, 4], "int32"),
-    "ol": ("dram", [4, 128, 4], "float32"), "ml": ("dram", [4, 128, 4], "float32"),
     "ss": ("dram", [4, 128, 256], "int32"), "ls": ("dram", [4, 128, 256], "int32"),
+    "ox": ("dram", [4, 128, 1024], "bfloat16"),
     "oa": ("dram", [4, 128, 256], "float32"), "ma": ("dram", [4, 128, 256], "float32"),
-    "ok": ("dram", [4, 128, 64], "float32"), "mk": ("dram", [4, 128, 64], "float32"),
-    "ox": ("dram", [4, 128, 1024], "bfloat16"), "oz": ("dram", [4, 128, 64], "bfloat16"),
+    "mz": ("dram", [4, 128, 256], "bfloat16"), "ml": ("dram", [4, 128, 128], "float32"),
 }
 for _h in range(2):
     SCRATCH.update({
         "xg%d" % _h: ("sbuf", [128, 2048], "bfloat16"), "yg%d" % _h: ("sbuf", [128, 4096], "bfloat16"),
         "ov%d" % _h: ("sbuf", [128, 2048], "bfloat16"),
         "ur%d" % _h: ("sbuf", [128, 512 * NRING], "bfloat16"), "vr%d" % _h: ("sbuf", [128, 512 * NRING], "bfloat16"),
-        "wb%d" % _h: ("sbuf", [128, 4864], "bfloat16"), "wf%d" % _h: ("sbuf", [128, 3200], "float32"),
+        "wb%d" % _h: ("sbuf", [128, 4608], "bfloat16"), "wf%d" % _h: ("sbuf", [128, 2176], "float32"),
         "wi%d" % _h: ("sbuf", [128, 1024], "int32"), "wu%d" % _h: ("sbuf", [128, 320], "uint16"),
+        "wh%d" % _h: ("sbuf", [128, 512], "float16"),
+        "VA%d" % _h: ("sbuf", [128, 256], "float32"), "VL%d" % _h: ("sbuf", [128, 256], "float32"),
+        "mv%d" % _h: ("dram", [4, 128, 256], "float32"), "mk%d" % _h: ("dram", [4, 128, 128], "float32"),
     })
 for _b in range(8):
     SCRATCH["ps%d" % _b] = ("psum", [128, 512], "float32")
 
-SEMAPHORES = ["P", "V", "A", "G", "stx0", "stx1", "stx2", "stx3", "stk", "sts", "snd",
+SEMAPHORES = ["P", "V", "A", "G", "stx0", "stx1", "stx2", "stx3", "stk", "sts", "snd", "own",
               "ax0", "ax1", "ax2", "ax3", "ak", "as_", "inx", "ink", "ins",
-              "ox0", "ox1", "ox2", "ox3", "oa", "ok",
-              "bx0", "bx1", "bx2", "bx3", "ba0", "ba1", "ba2", "ba3", "bk", "fin", "fin2"]
+              "ox", "oa", "bx", "ba", "nx", "ns", "nxo", "nso", "zl", "zlo", "yx", "ya", "yz", "yl"]
+for _h in range(2):
+    SEMAPHORES += [_s + str(_h) for _s in ("bv", "ov", "vl", "bu", "bk", "ok", "yk")]
 
 CYC, PCYC, LAT, FIX = 0.83, 0.42, 60.0, 55.0
 
 
-def build_ops(T, others=(1, 2, 3)):
+def build_ops(T, q=0, net=None):
     ops = []
+    others = [(q + d) % N for d in (1, 2, 3)]
+    rows = lambda r: slice(32 * r, 32 * r + 32)
 
     def add(alts, reads, writes, banks=()):
         ops.append({"alts": alts, "r": list(reads), "w": list(writes), "b": list(banks), "bias": bias[0],
@@ -89,13 +97,16 @@ def build_ops(T, others=(1, 2, 3)):
             return last
         add({"P": (cost, run)}, reads, writes, banks)
 
+    def group(mms):
+        return [(o, l, r, j == 0, j == len(mms) - 1, n, 128, f) for j, (o, l, r, n, f) in enumerate(mms)]
+
     def ts(out, in0, s1, s2, op0, op1, n, reads, writes, banks=(), rate=1.0, act=None):
         if op1 is None:
-            alts = {"V": (vc(n, rate), lambda g: g.vector.tensor_scalar(out, R(in0), s1, None, op0))}
+            alts = {"V": (vc(n, rate), lambda g: g.vector.tensor_scalar(R(out), R(in0), s1, None, op0))}
         else:
-            alts = {"V": (vc(n, rate), lambda g: g.vector.tensor_scalar(out, R(in0), s1, s2, op0, op1))}
+            alts = {"V": (vc(n, rate), lambda g: g.vector.tensor_scalar(R(out), R(in0), s1, s2, op0, op1))}
         if act is not None:
-            alts["A"] = (vc(n) + 15, lambda g: g.scalar.activation(out, R(in0), act[0], bias=act[1], scale=act[2]))
+            alts["A"] = (vc(n, max(rate, 1.0)) + 15, lambda g: g.scalar.activation(out, R(in0), act[0], bias=act[1], scale=act[2]))
         add(alts, reads, writes, banks)
 
     def tt(out, a, b, op, n, reads, writes, banks=(), rate=None):
@@ -112,8 +123,8 @@ def build_ops(T, others=(1, 2, 3)):
     def act(out, in_, func, n, reads, writes, banks=(), bias=0.0):
         add({"A": (vc(n) + 15, lambda g: g.scalar.activation(R(out), R(in_), func, bias=bias))}, reads, writes, banks)
 
-    def scan(out, d0, d1, op0, op1, n, reads, writes, banks=()):
-        add({"V": (vc(n), lambda g: g.vector.tensor_tensor_scan(out, d0, d1, 0.0, op0, op1))}, reads, writes, banks)
+    def scan(out, d0, d1, op0, op1, n, reads, writes, banks=(), rate=1.0):
+        add({"V": (vc(n, rate), lambda g: g.vector.tensor_tensor_scan(out, d0, d1, 0.0, op0, op1))}, reads, writes, banks)
 
     def iota(out, pat, base, cm, n, writes, isint=False):
         if isint:
@@ -121,10 +132,21 @@ def build_ops(T, others=(1, 2, 3)):
         else:
             add({"G": (130 + 2 * n * CYC, lambda g: g.iota(out, pat, base, cm, allow_small_or_imprecise_dtypes=True))}, [], writes)
 
-    def mset(ap, v, n, writes):
-        add({"V": (vc(n), lambda g: g.vector.memset(ap, v))}, [], writes)
+    def mset(ap, v, n, writes, rate=0.5):
+        add({"V": (vc(n, rate), lambda g: g.vector.memset(ap, v))}, [], writes)
 
-    pos = {"CB": 0, "CF": 0, "TF": 0}
+    def dma(e, pairs, sem, lat, reads, writes):
+        def run(g):
+            for o, i in pairs:
+                (g.sync if e == "S" else g.scalar).dma_start(o, i).then_inc(T.sem[sem], 16)
+        add({e: (60.0 * len(pairs), run)}, reads, writes)
+        ops[-1].update({"sem": sem, "val": 16 * len(pairs), "lat": lat})
+
+    def remote(kind, items, sem, lat, reads, writes):
+        add({"G": (200.0, lambda g: net[kind](items, T.sem[sem]))}, reads, writes)
+        ops[-1].update({"sem": sem, "val": net["in"][kind] if net else 0, "lat": lat, "far": 1})
+
+    pos = {"CB": 0, "CF": 0, "TB": 0, "C16": 0}
     C = {}
 
     def alloc(buf, name, n):
@@ -135,18 +157,21 @@ def build_ops(T, others=(1, 2, 3)):
         t, o, n = C[name]
         return t[p0:p1, o + a:o + (n if b is None else b)]
 
-    for nm, n in (("II", 256), ("nII", 256), ("I22", 128), ("ONES", 128), ("B8", 8), ("Wd", 8), ("Ww", 8), ("W32", 16),
-                  ("CH", 256), ("CR", 256), ("MM16", 128), ("WV", 128), ("W4", 256), ("TK", 128), ("KX0", 128), ("KX1", 128), ("TRT", 512), ("W21h", 256), ("W21l", 256),
-                  ("MK", 256), ("MKp", 128), ("WV8", 8), ("EX0", 256), ("MKt", 128), ("W32n", 8), ("W64", 8), ("TRI", 512),
-                  ("Z8", 240), ("Zw", 144), ("THN", 128), ("LS", 128), ("LW", 8), ("EXb", 128)):
+    for nm, n in (("II", 256), ("nII", 256), ("sI", 128), ("nsI", 128), ("IH", 128), ("I16", 128), ("PM", 256), ("ONES", 128),
+                  ("MM", 256), ("BB", 256), ("B8", 16), ("nB8", 8), ("Wd", 8), ("Ww", 8), ("Wn", 16), ("W2", 16), ("LWa", 128), ("LWb", 128),
+                  ("W4V", 8), ("CH", 256), ("THN", 128), ("WV", 128), ("W4", 256), ("W21h", 256), ("W21l", 256), ("nBD", 128),
+                  ("MM16", 128), ("MK", 256), ("MK2", 128), ("MKp", 128), ("MKt", 128), ("hold", 256), ("rst", 128), ("rstr", 128),
+                  ("HP", 128), ("CR", 256), ("EX0", 256), ("EXb", 128), ("EXa", 128), ("EXK", 128), ("TRT", 512), ("Z8", 240),
+                  ("LS", 128), ("CT", 256), ("NH", 128), ("C2", 16), ("SEL", 1024), ("nSEL", 1024), ("cb", 16)):
         alloc("CB", nm, n)
-    for nm, n in (("IIf", 256), ("I20", 128), ("B8f", 16), ("BBf", 256), ("MM", 256), ("hold", 256), ("holdr", 256),
-                  ("TR", 128), ("col", 32)):
+    for nm, n in (("I20", 128), ("TR", 128), ("t4", 64), ("t5", 128), ("col", 32)):
         alloc("CF", nm, n)
-    for nm, n in (("t0", 256), ("t1", 256), ("t2", 256), ("t3", 256), ("t4", 256), ("t5", 256), ("t6", 144)):
-        alloc("TF", nm, n)
-    colnames = ["p", "pm", "pb", "w", "pw", "th", "thn", "w21", "w21h", "w21l", "n1024", "n5120", "trash", "p16",
-                "e0", "e1", "b0", "b1", "b2", "bc", "w4", "m15"]
+    for nm, n in (("IIh", 256), ("BBh", 256), ("B8h", 8)):
+        alloc("C16", nm, n)
+    for nm, n in (("t0", 256), ("t1", 256), ("t2", 256), ("t3", 16), ("t6", 128), ("tb", 1024)):
+        alloc("TB", nm, n)
+    colnames = ["p", "pm", "pb", "p7", "h8", "w", "pw", "th", "nth", "thn", "w21", "w21l", "p16", "w4", "m15", "wsel", "lwa", "lwb",
+                "sp", "e0", "e1", "e2", "b0", "b1", "b2", "b3", "f0", "f1", "f2", "f3"]
 
     def col(nm, p0=0, p1=128):
         k = colnames.index(nm)
@@ -154,117 +179,110 @@ def build_ops(T, others=(1, 2, 3)):
 
     CI = T.CI
     iota(CI[:, 0:1], [[0, 1]], 0, 1, 1, ["ci0"], True)
+    iota(c("t0"), [[0, 2], [1, 128]], 0, 0, 256, ["t0"])
+    iota(c("t2"), [[0, 16], [1, 16]], 0, 0, 256, ["t2"])
+    iota(c("t3"), [[0, 2], [1, 8]], 0, 0, 16, ["t3"])
+    iota(c("t1"), [[0, 2], [1, 8], [0, 16]], 0, 0, 256, ["t1"])
+    iota(c("tb"), [[1, 8], [0, 128]], 0, 0, 1024, ["tb"])
+    ops[-1]["late"] = 1
     cp(col("p"), CI[:, 0:1], 1, ["ci0"], ["c.p"])
-    ts(CI[:, 1:2], CI[:, 0:1], 15, None, OP.bitwise_and, None, 1, ["ci0"], ["ci1"])
-    ts(CI[:, 2:3], CI[:, 0:1], 4, None, OP.arith_shift_right, None, 1, ["ci0"], ["ci2"])
-    cp(col("pm"), CI[:, 1:2], 1, ["ci1"], ["c.pm"])
-    cp(col("pb"), CI[:, 2:3], 1, ["ci2"], ["c.pb"])
+    for j, (nm, s1, s2) in enumerate((("pm", 0, 15), ("pb", 4, 7), ("p7", 0, 7), ("h8", 3, 1))):
+        ts(CI[:, 1 + j:2 + j], CI[:, 0:1], s1, s2, OP.arith_shift_right, OP.bitwise_and, 1, ["ci0"], ["ci%d" % (1 + j)])
+        cp(col(nm), CI[:, 1 + j:2 + j], 1, ["ci%d" % (1 + j)], ["c." + nm])
 
     def cts(nm, src, s1, s2, o0, o1):
-        ts(col(nm), col(src), s1, s2, o0, o1, 1, ["c." + src], ["c." + nm])
-    iota(c("t0"), [[0, 2], [1, 128]], 0, 0, 256, ["t0"])
-    iota(c("t1"), [[0, 2], [1, 8], [0, 16]], 0, 0, 256, ["t1"])
-    iota(c("t2"), [[0, 16], [1, 16]], 0, 0, 256, ["t2"])
-    iota(c("t3", 0, 16), [[0, 2], [1, 8]], 0, 0, 16, ["t3"])
+        rd = ["c." + s for s in (src, s1, s2) if isinstance(s, str)]
+        ts(col(nm), col(src), col(s1) if isinstance(s1, str) else s1, col(s2) if isinstance(s2, str) else s2, o0, o1, 1, rd, ["c." + nm])
 
-    def eq(dst, src, cn, mul, n, a=0):
+    def eq(dst, src, cn, mul=None, n=None):
+        n = n or C[dst][2]
         if mul is None:
-            ts(c(dst, a, a + n), c(src, 0, n), col(cn), None, OP.is_equal, None, n, [src, "c." + cn], [dst])
+            ts(c(dst, 0, n), c(src, 0, n), col(cn), None, OP.is_equal, None, n, [src, "c." + cn], [dst], rate=0.5)
         else:
             rd = [src, "c." + cn] + (["c." + mul] if isinstance(mul, str) else [])
-            ts(c(dst, a, a + n), c(src, 0, n), col(cn), col(mul) if isinstance(mul, str) else mul, OP.is_equal, OP.mult, n, rd, [dst])
-    eq("II", "t0", "p", None, 256)
-    eq("nII", "t0", "p", -1.0, 256)
-    eq("MM", "t2", "pm", None, 256)
-    eq("B8f", "t3", "pb", None, 16)
-    eq("B8", "t3", "pb", None, 8)
-    eq("Wd", "t3", "pb", -2048.0, 8)
+            ts(c(dst, 0, n), c(src, 0, n), col(cn), col(mul) if isinstance(mul, str) else mul, OP.is_equal, OP.mult, n, rd, [dst], rate=0.5)
+
+    def lin(dst, src, mul, off=0.0, a=0, n=None, rate=0.5, flex=True):
+        n = n or C[dst][2]
+        m = col(mul) if isinstance(mul, str) else mul
+        o = col(off) if isinstance(off, str) else off
+        rd = [src] + ["c." + s for s in (mul, off) if isinstance(s, str)]
+        ts(c(dst, a, a + n), c(src, 0, n), m, o, OP.mult, OP.add, n, rd, [dst], rate=rate, act=(AF.Identity, o, m) if flex else None)
+
+    eq("II", "t0", "p")
+    eq("MM", "t2", "pm")
+    eq("BB", "t1", "pb")
+    eq("B8", "t3", "pb")
+    lin("nII", "II", -1.0); lin("sI", "II", S97); lin("nsI", "II", -S97); lin("IH", "II", 0.5); lin("I16", "II", 65536.0)
+    lin("PM", "II", -8192.0, n=128); lin("PM", "II", 8192.0, a=128, n=128)
+    lin("I20", "II", 20.0, rate=1.0); lin("IIh", "II", 1.0, flex=False); lin("BBh", "BB", 1.0, flex=False); lin("B8h", "B8", 1.0, flex=False)
     mset(c("t4", 0, 16), 0.5, 16, ["t4"])
     mset(c("t4", 16, 32), 0.0, 16, ["t4"])
     add({"V": (vc(16), lambda g: g.vector.tensor_tensor_scan(c("t4", 32, 48), c("t4", 0, 16), c("t4", 16, 32), 65536.0, OP.mult, OP.add))}, ["t4"], ["t4b"])
     tt(c("t4", 48, 64), c("t4", 32, 48), c("MM", 0, 16), OP.mult, 16, ["t4b", "MM"], ["t4c"])
     add({"V": (vc(16), lambda g: g.vector.tensor_reduce(col("th"), c("t4", 48, 64), AxisListType.X, OP.add))}, ["t4c"], ["c.th"])
-    cts("m15", "pm", 15.0, None, OP.is_lt, None)
-    ts(col("pw"), col("th"), 0.5, col("m15"), OP.mult, OP.mult, 1, ["c.th", "c.m15"], ["c.pw"])
-    eq("Ww", "t3", "pb", "pw", 8)
+    cts("m15", "pm", 15.0, 0.5, OP.is_lt, OP.mult)
+    cts("pw", "th", "m15", None, OP.mult, None)
     cts("e0", "pm", 15.0, -32768.0, OP.is_equal, OP.mult)
-    tt(col("thn"), col("e0"), col("pw"), OP.subtract, 1, ["c.e0", "c.pw"], ["c.thn"])
-    cts("e1", "th", -1.0, None, OP.mult, None)
-    eq("CH", "t1", "pb", "e1", 128, 128)
+    cts("thn", "e0", "pw", None, OP.subtract, None)
+    cts("nth", "th", -1.0, None, OP.mult, None)
+    lin("nB8", "B8", -1.0); lin("Wd", "B8", -16.0); lin("Ww", "B8", "pw"); lin("Wn", "B8", -U); lin("W2", "B8", 2 * U)
+    lin("CH", "BB", "nth", a=128, n=128); lin("THN", "BB", "thn"); lin("nBD", "BB", -U)
     cts("b0", "pb", 0.0, None, OP.is_equal, None)
-    cts("b1", "pb", 1.0, -2048.0, OP.is_equal, OP.mult)
-    cts("b2", "pb", 2.0, -4194304.0, OP.is_equal, OP.mult)
-    tt(col("bc"), col("b1"), col("b2"), OP.add, 1, ["c.b1", "c.b2"], ["c.bc"])
-    ts(c("CH", 0, 128), c("t2", 0, 128), col("b0"), col("bc"), OP.mult, OP.add, 128, ["t2", "c.b0", "c.bc"], ["CH"])
-    eq("I22", "t0", "p", 4194304.0, 128)
+    cts("b1", "pb", 1.0, -16.0, OP.is_equal, OP.mult)
+    cts("b2", "pb", 2.0, -65536.0, OP.is_equal, OP.mult)
+    cts("b3", "b1", "b2", None, OP.add, None)
+    lin("CH", "t2", "b0", "b3", n=128)
     cts("p16", "p", 16.0, None, OP.mult, None)
-    eq("MM16", "t2", "pm", "p16", 128)
-    ts(c("hold"), c("t2"), 0.0, None, OP.not_equal, None, 256, ["t2"], ["hold"])
-    ts(c("holdr"), c("t2"), 15.0, None, OP.not_equal, None, 256, ["t2"], ["holdr"])
-    eq("IIf", "t0", "p", None, 256)
-    eq("I20", "t0", "p", 20.0, 128)
-    eq("BBf", "t1", "pb", None, 256)
+    lin("MM16", "MM", "p16")
+    ts(c("hold"), c("t2"), 0.0, None, OP.not_equal, None, 256, ["t2"], ["hold"], rate=0.5)
+    ts(c("rst"), c("t2", 0, 128), 0.0, 4.0, OP.is_equal, OP.mult, 128, ["t2"], ["rst"], rate=0.5)
+    ts(c("rstr"), c("t2", 0, 128), 15.0, 4.0, OP.is_equal, OP.mult, 128, ["t2"], ["rstr"], rate=0.5)
+    ts(c("t6"), c("t2", 0, 128), col("pm"), None, OP.is_le, None, 128, ["t2", "c.pm"], ["t6"], rate=0.5)
+    tt(c("HP"), c("t6"), c("hold", 0, 128), OP.mult, 128, ["t6", "hold"], ["HP"])
     cts("w", "pm", 15.0, 7.0, OP.mult, OP.add)
     cts("w4", "w", 4.0, None, OP.mult, None)
     cts("w21", "w", 21.0, None, OP.mult, None)
-    eq("WV", "t1", "pb", "w", 128)
-    eq("W4", "t1", "pb", "w4", 256)
-    eq("WV8", "t3", "pb", "w", 8)
-    eq("W21h", "t1", "pb", "w21", 256)
-    ts(c("t5"), c("BBf"), col("w21"), None, OP.mult, None, 256, ["BBf", "c.w21"], ["t5"])
-    tt(c("W21l"), c("t5"), c("W21h"), OP.subtract, 256, ["t5", "W21h"], ["W21l"])
-    ts(c("MK"), c("MM"), -1.0, 16777216.0, OP.add, OP.mult, 256, ["MM"], ["MK"])
-    ts(c("t5", 0, 128), c("MM", 0, 128), -0.5, None, OP.mult, None, 128, ["MM"], ["t5"])
-    tt(c("MKp"), c("t5", 0, 128), c("MK", 0, 128), OP.subtract, 128, ["t5", "MK"], ["MKp"])
+    cp(c("cb", 0, 1), col("w21"), 1, ["c.w21"], ["cb"])
+    ts(col("w21l"), col("w21"), c("cb", 0, 1), None, OP.subtract, None, 1, ["c.w21", "cb"], ["c.w21l"])
+    lin("WV", "BB", "w"); lin("W4", "BB", "w4"); lin("W21h", "BB", "w21"); lin("W21l", "BB", "w21l"); lin("W4V", "B8", "w4")
+    big = 16777216.0
+    lin("MK", "MM", big, -big); lin("MK2", "MM", big + 2048.0, -big, flex=False); lin("MKp", "MM", 8192.0 - big, big, flex=False)
+    tt(c("MKt"), c("MK", 0, 128), c("t0", 0, 128), OP.add, 128, ["MK", "t0"], ["MKt"])
     mset(c("ONES"), 1.0, 128, ["ONES"])
-    eq("W32", "t3", "pb", 32.0, 16)
-    cts("b0", "p", 0.0, None, OP.is_equal, None)
-    cts("b1", "p", 1.0, -262144.0, OP.is_equal, OP.mult)
-    ts(c("CR"), c("t2"), col("b0"), col("b1"), OP.mult, OP.add, 256, ["t2", "c.b0", "c.b1"], ["CR"])
-    ts(CI[:, 3:4], CI[:, 0:1], 7, None, OP.bitwise_and, None, 1, ["ci0"], ["ci3"])
-    cp(col("b2"), CI[:, 3:4], 1, ["ci3"], ["c.b2"])
-    cts("b0", "p", 8.0, 128.0, OP.is_lt, OP.mult)
-    cts("b1", "b0", 128.0, None, OP.add, None)
-    eq("EX0", "t1", "b2", "b1", 256)
-    eq("EXb", "t1", "p", None, 128)
-    for q in range(2):
-        ts(c("TRI", 256 * q, 256 * q + 256), c("t0"), col("p"), -64.0, OP.is_ge, OP.mult, 256, ["t0", "c.p"], ["TRI"])
-    ts(c("TRT"), c("TRI"), -1.0, 15.5, OP.mult, OP.add, 512, ["TRI"], ["TRT"], rate=0.5)
+    cts("f0", "p", 0.0, U / 32, OP.is_equal, OP.mult)
+    cts("f1", "p", 1.0, -TH * U, OP.is_equal, OP.mult)
+    cts("f2", "p", 2.0, -U / 2, OP.is_equal, OP.mult)
+    cts("f3", "f1", "f2", None, OP.add, None)
+    lin("CR", "t2", "f0", "f1", n=128); lin("CR", "t2", "f0", "f3", a=128, n=128)
+    cts("e1", "h8", -128.0, 256.0, OP.mult, OP.add)
+    eq("EX0", "t1", "p7", "e1")
+    cts("e2", "h8", -4096.75, -4096.25, OP.mult, OP.add)
+    cts("b0", "p", 16.0, "e2", OP.is_lt, OP.mult)
+    cts("b1", "h8", 0.75, 0.25, OP.mult, OP.add)
+    cts("wsel", "b0", "b1", None, OP.add, None)
+    eq("EXK", "t1", "p7", "wsel")
+    eq("SEL", "tb", "p7", "wsel")
+    lin("nSEL", "SEL", -1.0)
+    eq("EXb", "t1", "p")
+    lin("EXa", "EXb", -U)
+    for j in range(2):
+        ts(c("TRT", 256 * j, 256 * j + 256), c("t0"), col("p"), 0.25, OP.is_ge, OP.mult, 256, ["t0", "c.p"], ["TRT"], rate=0.5)
     mset(c("Z8"), 0.0, 240, ["Z8"])
     mset(c("Z8", 112, 128), 8192.0, 16, ["Z8"])
-    iota(c("t6", 0, 144), [[1, 144]], -16, 0, 144, ["t6"])
-    cts("b2", "pb", 16.0, None, OP.mult, None)
-    eq("Zw", "t6", "b2", "pw", 144)
-    eq("THN", "t1", "pb", "thn", 128)
     cts("e0", "pm", 15.0, -16.0, OP.is_equal, OP.mult)
-    ts(col("e1"), col("p"), 1.0, col("e0"), OP.add, OP.add, 1, ["c.p", "c.e0"], ["c.e1"])
-    eq("LS", "t0", "e1", None, 128)
-    eq("W32n", "t3", "pb", -32.0, 8)
-    eq("W64", "t3", "pb", 64.0, 8)
-    tt(c("t5", 0, 128), c("t0", 0, 128), c("MM", 0, 128), OP.mult, 128, ["t0", "MM"], ["t5"])
-    tt(c("MKt"), c("t5", 0, 128), c("MK", 0, 128), OP.add, 128, ["t5", "MK"], ["MKt"])
-    eq("LW", "t3", "pb", "pm", 8)
-    cts("n1024", "p", -1.0, -1024.0, OP.mult, OP.add)
-    cts("n5120", "p", -1.0, -5120.0, OP.mult, OP.add)
-    cts("b0", "p", 0.0, None, OP.is_equal, None)
-    cts("b1", "p", 1.0, 5120.0, OP.is_equal, OP.mult)
-    cts("b2", "p", 2.0, 0.5, OP.is_equal, OP.mult)
-    tt(col("trash"), col("b1"), col("b2"), OP.add, 1, ["c.b1", "c.b2"], ["c.trash"])
-    ts(c("TK"), c("t0", 0, 128), col("b0"), col("trash"), OP.mult, OP.add, 128, ["t0", "c.b0", "c.trash"], ["TK"])
-    ts(c("t5", 0, 128), c("t0", 0, 128), col("pm"), 5120.0, OP.add, OP.add, 128, ["t0", "c.pm"], ["t5"])
-    ts(c("TR"), c("hold", 0, 128), -1.0, 1.0, OP.mult, OP.add, 128, ["hold"], ["TR"])
-    tt(c("TR"), c("TR"), c("t5", 0, 128), OP.mult, 128, ["TR", "t5"], ["TR"])
-    for q in range(8):
-        ts(c("t5", 16 * q, 16 * q + 16), c("t4", 32, 48), (1.0 if q % 2 == 0 else -1.0) / 65536.0, None, OP.mult, None, 16, ["t4b"], ["t5"])
-    iota(c("t3", 128, 256), [[1, 4], [0, 32]], 0, 0, 128, ["t3b"])
-    for q in range(2):
-        cts("b2", "p", -4.0 * q, None, OP.add, None)
-        ts(c("KX%d" % q), c("t3", 128, 256), col("b2"), None, OP.is_equal, None, 128, ["t3b", "c.b2"], ["KX%d" % q])
-        tt(c("KX%d" % q), c("KX%d" % q), c("t5", 0, 128), OP.mult, 128, ["KX%d" % q, "t5"], ["KX%d" % q])
+    cts("e1", "p", 1.0, "e0", OP.add, OP.add)
+    eq("LS", "t0", "e1")
+    mset(c("CT", 0, 128), 2048.0, 128, ["CT"]); mset(c("CT", 128, 256), -6144.0, 128, ["CT"])
+    mset(c("NH"), -0.5, 128, ["NH"])
+    mset(c("C2", 0, 8), 0.0, 8, ["C2"]); mset(c("C2", 8, 16), 16.0, 8, ["C2"])
+    cts("sp", "pm", 5120.0, None, OP.add, None)
+    ts(c("t5"), c("t0", 0, 128), col("sp"), 0.25, OP.add, OP.mult, 128, ["t0", "c.sp"], ["t5"])
+    tt(c("TR"), c("t5"), c("rst"), OP.mult, 128, ["t5", "rst"], ["TR"])
 
-    X, S, Ku, Kf, z, Lh, at, ai = T.X, T.S, T.Ku, T.Kf, T.z, T.Lh, T.at, T.ai
-    mset(at[:, 0:8], 0.0, 8, ["atot"])
-    mset(at[:, 8:16], 16.0, 8, ["athr"])
+    X, S, Ku, Kf, z, at, ai, AR = T.X, T.S, T.Ku, T.Kf, T.z, T.at, T.ai, T.AR
+    mset(AR[0:8, :], 0.0, 128, ["AR"])
+    mset(ai[0:8, 0:1], 0, 1, ["ai0"], rate=1.0)
 
     def zwin(h, rnd, j, n=1):
         o = 3072 + 384 * (rnd % 2) + 128 * (3 - n - j)
@@ -275,7 +293,7 @@ def build_ops(T, others=(1, 2, 3)):
         return T["wb%d" % h][:, o:o + 128 * n]
 
     def kwin(h, rnd, j, n=1):
-        o = 2432 + 384 * (rnd % 2) + 128 * (3 - n - j)
+        o = 1408 + 384 * (rnd % 2) + 128 * (3 - n - j)
         return T["wf%d" % h][:, o:o + 128 * n]
 
     def skeys(h, rnd):
@@ -284,32 +302,33 @@ def build_ops(T, others=(1, 2, 3)):
     for h in range(2):
         L = slice(128 * h, 128 * h + 128)
         zk, lk, kk_ = skeys(h, 0)
+        mset(T["wb%d" % h][:, 1216:1520], 0.0, 304, ["kd%d" % h, "ks%d" % h])
         cp(Ku[:, L], T.Ki[:, L], 128, ["in0"], ["Ku%d" % h])
-        cp(kwin(h, 0, 1), T.Ki[:, L], 128, ["in0"], [kk_])
-        cp(zwin(h, 0, 0), z[:, L], 128, ["in0", "z%d" % h], [zk], rate=0.5)
+        ts(kwin(h, 0, 1), T.Ki[:, L], -2048.0, None, OP.add, None, 128, ["in0"], [kk_])
+        cp(zwin(h, 0, 0), z[:, L], 128, ["in0", "z%d" % h], [zk], rate=0.5, flex=True)
         cp(T.Lb[0:8, L], T.Li[0:8, L], 128, ["in0"], ["Lb%d" % h])
         m = T["ps%d" % (6 + h)]
         pe([(m[:, 0:128], c("EXb", 0, 128, 0, 8), T.Lb[0:8, L], True, True, 128, 128, 0)], ["EXb", "Lb%d" % h], ["m0%d" % h], [6 + h])
         ts(lwin(h, 0, 0), m[:, 0:128], col("pm"), None, OP.is_equal, None, 128, ["m0%d" % h, "c.pm"], [lk], [6 + h])
-        cp(lwin(h, 0, 1), lwin(h, 0, 0), 128, [lk], [lk + "b"], rate=0.5)
-    cp(S[:, W:W + A], T.Si[:, :], A, ["in2", "Spad"], ["S"])
+        cp(lwin(h, 0, 1), lwin(h, 0, 0), 128, [lk], [lk + "b"], rate=0.5, flex=True)
+    cp(S[:, W:W + A], T.Si[:, :], A, ["in2"], ["S"])
 
     ring = [0, 0]
+    I = c("II", 0, 128)
 
     def names(h):
         return lambda s: "%s%d" % (s, h)
 
     def bufs(h):
-        wb, wf, wi, wu = T["wb%d" % h], T["wf%d" % h], T["wi%d" % h], T["wu%d" % h]
-        return wb, wf, wi, wu
+        return T["wb%d" % h], T["wf%d" % h], T["wi%d" % h], T["wu%d" % h], T["wh%d" % h]
 
-    def sub_chunk(h, src, skeys, base, ch, lz, rz, zkeys):
+    def sub_chunk(h, src, skeys, base, ch, lx, lz, rz, zkeys):
         s = session(h)
         mms = []
         for kk in range(4):
-            mms.append((sap(s, 128 * kk, 128 * kk + 128), c("II", 0, 128), src[:, base + 4 * ch + kk:base + 2048:16], True, False, 128, 128, 0))
+            mms.append((sap(s, 128 * kk, 128 * kk + 128), lx, src[:, base + 4 * ch + kk:base + 2048:16], True, False, 128, 128, 0))
             mms.append((sap(s, 128 * kk, 128 * kk + 128), lz, rz, False, True, 128, 128, 0))
-        pe(mms, ["II", "nII"] + skeys + zkeys, ["sl%d" % s["id"]], [s])
+        pe(mms, ["II", "nII", "sI", "nsI"] + skeys + zkeys, ["sl%d" % s["id"]], [s])
         return s, "sl%d" % s["id"]
 
     def ringbuf(h):
@@ -317,28 +336,33 @@ def build_ops(T, others=(1, 2, 3)):
         ring[h] = (r + 1) % NRING
         return r
 
-    def gather(out, win, off, n, reads, writes, flex=True):
-        cp(out, win.indirect(off), n, reads, writes, rate=GAM, flex=flex)
+    def gather(out, win, off, n, reads, writes, flex=True, plus=None):
+        if plus is None:
+            cp(out, win.indirect(off), n, reads, writes, rate=GAM, flex=flex)
+        else:
+            ts(out, win.indirect(off), plus, None, OP.add, None, n, reads, writes, rate=GAM, act=(AF.Identity, plus, 1.0) if flex else None)
         ops[-1]["ng"] = n * CYC
 
-    def perm(h, out, wide, src, back, f):
+    def perm(h, out, wide, src, back):
         mms = []
         for cl in range(3):
             o = (cl - 128 * h) % 3
             s = 32 * (cl + 1) if back else 128 - 32 * (cl + 1)
-            mms.append((out(o), wide(s), src(o), True, True, 43, 128, f))
+            mms.append((out(o), wide(s), src(o), 43, 0))
         return mms
+
+    def singles(mms):
+        return [mm for x in mms for mm in group([x])]
 
     def stage_a(h, rnd):
         bias[0] = BIAS[0] * (1 - h)
         k = names(h)
-        wb, wf, wi, wu = bufs(h)
+        wb, wf, wi, wu, wh = bufs(h)
         xg, acc, m = T["xg%d" % h], T["ps%d" % (4 + h)], T["ps%d" % (6 + h)]
         ab, mb = [4 + h], [6 + h]
-        L = slice(128 * h, 128 * h + 128)
         l0 = 128 * h
-        for q in range(2):
-            gather(xg[:, 1024 * q:1024 * q + 1024], X[:, 0:W], Ku[:, l0 + 64 * q:l0 + 64 * q + 64], 1024, ["X", "in1", k("Ku")], [k("xg%d" % q)])
+        for j in range(2):
+            gather(xg[:, 1024 * j:1024 * j + 1024], X[:, 0:W], Ku[:, l0 + 64 * j:l0 + 64 * j + 64], 1024, ["X", "in1", k("Ku")], [k("xg%d" % j)])
         allm = [k("m0"), k("m1"), k("m2"), k("m3")]
         zk, lk, kk_ = skeys(h, rnd)
         zc, lc = zwin(h, rnd, 0), lwin(h, rnd, 0)
@@ -347,7 +371,7 @@ def build_ops(T, others=(1, 2, 3)):
         pe([(acc[:, 0:128], lc, c("CH", 0, 128), True, False, 128, 128, 0),
             (m[:, 0:128], lc, c("CH", 128, 256), True, False, 128, 128, 0)], [lk, "CH"], [k("acc")] + allm, ab + mb)
         for ch in range(4):
-            s, sl = sub_chunk(h, xg, [k("xg0"), k("xg1")], 0, ch, c("nII", 0, 128), zc, [zk])
+            s, sl = sub_chunk(h, xg, [k("xg0"), k("xg1")], 0, ch, I, c("nII", 0, 128), zc, [zk])
             r = ringbuf(h)
             u, v = T["ur%d" % h][:, 512 * r:512 * r + 512], T["vr%d" % h][:, 512 * r:512 * r + 512]
             act(u, sap(s), AF.Abs, 512, [sl], [k("u%d" % r)], [s])
@@ -360,241 +384,230 @@ def build_ops(T, others=(1, 2, 3)):
             pe(mu + mv, [k("u%d" % r), k("v%d" % r), "Wd", "Ww", k("acc")], [k("acc")] + allm, ab + mb)
         bias[0] = BIAS[1] * (1 - h) + BIAS[11]
         act(wb[:, 0:128], m[:, 0:128], AF.Sign, 128, [k("m0")], [k("sg")], mb, bias=0.5)
-        pe([(acc[:, 0:128], c("I22"), wb[:, 0:128], False, True, 128, 128, 0)], [k("sg"), "I22", k("acc")], [k("acc")], ab)
-        scan(wf[:, 0:128], c("hold", 0, 128), acc[:, 0:128], OP.mult, OP.min, 128, [k("acc"), "hold"], [k("s1")], ab)
-        o = C["holdr"][1]
-        scan(acc[:, 383:255:-1], T.CF[:, o + 127:o - 1:-1], wf[:, 127::-1], OP.mult, OP.min, 128, [k("s1"), "holdr"], [k("acc")], ab)
-        tt(wf[:, 512:640], acc[:, 256:384], c("MM", 0, 128), OP.mult, 128, [k("acc"), "MM"], [k("s3")], ab)
-        pe([(m[:, 0:8], wf[:, 512:640], c("B8f", 0, 8), True, False, 8, 128, 1),
-            (m[:, 0:8], c("MM16"), c("B8"), False, True, 8, 128, 0)], [k("s3"), "B8f", "B8", "MM16"], [k("m0")], mb)
-        cp(wi[:, 0:8], m[:, 0:8], 8, [k("m0")], [k("i0")], mb)
-        ts(wi[:, 8:16], wi[:, 0:8], 2047, None, OP.bitwise_and, None, 8, [k("i0")], [k("i1")])
-        cp(wu[:, 0:8], wi[:, 8:16], 8, [k("i1")], [k("ou")])
+        pe([(acc[:, 0:128], c("I16"), wb[:, 0:128], False, True, 128, 128, 0)], [k("sg"), "I16", k("acc")], [k("acc")], ab)
+        scan(wi[:, 0:128], c("hold", 0, 128), acc[:, 0:128], OP.mult, OP.min, 128, [k("acc"), "hold"], [k("s0")], ab)
+        ts(wi[:, 128:136], wi[:, 15:128:16], 15, None, OP.bitwise_and, None, 8, [k("s0")], [k("i0")])
+        cp(wb[:, 1216:1344:16], wi[:, 128:136], 8, [k("i0")], [k("kd")])
+        scan(wb[:, 1376:1504], c("HP"), wb[:, 1216:1344], OP.mult, OP.add, 128, [k("kd"), "HP"], [k("ks")], rate=0.5)
+        b8 = c("B8", 0, 8)
+        pe(group([(m[:, 0:8], c("MM16"), b8, 8, 0), (m[:, 0:8], wb[:, 1217:1345], b8, 8, 0),
+                  (m[:, 0:8], wb[:, 1376:1504], b8, 8, 0), (m[:, 0:8], wb[:, 1377:1505], c("nB8"), 8, 0)]),
+           [k("ks"), k("kd"), "B8", "nB8", "MM16"], [k("m0")], mb)
+        cp(wu[:, 0:8], m[:, 0:8], 8, [k("m0")], [k("ou")], mb)
         tt(wb[:, 128:256], xg[:, 0:2048].indirect(wu[:, 0:8]), zc, OP.subtract, 128, [k("xg0"), k("xg1"), k("ou"), zk], [k("as")], rate=GAM)
         act(wb[:, 256:384], wb[:, 128:256], AF.Abs, 128, [k("as")], [k("D")])
         z0 = 3072 + 384 * (rnd % 2) + 256
-        mms = [(m[:, 0:256], c("II", 0, 128), c("MK"), True, False, 256, 128, 0)]
+        mms = [(m[:, 0:256], I, c("MK"), 256, 0)]
         for wt, o0, sh in (("W4", 0, 0), ("W21h", 128, 96), ("W21l", 128, 96)):
-            for mm in perm(h, lambda o: m[:, o0 + o:o0 + 128:3], lambda s: c(wt, (s + sh) % 128, (s + sh) % 128 + 128),
-                           lambda o: wb[:, 256 + o:384:3], False, 0):
-                mms.append(mm[:3] + (False, len(mms) == 9) + mm[5:])
-        pe(mms, ["II", "MK", "W4", "W21h", "W21l", k("D")], [k("m0"), k("m1")], mb)
-        pe(perm(h, lambda o: acc[:, 256 + o:384:3], lambda s: c("II", s, s + 128), lambda o: wb[:, z0 + o:z0 + 128:3], False, 0)
-           + perm(h, lambda o: acc[:, 384 + o:512:3], lambda s: c("II", s, s + 128), lambda o: wb[:, 256 + o:384:3], False, 0),
+            mms += perm(h, lambda o: m[:, o0 + o:o0 + 128:3], lambda s: c(wt, (s + sh) % 128, (s + sh) % 128 + 128),
+                        lambda o: wb[:, 256 + o:384:3], False)
+        pe(group(mms), ["II", "MK", "W4", "W21h", "W21l", k("D")], [k("m0"), k("m1")], mb)
+        pe(singles(perm(h, lambda o: acc[:, 256 + o:384:3], lambda s: c("II", s, s + 128), lambda o: wb[:, z0 + o:z0 + 128:3], False)
+                   + perm(h, lambda o: acc[:, 384 + o:512:3], lambda s: c("II", s, s + 128), lambda o: wb[:, 256 + o:384:3], False)),
            ["II", zk, k("D")], [k("acc")], ab)
         cp(wb[:, 384:640], acc[:, 256:512], 256, [k("acc")], [k("zD")], ab, flex=True)
-        DB = wb[:, 512:640]
         scan(wi[:, 640:896], c("hold"), m[:, 0:256], OP.mult, OP.max, 256, [k("m0"), k("m1"), "hold"], [k("r1")], mb)
-        ts(wi[:, 32:48], wi[:, 655:896:16], 2, 1023, OP.arith_shift_right, OP.bitwise_and, 16, [k("r1")], [k("i3")])
-        cp(wu[:, 8:24], wi[:, 32:48], 16, [k("i3")], [k("cu")])
+        ts(wi[:, 136:152], wi[:, 655:896:16], 2, 1023, OP.arith_shift_right, OP.bitwise_and, 16, [k("r1")], [k("i3")])
+        cp(wu[:, 8:24], wi[:, 136:152], 16, [k("i3")], [k("cu")])
         gather(wu[:, 64:320], S[:, W:W + A], wu[:, 8:24], 256, ["S", k("cu")], [k("Pu")], flex=False)
-        gather(wf[:, 896:1152], S[:, W:W + A], wu[:, 8:24], 256, ["S", k("cu"), k("Pu")], [k("Pf")])
-        ops[-1]["alts"]["V"] = (vc(256), lambda g: g.vector.tensor_copy(wf[:, 896:1152], wu[:, 64:320]))
-        ops[-1]["ng"] = 0.0
-        pe([(m[:, 256:264], DB, c("WV8"), True, True, 8, 128, 0),
-            (m[:, 384:512], c("WV"), wb[:, 256:384], True, False, 128, 128, 0),
-            (m[:, 384:512], c("I20"), kwin(h, rnd, 1), False, True, 128, 128, 1)],
-           ["WV8", "WV", "I20", k("zD"), k("D"), kk_], [k("m2"), k("m3")], mb)
-        cp(wi[:, 48:56], m[:, 256:264], 8, [k("m2")], [k("i4")], mb)
-        ts(wi[:, 56:64], wi[:, 48:56], 1023, None, OP.bitwise_and, None, 8, [k("i4")], [k("i5")])
-        ts(wf[:, 1152:1160], wi[:, 56:64], col("n1024"), None, OP.add, None, 8, [k("i5"), "c.n1024"], [k("kc")])
-        cp(wi[:, 128:256], m[:, 384:512], 128, [k("m3")], [k("k1")], mb)
-        ts(wi[:, 256:384], wi[:, 128:256], 2, 4095, OP.arith_shift_right, OP.bitwise_and, 128, [k("k1")], [k("k2")])
-        cp(kwin(h, rnd, 0), wi[:, 256:384], 128, [k("k2")], [k("K5")])
-        ts(wi[:, 384:512], wb[:, 128:256], 0.5, -0.25, OP.mult, OP.add, 128, [k("as")], [k("hfi")])
-        tt(zwin(h, rnd, 1), wi[:, 384:512], zc, OP.add, 128, [k("hfi"), zk], [k("zf")])
-        pe(perm(h, lambda o: m[:, 384 + o:512:3], lambda s: c("IIf", s, s + 128), lambda o: wf[:, 896 + o:1024:3], True, 1),
-           ["IIf", k("Pf")], [k("m3")], mb)
-        tt(wf[:, 1664:1792], m[:, 384:512], kwin(h, rnd, 1), OP.subtract, 128, [k("m3"), kk_], [k("d2")], mb)
-        if NV[h]:
-            cp(wb[:, 1536:1664], DB, 128, [k("zD")], [k("D4")], rate=0.5, flex=True)
-            cp(wb[:, 1664:1792], DB, 128, [k("zD")], [k("D4")], rate=0.5, flex=True)
-            cp(wb[:, 1792:2048], wb[:, 1536:1792], 256, [k("D4")], [k("D4")], rate=0.5, flex=True)
+        ts(wh[:, 0:256], wu[:, 64:320], -2048.0, None, OP.add, None, 256, [k("Pu")], [k("Pc")], rate=0.5)
+        pe(group([(m[:, 384:512], c("WV"), wb[:, 256:384], 128, 0), (m[:, 384:512], c("I20"), kwin(h, rnd, 1), 128, 1)]),
+           ["WV", "I20", k("D"), kk_], [k("m3")], mb)
+        ts(wi[:, 256:384], m[:, 384:512], 40960.0, None, OP.add, None, 128, [k("m3")], [k("k1")], mb)
+        ts(wi[:, 384:512], wi[:, 256:384], 2, 4095, OP.arith_shift_right, OP.bitwise_and, 128, [k("k1")], [k("k2")])
+        ts(kwin(h, rnd, 0), wi[:, 384:512], -2048.0, None, OP.add, None, 128, [k("k2")], [k("K5")])
+        pe(group([(m[:, 256:384], c("IH"), c("NH"), 128, 0), (m[:, 256:384], I, zc, 128, 0), (m[:, 256:384], c("IH"), wb[:, 128:256], 128, 0)]),
+           ["IH", "NH", "II", zk, k("as")], [k("m2")], mb)
+        ts(zwin(h, rnd, 1), m[:, 256:384], MAGIC, -MAGIC, OP.add, OP.add, 128, [k("m2")], [k("zf")], mb)
+        pe(singles(perm(h, lambda o: m[:, 384 + o:512:3], lambda s: c("IIh", s, s + 128), lambda o: wh[:, o:128:3], True)),
+           ["IIh", k("Pc")], [k("m3")], mb)
+        tt(wf[:, 896:1024], m[:, 384:512], kwin(h, rnd, 1), OP.subtract, 128, [k("m3"), kk_], [k("d2")], mb)
 
     def stage_c(h, rnd):
+        last = rnd == RO - 1
         bias[0] = BIAS[2] * (1 - h)
         k = names(h)
-        wb, wf, wi, wu = bufs(h)
+        wb, wf, wi, wu, wh = bufs(h)
         yg, acc, m = T["yg%d" % h], T["ps%d" % (4 + h)], T["ps%d" % (6 + h)]
         ab, mb = [4 + h], [6 + h]
-        L = slice(128 * h, 128 * h + 128)
-        l0 = 128 * h
         zB, DB = wb[:, 384:512], wb[:, 512:640]
-        for q in range(4):
-            gather(yg[:, 1024 * q:1024 * q + 1024], X[:, 0:W], wu[:, 64 + 64 * q:128 + 64 * q], 1024, ["X", k("Pu")], [k("yg%d" % q)])
-        I = c("II", 0, 128)
-        ho = C["holdr"][1]
+        for j in range(4):
+            gather(yg[:, 1024 * j:1024 * j + 1024], X[:, 0:W], wu[:, 64 + 64 * j:128 + 64 * j], 1024, ["X", k("Pu")], [k("yg%d" % j)])
+        ro = C["rstr"][1]
 
         def best(role):
             a, n = 128 * role, "BC"[role]
-            scan(wf[:, a:a + 128], c("hold", 0, 128), acc[:, a:a + 128], OP.mult, OP.min, 128, [k("acc"), "hold"], [k("s1" + n[:role])], ab)
+            scan(wf[:, a:a + 128], c("rst"), acc[:, a:a + 128], OP.add, OP.min, 128, [k("acc"), "rst"], [k("s1" + n)], ab)
             src = wf[:, 127::-1] if role == 0 else wf[:, 255:127:-1]
-            scan(wf[:, 383 + a:255 + a:-1], T.CF[:, ho + 127:ho - 1:-1], src, OP.mult, OP.min, 128, [k("s1" + n[:role]), "holdr"], [k("s2" + n)])
+            scan(wf[:, 383 + a:255 + a:-1], T.CB[:, ro + 127:ro - 1:-1], src, OP.add, OP.min, 128, [k("s1" + n), "rstr"], [k("s2" + n)])
             tt(wb[:, 640 + a:768 + a], acc[:, a:a + 128], wf[:, 256 + a:384 + a], OP.is_equal, 128, [k("acc"), k("s2" + n)], [k("oh" + n)], ab)
 
         def partner():
             best(0)
-            pe([(m[:, 0:128], wb[:, 640:768], I, True, True, 128, 128, 0)], ["II", k("ohB")], [k("m0")], mb)
-            tt(wf[:, 1792:1920], m[:, 0:128], wf[:, 896:1024], OP.mult, 128, [k("m0"), k("Pf")], [k("pay")], mb)
-            pe([(m[:, 256:384], I, c("MK", 0, 128), True, False, 128, 128, 0),
-                (m[:, 256:384], c("BBf", 0, 128), wf[:, 1792:1920], False, True, 128, 128, 1),
-                (m[:, 128:136], wf[:, 1792:1920], c("B8f", 0, 8), True, True, 8, 128, 1)], ["II", "MK", "BBf", "B8f", k("pay")], [k("m1"), k("m2")], mb)
+            pe(group([(m[:, 0:128], wb[:, 640:768], I, 128, 0)]), ["II", k("ohB")], [k("m0")], mb)
+            tt(wh[:, 256:384], m[:, 0:128], wh[:, 0:128], OP.mult, 128, [k("m0"), k("Pc")], [k("pay")], mb)
+            pe(group([(m[:, 256:384], I, c("MK2"), 128, 0), (m[:, 256:384], c("BBh", 0, 128), wh[:, 256:384], 128, 0)])
+               + group([(m[:, 128:144], c("ONES"), c("C2"), 16, 0), (m[:, 128:136], DB, c("W4V"), 8, 0),
+                        (m[:, 136:144], wh[:, 256:384], c("B8h"), 8, 0)]),
+               ["II", "MK2", "BBh", "B8h", "ONES", "C2", "W4V", k("zD"), k("pay")], [k("m1"), k("m2")], mb)
             scan(wf[:, 640:768], c("hold", 0, 128), m[:, 256:384], OP.mult, OP.max, 128, [k("m2"), "hold"], [k("sc")], mb)
             cp(wu[:, 24:32], wf[:, 655:768:16], 8, [k("sc")], [k("ju")])
             gather(wb[:, 896:1024], X[:, 0:W], wu[:, 24:32], 128, ["X", k("ju")], [k("yj")])
-            ts(wf[:, 1160:1168], m[:, 128:136], col("n5120"), None, OP.add, None, 8, [k("m1"), "c.n5120"], [k("kw")], mb,
-               act=(AF.Identity, col("n5120"), 1.0))
-            pe(perm(h, lambda o: m[:, 256 + o:384:3], lambda s: c("II", s, s + 128), lambda o: wb[:, 896 + o:1024:3], True, 0)
-               + [(m[:, 384:512], I, wb[:, 896:1024], True, False, 128, 128, 0), (m[:, 384:512], I, DB, False, True, 128, 128, 0)],
-               ["II", k("yj"), k("zD")], [k("m2"), k("m3")], mb)
+            cp(wi[:, 152:168], m[:, 128:144], 16, [k("m1")], [k("i4")], mb)
+            ts(wi[:, 168:184], wi[:, 152:168], 4032, None, OP.bitwise_and, None, 16, [k("i4")], [k("hi")])
+            ts(wi[:, 184:200], wi[:, 152:168], 63, None, OP.bitwise_and, None, 16, [k("i4")], [k("lo")])
+            mms = singles(perm(h, lambda o: m[:, 256 + o:384:3], lambda s: c("II", s, s + 128), lambda o: wb[:, 896 + o:1024:3], True))
+            if last:
+                mms += group([(m[:, 384:512], c("IH"), x, 128, 0) for x in (c("NH"), DB, wb[:, 896:1024])])
+            else:
+                mms += group([(m[:, 384:512], I, x, 128, 0) for x in (DB, wb[:, 896:1024])])
+            pe(mms, ["II", "IH", "NH", k("yj"), k("zD")], [k("m2"), k("m3")], mb)
             cp(zwin(h, rnd, 2), m[:, 256:384], 128, [k("m2")], [k("yh")], mb, flex=True)
-            ts(wi[:, 512:640], m[:, 384:512], 0.5, -0.25, OP.mult, OP.add, 128, [k("m3")], [k("nw")], mb)
-            ts(wb[:, 1184:1192], wf[:, 15:128:16], float(32 * TH - 262144), None, OP.is_ge, None, 8, [k("s1")], [k("ge")])
+            if last:
+                ts(T["VA%d" % h][:, 0:128], m[:, 384:512], MAGIC, -MAGIC, OP.add, OP.add, 128, [k("m3")], [k("nw")], mb)
+            else:
+                ts(wi[:, 512:640], m[:, 384:512], 0.5, -0.25, OP.mult, OP.add, 128, [k("m3")], [k("nw")], mb)
 
         for role in range(2):
             if role == 1:
                 bias[0] = BIAS[12] * (1 - h) + BIAS[13]
                 partner()
                 bias[0] = BIAS[2] * (1 - h)
-            pe([(acc[:, 128 * role:128 * role + 128], c("ONES"), c("CR", 0, 128), True, False, 128, 128, 0)], ["ONES", "CR"], [k("acc")], ab)
+            o = acc[:, 128 * role:128 * role + 128]
+            mms = [(o, c("ONES"), c("CR", 128 * role, 128 * role + 128), True, False, 128, 128, 0), (o, DB, c("nBD"), False, False, 128, 128, 0)]
+            if role:
+                mms.append((o, AR[0:8, :], c("EXa", 0, 128, 0, 8), False, False, 128, 128, 0))
+            pe(mms, ["ONES", "CR", "nBD", "EXa", k("zD")] + ["AR"] * role, [k("acc")], ab)
+            sd = session(6 + h)
+            pe(singles([(sap(sd, 128 * kk, 128 * kk + 128), c("II", 96 * role, 96 * role + 128), DB, 128, 0) for kk in range(4)]),
+               ["II", k("zD"), k("yg%d" % (2 * role))], [k("D4")], [sd])
             lz = c("nII", 96 * role, 96 * role + 128)
             for ch in range(4):
-                s, sl = sub_chunk(h, yg, [k("yg%d" % (2 * role)), k("yg%d" % (2 * role + 1))], 2048 * role, ch, lz, zB, [k("zD")])
+                s, sl = sub_chunk(h, yg, [k("yg%d" % (2 * role)), k("yg%d" % (2 * role + 1))], 2048 * role, ch, I, lz, zB, [k("zD")])
                 r = ringbuf(h)
                 u, v = T["ur%d" % h][:, 512 * r:512 * r + 512], T["vr%d" % h][:, 512 * r:512 * r + 512]
-                if role == 0 and ch >= 4 - NV[h]:
-                    act(sap(s), sap(s), AF.Abs, 512, [sl], [sl], [s])
-                    tt(u, sap(s), wb[:, 1536:2048], OP.subtract, 512, [sl, k("D4")], [k("u%d" % r)], [s])
-                    ts(v, u, 0.0, None, OP.max, None, 512, [k("u%d" % r)], [k("v%d" % r)], rate=0.5, act=(AF.Relu, 0.0, 1.0))
-                    mv = []
+                act(u, sap(s), AF.Abs, 512, [sl], [k("u%d" % r)], [s])
+                tt(v, u, sap(sd), OP.max, 512, [k("u%d" % r), k("D4")], [k("v%d" % r)], [sd])
+                mv = []
+                for buf, wt in (("ur", "Wn"), ("vr", "W2")):
                     for kk in range(4):
                         kq = 4 * ch + kk
-                        for buf, wt in (("ur", "W32n"), ("vr", "W64")):
-                            mv.append((acc[:, kq:128:16], T["%s%d" % (buf, h)][:, 512 * r + 128 * kk:512 * r + 128 * kk + 128],
-                                       c(wt), False, kq == 15 and buf == "vr", 8, 128, 0))
-                    pe(mv, [k("u%d" % r), k("v%d" % r), "W32n", "W64", k("acc")], [k("acc")], ab)
-                    continue
-                act(u, sap(s), AF.Abs, 512, [sl], [k("u%d" % r)], [s])
-                mms = [(sap(s), c("II", 0, 128), u, True, False, 512, 128, 0)]
-                for kk in range(4):
-                    mms.append((sap(s, 128 * kk, 128 * kk + 128), lz, DB, False, kk == 3, 128, 128, 0))
-                pe(mms, ["II", "nII", k("zD"), sl, k("u%d" % r)], [sl], [s])
-                act(v, sap(s), AF.Abs, 512, [sl], [k("v%d" % r)], [s])
-                mv = []
-                for kk in range(4):
-                    kq = 4 * ch + kk
-                    mv.append((acc[:, 128 * role + kq:128 * role + 128:16], T["vr%d" % h][:, 512 * r + 128 * kk:512 * r + 128 * kk + 128],
-                               c("W32", 2 * role, 2 * role + 8), False, kq == 15, 8, 128, 0))
-                pe(mv, [k("v%d" % r), "W32", k("acc")], [k("acc")], ab)
+                        mv.append((acc[:, 128 * role + kq:128 * role + 128:16], T["%s%d" % (buf, h)][:, 512 * r + 128 * kk:512 * r + 128 * kk + 128],
+                                   c(wt, 2 * role, 2 * role + 8), False, kq == 15 and buf == "vr", 8, 128, 0))
+                pe(mv, [k("u%d" % r), k("v%d" % r), "Wn", "W2", k("acc")], [k("acc")], ab)
         bias[0] = BIAS[3] * (1 - h) + BIAS[10]
-        tt(wf[:, 1168:1176], wf[:, 15:128:16], at[:, 8:16], OP.add, 8, [k("s1"), "athr"], [k("dt")])
         best(1)
-        tt(wb[:, 1152:1160], wf[:, 143:256:16], wf[:, 1168:1176], OP.is_le, 8, [k("dt"), k("s1C")], [k("hit")])
+        tt(wb[:, 1152:1160], wf[:, 143:256:16], wf[:, 15:128:16], OP.is_le, 8, [k("s1B"), k("s1C")], [k("hit")])
+        tt(wb[:, 1160:1168], wb[:, 1152:1160], wf[:, 15:128:16], OP.is_le, 8, [k("s1B"), k("hit")], [k("nei")])
+        tt(wb[:, 1168:1184], wi[:, 168:184], wb[:, 1152:1168], OP.mult, 16, [k("hit"), k("nei"), k("hi")], [k("kh")])
+        tt(wb[:, 1184:1200], wi[:, 184:200], wb[:, 1152:1168], OP.mult, 16, [k("hit"), k("nei"), k("lo")], [k("kl")])
         bias[0] = BIAS[14]
         pe([(m[32:64, 384:512], wb[:, 768:800], I, True, True, 128, 32, 0),
             (m[64:128, 384:512], wb[:, 800:864], I, True, True, 128, 64, 0),
             (m[0:32, 384:512], wb[:, 864:896], I, True, True, 128, 32, 0)], ["II", k("ohC")], [k("m3")], mb)
-        tt(wf[:, 1920:2048], m[:, 384:512], wf[:, 1024:1152], OP.mult, 128, [k("m3"), k("Pf")], [k("payC")], mb)
-        pe([(m[:, 384:512], c("BBf", 32, 160), wf[:, 1920:2048], True, True, 128, 128, 1)], ["BBf", k("payC")], [k("m3")], mb)
-        tt(wf[:, 2048:2176], m[:, 384:512], wf[:, 896:1024], OP.subtract, 128, [k("m3"), k("Pf")], [k("c1")], mb)
-        tt(wf[:, 2176:2304], m[:, 0:128], wf[:, 2048:2176], OP.mult, 128, [k("m0"), k("c1")], [k("c2")], mb)
-        bias[0] = BIAS[3] * (1 - h) + BIAS[10]
-        tt(wb[:, 1160:1168], wb[:, 1184:1192], wb[:, 1152:1160], OP.is_gt, 8, [k("ge"), k("hit")], [k("nei")])
-        tt(wf[:, 1176:1192], wb[:, 1152:1168], wf[:, 1152:1168], OP.mult, 16, [k("hit"), k("nei"), k("kc"), k("kw")], [k("km")])
-        tt(wf[:, 1200:1208], wf[:, 1176:1184], wf[:, 1184:1192], OP.add, 8, [k("km")], [k("key")])
+        tt(wh[:, 384:512], m[:, 384:512], wh[:, 128:256], OP.mult, 128, [k("m3"), k("Pc")], [k("payC")], mb)
+        pe(group([(m[:, 256:512], I, c("CT"), 256, 0), (m[:, 256:512], wb[:, 640:768], c("PM"), 256, 0),
+                  (m[:, 256:384], c("IIh", 0, 128), wh[:, 0:128], 128, 0), (m[:, 384:512], c("BBh", 32, 160), wh[:, 384:512], 128, 0)]),
+           ["II", "CT", "PM", "IIh", "BBh", k("ohB"), k("Pc"), k("payC")], [k("m2"), k("m3")], mb)
+        if last:
+            cp(wf[:, 1024:1152], m[:, 256:384], 128, [k("m2")], [k("tu")], mb, flex=True)
+            tt(T["VA%d" % h][:, 128:256], m[:, 384:512], wf[:, 1024:1152], OP.max, 128, [k("m3"), k("tu")], [k("nc")], mb)
+            remote("all", [(T["VA%d" % h][:, :], T["mv%d" % h])], k("bv"), 3000.0, [k("nw"), k("nc")], [k("mv")])
+            dma("S", [(T["mv%d" % h][q], T["VA%d" % h][:, :])], k("ov"), 2000.0, [k("nw"), k("nc")], [k("mvo")])
+            dma("S", [(T["VL%d" % h][:, :], T["mv%d" % h][:, rows(q), :])], k("vl"), 2200.0, [k("mv"), k("mvo")], [k("VL")])
+        else:
+            cp(wf[:, 1024:1280], m[:, 256:512], 256, [k("m2"), k("m3")], [k("tu")], mb, flex=True)
 
     def stage_e(h, rnd):
         last = rnd == RO - 1
         zk, lk, kk_ = skeys(h, rnd)
         zn, ln, kn = skeys(h, rnd + 1)
-        bias[0] = BIAS[4] * (1 - h) + BIAS[9]
+        bias[0] = BIAS[5] * (1 - h) + BIAS[6]
         k = names(h)
-        wb, wf, wi, wu = bufs(h)
+        wb, wf, wi, wu, wh = bufs(h)
         xg, acc, m = T["xg%d" % h], T["ps%d" % (4 + h)], T["ps%d" % (6 + h)]
         ab, mb = [4 + h], [6 + h]
         L = slice(128 * h, 128 * h + 128)
-        I = c("II", 0, 128)
-        pe([(m[0:8, 128:256], c("ONES", 0, 8), c("TK"), True, False, 128, 8, 0),
-            (m[0:8, 128:256], wf[:, 1200:1208], c("IIf", 0, 128), False, True, 128, 8, 1)], ["IIf", "ONES", "TK", k("key")], [k("m1")], mb)
-        Rh, Rl = wb[0:8, 4608:4736], wb[0:8, 4736:4864]
-        cp(Rh, m[0:8, 128:256], 128, [k("m1")], [k("Rf")], mb, flex=True)
-        tt(Rl, m[0:8, 128:256], Rh, OP.subtract, 128, [k("m1"), k("Rf")], [k("Rl")], mb)
-        s = session(2 + h)
-        sl = "sl%d" % s["id"]
-        pe([(sap(s, 128 * q, 128 * q + 128), c("KX%d" % q, 0, 128, 0, 8), (Rh, Rl)[j], j == 0, j == 1, 128, 128, 0) for q in range(2) for j in range(2)],
-           ["KX0", "KX1", k("Rf"), k("Rl")], [sl], [s])
-        cp(wi[:, 640:896], sap(s, 0, 256), 256, [sl], [k("r1")], [s])
-        tt(wb[:, 1280:1536], wi[:, 640:896], sap(s, 0, 256), OP.is_gt, 256, [sl, k("r1")], [k("bits")], [s])
-        for q in range(2):
-            s = session(2 + h)
-            sl = "sl%d" % s["id"]
-            onv = q < NE[h]
-            mms = [] if onv else [(sap(s), I, c("TRI"), True, False, 512, 128, 0)]
-            for a in range(4):
-                bt = wb[32 * a:32 * a + 32, 1280 + 128 * q:1408 + 128 * q]
-                mms.append((sap(s, 128 * a, 128 * a + 128), bt, bt, onv, onv or a == 3, 128, 128, 0))
-                pe(mms, ["II", "TRI", k("bits"), sl], [sl], [s])
-                ops[-1]["fence"] = 1
-                mms = []
-            if onv:
-                tt(wb[:, 2048 + 512 * q:2560 + 512 * q], sap(s), c("TRT"), OP.is_gt, 512, [sl, "TRT"], [k("e%d" % q)], [s])
-            else:
-                ts(wb[:, 2048 + 512 * q:2560 + 512 * q], sap(s), -15.0, 0.0, OP.add, OP.max, 512, [sl], [k("e%d" % q)], [s],
-                   act=(AF.Relu, -15.0, 1.0))
-        mms = [(m[:, 128:256], I, c("MKp"), True, False, 128, 128, 0),
-               (m[:, 128:256], c("EXb", 0, 128, 0, 8), Rh, False, False, 128, 128, 0),
-               (m[:, 128:256], c("EXb", 0, 128, 0, 8), Rl, False, False, 128, 128, 0)]
-        for b in range(8):
-            mms.append((m[:, 128:256], c("Z8", 112 - 16 * b, 240 - 16 * b), wb[:, 2048 + 128 * b:2176 + 128 * b], False, b == 7, 128, 128, 0))
-        pe(mms, ["II", "MKp", "EXb", "Z8", k("Rf"), k("Rl"), k("e0"), k("e1")], [k("m1")], mb)
-        scan(wf[:, 640:768], c("TR"), m[:, 128:256], OP.max, OP.min, 128, [k("m1"), "TR"], [k("sc")], mb)
-        cp(wu[:, 32:40], wf[:, 655:768:16], 8, [k("sc")], [k("ku")])
-        bias[0] = BIAS[5] * (1 - h) + BIAS[6]
-        pe([(m[0:16, 256:384], wb[:, 1152:1168], I, True, True, 128, 16, 0)], ["II", k("hit"), k("nei")], [k("m2")], mb)
-        cp(wb[0:16, 1024:1152], m[0:16, 256:384], 128, [k("m2")], [k("Rb")], mb, flex=True)
-        if not last:
-            pe([(m[:, 384:392], c("ONES"), wb[:, 1152:1160], True, True, 8, 128, 0)], ["ONES", k("hit")], [k("m3")], mb)
-            tt(at[:, 0:8], m[:, 384:392], at[:, 0:8], OP.add, 8, [k("m3"), "atot"], ["atot"], mb)
-        mms = [(m[:, 256:384], I, c("MKt"), True, False, 128, 128, 0)]
-        for j, mm in enumerate(perm(h, lambda o: m[:, 256 + o:384:3], lambda s: c("EX0", s, s + 128, 0, 16), lambda o: wb[0:16, 1024 + o:1152:3], True, 0)):
-            mms.append(mm[:3] + (False, j == 2) + mm[5:])
-        pe(mms, ["II", "MKt", "EX0", k("Rb")], [k("m2")], mb)
-        scan(wf[:, 768:896], c("hold", 0, 128), m[:, 256:384], OP.mult, OP.max, 128, [k("m2"), "hold"], [k("sc2")], mb)
+        RT = wb[0:48, 1024:1152]
+        pe([(m[0:48, 128:256], wb[:, 1152:1200], I, True, True, 128, 48, 0)], ["II", k("hit"), k("nei"), k("kh"), k("kl")], [k("m1")], mb)
+        if last:
+            cp(RT, m[0:48, 128:256], 128, [k("m1")], [k("RT")], mb, flex=True)
+        else:
+            add({"A": (vc(128) + 35, lambda g: g.scalar.activation(RT, m[0:48, 128:256], AF.Copy, accum_out=at[0:48, h:h + 1]))},
+                [k("m1")], [k("RT"), k("cnt")], mb)
+        pe(group([(m[:, 0:128], I, c("MKt"), 128, 0)]
+                 + perm(h, lambda o: m[:, o:128:3], lambda s: c("EX0", s, s + 128, 0, 16), lambda o: wb[0:16, 1024 + o:1152:3], True)),
+           ["II", "MKt", "EX0", k("RT")], [k("m0")], mb)
+        scan(wf[:, 768:896], c("hold", 0, 128), m[:, 0:128], OP.mult, OP.max, 128, [k("m0"), "hold"], [k("sc2")], mb)
         cp(wu[:, 40:48], wf[:, 783:896:16], 8, [k("sc2")], [k("su")])
         su = wu[:, 40:48]
         gather(z[:, L] if last else zwin(h, rnd + 1, 0), zwin(h, rnd, 0, 3), su, 128, [k("su"), zk, k("zf"), k("yh")], [k("z") if last else zn])
         gather(lwin(h, rnd + 1, 0), lwin(h, rnd, 0, 3), su, 128, [k("su"), lk, lk + "b", k("dL")], [ln])
         if not last:
             cp(lwin(h, rnd + 1, 1), lwin(h, rnd + 1, 0), 128, [ln], [ln + "b"], rate=0.5, flex=True)
+        bias[0] = BIAS[4] * (1 - h) + BIAS[9]
+        for j in range(2):
+            s = session(2 + h)
+            sl = "sl%d" % s["id"]
+            pe(group([(sap(s), RT, c("nSEL", 512 * j, 512 * j + 512, 0, 48), 512, 0)]
+                     + [(sap(s, 128 * a, 128 * a + 128), c("SEL", 512 * j + 128 * a, 512 * j + 128 * a + 128, 0, 48), RT, 128, 0) for a in range(4)]),
+               ["SEL", "nSEL", k("RT")], [sl], [s])
+            tt(wb[:, 2048 + 512 * j:2560 + 512 * j], sap(s), c("TRT"), OP.is_equal, 512, [sl, "TRT"], [k("e%d" % j)], [s])
+        pe(group([(m[:, 128:256], I, c("MKp"), 128, 0), (m[:, 128:256], c("EXK", 0, 128, 0, 48), RT, 128, 0)]
+                 + [(m[:, 128:256], c("Z8", 112 - 16 * b, 240 - 16 * b), wb[:, 2048 + 128 * b:2176 + 128 * b], 128, 0) for b in range(8)]),
+           ["II", "MKp", "EXK", "Z8", k("RT"), k("e0"), k("e1")], [k("m1")], mb)
+        scan(wf[:, 640:768], c("TR"), m[:, 128:256], OP.max, OP.min, 128, [k("m1"), "TR"], [k("sc")], mb)
+        cp(wu[:, 32:40], wf[:, 655:768:16], 8, [k("sc")], [k("ku")])
         bias[0] = BIAS[7] * (1 - h) + BIAS[8]
         ov = T["ov%d" % h]
         for ch in range(4):
-            s, sl = sub_chunk(4 + h, xg, [k("xg0"), k("xg1")], 0, ch, c("nII", 0, 128), zwin(h, rnd, 2), [k("yh")])
-            act(ov[:, 512 * ch:512 * ch + 512], sap(s), AF.Abs, 512, [sl], [k("ov%d" % ch)], [s])
-            if ch % 2:
-                u = ov[:, 512 * ch - 512:512 * ch + 512]
-                ts(u, u, 48.0, None, OP.is_gt, None, 1024, [k("ov%d" % (ch - 1)), k("ov%d" % ch)], [k("ov%d" % (ch - 1)), k("ov%d" % ch)], rate=0.5)
-                mv = [(acc[:, 0:128], c("THN"), lwin(h, rnd, 0), True, False, 128, 128, 0)] if ch == 1 else []
-                for kq in range(4 * ch - 4, 4 * ch + 4):
-                    mv.append((acc[:, 0:128], c("Zw", 16 - kq, 144 - kq), ov[:, 128 * kq:128 * kq + 128], False, kq == 15, 128, 128, 0))
-                pe(mv, [k("ov%d" % (ch - 1)), k("ov%d" % ch), "Zw", "THN", lk, k("acc")], [k("acc")], ab)
-        ts(acc[:, 0:128], acc[:, 0:128], -0.5, None, OP.is_gt, None, 128, [k("acc")], [k("acc")], ab)
-        tt(acc[:, 0:128], acc[:, 0:128], wf[:, 1664:1792], OP.mult, 128, [k("acc"), k("d2")], [k("acc")], ab)
-        tt(kwin(h, rnd, 2), acc[:, 0:128], kwin(h, rnd, 1), OP.add, 128, [k("acc"), kk_], [k("Kc")], ab)
-        if not last:
-            gather(Ku[:, L], kwin(h, rnd, 0, 3), su, 128, [k("su"), kk_, k("K5"), k("Kc")], [k("Ku")], flex=False)
-        gather(Kf[:, L] if last else kwin(h, rnd + 1, 1), kwin(h, rnd, 0, 3), su, 128, [k("su"), kk_, k("K5"), k("Kc")], [k("Kf") if last else kn])
+            o = ov[:, 512 * ch:512 * ch + 512]
+            if ch < NE[h]:
+                s, sl = sub_chunk(4 + h, xg, [k("xg0"), k("xg1")], 0, ch, I, c("nII", 0, 128), zwin(h, rnd, 2), [k("yh")])
+                act(o, sap(s), AF.Abs, 512, [sl], [k("ov%d" % ch)], [s])
+                ts(o, o, 48.0, None, OP.is_gt, None, 512, [k("ov%d" % ch)], [k("ov%d" % ch)], rate=0.5)
+            else:
+                s, sl = sub_chunk(4 + h, xg, [k("xg0"), k("xg1")], 0, ch, c("sI"), c("nsI"), zwin(h, rnd, 2), [k("yh")])
+                ts(o, sap(s), MAGIC, MAGIC, OP.add, OP.not_equal, 512, [sl], [k("ov%d" % ch)], [s])
+            mv = [(acc[:, 0:128], lwin(h, rnd, 0), c("THN"), True, False, 128, 128, 0)] if ch == 0 else []
+            for kq in range(4 * ch, 4 * ch + 4):
+                mv.append((acc[:, kq:128:16], ov[:, 128 * kq:128 * kq + 128], c("Ww"), False, kq == 15, 8, 128, 0))
+            pe(mv, [k("ov%d" % ch), "Ww", "THN", lk, k("acc")], [k("acc")], ab)
+        ts(wb[:, 1536:1664], acc[:, 0:128], -0.5, None, OP.is_gt, None, 128, [k("acc")], [k("off")], ab)
+        pe(group([(acc[:, 128:256], wb[:, 1536:1664], I, 128, 0)]), ["II", k("off")], [k("acc")], ab)
+        tt(acc[:, 128:256], acc[:, 128:256], wf[:, 896:1024], OP.mult, 128, [k("acc"), k("d2")], [k("acc")], ab)
+        tt(kwin(h, rnd, 2), acc[:, 128:256], kwin(h, rnd, 1), OP.add, 128, [k("acc"), kk_], [k("Kc")], ab)
+        rd = [k("su"), kk_, k("K5"), k("Kc")]
         if last:
-            pe([(m[0:8, 0:128], c("LW"), lwin(h, rnd + 1, 0), True, True, 128, 8, 0)], ["LW", ln], [k("m0")], mb)
-            cp(T.Lo[0:8, L], m[0:8, 0:128], 128, [k("m0")], [k("Lo")], mb, flex=True)
+            gather(Kf[:, L], kwin(h, rnd, 0, 3), su, 128, rd, [k("Kf")], plus=2048.0)
+            remote("all", [(Kf[:, L], T["mk%d" % h])], k("bk"), 2800.0, [k("Kf")], [k("mk")])
+            dma("S", [(T["mk%d" % h][q], Kf[:, L])], k("ok"), 2000.0, [k("Kf")], [k("mko")])
+            dma("S", [(T.yk[:, L], T["mk%d" % h][:, rows(q), :])], k("yk"), 2200.0, [k("mk"), k("mko")], [k("yk")])
+        else:
+            gather(Ku[:, L], kwin(h, rnd, 0, 3), su, 128, rd, [k("Ku")], flex=False, plus=2048.0)
+            gather(kwin(h, rnd + 1, 1), kwin(h, rnd, 0, 3), su, 128, rd, [kn])
 
     def writes(h):
         k = names(h)
-        wb, wf, wi, wu = bufs(h)
-        cp(X[:, 0:WX].indirect(wu[:, 32:40]), wi[:, 512:640], 128, [k("ku"), k("nw"), "Xpad", "X"], ["X"], rate=SCA)
-        tt(S[:, 0:WX].indirect(wu[:, 32:40]), wf[:, 2176:2304], wf[:, 896:1024], OP.add, 128, [k("ku"), k("c2"), k("Pf"), "S"], ["S"], rate=SCA)
+        wb, wf, wi, wu, wh = bufs(h)
+        cp(X[:, 0:WX].indirect(wu[:, 32:40]), wi[:, 512:640], 128, [k("ku"), k("nw"), "X"], ["X"], rate=SCA)
+        tt(S[:, 0:WX].indirect(wu[:, 32:40]), wf[:, 1024:1152], wf[:, 1152:1280], OP.max, 128, [k("ku"), k("tu"), "S"], ["S"], rate=SCA)
         ops[-1]["ns"] = ops[-2]["ns"] = 128 * CYC
 
+    def last_writes(h):
+        k = names(h)
+        wu = T["wu%d" % h]
+        remote("near", [(wu[:, 32:40], [T.LK[:, 32 * h + 8 * r:32 * h + 8 * r + 8] for r in range(N)])], k("bu"), 2500.0, [k("ku")], [k("LK")])
+        for r in range(N):
+            src = wu[rows(q), 32:40] if r == q else T.LK[rows(q), 32 * h + 8 * r:32 * h + 8 * r + 8]
+            cp(T.KU[rows(r), 8 * h:8 * h + 8], src, 8, [k("ku") if r == q else k("LK")], [k("KU%d" % r)])
+        rd = [k("KU%d" % r) for r in range(N)] + [k("VL")]
+        ku = T.KU[:, 8 * h:8 * h + 8]
+        cp(T.NX[:, 0:WX].indirect(ku), T["VL%d" % h][:, 0:128], 128, rd + ["NX", "NXo"], ["NX"], rate=SCA)
+        cp(T.NS[:, 0:WX].indirect(ku), T["VL%d" % h][:, 128:256], 128, rd + ["NS", "NSo"], ["NS"], rate=SCA)
+        ops[-1]["ns"] = ops[-2]["ns"] = 128 * CYC
+
+    SA = slice(W, W + A)
     for rnd in range(RO):
         last = rnd == RO - 1
         for j, stage in enumerate((stage_a, stage_c, stage_e)):
@@ -603,26 +616,48 @@ def build_ops(T, others=(1, 2, 3)):
                 stage(h, rnd)
         base[0] = len(ops) - 600
         bias[0] = 0.0
-        writes(0); writes(1)
         if not last:
-            cp(ai[:, 0:8], at[:, 0:8], 8, ["atot"], ["ai0"])
-            ts(ai[:, 8:16], ai[:, 0:8], 31, None, OP.bitwise_and, None, 8, ["ai0"], ["ai1"])
-            ts(at[:, 8:16], ai[:, 8:16], 32.0, 16.0, OP.mult, OP.add, 8, ["ai1"], ["athr"])
-    for r in others:
-        bias[0] = -3000.0 * others.index(r)
-        for cq in range(4):
-            cp(T.OX[32 * cq:32 * cq + 32, 1024 * r:1024 * r + 1024], X[32 * r:32 * r + 32, 1024 * cq:1024 * cq + 1024], 1024,
-               ["X"], ["OX%d%d" % (r, cq)], rate=0.5, flex=True)
-        for cq in range(4):
-            cp(T.OS[32 * cq:32 * cq + 32, 256 * r:256 * r + 256], S[32 * r:32 * r + 32, W + 256 * cq:W + 256 * cq + 256], 256,
-               ["S"], ["OS%d%d" % (r, cq)], flex=True)
+            writes(0); writes(1)
+            ts(ai[0:8, 1:2], ai[0:8, 0:1], at[0:8, 0:1], at[0:8, 1:2], OP.add, OP.add, 1, ["ai0", "cnt0", "cnt1"], ["ai1"])
+            ts(ai[0:8, 0:1], ai[0:8, 1:2], 31, None, OP.bitwise_and, None, 1, ["ai1"], ["ai0"])
+            cp(at[0:8, 2:3], ai[0:8, 0:1], 1, ["ai0"], ["af"])
+            ts(AR[0:8, :], c("ONES", 0, 128, 0, 8), at[0:8, 2:3], None, OP.mult, None, 128, ["ONES", "af"], ["AR"], rate=0.5)
+        if rnd == RO - 2:
+            base[0] = len(ops) - 620
+            dma("S", [(T.ox[:, :, :], X[:, 0:W])], "ox", 6000.0, ["X"], ["ox"])
+            dma("S", [(T.oa[:, :, :], S[:, SA])], "oa", 4000.0, ["S"], ["oa"])
+            remote("each", [(T.ox, T.mx)], "bx", 6000.0, ["ox"], ["mx"])
+            remote("each", [(T.oa, T.ma)], "ba", 4000.0, ["oa"], ["ma"])
+            dma("S", [(T.NX[rows(q), 0:W], T.ox[q])], "nxo", 3000.0, ["ox"], ["NXo"])
+            dma("S", [(T.NS[rows(q), SA], T.oa[q])], "nso", 3000.0, ["oa"], ["NSo"])
+            dma("S", [(T.NX[rows(r), 0:W], T.mx[r]) for r in others], "nx", 5000.0, ["mx"], ["NX"])
+            dma("S", [(T.NS[rows(r), SA], T.ma[r]) for r in others], "ns", 4000.0, ["ma"], ["NS"])
+    base[0] = len(ops) - 640
+    bias[0] = -20000.0
+    ts(c("t6"), c("t2", 0, 128), 8.0, col("pm"), OP.is_lt, OP.mult, 128, ["t2", "c.pm", "HP"], ["t6"], rate=0.5)
+    tt(c("LWa"), c("t6"), c("BB", 0, 128), OP.mult, 128, ["t6", "BB"], ["LWa"])
+    ts(c("t6"), c("t2", 0, 128), 8.0, col("pm"), OP.is_ge, OP.mult, 128, ["t2", "c.pm"], ["t6"], rate=0.5)
+    tt(c("LWb"), c("t6"), c("BB", 0, 128), OP.mult, 128, ["t6", "BB"], ["LWb"])
+    bias[0] = 0.0
+    m = T.ps7
+    pe(group([(m[:, 0:128], c("LWa"), lwin(0, RO, 0), 128, 0), (m[:, 0:128], c("LWb"), lwin(1, RO, 0), 128, 0)]),
+       ["LWa", "LWb", skeys(0, RO)[1], skeys(1, RO)[1]], ["m01"], [7])
+    cp(T.Lo[:, :], m[:, 0:128], 128, ["m01"], ["Lo"], [7], flex=True)
+    remote("two", [(z[:, :], T.mz), (T.Lo[:, :], T.ml)], "zl", 2800.0, ["z0", "z1", "Lo"], ["mz"])
+    dma("S", [(T.mz[q], z[:, :]), (T.ml[q], T.Lo[:, :])], "zlo", 2000.0, ["z0", "z1", "Lo"], ["mzo"])
+    dma("S", [(T.yz[:, :], T.mz[:, rows(q), :])], "yz", 2200.0, ["mz", "mzo"], ["yz"])
+    dma("S", [(T.yl[:, :], T.ml[:, 32 * q:32 * q + 32:8, :])], "yl", 2200.0, ["mz", "mzo"], ["yl"])
+    last_writes(0); last_writes(1)
+    dma("S", [(T.yx[:, :], T.NX[:, 0:W])], "yx", 6000.0, ["NX", "NXo"], ["yx"])
+    dma("A", [(T.ya[:, :], T.NS[:, SA])], "ya", 5000.0, ["NS", "NSo"], ["ya"])
     return ops
 
 
 READY = {"in0": 10000.0, "in1": 13000.0, "in2": 16000.0}
+ENG = ("P", "V", "A", "G", "S")
 
 
-def schedule(ops):
+def links(ops):
     n = len(ops)
     deps = [set() for _ in range(n)]
     lastw, readers = {}, {}
@@ -640,59 +675,81 @@ def schedule(ops):
             lastw[key] = i
             readers[key] = []
         deps[i].discard(i)
-    first = {}
-    for o in ops:
-        for b in o["b"]:
-            if isinstance(b, dict):
-                b["bank"], b["left"] = None, 0
+    first, seen = {}, set()
     for i, o in enumerate(ops):
         for b in o["b"]:
-            if isinstance(b, dict):
-                if b["left"] == 0:
-                    if b["h"] in first and first[b["h"]] not in deps[i]:
-                        deps[i].add(first[b["h"]])
-                    first[b["h"]] = i
-                b["left"] += 1
+            if isinstance(b, dict) and b["id"] not in seen:
+                seen.add(b["id"])
+                if b["h"] in first:
+                    deps[i].add(first[b["h"]])
+                first[b["h"]] = i
     succ = [[] for _ in range(n)]
     for i in range(n):
         for d in deps[i]:
             succ[d].append(i)
     prio = [0.0] * n
     for i in range(n - 1, -1, -1):
-        prio[i] = min(a[0] for a in ops[i]["alts"].values()) + LAT + max([prio[s] for s in succ[i]], default=0.0)
+        prio[i] = min(a[0] for a in ops[i]["alts"].values()) + ops[i].get("lat", LAT) + max([prio[s] for s in succ[i]], default=0.0)
+    for o in ops:
+        o["in"] = max([READY.get(key, 0.0) for key in o["r"]], default=0.0)
+        if "late" in o:
+            o["in"] = 9000.0
+    return deps, succ, prio
+
+
+def schedule(ops, lk):
+    n = len(ops)
+    deps, succ = [set(d) for d in lk[0]], lk[1]
+    for o in ops:
+        for b in o["b"]:
+            if isinstance(b, dict):
+                b["bank"], b["left"] = None, 0
+    for o in ops:
+        for b in o["b"]:
+            if isinstance(b, dict):
+                b["left"] += 1
     left = [len(deps[i]) for i in range(n)]
     ready = [i for i in range(n) if left[i] == 0]
-    dready = [max([READY.get(key, 0.0) for key in ops[i]["r"]], default=0.0) for i in range(n)]
-    efree = {"P": 0.0, "V": 0.0, "A": 0.0, "G": 0.0}
+    dready = [o["in"] for o in ops]
+    efree = {e: 0.0 for e in ENG}
     bfree, blast = [0.0] * 8, [None] * 8
     eng, end, order = [None] * n, [0.0] * n, []
     held = [False] * 4
-    for i in range(n):
-        prio[i] += ops[i]["bias"] + 500.0 * NUDGE.get(ops[i]["pos"], 0)
+    prio = [lk[2][i] + ops[i]["bias"] + 500.0 * NUDGE.get(ops[i]["pos"], 0) for i in range(n)]
     while ready:
         best = None
         cand = []
-        free = sorted([b for b in range(4) if not held[b]], key=lambda b: bfree[b])
+        t0 = 1e18
+        free = None
+        for b in range(4):
+            if not held[b] and (free is None or bfree[b] < bfree[free]):
+                free = b
         for i in ready:
+            dr = dready[i]
+            if dr > t0 + WIN:
+                continue
             o = ops[i]
             banks = []
             for b in o["b"]:
                 if isinstance(b, dict):
-                    b = b["bank"] if b["bank"] is not None else (free[0] if free else None)
+                    b = b["bank"] if b["bank"] is not None else free
                 banks.append(b)
             if None in banks:
                 continue
             pick = None
             for e, (cost, _) in o["alts"].items():
-                st = max(efree[e], dready[i])
+                st = efree[e] if efree[e] > dr else dr
                 for b in banks:
                     if blast[b] is not None:
-                        st = max(st, bfree[b] + (LAT if eng[blast[b]] != e else 0.0))
+                        t = bfree[b] + (LAT if eng[blast[b]] != e else 0.0)
+                        if t > st:
+                            st = t
                 val = st + cost + (VPEN + 400.0 * LEAN.get(o["pos"], 0) if e == "V" else 0.0)
                 if pick is None or val < pick[3]:
                     pick = (st, e, cost, val)
+            if pick[0] < t0:
+                t0 = pick[0]
             cand.append((pick[0], i, pick[1], pick[2], banks))
-        t0 = min(x[0] for x in cand)
         for x in cand:
             if x[0] <= t0 + WIN and (best is None or prio[x[1]] > prio[best[1]]):
                 best = x
@@ -709,44 +766,47 @@ def schedule(ops):
                 deps[i].add(blast[b])
             blast[b], bfree[b] = i, end[i]
         order.append(i)
+        done = end[i] + ops[i].get("lat", LAT)
         for s in succ[i]:
             left[s] -= 1
-            dready[s] = max(dready[s], end[i] + LAT)
+            if done > dready[s]:
+                dready[s] = done
             if left[s] == 0:
                 ready.append(s)
-    return order, eng, deps, end, lastw
+    return order, eng, deps, end
 
 
-SPREAD = [(1.5, 3.8, 60.0, 1.0), (1.04, 1.6, 40.0, 1.0), (2.08, 6.0, 60.0, 1.0), (1.9, 5.0, 120.0, 1.0)]
+SPREAD = [(1.5, 3.8, 60.0), (1.04, 1.6, 40.0), (2.08, 6.0, 60.0), (1.9, 5.0, 120.0)]
 TUNED = []
 
 
-def span(ops):
-    order, eng, deps, end, lastw = schedule(ops)
+def span(ops, lk):
+    order, eng, deps, end = schedule(ops, lk)
     tot = 0.0
-    for gam, sca, lat, f in SPREAD:
-        fin, free = [0.0] * len(ops), {"P": 0.0, "V": 0.0, "A": 0.0, "G": 0.0}
+    for gam, sca, lat in SPREAD:
+        fin, free, most = [0.0] * len(ops), {e: 0.0 for e in ENG}, 0.0
         for i in order:
             o, e = ops[i], eng[i]
             st = free[e]
             if o["in"] > st:
                 st = o["in"]
             for d in deps[i]:
-                t = fin[d] + (0.0 if e == "P" and eng[d] == "P" and "fence" not in o else lat)
+                t = fin[d] + (0.0 if e == "P" and eng[d] == "P" else lat)
                 if t > st:
                     st = t
-            fin[i] = free[e] = st + f * (o["alts"][e][0] + o.get("ng", 0) * (gam - GAM) + o.get("ns", 0) * (sca - SCA))
-        tot += max(fin) / f
+            free[e] = st + o["alts"][e][0] + o.get("ng", 0) * (gam - GAM) + o.get("ns", 0) * (sca - SCA)
+            fin[i] = free[e] + o.get("lat", 0.0)
+            if fin[i] > most:
+                most = fin[i]
+        tot += most
     return tot / len(SPREAD)
 
 
-def tune(ops, steps):
+def tune(ops, lk, steps):
     rng = np.random.RandomState(7)
-    for o in ops:
-        o["in"] = max([READY.get(key, 0.0) for key in o["r"]], default=0.0)
     poss = sorted({o["pos"] for o in ops if o["pos"] >= 0})
     flex = sorted({o["pos"] for o in ops if o["pos"] >= 0 and len(o["alts"]) > 1})
-    best = span(ops)
+    best = span(ops, lk)
     for _ in range(steps):
         keep = (dict(NUDGE), dict(LEAN))
         if rng.rand() < 0.65:
@@ -755,7 +815,7 @@ def tune(ops, steps):
                 NUDGE[j] = NUDGE.get(j, 0) + d
         else:
             LEAN[flex[rng.randint(len(flex))]] = (-4, -2, 0, 2, 4)[rng.randint(5)]
-        s = span(ops)
+        s = span(ops, lk)
         if s <= best:
             best = s
         else:
@@ -770,58 +830,72 @@ def rank_program(g, core, T, topo):
     sem = T.sem
     others = [(q + d) % N for d in (1, 2, 3)]
     rows = lambda r: slice(32 * r, 32 * r + 32)
+    sent = [0]
 
     def dst(r):
         rid, pid, _ = topo.addr(T.cores[r])
         return DstId(rid=rid, pnc=pid)
 
+    def shared(r):
+        return [e for e in topo.engines(T.cores[r], T.cores[(r + 1) % N])
+                if all(e in topo.engines(T.cores[r], T.cores[(r + d) % N]) for d in (2, 3))]
+
     def send(src, land, r, rsem):
         rid, pid, _ = topo.addr(T.cores[r])
         g.remote_dma(land, src, rsem, sem.snd, pid, rid, topo.mask(core, T.cores[r]))
-        return len(topo.engines(core, T.cores[r]))
+        sent[0] += len(topo.engines(core, T.cores[r]))
 
-    def fused(src, land, rsem):
-        trs, tot = [], 0
-        for j, r in enumerate(others):
-            en = topo.engines(core, T.cores[r])
-            w = len(en) // 4
-            mk = sum(1 << e for e in en[w * j:w * j + w])
-            trs.append(RemoteDMATransfer(dst_ids=[dst(r)], dma_engine_mask=mk, remote_sem=rsem, src=src[r], dst=land[q]))
-            tot += w
-        g.remote_dma_fused(trs, local_sem=sem.snd)
-        return tot
+    def each(items, rsem):
+        (src, land), = items
+        en = shared(q)
+        w = len(en) // 4
+        g.remote_dma_fused([RemoteDMATransfer(dst_ids=[dst(r)], dma_engine_mask=sum(1 << e for e in en[w * j:w * j + w]),
+                                              remote_sem=rsem, src=src[r], dst=land[q]) for j, r in enumerate(others)], local_sem=sem.snd)
+        sent[0] += 3 * w
 
-    def quarter(r):
-        return len(topo.engines(T.cores[r], core)) // 4
+    def spread(items, rsem):
+        en = shared(q)
+        w = len(en) // len(items)
+        g.remote_dma_fused([RemoteDMATransfer(dst_ids=[dst(r) for r in others], dma_engine_mask=sum(1 << e for e in en[w * j:w * j + w]),
+                                              remote_sem=rsem, srcs=[src], dsts=[land[q]] * 3) for j, (src, land) in enumerate(items)],
+                           local_sem=sem.snd)
+        sent[0] += w * len(items)
+
+    quarters = sum(len(shared(r)) // 4 for r in others)
+    whole = sum(len(shared(r)) for r in others)
+    net = {"each": each, "all": spread, "near": spread, "two": spread,
+           "in": {"each": quarters, "all": whole, "near": whole, "two": whole}}
 
     def full(r):
         return len(topo.engines(T.cores[r], core))
 
-    ops = build_ops(T, others)
+    ops = build_ops(T, q, net)
+    lk = links(ops)
     if not TUNED:
-        TUNED.append(tune(ops, STEPS))
-    order, eng, deps, end, lastw = schedule(ops)
-    Q = {"P": g.tensor, "V": g.vector, "A": g.scalar, "G": g}
+        TUNED.append(tune(ops, lk, STEPS))
+    order, eng, deps, end = schedule(ops, lk)
+    Q = {"P": g.tensor, "V": g.vector, "A": g.scalar, "G": g, "S": g.sync}
     idx, cnt = {}, {"P": 0, "V": 0, "A": 0, "G": 0}
     for i in order:
-        cnt[eng[i]] += 1
-        idx[i] = cnt[eng[i]]
+        if "sem" not in ops[i]:
+            cnt[eng[i]] += 1
+            idx[i] = cnt[eng[i]]
 
     for r in others:
         g.sync.dma_start(T.sx[r], T.x0[rows(r), :]).then_inc(sem["stx%d" % r], 16)
     g.scalar.dma_start(T.sk[:, :, :], T.kw[:]).then_inc(sem.stk, 16)
     g.scalar.dma_start(T.sl[:, :, :], T.l0[:]).then_inc(sem.stk, 16)
     g.scalar.dma_start(T.sz[:, :, :], T.z0[:]).then_inc(sem.stk, 16)
-    g.scalar.dma_start(T.z[rows(q), :], T.z0[rows(q), :]).then_inc(sem.ink, 16)
-    g.scalar.dma_start(T.Ki[rows(q), :], T.kw[rows(q), :]).then_inc(sem.ink, 16)
-    g.scalar.dma_start(T.Li[2 * q:2 * q + 2, :], T.l0[2 * q:2 * q + 2, :]).then_inc(sem.ink, 16)
+    g.scalar.dma_start(T.lz[q], T.z0[rows(q), :]).then_inc(sem.own, 16)
+    g.scalar.dma_start(T.lk[q], T.kw[rows(q), :]).then_inc(sem.own, 16)
+    g.scalar.dma_start(T.ll[q], T.l0[2 * q:2 * q + 2, :]).then_inc(sem.own, 16)
     g.sync.dma_start(T.X[rows(q), 0:W], T.x0[rows(q), :]).then_inc(sem.inx, 16)
     g.sync.wait_ge(sem["stx%d" % others[2]], 16)
     for r in others:
         g.sync.dma_start(T.ss[r], T.asc[rows(r), :]).then_inc(sem.sts, 16)
-    nin, nink, nins = 16 * N, 48 * N, 16 * N
+    nin, nink, nins = 16 * N, 48, 16 * N
 
-    known = {e: {"P": 0, "V": 0, "A": 0, "G": 0, "in0": 0, "in1": 0, "in2": 0} for e in Q}
+    known = {e: {} for e in Q}
     clock = {}
 
     def emit(i):
@@ -829,48 +903,51 @@ def rank_program(g, core, T, topo):
         kn = known[e]
         need = {}
         for d in deps[i]:
-            if e == "P" and eng[d] == "P" and not ("fence" in ops[i] and "fence" in ops[d]):
-                continue
-            if idx[d] > kn[eng[d]] and idx[d] > need.get(eng[d], (0, None))[0]:
+            if "sem" in ops[d]:
+                need[ops[d]["sem"]] = (ops[d]["val"], d)
+            elif not (e == "P" and eng[d] == "P") and idx[d] > need.get(eng[d], (0, None))[0]:
                 need[eng[d]] = (idx[d], d)
         for f, (v, d) in sorted(need.items(), key=lambda x: -end[x[1][1]]):
-            if v > kn[f]:
+            if v > kn.get(f, 0):
                 Q[e].wait_ge(sem[f], v)
                 kn[f] = v
-                for f2, v2 in clock[d].items():
-                    kn[f2] = max(kn[f2], v2)
+                if "far" not in ops[d]:
+                    for f2, v2 in clock[d].items():
+                        kn[f2] = max(kn.get(f2, 0), v2)
         for key, s, v in (("in0", sem.ink, nink), ("in1", sem.inx, nin), ("in2", sem.ins, nins)):
-            if key in ops[i]["r"] and not kn[key]:
+            if key in ops[i]["r"] and not kn.get(key, 0):
                 Q[e].wait_ge(s, v)
                 kn[key] = 1
-        ops[i]["alts"][e][1](g).then_inc(sem[e], 1)
+        if "sem" in ops[i]:
+            ops[i]["alts"][e][1](g)
+        else:
+            ops[i]["alts"][e][1](g).then_inc(sem[e], 1)
         clock[i] = dict(kn)
 
-    gfirst = [i for i in order if eng[i] == "G" and not deps[i]]
+    gfirst = [i for i in order if eng[i] == "G" and not deps[i] and "late" not in ops[i]]
     for i in gfirst:
         emit(i)
-    sent = 0
     g.wait_ge(sem.stk, 48)
-    sent += fused(T.sl, T.ll, sem.ak)
-    sent += fused(T.sk, T.lk, sem.ak)
-    sent += fused(T.sz, T.lz, sem.ak)
+    each([(T.sl, T.ll)], sem.ak)
+    each([(T.sk, T.lk)], sem.ak)
+    each([(T.sz, T.lz)], sem.ak)
     for j, r in enumerate(others):
         g.wait_ge(sem["stx%d" % r], 16)
-        sent += send(T.sx[r], T.lx[q], r, sem["ax%d" % q])
+        send(T.sx[r], T.lx[q], r, sem["ax%d" % q])
     g.wait_ge(sem.sts, 48)
-    sent += fused(T.ss, T.ls, sem.as_)
+    each([(T.ss, T.ls)], sem.as_)
     back = [(q - d) % N for d in (1, 2, 3)]
-    g.scalar.wait_ge(sem.ak, 3 * sum(quarter(r2) for r2 in others))
-    for r2 in back:
-        g.scalar.dma_start(T.Ki[rows(r2), :], T.lk[r2]).then_inc(sem.ink, 16)
-        g.scalar.dma_start(T.Li[2 * r2:2 * r2 + 2, :], T.ll[r2]).then_inc(sem.ink, 16)
-        g.scalar.dma_start(T.z[rows(r2), :], T.lz[r2]).then_inc(sem.ink, 16)
+    g.sync.wait_ge(sem.own, 48)
+    g.sync.wait_ge(sem.ak, 3 * quarters)
+    g.sync.dma_start(T.Ki[:, :], T.lk[:, :, :]).then_inc(sem.ink, 16)
+    g.sync.dma_start(T.Li[0:8, :], T.ll[:, :, :]).then_inc(sem.ink, 16)
+    g.sync.dma_start(T.z[:, :], T.lz[:, :, :]).then_inc(sem.ink, 16)
     for j, r in enumerate(back):
         g.sync.wait_ge(sem["ax%d" % r], full(r))
         g.sync.dma_start(T.X[rows(r), 0:W], T.lx[r]).then_inc(sem.inx, 16)
         if j == 0:
             g.sync.dma_start(T.Si[rows(q), :], T.asc[rows(q), :]).then_inc(sem.ins, 16)
-    g.sync.wait_ge(sem.as_, sum(quarter(r) for r in others))
+    g.sync.wait_ge(sem.as_, quarters)
     for r in back:
         g.sync.dma_start(T.Si[rows(r), :], T.ls[r]).then_inc(sem.ins, 16)
 
@@ -878,59 +955,9 @@ def rank_program(g, core, T, topo):
         if i not in gfirst:
             emit(i)
 
-    def after(queue, keys):
-        need = {}
-        for key in keys:
-            d = lastw[key]
-            need[eng[d]] = max(need.get(eng[d], 0), idx[d])
-        for f, v in need.items():
-            queue.wait_ge(sem[f], v)
-
-    SA = slice(W, W + A)
-    after(g.sync, ["X"])
-    g.sync.dma_start(T.yx[rows(q), :], T.X[rows(q), 0:W]).then_inc(sem.fin, 16)
-    after(g.sync, ["S"])
-    g.sync.dma_start(T.ya[rows(q), :], T.S[rows(q), SA]).then_inc(sem.fin, 16)
-    after(g.sync, ["Lo0", "Lo1", "z0", "z1"])
-    g.sync.dma_start(T.ol[:, :, :], T.Lo[0:8, :]).then_inc(sem.ok, 16)
-    g.sync.dma_start(T.oz[:, :, :], T.z[:, :]).then_inc(sem.ok, 16)
-    after(g.sync, ["Kf0", "Kf1"])
-    g.sync.dma_start(T.ok[:, :, :], T.Kf[:, :]).then_inc(sem.ok, 16)
-    after(g.scalar, ["Kf0", "Kf1", "Lo0", "Lo1", "z0", "z1"])
-    g.scalar.dma_start(T.yz[rows(q), :], T.z[rows(q), :]).then_inc(sem.fin2, 16)
-    g.scalar.dma_start(T.yk[rows(q), :], T.Kf[rows(q), :]).then_inc(sem.fin2, 16)
-    g.scalar.dma_start(T.yl[2 * q:2 * q + 2, :], T.Lo[2 * q:2 * q + 2, :]).then_inc(sem.fin2, 16)
-    for r in others:
-        after(g, ["OX%d%d" % (r, cq) for cq in range(4)])
-        sent += send(T.OX[:, 1024 * r:1024 * r + 1024], T.mx[q], r, sem["bx%d" % q])
-        after(g, ["OS%d%d" % (r, cq) for cq in range(4)])
-        sent += send(T.OS[:, 256 * r:256 * r + 256], T.ma[q], r, sem["ba%d" % q])
-        if r == others[1]:
-            g.wait_ge(sem.ok, 48)
-            sent += fused(T.ok, T.mk, sem.bk)
-            sent += fused(T.oz, T.mz, sem.bk)
-            sent += fused(T.ol, T.ml, sem.bk)
-    for r in back:
-        if r == back[2]:
-            g.sync.wait_ge(sem.bk, 3 * sum(quarter(r2) for r2 in others))
-            g.scalar.wait_ge(sem.bk, 3 * sum(quarter(r2) for r2 in others))
-            for j, r2 in enumerate(back):
-                g.sync.dma_start(T.yk[rows(r2), :], T.mk[r2]).then_inc(sem.fin, 16)
-                g.scalar.dma_start(T.yz[rows(r2), :], T.mz[r2]).then_inc(sem.fin2, 16)
-                if j % 2:
-                    g.scalar.dma_start(T.yl[2 * r2:2 * r2 + 2, :], T.ml[r2]).then_inc(sem.fin2, 16)
-                else:
-                    g.sync.dma_start(T.yl[2 * r2:2 * r2 + 2, :], T.ml[r2]).then_inc(sem.fin, 16)
-        g.sync.wait_ge(sem["bx%d" % r], full(r))
-        g.scalar.wait_ge(sem["bx%d" % r], full(r))
-        for cq in range(4):
-            (g.sync, g.scalar)[cq % 2].dma_start(T.yx[rows(r), 1024 * cq:1024 * cq + 1024], T.mx[r, rows(cq), :]).then_inc((sem.fin, sem.fin2)[cq % 2], 16)
-        g.sync.wait_ge(sem["ba%d" % r], full(r))
-        g.scalar.wait_ge(sem["ba%d" % r], full(r))
-        for cq in range(4):
-            (g.sync, g.scalar)[cq % 2].dma_start(T.ya[rows(r), 256 * cq:256 * cq + 256], T.ma[r, rows(cq), :]).then_inc((sem.fin, sem.fin2)[cq % 2], 16)
-    g.sync.wait_ge(sem.fin, 32 + 80 * (N - 1) + 32)
-    g.scalar.wait_ge(sem.fin2, 48 + 80 * (N - 1) + 16)
-    g.wait_ge(sem.snd, sent)
-    for f in Q:
+    for o in ops:
+        if "sem" in o and o["w"][0][0] == "y":
+            g.wait_ge(sem[o["sem"]], o["val"])
+    g.wait_ge(sem.snd, sent[0])
+    for f in cnt:
         g.wait_ge(sem[f], cnt[f])

@@ -4,16 +4,19 @@ from concourse.mybir import AluOpType as OP, AxisListType, ActivationFunctionTyp
 
 N, W, A, TL, RO, EPS, TH = 4, 4096, 1024, 256, 4, 48, 720
 WX = 5248
-NRING = 5
+NRING = 6
+PAIR = [[], []]
+BLK = [0, 2, 4, 6, 1, 3, 5, 7]
 BIAS = [8000, -3000, 12000, 8000, -1000, 3000, 3000, 2000, 0, 3000, 1000, 8000, 4000, 5000, 0]
 NE = [4, 4]
-STEPS = 3000
-WIN, VPEN = 40.0, 300.0
+S97 = 169.0 / 16384
+LASTB = [0, 0]
+STEPS, STEPS2 = 3500, 15000
+WIN, VPEN = 120.0, 150.0
 NUDGE = {}
 LEAN = {}
 GAM, SCA = 1.5, 3.8
 MAGIC = 12582912.0
-S97 = 169.0 / 16384
 U = 2.0 ** -13
 
 SCRATCH = {
@@ -23,11 +26,11 @@ SCRATCH = {
     "Lb": ("sbuf", [128, TL], "bfloat16"), "Lo": ("sbuf", [128, 128], "float32"),
     "Ku": ("sbuf", [128, TL], "uint16"), "Kf": ("sbuf", [128, TL], "float32"),
     "z": ("sbuf", [128, TL], "bfloat16"), "AR": ("sbuf", [128, 128], "bfloat16"),
-    "LK": ("sbuf", [128, 64], "uint16"), "KU": ("sbuf", [128, 16], "uint16"),
+    "KU": ("sbuf", [128, 16], "uint16"),
     "at": ("sbuf", [128, 16], "float32"), "ai": ("sbuf", [128, 16], "int32"),
-    "CB": ("sbuf", [128, 9344], "bfloat16"), "CF": ("sbuf", [128, 512], "float32"), "C16": ("sbuf", [128, 528], "float16"),
-    "CI": ("sbuf", [128, 16], "int32"), "TB": ("sbuf", [128, 2048], "bfloat16"),
-    "sx": ("dram", [4, 128, 1024], "bfloat16"), "lx": ("dram", [4, 128, 1024], "bfloat16"), "mx": ("dram", [4, 128, 1024], "bfloat16"),
+    "CB": ("sbuf", [128, 9984], "bfloat16"), "CF": ("sbuf", [128, 368], "float32"), "C16": ("sbuf", [128, 912], "float16"),
+    "CI": ("sbuf", [128, 16], "int32"), "TB": ("sbuf", [128, 1776], "bfloat16"),
+    "SX": ("sbuf", [128, 3072], "bfloat16"), "LX": ("sbuf", [128, 3072], "bfloat16"), "mx": ("dram", [4, 128, 1024], "bfloat16"),
     "sz": ("dram", [4, 128, 64], "bfloat16"), "lz": ("dram", [4, 128, 64], "bfloat16"),
     "sk": ("dram", [4, 128, 64], "int32"), "lk": ("dram", [4, 128, 64], "int32"),
     "sl": ("dram", [4, 128, 4], "int32"), "ll": ("dram", [4, 128, 4], "int32"),
@@ -44,19 +47,20 @@ for _h in range(2):
         "wb%d" % _h: ("sbuf", [128, 4608], "bfloat16"), "wf%d" % _h: ("sbuf", [128, 2176], "float32"),
         "wi%d" % _h: ("sbuf", [128, 1024], "int32"), "wu%d" % _h: ("sbuf", [128, 320], "uint16"),
         "wh%d" % _h: ("sbuf", [128, 512], "float16"),
-        "VA%d" % _h: ("sbuf", [128, 256], "float32"), "VL%d" % _h: ("sbuf", [128, 256], "float32"),
-        "mv%d" % _h: ("dram", [4, 128, 256], "float32"), "mk%d" % _h: ("dram", [4, 128, 128], "float32"),
+        "VA%d" % _h: ("sbuf", [128, 128], "bfloat16"), "VL%d" % _h: ("sbuf", [128, 128], "bfloat16"),
+        "MS%d" % _h: ("sbuf", [128, 272], "float32"), "LM%d" % _h: ("sbuf", [128, 544], "float32"),
+        "mv%d" % _h: ("dram", [4, 128, 128], "bfloat16"), "mk%d" % _h: ("dram", [4, 128, 128], "float32"),
     })
 for _b in range(8):
     SCRATCH["ps%d" % _b] = ("psum", [128, 512], "float32")
 
-SEMAPHORES = ["P", "V", "A", "G", "stx0", "stx1", "stx2", "stx3", "stk", "sts", "snd", "own",
-              "ax0", "ax1", "ax2", "ax3", "ak", "as_", "inx", "ink", "ins",
+SEMAPHORES = ["P", "V", "A", "G", "stx0", "stx1", "stx2", "stk", "sts", "snd", "own",
+              "ax0", "ax1", "ax2", "ak", "as_", "inx", "ink", "ins",
               "ox", "oa", "bx", "ba", "nx", "ns", "nxo", "nso", "zl", "zlo", "yx", "ya", "yz", "yl"]
 for _h in range(2):
     SEMAPHORES += [_s + str(_h) for _s in ("bv", "ov", "vl", "bu", "bk", "ok", "yk")]
 
-CYC, PCYC, LAT, FIX = 0.83, 0.42, 60.0, 55.0
+CYC, PCYC, LAT, FIX = 0.83, 0.42, 170.0, 15.0
 
 
 def build_ops(T, q=0, net=None):
@@ -66,9 +70,9 @@ def build_ops(T, q=0, net=None):
 
     def add(alts, reads, writes, banks=()):
         ops.append({"alts": alts, "r": list(reads), "w": list(writes), "b": list(banks), "bias": bias[0],
-                    "pos": len(ops) - base[0] if base[0] >= 0 else -1})
+                    "pos": -1 if base[0] is None else len(ops) - base[0], "rnd": turn[0]})
 
-    bias, base = [0.0], [-1]
+    bias, base, turn = [0.0], [None], [0]
 
     def vc(n, rate=1.0):
         return FIX + max(64, n * rate) * CYC
@@ -79,11 +83,22 @@ def build_ops(T, q=0, net=None):
         nsess[0] += 1
         return {"bank": None, "id": nsess[0], "h": h, "left": 0}
 
-    def sap(s, a=0, b=512):
-        return ("slot", s, a, b)
+    def sap(s, a=0, b=512, p0=None):
+        return ("slot", s, a, b, p0)
 
     def R(ap):
-        return T["ps%d" % ap[1]["bank"]][:, ap[2]:ap[3]] if isinstance(ap, tuple) else ap
+        if not isinstance(ap, tuple):
+            return ap
+        if ap[0] == "by":
+            return ap[2] if ap[1]["e"] == "V" else ap[3]
+        if ap[4] is None:
+            return T["ps%d" % ap[1]["bank"]][:, ap[2]:ap[3]]
+        return T["ps%d" % ap[1]["bank"]][ap[4]:ap[4] + 64, ap[2]:ap[3]]
+
+    def over(out, in_, thr, n, reads, writes, banks, rate, wv, wa):
+        add({"V": (vc(n, rate), lambda g: g.vector.tensor_scalar(out, in_, thr, 0.5, OP.is_gt, OP.subtract)),
+             "A": (vc(n) + 15, lambda g: g.scalar.activation(out, in_, AF.Sign, bias=-thr))}, reads, writes, banks)
+        return ("by", ops[-1], wv, wa)
 
     def pe(mms, reads, writes, banks):
         cost = 30.0
@@ -93,7 +108,7 @@ def build_ops(T, q=0, net=None):
         def run(g):
             last = None
             for (o, l, r, st, sp, n, m, f) in mms:
-                last = g.tensor.matmul(R(o), l, r, st, sp)
+                last = g.tensor.matmul(R(o), R(l), R(r), st, sp)
             return last
         add({"P": (cost, run)}, reads, writes, banks)
 
@@ -132,8 +147,14 @@ def build_ops(T, q=0, net=None):
         else:
             add({"G": (130 + 2 * n * CYC, lambda g: g.iota(out, pat, base, cm, allow_small_or_imprecise_dtypes=True))}, [], writes)
 
-    def mset(ap, v, n, writes, rate=0.5):
-        add({"V": (vc(n, rate), lambda g: g.vector.memset(ap, v))}, [], writes)
+    def mset(ap, v, n, writes, rate=0.5, late=False):
+        if late:
+            iota(ap, [[0, n]], int(v), 0, n, writes)
+        else:
+            add({"V": (vc(n, rate), lambda g: g.vector.memset(ap, v))}, [], writes)
+
+    def pick(out, in_, pat, op, fill, base, cm, n, reads, writes):
+        add({"G": (170 + 2 * n * CYC, lambda g: g.affine_select(out, in_, pat, op, fill, base, cm))}, reads, writes)
 
     def dma(e, pairs, sem, lat, reads, writes):
         def run(g):
@@ -157,20 +178,21 @@ def build_ops(T, q=0, net=None):
         t, o, n = C[name]
         return t[p0:p1, o + a:o + (n if b is None else b)]
 
-    for nm, n in (("II", 256), ("nII", 256), ("sI", 128), ("nsI", 128), ("IH", 128), ("I16", 128), ("PM", 256), ("ONES", 128),
-                  ("MM", 256), ("BB", 256), ("B8", 16), ("nB8", 8), ("Wd", 8), ("Ww", 8), ("Wn", 16), ("W2", 16), ("LWa", 128), ("LWb", 128),
-                  ("W4V", 8), ("CH", 256), ("THN", 128), ("WV", 128), ("W4", 256), ("W21h", 256), ("W21l", 256), ("nBD", 128),
-                  ("MM16", 128), ("MK", 256), ("MK2", 128), ("MKp", 128), ("MKt", 128), ("hold", 256), ("rst", 128), ("rstr", 128),
-                  ("HP", 128), ("CR", 256), ("EX0", 256), ("EXb", 128), ("EXa", 128), ("EXK", 128), ("TRT", 512), ("Z8", 240),
-                  ("LS", 128), ("CT", 256), ("NH", 128), ("C2", 16), ("SEL", 1024), ("nSEL", 1024), ("cb", 16)):
+    for nm, n in (("II", 256), ("nII", 128), ("IH", 128), ("I16", 128), ("I17", 128), ("PM", 256), ("PMh", 256), ("PT", 256), ("CK", 256), ("ONES", 128), ("Wv", 8),
+                  ("MM", 128), ("BB", 256), ("B8", 16), ("nB8", 8), ("Wd", 8), ("Ww", 8), ("Wn", 16), ("W2", 16), ("LWa", 128), ("LWb", 128),
+                  ("W4V", 8), ("CH", 256), ("THN", 128), ("WV", 128), ("W4", 256), ("nBD", 256),
+                  ("MM16", 128), ("MK", 256), ("MK2", 128), ("MKp", 128), ("MKt", 128), ("hold", 256), ("rst", 160), ("rstr", 128),
+                  ("HP", 128), ("CR", 128), ("CRC", 160), ("EX0", 256), ("EXb", 128), ("EXK", 128), ("TRT", 768), ("Z8", 240), ("Zq", 224),
+                  ("LS", 128), ("CT", 384), ("NH", 128), ("C2", 16), ("SEL", 1024), ("nSEL", 512),
+                  ("sI", 128), ("nsI", 128), ("THO0", 128), ("THO1", 128)):
         alloc("CB", nm, n)
-    for nm, n in (("I20", 128), ("TR", 128), ("t4", 64), ("t5", 128), ("col", 32)):
+    for nm, n in (("TR", 128), ("t4", 64), ("t5", 128), ("col", 32), ("sel", 8)):
         alloc("CF", nm, n)
-    for nm, n in (("IIh", 256), ("BBh", 256), ("B8h", 8)):
+    for nm, n in (("IIh", 128), ("I20", 256), ("BBh", 256), ("W21", 256), ("B8h", 8)):
         alloc("C16", nm, n)
-    for nm, n in (("t0", 256), ("t1", 256), ("t2", 256), ("t3", 16), ("t6", 128), ("tb", 1024)):
+    for nm, n in (("t0", 256), ("t1", 256), ("t2", 256), ("t3", 16), ("t6", 128), ("t7", 160), ("t8", 128), ("nONE", 64), ("zero", 512)):
         alloc("TB", nm, n)
-    colnames = ["p", "pm", "pb", "p7", "h8", "w", "pw", "th", "nth", "thn", "w21", "w21l", "p16", "w4", "m15", "wsel", "lwa", "lwb",
+    colnames = ["p", "pm", "pb", "p7", "h8", "w", "pw", "th", "nth", "thn", "w21", "p63", "p16", "w4", "m15", "wsel", "lwa", "lwb",
                 "sp", "e0", "e1", "e2", "b0", "b1", "b2", "b3", "f0", "f1", "f2", "f3"]
 
     def col(nm, p0=0, p1=128):
@@ -183,8 +205,12 @@ def build_ops(T, q=0, net=None):
     iota(c("t2"), [[0, 16], [1, 16]], 0, 0, 256, ["t2"])
     iota(c("t3"), [[0, 2], [1, 8]], 0, 0, 16, ["t3"])
     iota(c("t1"), [[0, 2], [1, 8], [0, 16]], 0, 0, 256, ["t1"])
-    iota(c("tb"), [[1, 8], [0, 128]], 0, 0, 1024, ["tb"])
-    ops[-1]["late"] = 1
+    for o in ops:
+        o["early"] = 1
+    iota(c("zero"), [[0, 512]], 0, 0, 512, ["zero"])
+
+    def eye(dst, v, a=0):
+        pick(c(dst, a, a + 128), c("zero", 0, 128), [[-1, 128]], OP.not_equal, v, 0, 1, 128, ["zero"], [dst])
     cp(col("p"), CI[:, 0:1], 1, ["ci0"], ["c.p"])
     for j, (nm, s1, s2) in enumerate((("pm", 0, 15), ("pb", 4, 7), ("p7", 0, 7), ("h8", 3, 1))):
         ts(CI[:, 1 + j:2 + j], CI[:, 0:1], s1, s2, OP.arith_shift_right, OP.bitwise_and, 1, ["ci0"], ["ci%d" % (1 + j)])
@@ -192,7 +218,13 @@ def build_ops(T, q=0, net=None):
 
     def cts(nm, src, s1, s2, o0, o1):
         rd = ["c." + s for s in (src, s1, s2) if isinstance(s, str)]
-        ts(col(nm), col(src), col(s1) if isinstance(s1, str) else s1, col(s2) if isinstance(s2, str) else s2, o0, o1, 1, rd, ["c." + nm])
+        a, b = (col(s) if isinstance(s, str) else s for s in (s1, s2))
+        alt = None
+        if o0 == OP.mult and o1 in (None, OP.add):
+            alt = (AF.Identity, 0.0 if o1 is None else b, a)
+        if o0 == OP.add and o1 is None:
+            alt = (AF.Identity, a, 1.0)
+        ts(col(nm), col(src), a, b, o0, o1, 1, rd, ["c." + nm], act=alt)
 
     def eq(dst, src, cn, mul=None, n=None):
         n = n or C[dst][2]
@@ -213,9 +245,10 @@ def build_ops(T, q=0, net=None):
     eq("MM", "t2", "pm")
     eq("BB", "t1", "pb")
     eq("B8", "t3", "pb")
-    lin("nII", "II", -1.0); lin("sI", "II", S97); lin("nsI", "II", -S97); lin("IH", "II", 0.5); lin("I16", "II", 65536.0)
-    lin("PM", "II", -8192.0, n=128); lin("PM", "II", 8192.0, a=128, n=128)
-    lin("I20", "II", 20.0, rate=1.0); lin("IIh", "II", 1.0, flex=False); lin("BBh", "BB", 1.0, flex=False); lin("B8h", "B8", 1.0, flex=False)
+    lin("nII", "II", -1.0); lin("IH", "II", 0.5); lin("I16", "II", 65536.0); lin("I17", "II", 131072.0)
+    for nm, v in (("PT", 8192.0), ("PMh", 81920.0), ("PM", 163840.0)):
+        eye(nm, -v); eye(nm, v, 128)
+    lin("I20", "II", 20.0, flex=False); lin("IIh", "II", 1.0, flex=False); lin("BBh", "BB", 1.0, flex=False); lin("B8h", "B8", 1.0, flex=False)
     mset(c("t4", 0, 16), 0.5, 16, ["t4"])
     mset(c("t4", 16, 32), 0.0, 16, ["t4"])
     add({"V": (vc(16), lambda g: g.vector.tensor_tensor_scan(c("t4", 32, 48), c("t4", 0, 16), c("t4", 16, 32), 65536.0, OP.mult, OP.add))}, ["t4"], ["t4b"])
@@ -226,7 +259,7 @@ def build_ops(T, q=0, net=None):
     cts("e0", "pm", 15.0, -32768.0, OP.is_equal, OP.mult)
     cts("thn", "e0", "pw", None, OP.subtract, None)
     cts("nth", "th", -1.0, None, OP.mult, None)
-    lin("nB8", "B8", -1.0); lin("Wd", "B8", -16.0); lin("Ww", "B8", "pw"); lin("Wn", "B8", -U); lin("W2", "B8", 2 * U)
+    lin("nB8", "B8", -1.0); lin("Wd", "B8", -16.0); lin("Ww", "B8", "pw"); lin("Wv", "Ww", 0.5); lin("Wn", "B8", -U); lin("W2", "B8", 2 * U)
     lin("CH", "BB", "nth", a=128, n=128); lin("THN", "BB", "thn"); lin("nBD", "BB", -U)
     cts("b0", "pb", 0.0, None, OP.is_equal, None)
     cts("b1", "pb", 1.0, -16.0, OP.is_equal, OP.mult)
@@ -236,25 +269,30 @@ def build_ops(T, q=0, net=None):
     cts("p16", "p", 16.0, None, OP.mult, None)
     lin("MM16", "MM", "p16")
     ts(c("hold"), c("t2"), 0.0, None, OP.not_equal, None, 256, ["t2"], ["hold"], rate=0.5)
-    ts(c("rst"), c("t2", 0, 128), 0.0, 4.0, OP.is_equal, OP.mult, 128, ["t2"], ["rst"], rate=0.5)
+    ts(c("rst"), c("t2", 0, 160), 0.0, 4.0, OP.is_equal, OP.mult, 160, ["t2"], ["rst"], rate=0.5)
     ts(c("rstr"), c("t2", 0, 128), 15.0, 4.0, OP.is_equal, OP.mult, 128, ["t2"], ["rstr"], rate=0.5)
     ts(c("t6"), c("t2", 0, 128), col("pm"), None, OP.is_le, None, 128, ["t2", "c.pm"], ["t6"], rate=0.5)
     tt(c("HP"), c("t6"), c("hold", 0, 128), OP.mult, 128, ["t6", "hold"], ["HP"])
     cts("w", "pm", 15.0, 7.0, OP.mult, OP.add)
     cts("w4", "w", 4.0, None, OP.mult, None)
     cts("w21", "w", 21.0, None, OP.mult, None)
-    cp(c("cb", 0, 1), col("w21"), 1, ["c.w21"], ["cb"])
-    ts(col("w21l"), col("w21"), c("cb", 0, 1), None, OP.subtract, None, 1, ["c.w21", "cb"], ["c.w21l"])
-    lin("WV", "BB", "w"); lin("W4", "BB", "w4"); lin("W21h", "BB", "w21"); lin("W21l", "BB", "w21l"); lin("W4V", "B8", "w4")
+    cts("e0", "w21", 2048.0, -4096.0, OP.is_ge, OP.mult)
+    cts("w21", "w21", "e0", None, OP.add, None)
+    lin("WV", "BB", "w"); lin("W4", "BB", "w4"); lin("W21", "BB", "w21", flex=False); lin("W4V", "B8", "w4")
     big = 16777216.0
-    lin("MK", "MM", big, -big); lin("MK2", "MM", big + 2048.0, -big, flex=False); lin("MKp", "MM", 8192.0 - big, big, flex=False)
+    lin("MK", "MM", big, -big, n=128); lin("MK", "MM", 1.5 * big, -big, a=128, n=128); lin("MK2", "MM", big + 2048.0, -big, flex=False); lin("MKp", "MM", 8192.0 - big, big, flex=False)
     tt(c("MKt"), c("MK", 0, 128), c("t0", 0, 128), OP.add, 128, ["MK", "t0"], ["MKt"])
     mset(c("ONES"), 1.0, 128, ["ONES"])
     cts("f0", "p", 0.0, U / 32, OP.is_equal, OP.mult)
     cts("f1", "p", 1.0, -TH * U, OP.is_equal, OP.mult)
-    cts("f2", "p", 2.0, -U / 2, OP.is_equal, OP.mult)
+    lin("CR", "t2", "f0", "f1")
+    cts("f0", "p", 8.0, U / 32, OP.is_equal, OP.mult)
+    cts("f1", "p", 9.0, -TH * U, OP.is_equal, OP.mult)
+    cts("f2", "p", 10.0, -U / 2, OP.is_equal, OP.mult)
     cts("f3", "f1", "f2", None, OP.add, None)
-    lin("CR", "t2", "f0", "f1", n=128); lin("CR", "t2", "f0", "f3", a=128, n=128)
+    lin("t7", "t2", "f0", "f3")
+    ts(c("CRC"), c("t1", 96, 256), col("p"), -U, OP.is_equal, OP.mult, 160, ["t1", "c.p"], ["CRC"], rate=0.5)
+    tt(c("CRC"), c("CRC"), c("t7"), OP.add, 160, ["CRC", "t7"], ["CRC"])
     cts("e1", "h8", -128.0, 256.0, OP.mult, OP.add)
     eq("EX0", "t1", "p7", "e1")
     cts("e2", "h8", -4096.75, -4096.25, OP.mult, OP.add)
@@ -262,27 +300,46 @@ def build_ops(T, q=0, net=None):
     cts("b1", "h8", 0.75, 0.25, OP.mult, OP.add)
     cts("wsel", "b0", "b1", None, OP.add, None)
     eq("EXK", "t1", "p7", "wsel")
-    eq("SEL", "tb", "p7", "wsel")
-    lin("nSEL", "SEL", -1.0)
+    ts(c("sel"), c("t3", 0, 8), col("p7"), col("wsel"), OP.is_equal, OP.mult, 8, ["t3", "c.p7", "c.wsel"], ["sel"])
+    mset(c("nONE"), -1.0, 64, ["nONE"])
+    for x, b in enumerate(BLK):
+        for dst, src, n, o in (("SEL", "ONES", 128, 128 * b), ("nSEL", "nONE", 64, 64 * x)):
+            ts(c(dst, o, o + n), c(src), c("sel", b, b + 1), None, OP.mult, None, n, [src, "sel"], ["%s%d" % (dst, b)], rate=0.5,
+               act=(AF.Identity, 0.0, c("sel", b, b + 1)))
+    sels = ["%s%d" % (s, b) for s in ("SEL", "nSEL") for b in range(8)]
     eq("EXb", "t1", "p")
-    lin("EXa", "EXb", -U)
-    for j in range(2):
-        ts(c("TRT", 256 * j, 256 * j + 256), c("t0"), col("p"), 0.25, OP.is_ge, OP.mult, 256, ["t0", "c.p"], ["TRT"], rate=0.5)
-    mset(c("Z8"), 0.0, 240, ["Z8"])
-    mset(c("Z8", 112, 128), 8192.0, 16, ["Z8"])
+    pick(c("TRT", 0, 512), c("zero"), [[0, 8], [-1, 64]], OP.is_gt, 0.25, 0, 1, 512, ["zero"], ["TRT"])
+    for p0 in (0, 64):
+        pick(c("TRT", 512, 768, p0, p0 + 64), c("zero", 0, 256, p0, p0 + 64), [[0, 4], [-1, 64]], OP.is_gt, 0.25, 0, 1, 256, ["zero"], ["TRT"])
+    mset(c("Z8", 0, 464), 0.0, 464, ["Z8", "Zq"], late=True)
+    mset(c("Z8", 112, 128), 8192.0, 16, ["Z8"], late=True)
+    mset(c("Zq", 96, 112, 0, 64), 8192.0, 16, ["Zq"], late=True)
+    mset(c("Zq", 112, 128, 64, 128), 8192.0, 16, ["Zq"], late=True)
+    for h in range(2):
+        if NE[h] < 4:
+            ts(c("THO%d" % h), c("t2", 0, 128), 4.0 * NE[h], -128.0, OP.is_ge, OP.mult, 128, ["t2"], ["THO%d" % h], rate=0.5)
+    if min(NE) < 4:
+        lin("sI", "II", S97); lin("nsI", "II", -S97)
+    mset(c("CK", 0, 128), 122880.0, 128, ["CK"], late=True); mset(c("CK", 128, 256), -40960.0, 128, ["CK"], late=True)
     cts("e0", "pm", 15.0, -16.0, OP.is_equal, OP.mult)
     cts("e1", "p", 1.0, "e0", OP.add, OP.add)
     eq("LS", "t0", "e1")
-    mset(c("CT", 0, 128), 2048.0, 128, ["CT"]); mset(c("CT", 128, 256), -6144.0, 128, ["CT"])
+    for j, v in enumerate((2048.0, -6144.0, -8192.0)):
+        mset(c("CT", 128 * j, 128 * j + 128), v, 128, ["CT"], late=True)
     mset(c("NH"), -0.5, 128, ["NH"])
-    mset(c("C2", 0, 8), 0.0, 8, ["C2"]); mset(c("C2", 8, 16), 16.0, 8, ["C2"])
+    iota(c("C2"), [[16, 2], [0, 8]], 0, 0, 16, ["C2"])
     cts("sp", "pm", 5120.0, None, OP.add, None)
     ts(c("t5"), c("t0", 0, 128), col("sp"), 0.25, OP.add, OP.mult, 128, ["t0", "c.sp"], ["t5"])
-    tt(c("TR"), c("t5"), c("rst"), OP.mult, 128, ["t5", "rst"], ["TR"])
+    tt(c("TR"), c("t5"), c("rst", 0, 128), OP.mult, 128, ["t5", "rst"], ["TR"])
+
+    lin("t8", "BB", "pm")
+    for nm, sg, b0 in (("LWa", -1, 7), ("LWb", 1, -8)):
+        pick(c(nm), c("t8"), [[0, 8], [sg, 16]], OP.is_ge, 0.0, b0, 0, 128, ["t8"], [nm])
 
     X, S, Ku, Kf, z, at, ai, AR = T.X, T.S, T.Ku, T.Kf, T.z, T.at, T.ai, T.AR
-    mset(AR[0:8, :], 0.0, 128, ["AR"])
-    mset(ai[0:8, 0:1], 0, 1, ["ai0"], rate=1.0)
+    mset(AR[0:32, :], 1.0, 128, ["AR"], late=True)
+    mset(AR[0:8, :], 0.0, 128, ["AR"], late=True)
+    iota(ai[0:8, 0:1], [[0, 1]], 0, 0, 1, ["ai0"], True)
 
     def zwin(h, rnd, j, n=1):
         o = 3072 + 384 * (rnd % 2) + 128 * (3 - n - j)
@@ -304,14 +361,20 @@ def build_ops(T, q=0, net=None):
         zk, lk, kk_ = skeys(h, 0)
         mset(T["wb%d" % h][:, 1216:1520], 0.0, 304, ["kd%d" % h, "ks%d" % h])
         cp(Ku[:, L], T.Ki[:, L], 128, ["in0"], ["Ku%d" % h])
-        ts(kwin(h, 0, 1), T.Ki[:, L], -2048.0, None, OP.add, None, 128, ["in0"], [kk_])
+        ts(kwin(h, 0, 1), T.Ki[:, L], 20.0, None, OP.mult, None, 128, ["in0"], [kk_])
         cp(zwin(h, 0, 0), z[:, L], 128, ["in0", "z%d" % h], [zk], rate=0.5, flex=True)
         cp(T.Lb[0:8, L], T.Li[0:8, L], 128, ["in0"], ["Lb%d" % h])
         m = T["ps%d" % (6 + h)]
         pe([(m[:, 0:128], c("EXb", 0, 128, 0, 8), T.Lb[0:8, L], True, True, 128, 128, 0)], ["EXb", "Lb%d" % h], ["m0%d" % h], [6 + h])
         ts(lwin(h, 0, 0), m[:, 0:128], col("pm"), None, OP.is_equal, None, 128, ["m0%d" % h, "c.pm"], [lk], [6 + h])
         cp(lwin(h, 0, 1), lwin(h, 0, 0), 128, [lk], [lk + "b"], rate=0.5, flex=True)
-    cp(S[:, W:W + A], T.Si[:, :], A, ["in2"], ["S"])
+    pick(S[:, W:W + A], T.Si[:, :], [[0, A]], OP.is_ge, 0.0, 0, 0, A, ["in2"], ["S"])
+    xq = []
+    for j in range(3):
+        for cq in range(4):
+            xq.append("X%d%d" % (j, cq))
+            cp(X[rows((q - 1 - j) % N), 1024 * cq:1024 * cq + 1024], T.LX[rows(cq), 1024 * j:1024 * j + 1024], 1024, ["inx%d" % j], xq[-1:],
+               rate=0.5, flex=True)
 
     ring = [0, 0]
     I = c("II", 0, 128)
@@ -328,7 +391,7 @@ def build_ops(T, q=0, net=None):
         for kk in range(4):
             mms.append((sap(s, 128 * kk, 128 * kk + 128), lx, src[:, base + 4 * ch + kk:base + 2048:16], True, False, 128, 128, 0))
             mms.append((sap(s, 128 * kk, 128 * kk + 128), lz, rz, False, True, 128, 128, 0))
-        pe(mms, ["II", "nII", "sI", "nsI"] + skeys + zkeys, ["sl%d" % s["id"]], [s])
+        pe(mms, ["II", "nII"] + skeys + zkeys, ["sl%d" % s["id"]], [s])
         return s, "sl%d" % s["id"]
 
     def ringbuf(h):
@@ -336,11 +399,8 @@ def build_ops(T, q=0, net=None):
         ring[h] = (r + 1) % NRING
         return r
 
-    def gather(out, win, off, n, reads, writes, flex=True, plus=None):
-        if plus is None:
-            cp(out, win.indirect(off), n, reads, writes, rate=GAM, flex=flex)
-        else:
-            ts(out, win.indirect(off), plus, None, OP.add, None, n, reads, writes, rate=GAM, act=(AF.Identity, plus, 1.0) if flex else None)
+    def gather(out, win, off, n, reads, writes, flex=True):
+        cp(out, win.indirect(off), n, reads, writes, rate=GAM, flex=flex)
         ops[-1]["ng"] = n * CYC
 
     def perm(h, out, wide, src, back):
@@ -362,7 +422,7 @@ def build_ops(T, q=0, net=None):
         ab, mb = [4 + h], [6 + h]
         l0 = 128 * h
         for j in range(2):
-            gather(xg[:, 1024 * j:1024 * j + 1024], X[:, 0:W], Ku[:, l0 + 64 * j:l0 + 64 * j + 64], 1024, ["X", "in1", k("Ku")], [k("xg%d" % j)])
+            gather(xg[:, 1024 * j:1024 * j + 1024], X[:, 0:W], Ku[:, l0 + 64 * j:l0 + 64 * j + 64], 1024, ["X", "in1", k("Ku")] + xq, [k("xg%d" % j)])
         allm = [k("m0"), k("m1"), k("m2"), k("m3")]
         zk, lk, kk_ = skeys(h, rnd)
         zc, lc = zwin(h, rnd, 0), lwin(h, rnd, 0)
@@ -375,16 +435,22 @@ def build_ops(T, q=0, net=None):
             r = ringbuf(h)
             u, v = T["ur%d" % h][:, 512 * r:512 * r + 512], T["vr%d" % h][:, 512 * r:512 * r + 512]
             act(u, sap(s), AF.Abs, 512, [sl], [k("u%d" % r)], [s])
-            ts(v, u, 48.0, None, OP.is_gt, None, 512, [k("u%d" % r)], [k("v%d" % r)], rate=0.5)
+            if ch in PAIR[h]:
+                continue
+            nc = 2 if ch - 1 in PAIR[h] else 1
+            r0 = r + 1 - nc
+            us, vs = [k("u%d" % j) for j in range(r0, r + 1)], [k("v%d" % j) for j in range(r0, r + 1)]
+            u, v = T["ur%d" % h], T["vr%d" % h]
+            wt = over(v[:, 512 * r0:512 * r + 512], u[:, 512 * r0:512 * r + 512], 48.5, 512 * nc, us, vs, (), 0.5, c("Ww"), c("Wv"))
             mu, mv = [], []
-            for kk in range(4):
-                kq = 4 * ch + kk
-                mu.append((acc[:, kq:128:16], T["ur%d" % h][:, 512 * r + 128 * kk:512 * r + 128 * kk + 128], c("Wd"), False, False, 8, 128, 0))
-                mv.append((m[:, kq:128:16], T["vr%d" % h][:, 512 * r + 128 * kk:512 * r + 128 * kk + 128], c("Ww"), False, kq == 15, 8, 128, 0))
-            pe(mu + mv, [k("u%d" % r), k("v%d" % r), "Wd", "Ww", k("acc")], [k("acc")] + allm, ab + mb)
+            for kk in range(4 * nc):
+                kq = 4 * (ch + 1 - nc) + kk
+                mu.append((acc[:, kq:128:16], u[:, 512 * r0 + 128 * kk:512 * r0 + 128 * kk + 128], c("Wd"), False, False, 8, 128, 0))
+                mv.append((m[:, kq:128:16], v[:, 512 * r0 + 128 * kk:512 * r0 + 128 * kk + 128], wt, False, kq == 15, 8, 128, 0))
+            pe(mu + mv, us + vs + ["Wd", "Ww", "Wv", k("acc")], [k("acc")] + allm, ab + mb)
         bias[0] = BIAS[1] * (1 - h) + BIAS[11]
-        act(wb[:, 0:128], m[:, 0:128], AF.Sign, 128, [k("m0")], [k("sg")], mb, bias=0.5)
-        pe([(acc[:, 0:128], c("I16"), wb[:, 0:128], False, True, 128, 128, 0)], [k("sg"), "I16", k("acc")], [k("acc")], ab)
+        wt = over(wb[:, 0:128], m[:, 0:128], -16384.0, 128, [k("m0")], [k("sg")], mb, 1.0, c("I17"), c("I16"))
+        pe([(acc[:, 0:128], wt, wb[:, 0:128], False, True, 128, 128, 0)], [k("sg"), "I16", "I17", k("acc")], [k("acc")], ab)
         scan(wi[:, 0:128], c("hold", 0, 128), acc[:, 0:128], OP.mult, OP.min, 128, [k("acc"), "hold"], [k("s0")], ab)
         ts(wi[:, 128:136], wi[:, 15:128:16], 15, None, OP.bitwise_and, None, 8, [k("s0")], [k("i0")])
         cp(wb[:, 1216:1344:16], wi[:, 128:136], 8, [k("i0")], [k("kd")])
@@ -398,10 +464,10 @@ def build_ops(T, q=0, net=None):
         act(wb[:, 256:384], wb[:, 128:256], AF.Abs, 128, [k("as")], [k("D")])
         z0 = 3072 + 384 * (rnd % 2) + 256
         mms = [(m[:, 0:256], I, c("MK"), 256, 0)]
-        for wt, o0, sh in (("W4", 0, 0), ("W21h", 128, 96), ("W21l", 128, 96)):
+        for wt, o0, sh in (("W4", 0, 0), ("W21", 128, 96)):
             mms += perm(h, lambda o: m[:, o0 + o:o0 + 128:3], lambda s: c(wt, (s + sh) % 128, (s + sh) % 128 + 128),
                         lambda o: wb[:, 256 + o:384:3], False)
-        pe(group(mms), ["II", "MK", "W4", "W21h", "W21l", k("D")], [k("m0"), k("m1")], mb)
+        pe(group(mms), ["II", "MK", "W4", "W21", k("D")], [k("m0"), k("m1")], mb)
         pe(singles(perm(h, lambda o: acc[:, 256 + o:384:3], lambda s: c("II", s, s + 128), lambda o: wb[:, z0 + o:z0 + 128:3], False)
                    + perm(h, lambda o: acc[:, 384 + o:512:3], lambda s: c("II", s, s + 128), lambda o: wb[:, 256 + o:384:3], False)),
            ["II", zk, k("D")], [k("acc")], ab)
@@ -409,19 +475,17 @@ def build_ops(T, q=0, net=None):
         scan(wi[:, 640:896], c("hold"), m[:, 0:256], OP.mult, OP.max, 256, [k("m0"), k("m1"), "hold"], [k("r1")], mb)
         ts(wi[:, 136:152], wi[:, 655:896:16], 2, 1023, OP.arith_shift_right, OP.bitwise_and, 16, [k("r1")], [k("i3")])
         cp(wu[:, 8:24], wi[:, 136:152], 16, [k("i3")], [k("cu")])
-        gather(wu[:, 64:320], S[:, W:W + A], wu[:, 8:24], 256, ["S", k("cu")], [k("Pu")], flex=False)
+        if rnd == 0:
+            gather(wu[:, 64:320], T.Si[:, 0:A], wu[:, 8:24], 256, ["in2", k("cu")], [k("Pu")], flex=False)
+        else:
+            gather(wu[:, 64:320], S[:, W:W + A], wu[:, 8:24], 256, ["S", k("cu")], [k("Pu")], flex=False)
         ts(wh[:, 0:256], wu[:, 64:320], -2048.0, None, OP.add, None, 256, [k("Pu")], [k("Pc")], rate=0.5)
-        pe(group([(m[:, 384:512], c("WV"), wb[:, 256:384], 128, 0), (m[:, 384:512], c("I20"), kwin(h, rnd, 1), 128, 1)]),
-           ["WV", "I20", k("D"), kk_], [k("m3")], mb)
-        ts(wi[:, 256:384], m[:, 384:512], 40960.0, None, OP.add, None, 128, [k("m3")], [k("k1")], mb)
+        pe(group([(m[:, 256:384], c("IH"), c("NH"), 128, 0), (m[:, 256:384], I, zc, 128, 0), (m[:, 256:384], c("IH"), wb[:, 128:256], 128, 0)])
+           + group([(m[:, 384:512], c("WV"), wb[:, 256:384], 128, 0)]), ["IH", "NH", "II", "WV", zk, k("as"), k("D")], [k("m2"), k("m3")], mb)
+        tt(wi[:, 256:384], m[:, 384:512], kwin(h, rnd, 1), OP.add, 128, [k("m3"), kk_], [k("k1")], mb)
         ts(wi[:, 384:512], wi[:, 256:384], 2, 4095, OP.arith_shift_right, OP.bitwise_and, 128, [k("k1")], [k("k2")])
-        ts(kwin(h, rnd, 0), wi[:, 384:512], -2048.0, None, OP.add, None, 128, [k("k2")], [k("K5")])
-        pe(group([(m[:, 256:384], c("IH"), c("NH"), 128, 0), (m[:, 256:384], I, zc, 128, 0), (m[:, 256:384], c("IH"), wb[:, 128:256], 128, 0)]),
-           ["IH", "NH", "II", zk, k("as")], [k("m2")], mb)
+        ts(kwin(h, rnd, 0), wi[:, 384:512], 20.0, None, OP.mult, None, 128, [k("k2")], [k("K5")])
         ts(zwin(h, rnd, 1), m[:, 256:384], MAGIC, -MAGIC, OP.add, OP.add, 128, [k("m2")], [k("zf")], mb)
-        pe(singles(perm(h, lambda o: m[:, 384 + o:512:3], lambda s: c("IIh", s, s + 128), lambda o: wh[:, o:128:3], True)),
-           ["IIh", k("Pc")], [k("m3")], mb)
-        tt(wf[:, 896:1024], m[:, 384:512], kwin(h, rnd, 1), OP.subtract, 128, [k("m3"), kk_], [k("d2")], mb)
 
     def stage_c(h, rnd):
         last = rnd == RO - 1
@@ -436,11 +500,11 @@ def build_ops(T, q=0, net=None):
         ro = C["rstr"][1]
 
         def best(role):
-            a, n = 128 * role, "BC"[role]
-            scan(wf[:, a:a + 128], c("rst"), acc[:, a:a + 128], OP.add, OP.min, 128, [k("acc"), "rst"], [k("s1" + n)], ab)
-            src = wf[:, 127::-1] if role == 0 else wf[:, 255:127:-1]
-            scan(wf[:, 383 + a:255 + a:-1], T.CB[:, ro + 127:ro - 1:-1], src, OP.add, OP.min, 128, [k("s1" + n), "rstr"], [k("s2" + n)])
-            tt(wb[:, 640 + a:768 + a], acc[:, a:a + 128], wf[:, 256 + a:384 + a], OP.is_equal, 128, [k("acc"), k("s2" + n)], [k("oh" + n)], ab)
+            a, n, wd = 128 * role, "BC"[role], 128 + 32 * role
+            scan(wf[:, 3 * a:3 * a + wd], c("rst", 0, wd), acc[:, a:a + wd], OP.add, OP.min, wd, [k("acc"), "rst"], [k("s1" + n)], ab)
+            src = wf[:, 127::-1] if role == 0 else wf[:, 511:383:-1]
+            scan(wf[:, 255 + a:127 + a:-1], T.CB[:, ro + 127:ro - 1:-1], src, OP.add, OP.min, 128, [k("s1" + n), "rstr"], [k("s2" + n)])
+            tt(wb[:, 640 + a:768 + a], acc[:, a:a + 128], wf[:, 128 + a:256 + a], OP.is_equal, 128, [k("acc"), k("s2" + n)], [k("oh" + n)], ab)
 
         def partner():
             best(0)
@@ -464,7 +528,11 @@ def build_ops(T, q=0, net=None):
             pe(mms, ["II", "IH", "NH", k("yj"), k("zD")], [k("m2"), k("m3")], mb)
             cp(zwin(h, rnd, 2), m[:, 256:384], 128, [k("m2")], [k("yh")], mb, flex=True)
             if last:
-                ts(T["VA%d" % h][:, 0:128], m[:, 384:512], MAGIC, -MAGIC, OP.add, OP.add, 128, [k("m3")], [k("nw")], mb)
+                va, mv = T["VA%d" % h][:, :], T["mv%d" % h]
+                ts(va, m[:, 384:512], MAGIC, -MAGIC, OP.add, OP.add, 128, [k("m3")], [k("nw")], mb)
+                remote("all", [(va, mv)], k("bv"), 3000.0, [k("nw")], [k("mv")])
+                dma("S", [(mv[q], va)], k("ov"), 2000.0, [k("nw")], [k("mvo")])
+                dma("S", [(T["VL%d" % h][:, :], mv[:, rows(q), :])], k("vl"), 2200.0, [k("mv"), k("mvo")], [k("VL")])
             else:
                 ts(wi[:, 512:640], m[:, 384:512], 0.5, -0.25, OP.mult, OP.add, 128, [k("m3")], [k("nw")], mb)
 
@@ -473,17 +541,20 @@ def build_ops(T, q=0, net=None):
                 bias[0] = BIAS[12] * (1 - h) + BIAS[13]
                 partner()
                 bias[0] = BIAS[2] * (1 - h)
-            o = acc[:, 128 * role:128 * role + 128]
-            mms = [(o, c("ONES"), c("CR", 128 * role, 128 * role + 128), True, False, 128, 128, 0), (o, DB, c("nBD"), False, False, 128, 128, 0)]
+            wd = 128 + 32 * role
+            o = acc[:, 128 * role:128 * role + wd]
             if role:
-                mms.append((o, AR[0:8, :], c("EXa", 0, 128, 0, 8), False, False, 128, 128, 0))
-            pe(mms, ["ONES", "CR", "nBD", "EXa", k("zD")] + ["AR"] * role, [k("acc")], ab)
-            sd = session(6 + h)
-            pe(singles([(sap(sd, 128 * kk, 128 * kk + 128), c("II", 96 * role, 96 * role + 128), DB, 128, 0) for kk in range(4)]),
-               ["II", k("zD"), k("yg%d" % (2 * role))], [k("D4")], [sd])
-            lz = c("nII", 96 * role, 96 * role + 128)
+                mms = [(o, AR[0:11, :], c("CRC", 0, 160, 0, 11), True, False, wd, 128, 0)]
+            else:
+                mms = [(o, c("ONES"), c("CR"), True, False, wd, 128, 0)]
+            mms.append((o, DB, c("nBD", 96 * role, 96 * role + wd), False, False, wd, 128, 0))
+            pe(mms, ["ONES", "CR", "CRC", "nBD", k("zD")] + ["AR"] * role, [k("acc")], ab)
+            if role == 0:
+                sd = session(6 + h)
+                pe(singles([(sap(sd, 128 * kk, 128 * kk + 128), I, DB, 128, 0) for kk in range(4)]), ["II", k("zD"), k("yg0")], [k("D4")], [sd])
             for ch in range(4):
-                s, sl = sub_chunk(h, yg, [k("yg%d" % (2 * role)), k("yg%d" % (2 * role + 1))], 2048 * role, ch, I, lz, zB, [k("zD")])
+                s, sl = sub_chunk(h, yg, [k("yg%d" % (2 * role)), k("yg%d" % (2 * role + 1))], 2048 * role, ch,
+                                  c("II", 32 * role, 32 * role + 128), c("nII"), zB, [k("zD")])
                 r = ringbuf(h)
                 u, v = T["ur%d" % h][:, 512 * r:512 * r + 512], T["vr%d" % h][:, 512 * r:512 * r + 512]
                 act(u, sap(s), AF.Abs, 512, [sl], [k("u%d" % r)], [s])
@@ -492,31 +563,27 @@ def build_ops(T, q=0, net=None):
                 for buf, wt in (("ur", "Wn"), ("vr", "W2")):
                     for kk in range(4):
                         kq = 4 * ch + kk
-                        mv.append((acc[:, 128 * role + kq:128 * role + 128:16], T["%s%d" % (buf, h)][:, 512 * r + 128 * kk:512 * r + 128 * kk + 128],
-                                   c(wt, 2 * role, 2 * role + 8), False, kq == 15 and buf == "vr", 8, 128, 0))
+                        mv.append((acc[:, 128 * role + kq:128 * role + wd:16], T["%s%d" % (buf, h)][:, 512 * r + 128 * kk:512 * r + 128 * kk + 128],
+                                   c(wt, 6 * role, 8 + 8 * role), False, kq == 15 and buf == "vr", 8, 128, 0))
                 pe(mv, [k("u%d" % r), k("v%d" % r), "Wn", "W2", k("acc")], [k("acc")], ab)
         bias[0] = BIAS[3] * (1 - h) + BIAS[10]
         best(1)
-        tt(wb[:, 1152:1160], wf[:, 143:256:16], wf[:, 15:128:16], OP.is_le, 8, [k("s1B"), k("s1C")], [k("hit")])
+        tt(wb[:, 1152:1160], wf[:, 431:544:16], wf[:, 15:128:16], OP.is_le, 8, [k("s1B"), k("s1C")], [k("hit")])
         tt(wb[:, 1160:1168], wb[:, 1152:1160], wf[:, 15:128:16], OP.is_le, 8, [k("s1B"), k("hit")], [k("nei")])
         tt(wb[:, 1168:1184], wi[:, 168:184], wb[:, 1152:1168], OP.mult, 16, [k("hit"), k("nei"), k("hi")], [k("kh")])
         tt(wb[:, 1184:1200], wi[:, 184:200], wb[:, 1152:1168], OP.mult, 16, [k("hit"), k("nei"), k("lo")], [k("kl")])
         bias[0] = BIAS[14]
-        pe([(m[32:64, 384:512], wb[:, 768:800], I, True, True, 128, 32, 0),
-            (m[64:128, 384:512], wb[:, 800:864], I, True, True, 128, 64, 0),
-            (m[0:32, 384:512], wb[:, 864:896], I, True, True, 128, 32, 0)], ["II", k("ohC")], [k("m3")], mb)
+        pe(group([(m[:, 384:512], wb[:, 768:896], I, 128, 0)]), ["II", k("ohC")], [k("m3")], mb)
         tt(wh[:, 384:512], m[:, 384:512], wh[:, 128:256], OP.mult, 128, [k("m3"), k("Pc")], [k("payC")], mb)
-        pe(group([(m[:, 256:512], I, c("CT"), 256, 0), (m[:, 256:512], wb[:, 640:768], c("PM"), 256, 0),
-                  (m[:, 256:384], c("IIh", 0, 128), wh[:, 0:128], 128, 0), (m[:, 384:512], c("BBh", 32, 160), wh[:, 384:512], 128, 0)]),
-           ["II", "CT", "PM", "IIh", "BBh", k("ohB"), k("Pc"), k("payC")], [k("m2"), k("m3")], mb)
+        pe(group([(m[:, 256:512], wb[:, 640:768], c("PT"), 256, 0)]
+                 + [(m[:, 256:512], I, c("CT", 0, 256), 256, 0) if last else (m[:, 384:512], I, c("CT", 256, 384), 128, 0)]
+                 + [(m[:, 256:384], c("IIh"), wh[:, 0:128], 128, 0), (m[:, 384:512], c("BBh", 32, 160), wh[:, 384:512], 128, 0)]),
+           ["II", "CT", "PT", "IIh", "BBh", k("ohB"), k("Pc"), k("payC")], [k("m2"), k("m3")], mb)
         if last:
             cp(wf[:, 1024:1152], m[:, 256:384], 128, [k("m2")], [k("tu")], mb, flex=True)
-            tt(T["VA%d" % h][:, 128:256], m[:, 384:512], wf[:, 1024:1152], OP.max, 128, [k("m3"), k("tu")], [k("nc")], mb)
-            remote("all", [(T["VA%d" % h][:, :], T["mv%d" % h])], k("bv"), 3000.0, [k("nw"), k("nc")], [k("mv")])
-            dma("S", [(T["mv%d" % h][q], T["VA%d" % h][:, :])], k("ov"), 2000.0, [k("nw"), k("nc")], [k("mvo")])
-            dma("S", [(T["VL%d" % h][:, :], T["mv%d" % h][:, rows(q), :])], k("vl"), 2200.0, [k("mv"), k("mvo")], [k("VL")])
+            tt(T["MS%d" % h][:, 0:128], m[:, 384:512], wf[:, 1024:1152], OP.max, 128, [k("m3"), k("tu")], [k("nc")], mb)
         else:
-            cp(wf[:, 1024:1280], m[:, 256:512], 256, [k("m2"), k("m3")], [k("tu")], mb, flex=True)
+            ts(wf[:, 1024:1280], m[:, 256:512], 2048.0, None, OP.add, None, 256, [k("m2"), k("m3")], [k("tu")], mb, act=(AF.Identity, 2048.0, 1.0))
 
     def stage_e(h, rnd):
         last = rnd == RO - 1
@@ -546,45 +613,64 @@ def build_ops(T, q=0, net=None):
         if not last:
             cp(lwin(h, rnd + 1, 1), lwin(h, rnd + 1, 0), 128, [ln], [ln + "b"], rate=0.5, flex=True)
         bias[0] = BIAS[4] * (1 - h) + BIAS[9]
-        for j in range(2):
-            s = session(2 + h)
-            sl = "sl%d" % s["id"]
-            pe(group([(sap(s), RT, c("nSEL", 512 * j, 512 * j + 512, 0, 48), 512, 0)]
-                     + [(sap(s, 128 * a, 128 * a + 128), c("SEL", 512 * j + 128 * a, 512 * j + 128 * a + 128, 0, 48), RT, 128, 0) for a in range(4)]),
-               ["SEL", "nSEL", k("RT")], [sl], [s])
-            tt(wb[:, 2048 + 512 * j:2560 + 512 * j], sap(s), c("TRT"), OP.is_equal, 512, [sl, "TRT"], [k("e%d" % j)], [s])
+        blk = BLK
+        lo, hi = wb[0:48, 1024:1088], wb[0:48, 1088:1152]
+        sel = lambda b, n: c("SEL", 128 * b, 128 * b + n, 0, 48)
+        s = session(2 + h)
+        sl = "sl%d" % s["id"]
+        pe(group([(sap(s), RT, c("nSEL", 0, 512, 0, 48), 512, 0)] + [(sap(s, 64 * x, 64 * x + 64), sel(blk[x], 128), lo, 64, 0) for x in range(8)]),
+           sels + [k("RT")], [sl], [s])
+        tt(wb[:, 2048:2560], sap(s), c("TRT", 0, 512), OP.is_equal, 512, [sl, "TRT"], [k("e0")], [s])
+        s = session(2 + h)
+        sl = "sl%d" % s["id"]
+        pe([mm for j in range(2) for mm in group([(sap(s, 0, 256, 64 * j), hi, c("nSEL", 256 * j, 256 * j + 256, 0, 48), 256, 0)]
+                                                 + [(sap(s, 64 * x, 64 * x + 64, 64 * j), sel(2 * x + j, 64), hi, 64, 0) for x in range(4)])],
+           sels + [k("RT")], [sl], [s])
+        tt(wb[:, 2560:2816], sap(s, 0, 256), c("TRT", 512, 768), OP.is_equal, 256, [sl, "TRT"], [k("e1")], [s])
         pe(group([(m[:, 128:256], I, c("MKp"), 128, 0), (m[:, 128:256], c("EXK", 0, 128, 0, 48), RT, 128, 0)]
-                 + [(m[:, 128:256], c("Z8", 112 - 16 * b, 240 - 16 * b), wb[:, 2048 + 128 * b:2176 + 128 * b], 128, 0) for b in range(8)]),
-           ["II", "MKp", "EXK", "Z8", k("RT"), k("e0"), k("e1")], [k("m1")], mb)
+                 + [(m[:, 192:256], c("Zq", 96 - 32 * x, 224 - 32 * x), wb[:, 2560 + 64 * x:2624 + 64 * x], 64, 0) for x in range(4)]
+                 + [(m[:, 128:192], c("Z8", 112 - 16 * blk[x], 240 - 16 * blk[x]), wb[:, 2048 + 64 * x:2112 + 64 * x], 64, 0) for x in range(8)]),
+           ["II", "MKp", "EXK", "Z8", "Zq", k("RT"), k("e0"), k("e1")], [k("m1")], mb)
         scan(wf[:, 640:768], c("TR"), m[:, 128:256], OP.max, OP.min, 128, [k("m1"), "TR"], [k("sc")], mb)
-        cp(wu[:, 32:40], wf[:, 655:768:16], 8, [k("sc")], [k("ku")])
-        bias[0] = BIAS[7] * (1 - h) + BIAS[8]
+        cp(T["MS%d" % h][:, 128:136] if last else wu[:, 32:40], wf[:, 655:768:16], 8, [k("sc")], [k("ku")], flex=last)
+        bias[0] = LASTB[h] if last else BIAS[7] * (1 - h) + BIAS[8]
         ov = T["ov%d" % h]
+        c0 = 0
         for ch in range(4):
             o = ov[:, 512 * ch:512 * ch + 512]
             if ch < NE[h]:
                 s, sl = sub_chunk(4 + h, xg, [k("xg0"), k("xg1")], 0, ch, I, c("nII", 0, 128), zwin(h, rnd, 2), [k("yh")])
                 act(o, sap(s), AF.Abs, 512, [sl], [k("ov%d" % ch)], [s])
-                ts(o, o, 48.0, None, OP.is_gt, None, 512, [k("ov%d" % ch)], [k("ov%d" % ch)], rate=0.5)
+                if ch % 2 == 0 and ch + 1 < NE[h]:
+                    continue
+                o, ks = ov[:, 512 * c0:512 * ch + 512], [k("ov%d" % j) for j in range(c0, ch + 1)]
+                wt = over(o, o, 48.5, 512 * (ch + 1 - c0), ks, ks, (), 0.5, c("Ww"), c("Wv"))
             else:
-                s, sl = sub_chunk(4 + h, xg, [k("xg0"), k("xg1")], 0, ch, c("sI"), c("nsI"), zwin(h, rnd, 2), [k("yh")])
-                ts(o, sap(s), MAGIC, MAGIC, OP.add, OP.not_equal, 512, [sl], [k("ov%d" % ch)], [s])
-            mv = [(acc[:, 0:128], lwin(h, rnd, 0), c("THN"), True, False, 128, 128, 0)] if ch == 0 else []
-            for kq in range(4 * ch, 4 * ch + 4):
-                mv.append((acc[:, kq:128:16], ov[:, 128 * kq:128 * kq + 128], c("Ww"), False, kq == 15, 8, 128, 0))
-            pe(mv, [k("ov%d" % ch), "Ww", "THN", lk, k("acc")], [k("acc")], ab)
-        ts(wb[:, 1536:1664], acc[:, 0:128], -0.5, None, OP.is_gt, None, 128, [k("acc")], [k("off")], ab)
-        pe(group([(acc[:, 128:256], wb[:, 1536:1664], I, 128, 0)]), ["II", k("off")], [k("acc")], ab)
-        tt(acc[:, 128:256], acc[:, 128:256], wf[:, 896:1024], OP.mult, 128, [k("acc"), k("d2")], [k("acc")], ab)
-        tt(kwin(h, rnd, 2), acc[:, 128:256], kwin(h, rnd, 1), OP.add, 128, [k("acc"), kk_], [k("Kc")], ab)
+                s, sl = sub_chunk(4 + h, xg, [k("xg0"), k("xg1")], 0, ch, c("sI"), c("nsI"), zwin(h, rnd, 2), [k("yh"), "sI", "nsI"])
+                ks, wt = [k("ov%d" % ch)], c("Ww")
+                ts(o, sap(s), MAGIC, MAGIC, OP.add, OP.not_equal, 512, [sl], ks, [s])
+            mv = [(acc[:, 0:128], lwin(h, rnd, 0), c("THN"), True, False, 128, 128, 0)] if c0 == 0 else []
+            if c0 == 0 and NE[h] < 4:
+                mv.append((acc[:, 0:128], c("ONES"), c(k("THO")), False, False, 128, 128, 0))
+            for kq in range(4 * c0, 4 * ch + 4):
+                mv.append((acc[:, kq:128:16], ov[:, 128 * kq:128 * kq + 128], wt, False, kq == 15, 8, 128, 0))
+            pe(mv, ks + ["Ww", "Wv", "THN", "ONES", k("THO"), lk, k("acc")], [k("acc")], ab)
+            c0 = ch + 1
+        wt = over(wb[:, 1536:1664], acc[:, 0:128], -16384.25, 128, [k("acc")], [k("off")], ab, 1.0, c("PM"), c("PMh"))
+        pe(group([(acc[:, 128:384], I, c("CK"), 256, 0), (acc[:, 128:384], wb[:, 1536:1664], wt, 256, 0)]
+                 + [mm for a in (128, 256) for mm in perm(h, lambda o: acc[:, a + o:a + 128:3], lambda s: c("I20", s, s + 128), lambda o: wh[:, o:128:3], True)]),
+           ["II", "I20", "CK", "PM", "PMh", k("off"), k("Pc")], [k("acc")], ab)
+        tt(wf[:, 896:1024], acc[:, 128:256], kwin(h, rnd, 1), OP.min, 128, [k("acc"), kk_], [k("d2")], ab)
+        tt(kwin(h, rnd, 2), acc[:, 256:384], wf[:, 896:1024], OP.max, 128, [k("acc"), k("d2")], [k("Kc")], ab)
         rd = [k("su"), kk_, k("K5"), k("Kc")]
+        ts(Ku[:, L], kwin(h, rnd, 0, 3).indirect(su), 0.05, 0.25, OP.mult, OP.add, 128, rd, [k("Ku")], rate=GAM)
+        ops[-1]["ng"] = 128 * CYC
         if last:
-            gather(Kf[:, L], kwin(h, rnd, 0, 3), su, 128, rd, [k("Kf")], plus=2048.0)
+            cp(Kf[:, L], Ku[:, L], 128, [k("Ku")], [k("Kf")])
             remote("all", [(Kf[:, L], T["mk%d" % h])], k("bk"), 2800.0, [k("Kf")], [k("mk")])
             dma("S", [(T["mk%d" % h][q], Kf[:, L])], k("ok"), 2000.0, [k("Kf")], [k("mko")])
             dma("S", [(T.yk[:, L], T["mk%d" % h][:, rows(q), :])], k("yk"), 2200.0, [k("mk"), k("mko")], [k("yk")])
         else:
-            gather(Ku[:, L], kwin(h, rnd, 0, 3), su, 128, rd, [k("Ku")], flex=False, plus=2048.0)
             gather(kwin(h, rnd + 1, 1), kwin(h, rnd, 0, 3), su, 128, rd, [kn])
 
     def writes(h):
@@ -596,23 +682,25 @@ def build_ops(T, q=0, net=None):
 
     def last_writes(h):
         k = names(h)
-        wu = T["wu%d" % h]
-        remote("near", [(wu[:, 32:40], [T.LK[:, 32 * h + 8 * r:32 * h + 8 * r + 8] for r in range(N)])], k("bu"), 2500.0, [k("ku")], [k("LK")])
-        for r in range(N):
-            src = wu[rows(q), 32:40] if r == q else T.LK[rows(q), 32 * h + 8 * r:32 * h + 8 * r + 8]
-            cp(T.KU[rows(r), 8 * h:8 * h + 8], src, 8, [k("ku") if r == q else k("LK")], [k("KU%d" % r)])
-        rd = [k("KU%d" % r) for r in range(N)] + [k("VL")]
+        ms, lm = T["MS%d" % h], T["LM%d" % h]
+        remote("all", [(ms[:, 0:136], [lm[:, 136 * r:136 * r + 136] for r in range(N)])], k("bu"), 3000.0, [k("ku"), k("nc")], [k("LM")])
+        for j, r in enumerate([q] + others):
+            src = ms[rows(q), 0:136] if r == q else lm[rows(q), 136 * r:136 * r + 136]
+            cp(ms[rows(r), 136:272], src, 136, [k("ku"), k("nc")] if r == q else [k("LM")], [k("MT%d" % j)], flex=True)
+        rd = [k("MT%d" % j) for j in range(N)]
         ku = T.KU[:, 8 * h:8 * h + 8]
-        cp(T.NX[:, 0:WX].indirect(ku), T["VL%d" % h][:, 0:128], 128, rd + ["NX", "NXo"], ["NX"], rate=SCA)
-        cp(T.NS[:, 0:WX].indirect(ku), T["VL%d" % h][:, 128:256], 128, rd + ["NS", "NSo"], ["NS"], rate=SCA)
+        cp(ku, ms[:, 264:272], 8, rd, [k("KU")])
+        cp(T.NX[:, 0:WX].indirect(ku), T["VL%d" % h][:, :], 128, [k("KU"), k("VL"), "NX", "NXo"], ["NX"], rate=SCA)
+        cp(T.NS[:, 0:WX].indirect(ku), ms[:, 136:264], 128, [k("KU"), "NS", "NSo"], ["NS"], rate=SCA)
         ops[-1]["ns"] = ops[-2]["ns"] = 128 * CYC
 
     SA = slice(W, W + A)
     for rnd in range(RO):
         last = rnd == RO - 1
+        turn[0] = rnd
         for j, stage in enumerate((stage_a, stage_c, stage_e)):
             for h in range(2):
-                base[0] = len(ops) - 100 * (2 * j + h)
+                base[0] = len(ops) - 100 * (2 * j + h) - 1000 * last
                 stage(h, rnd)
         base[0] = len(ops) - 600
         bias[0] = 0.0
@@ -624,26 +712,20 @@ def build_ops(T, q=0, net=None):
             ts(AR[0:8, :], c("ONES", 0, 128, 0, 8), at[0:8, 2:3], None, OP.mult, None, 128, ["ONES", "af"], ["AR"], rate=0.5)
         if rnd == RO - 2:
             base[0] = len(ops) - 620
-            dma("S", [(T.ox[:, :, :], X[:, 0:W])], "ox", 6000.0, ["X"], ["ox"])
-            dma("S", [(T.oa[:, :, :], S[:, SA])], "oa", 4000.0, ["S"], ["oa"])
-            remote("each", [(T.ox, T.mx)], "bx", 6000.0, ["ox"], ["mx"])
-            remote("each", [(T.oa, T.ma)], "ba", 4000.0, ["oa"], ["ma"])
-            dma("S", [(T.NX[rows(q), 0:W], T.ox[q])], "nxo", 3000.0, ["ox"], ["NXo"])
-            dma("S", [(T.NS[rows(q), SA], T.oa[q])], "nso", 3000.0, ["oa"], ["NSo"])
+            dma("S", [(T.ox[r], X[rows(r), 0:W]) for r in others], "ox", 6000.0, ["X"], ["ox"])
+            dma("S", [(T.oa[r], S[rows(r), SA]) for r in others], "oa", 4000.0, ["S"], ["oa"])
+            remote("turn", [(T.ox, T.mx)], "bx", 6000.0, ["ox"], ["mx"])
+            remote("turn", [(T.oa, T.ma)], "ba", 4000.0, ["oa"], ["ma"])
+            dma("S", [(T.NX[rows(q), 0:W], X[rows(q), 0:W])], "nxo", 3000.0, ["X", "ox"], ["NXo"])
+            dma("S", [(T.NS[rows(q), SA], S[rows(q), SA])], "nso", 3000.0, ["S", "oa"], ["NSo"])
             dma("S", [(T.NX[rows(r), 0:W], T.mx[r]) for r in others], "nx", 5000.0, ["mx"], ["NX"])
             dma("S", [(T.NS[rows(r), SA], T.ma[r]) for r in others], "ns", 4000.0, ["ma"], ["NS"])
     base[0] = len(ops) - 640
-    bias[0] = -20000.0
-    ts(c("t6"), c("t2", 0, 128), 8.0, col("pm"), OP.is_lt, OP.mult, 128, ["t2", "c.pm", "HP"], ["t6"], rate=0.5)
-    tt(c("LWa"), c("t6"), c("BB", 0, 128), OP.mult, 128, ["t6", "BB"], ["LWa"])
-    ts(c("t6"), c("t2", 0, 128), 8.0, col("pm"), OP.is_ge, OP.mult, 128, ["t2", "c.pm"], ["t6"], rate=0.5)
-    tt(c("LWb"), c("t6"), c("BB", 0, 128), OP.mult, 128, ["t6", "BB"], ["LWb"])
-    bias[0] = 0.0
     m = T.ps7
     pe(group([(m[:, 0:128], c("LWa"), lwin(0, RO, 0), 128, 0), (m[:, 0:128], c("LWb"), lwin(1, RO, 0), 128, 0)]),
        ["LWa", "LWb", skeys(0, RO)[1], skeys(1, RO)[1]], ["m01"], [7])
     cp(T.Lo[:, :], m[:, 0:128], 128, ["m01"], ["Lo"], [7], flex=True)
-    remote("two", [(z[:, :], T.mz), (T.Lo[:, :], T.ml)], "zl", 2800.0, ["z0", "z1", "Lo"], ["mz"])
+    remote("all", [(z[:, :], T.mz), (T.Lo[:, :], T.ml)], "zl", 2800.0, ["z0", "z1", "Lo"], ["mz"])
     dma("S", [(T.mz[q], z[:, :]), (T.ml[q], T.Lo[:, :])], "zlo", 2000.0, ["z0", "z1", "Lo"], ["mzo"])
     dma("S", [(T.yz[:, :], T.mz[:, rows(q), :])], "yz", 2200.0, ["mz", "mzo"], ["yz"])
     dma("S", [(T.yl[:, :], T.ml[:, 32 * q:32 * q + 32:8, :])], "yl", 2200.0, ["mz", "mzo"], ["yl"])
@@ -653,7 +735,7 @@ def build_ops(T, q=0, net=None):
     return ops
 
 
-READY = {"in0": 10000.0, "in1": 13000.0, "in2": 16000.0}
+READY = {"in0": 9000.0, "in1": 7000.0, "in2": 16000.0, "inx0": 7500.0, "inx1": 9000.0, "inx2": 10500.0}
 ENG = ("P", "V", "A", "G", "S")
 
 
@@ -692,8 +774,8 @@ def links(ops):
         prio[i] = min(a[0] for a in ops[i]["alts"].values()) + ops[i].get("lat", LAT) + max([prio[s] for s in succ[i]], default=0.0)
     for o in ops:
         o["in"] = max([READY.get(key, 0.0) for key in o["r"]], default=0.0)
-        if "late" in o:
-            o["in"] = 9000.0
+        if "G" in o["alts"] and "early" not in o:
+            o["in"] = max(o["in"], 10000.0)
     return deps, succ, prio
 
 
@@ -756,6 +838,7 @@ def schedule(ops, lk):
         st, i, e, cost, banks = best
         ready.remove(i)
         eng[i], end[i] = e, st + cost
+        ops[i]["e"] = e
         efree[e] = end[i]
         for b0, b in zip(ops[i]["b"], banks):
             if isinstance(b0, dict):
@@ -776,7 +859,7 @@ def schedule(ops, lk):
     return order, eng, deps, end
 
 
-SPREAD = [(1.5, 3.8, 60.0), (1.04, 1.6, 40.0), (2.08, 6.0, 60.0), (1.9, 5.0, 120.0)]
+SPREAD = [(1.5, 3.8, 170.0), (1.9, 5.0, 130.0)]
 TUNED = []
 
 
@@ -823,6 +906,117 @@ def tune(ops, lk, steps):
     return best
 
 
+def polish(ops, lk, steps):
+    order, eng, _, _ = schedule(ops, lk)
+    n = len(ops)
+    banks = [[b["bank"] if isinstance(b, dict) else b for b in o["b"]] for o in ops]
+    fixed = [set(d) for d in lk[0]]
+    stay, members = {}, {}
+    for i in order:
+        for b in ops[i]["b"]:
+            if isinstance(b, dict):
+                if b["id"] not in members:
+                    members[b["id"]] = []
+                    if b["bank"] in stay:
+                        fixed[i].update(members[stay[b["bank"]]])
+                    stay[b["bank"]] = b["id"]
+                members[b["id"]].append(i)
+    fixed = [sorted(d) for d in fixed]
+    latm = [[o.get("lat", 0.0) * x[3] for o in ops] for x in POLISH]
+    inm = [[o["in"] * x[4] for o in ops] for x in POLISH]
+    cost = [[{e: a[0] + o.get("ng", 0) * (x[0] - GAM) + o.get("ns", 0) * (x[1] - SCA) for e, a in o["alts"].items()} for o in ops]
+            for x in POLISH]
+
+    def walk(order, eng, m):
+        lat, co, lats, ins = POLISH[m][2], cost[m], latm[m], inm[m]
+        fin, why = [0.0] * n, [-1] * n
+        free, elast, blast = {e: 0.0 for e in ENG}, {e: -1 for e in ENG}, [-1] * 8
+        most, last = 0.0, -1
+        for i in order:
+            e = eng[i]
+            st, w = free[e], elast[e]
+            if ins[i] > st:
+                st, w = ins[i], -1
+            pe_ = e == "P"
+            for d in fixed[i]:
+                t = fin[d] if pe_ and eng[d] == "P" else fin[d] + lat
+                if t > st:
+                    st, w = t, d
+            for b in banks[i]:
+                d = blast[b]
+                if d >= 0:
+                    t = fin[d] if pe_ and eng[d] == "P" else fin[d] + lat
+                    if t > st:
+                        st, w = t, d
+                blast[b] = i
+            t = free[e] = st + co[i][e]
+            elast[e] = i
+            t += lats[i]
+            fin[i], why[i] = t, w
+            if t > most:
+                most, last = t, i
+        return most, why, last
+
+    def lift(order, i, j):
+        a, b = order.index(j), order.index(i)
+        need, up, rest = set(fixed[i]), [i], []
+        for x in order[b - 1:a - 1 if a else None:-1]:
+            if x in need:
+                up.append(x)
+                need.update(fixed[x])
+            else:
+                rest.append(x)
+        if j in up:
+            return None
+        return order[:a] + up[::-1] + rest[::-1] + order[b + 1:]
+
+    place = {(o["pos"], o["rnd"]): i for i, o in enumerate(ops) if o["pos"] >= 0}
+
+    def twin(i, s):
+        return i if s == 0 else place.get((ops[i]["pos"], ops[i]["rnd"] + s))
+
+    rng = np.random.RandomState(11)
+    res = [walk(order, eng, m) for m in range(len(POLISH))]
+    now = best = sum(r[0] for r in res)
+    keep = (order, list(eng))
+    for step in range(steps):
+        _, why, i = res[rng.randint(len(res))]
+        pairs = []
+        while why[i] >= 0:
+            if why[i] not in fixed[i] or len(ops[i]["alts"]) > 1:
+                pairs.append((i, why[i]))
+            i = why[i]
+        i, j = pairs[rng.randint(len(pairs))]
+        new, ne = order, eng
+        shifts = range(1 - RO, RO) if rng.rand() < ALIKE else [0]
+        flip = [x for x in (i, j) if len(ops[x]["alts"]) > 1]
+        if flip and (j in fixed[i] or rng.rand() < 0.3):
+            x = flip[rng.randint(len(flip))]
+            ne = list(eng)
+            for s in shifts:
+                y = twin(x, s)
+                if y is not None:
+                    ne[y] = "V" if eng[x] == "A" else "A"
+        else:
+            for s in shifts:
+                x, y = twin(i, s), twin(j, s)
+                if x is not None and y is not None and new.index(y) < new.index(x):
+                    new = lift(new, x, y) or new
+            if new is order:
+                continue
+        r = [walk(new, ne, m) for m in range(len(POLISH))]
+        s = sum(x[0] for x in r)
+        if s <= now + HEAT * (1.0 - step / steps) * rng.exponential():
+            order, eng, res, now = new, ne, r, s
+            if s < best:
+                best, keep = s, (order, list(eng))
+    return keep[0], keep[1], banks, fixed, best / len(POLISH)
+
+
+POLISH = [(1.5, 3.8, 170.0, 1.0, 0.9), (1.8, 5.0, 120.0, 1.5, 1.0)]
+HEAT, ALIKE = 60.0, 0.7
+
+
 def rank_program(g, core, T, topo):
     q = T.rank_of(core)
     if q is None:
@@ -863,17 +1057,32 @@ def rank_program(g, core, T, topo):
 
     quarters = sum(len(shared(r)) // 4 for r in others)
     whole = sum(len(shared(r)) for r in others)
-    net = {"each": each, "all": spread, "near": spread, "two": spread,
-           "in": {"each": quarters, "all": whole, "near": whole, "two": whole}}
+
+    def turn(items, rsem):
+        (src, land), = items
+        for r in others:
+            send(src[r], land[q], r, rsem)
 
     def full(r):
         return len(topo.engines(T.cores[r], core))
 
+    net = {"turn": turn, "all": spread, "in": {"turn": sum(full(r) for r in others), "all": whole}}
+
     ops = build_ops(T, q, net)
-    lk = links(ops)
     if not TUNED:
-        TUNED.append(tune(ops, lk, STEPS))
-    order, eng, deps, end = schedule(ops, lk)
+        lk = links(ops)
+        tune(ops, lk, STEPS)
+        TUNED.extend(polish(ops, lk, STEPS2))
+    order, eng, banks, fixed = TUNED[:4]
+    deps, end, blast = [set(d) for d in fixed], {}, {}
+    for j, i in enumerate(order):
+        ops[i]["e"], end[i] = eng[i], j
+        for b0, b in zip(ops[i]["b"], banks[i]):
+            if isinstance(b0, dict):
+                b0["bank"] = b
+            if b in blast:
+                deps[i].add(blast[b])
+            blast[b] = i
     Q = {"P": g.tensor, "V": g.vector, "A": g.scalar, "G": g, "S": g.sync}
     idx, cnt = {}, {"P": 0, "V": 0, "A": 0, "G": 0}
     for i in order:
@@ -881,8 +1090,9 @@ def rank_program(g, core, T, topo):
             cnt[eng[i]] += 1
             idx[i] = cnt[eng[i]]
 
-    for r in others:
-        g.sync.dma_start(T.sx[r], T.x0[rows(r), :]).then_inc(sem["stx%d" % r], 16)
+    for j, r in enumerate(others):
+        for cq in range(4):
+            g.sync.dma_start(T.SX[rows(cq), 1024 * j:1024 * j + 1024], T.x0[rows(r), 1024 * cq:1024 * cq + 1024]).then_inc(sem["stx%d" % j], 16)
     g.scalar.dma_start(T.sk[:, :, :], T.kw[:]).then_inc(sem.stk, 16)
     g.scalar.dma_start(T.sl[:, :, :], T.l0[:]).then_inc(sem.stk, 16)
     g.scalar.dma_start(T.sz[:, :, :], T.z0[:]).then_inc(sem.stk, 16)
@@ -890,10 +1100,12 @@ def rank_program(g, core, T, topo):
     g.scalar.dma_start(T.lk[q], T.kw[rows(q), :]).then_inc(sem.own, 16)
     g.scalar.dma_start(T.ll[q], T.l0[2 * q:2 * q + 2, :]).then_inc(sem.own, 16)
     g.sync.dma_start(T.X[rows(q), 0:W], T.x0[rows(q), :]).then_inc(sem.inx, 16)
-    g.sync.wait_ge(sem["stx%d" % others[2]], 16)
+    g.sync.wait_ge(sem.stx2, 64)
     for r in others:
         g.sync.dma_start(T.ss[r], T.asc[rows(r), :]).then_inc(sem.sts, 16)
-    nin, nink, nins = 16 * N, 48, 16 * N
+    back = [(q - d) % N for d in (1, 2, 3)]
+    landed = [("in0", sem.ink, 48), ("in1", sem.inx, 16), ("in2", sem.ins, 16 * N)]
+    landed += [("inx%d" % j, sem["ax%d" % j], full(r)) for j, r in enumerate(back)]
 
     known = {e: {} for e in Q}
     clock = {}
@@ -914,7 +1126,10 @@ def rank_program(g, core, T, topo):
                 if "far" not in ops[d]:
                     for f2, v2 in clock[d].items():
                         kn[f2] = max(kn.get(f2, 0), v2)
-        for key, s, v in (("in0", sem.ink, nink), ("in1", sem.inx, nin), ("in2", sem.ins, nins)):
+        if e == "G" and i in idx and idx[i] - 1 > kn.get("G", 0):
+            g.wait_ge(sem.G, idx[i] - 1)
+            kn["G"] = idx[i] - 1
+        for key, s, v in landed:
             if key in ops[i]["r"] and not kn.get(key, 0):
                 Q[e].wait_ge(s, v)
                 kn[key] = 1
@@ -924,7 +1139,7 @@ def rank_program(g, core, T, topo):
             ops[i]["alts"][e][1](g).then_inc(sem[e], 1)
         clock[i] = dict(kn)
 
-    gfirst = [i for i in order if eng[i] == "G" and not deps[i] and "late" not in ops[i]]
+    gfirst = [i for i in order if "early" in ops[i]]
     for i in gfirst:
         emit(i)
     g.wait_ge(sem.stk, 48)
@@ -932,22 +1147,17 @@ def rank_program(g, core, T, topo):
     each([(T.sk, T.lk)], sem.ak)
     each([(T.sz, T.lz)], sem.ak)
     for j, r in enumerate(others):
-        g.wait_ge(sem["stx%d" % r], 16)
-        send(T.sx[r], T.lx[q], r, sem["ax%d" % q])
+        g.wait_ge(sem["stx%d" % j], 64)
+        send(T.SX[:, 1024 * j:1024 * j + 1024], T.LX[:, 1024 * j:1024 * j + 1024], r, sem["ax%d" % j])
     g.wait_ge(sem.sts, 48)
-    each([(T.ss, T.ls)], sem.as_)
-    back = [(q - d) % N for d in (1, 2, 3)]
+    turn([(T.ss, T.ls)], sem.as_)
     g.sync.wait_ge(sem.own, 48)
     g.sync.wait_ge(sem.ak, 3 * quarters)
     g.sync.dma_start(T.Ki[:, :], T.lk[:, :, :]).then_inc(sem.ink, 16)
     g.sync.dma_start(T.Li[0:8, :], T.ll[:, :, :]).then_inc(sem.ink, 16)
     g.sync.dma_start(T.z[:, :], T.lz[:, :, :]).then_inc(sem.ink, 16)
-    for j, r in enumerate(back):
-        g.sync.wait_ge(sem["ax%d" % r], full(r))
-        g.sync.dma_start(T.X[rows(r), 0:W], T.lx[r]).then_inc(sem.inx, 16)
-        if j == 0:
-            g.sync.dma_start(T.Si[rows(q), :], T.asc[rows(q), :]).then_inc(sem.ins, 16)
-    g.sync.wait_ge(sem.as_, quarters)
+    g.sync.dma_start(T.Si[rows(q), :], T.asc[rows(q), :]).then_inc(sem.ins, 16)
+    g.sync.wait_ge(sem.as_, net["in"]["turn"])
     for r in back:
         g.sync.dma_start(T.Si[rows(r), :], T.ls[r]).then_inc(sem.ins, 16)
 

import numpy as np
from concourse.bass import DstId, RemoteDMATransfer
from concourse.mybir import AluOpType as OP, AxisListType, ActivationFunctionType as AF

N, W, A, TL, RO, EPS, TH = 4, 4096, 1024, 256, 4, 48, 720
WX = 5248
NRING = 6
PAIR = [[], []]
BLK = [0, 2, 4, 6, 1, 3, 5, 7]
BIAS = [8000, -3000, 12000, 8000, -1000, 3000, 3000, 2000, 0, 3000, 1000, 8000, 4000, 5000, 0]
NE = [4, 4]
S97 = 169.0 / 16384
LASTB = [0, 0]
STEPS, STEPS2 = 3500, 15000
WIN, VPEN = 120.0, 150.0
NUDGE = {}
LEAN = {}
GAM, SCA = 1.5, 3.8
MAGIC = 12582912.0
U = 2.0 ** -13

SCRATCH = {
    "X": ("sbuf", [128, WX], "bfloat16"), "S": ("sbuf", [128, WX], "float32"),
    "NX": ("sbuf", [128, WX], "bfloat16"), "NS": ("sbuf", [128, WX], "float32"),
    "Si": ("sbuf", [128, A], "int32"), "Ki": ("sbuf", [128, TL], "int32"), "Li": ("sbuf", [128, TL], "int32"),
    "Lb": ("sbuf", [128, TL], "bfloat16"), "Lo": ("sbuf", [128, 128], "float32"),
    "Ku": ("sbuf", [128, TL], "uint16"), "Kf": ("sbuf", [128, TL], "float32"),
    "z": ("sbuf", [128, TL], "bfloat16"), "AR": ("sbuf", [128, 128], "bfloat16"),
    "KU": ("sbuf", [128, 16], "uint16"),
    "at": ("sbuf", [128, 16], "float32"), "ai": ("sbuf", [128, 16], "int32"),
    "CB": ("sbuf", [128, 9984], "bfloat16"), "CF": ("sbuf", [128, 368], "float32"), "C16": ("sbuf", [128, 912], "float16"),
    "CI": ("sbuf", [128, 16], "int32"), "TB": ("sbuf", [128, 1776], "bfloat16"),
    "SX": ("sbuf", [128, 3072], "bfloat16"), "LX": ("sbuf", [128, 3072], "bfloat16"), "mx": ("dram", [4, 128, 1024], "bfloat16"),
    "sz": ("dram", [4, 128, 64], "bfloat16"), "lz": ("dram", [4, 128, 64], "bfloat16"),
    "sk": ("dram", [4, 128, 64], "int32"), "lk": ("dram", [4, 128, 64], "int32"),
    "sl": ("dram", [4, 128, 4], "int32"), "ll": ("dram", [4, 128, 4], "int32"),
    "ss": ("dram", [4, 128, 256], "int32"), "ls": ("dram", [4, 128, 256], "int32"),
    "ox": ("dram", [4, 128, 1024], "bfloat16"),
    "oa": ("dram", [4, 128, 256], "float32"), "ma": ("dram", [4, 128, 256], "float32"),
    "mz": ("dram", [4, 128, 256], "bfloat16"), "ml": ("dram", [4, 128, 128], "float32"),
}
for _h in range(2):
    SCRATCH.update({
        "xg%d" % _h: ("sbuf", [128, 2048], "bfloat16"), "yg%d" % _h: ("sbuf", [128, 4096], "bfloat16"),
        "ov%d" % _h: ("sbuf", [128, 2048], "bfloat16"),
        "ur%d" % _h: ("sbuf", [128, 512 * NRING], "bfloat16"), "vr%d" % _h: ("sbuf", [128, 512 * NRING], "bfloat16"),
        "wb%d" % _h: ("sbuf", [128, 4608], "bfloat16"), "wf%d" % _h: ("sbuf", [128, 2176], "float32"),
        "wi%d" % _h: ("sbuf", [128, 1024], "int32"), "wu%d" % _h: ("sbuf", [128, 320], "uint16"),
        "wh%d" % _h: ("sbuf", [128, 512], "float16"),
        "VA%d" % _h: ("sbuf", [128, 128], "bfloat16"), "VL%d" % _h: ("sbuf", [128, 128], "bfloat16"),
        "MS%d" % _h: ("sbuf", [128, 272], "float32"), "LM%d" % _h: ("sbuf", [128, 544], "float32"),
        "mv%d" % _h: ("dram", [4, 128, 128], "bfloat16"), "mk%d" % _h: ("dram", [4, 128, 128], "float32"),
    })
for _b in range(8):
    SCRATCH["ps%d" % _b] = ("psum", [128, 512], "float32")

SEMAPHORES = ["P", "V", "A", "G", "stx0", "stx1", "stx2", "stk", "sts", "snd", "own",
              "ax0", "ax1", "ax2", "ak", "as_", "inx", "ink", "ins",
              "ox", "oa", "bx", "ba", "nx", "ns", "nxo", "nso", "zl", "zlo", "yx", "ya", "yz", "yl"]
for _h in range(2):
    SEMAPHORES += [_s + str(_h) for _s in ("bv", "ov", "vl", "bu", "bk", "ok", "yk")]

CYC, PCYC, LAT, FIX = 0.83, 0.42, 170.0, 15.0


def build_ops(T, q=0, net=None):
    ops = []
    others = [(q + d) % N for d in (1, 2, 3)]
    rows = lambda r: slice(32 * r, 32 * r + 32)

    def add(alts, reads, writes, banks=()):
        ops.append({"alts": alts, "r": list(reads), "w": list(writes), "b": list(banks), "bias": bias[0],
                    "pos": -1 if base[0] is None else len(ops) - base[0], "rnd": turn[0]})

    bias, base, turn = [0.0], [None], [0]

    def vc(n, rate=1.0):
        return FIX + max(64, n * rate) * CYC

    nsess = [0]

    def session(h):
        nsess[0] += 1
        return {"bank": None, "id": nsess[0], "h": h, "left": 0}

    def sap(s, a=0, b=512, p0=None):
        return ("slot", s, a, b, p0)

    def R(ap):
        if not isinstance(ap, tuple):
            return ap
        if ap[0] == "by":
            return ap[2] if ap[1]["e"] == "V" else ap[3]
        if ap[4] is None:
            return T["ps%d" % ap[1]["bank"]][:, ap[2]:ap[3]]
        return T["ps%d" % ap[1]["bank"]][ap[4]:ap[4] + 64, ap[2]:ap[3]]

    def over(out, in_, thr, n, reads, writes, banks, rate, wv, wa):
        add({"V": (vc(n, rate), lambda g: g.vector.tensor_scalar(out, in_, thr, 0.5, OP.is_gt, OP.subtract)),
             "A": (vc(n) + 15, lambda g: g.scalar.activation(out, in_, AF.Sign, bias=-thr))}, reads, writes, banks)
        return ("by", ops[-1], wv, wa)

    def pe(mms, reads, writes, banks):
        cost = 30.0
        for (o, l, r, st, sp, n, m, f) in mms:
            cost += max(min(64, m), n) * (4 if f else 1) * PCYC

        def run(g):
            last = None
            for (o, l, r, st, sp, n, m, f) in mms:
                last = g.tensor.matmul(R(o), R(l), R(r), st, sp)
            return last
        add({"P": (cost, run)}, reads, writes, banks)

    def group(mms):
        return [(o, l, r, j == 0, j == len(mms) - 1, n, 128, f) for j, (o, l, r, n, f) in enumerate(mms)]

    def ts(out, in0, s1, s2, op0, op1, n, reads, writes, banks=(), rate=1.0, act=None):
        if op1 is None:
            alts = {"V": (vc(n, rate), lambda g: g.vector.tensor_scalar(R(out), R(in0), s1, None, op0))}
        else:
            alts = {"V": (vc(n, rate), lambda g: g.vector.tensor_scalar(R(out), R(in0), s1, s2, op0, op1))}
        if act is not None:
            alts["A"] = (vc(n, max(rate, 1.0)) + 15, lambda g: g.scalar.activation(out, R(in0), act[0], bias=act[1], scale=act[2]))
        add(alts, reads, writes, banks)

    def tt(out, a, b, op, n, reads, writes, banks=(), rate=None):
        if rate is None:
            rate = 1.0 if banks else 2.0
        add({"V": (vc(n, rate), lambda g: g.vector.tensor_tensor(out, R(a), R(b), op))}, reads, writes, banks)

    def cp(out, in_, n, reads, writes, banks=(), rate=1.0, flex=False):
        alts = {"V": (vc(n, rate), lambda g: g.vector.tensor_copy(out, R(in_)))}
        if flex:
            alts["A"] = (vc(n, max(rate, 1.0)) + 15, lambda g: g.scalar.activation(out, R(in_), AF.Copy))
        add(alts, reads, writes, banks)

    def act(out, in_, func, n, reads, writes, banks=(), bias=0.0):
        add({"A": (vc(n) + 15, lambda g: g.scalar.activation(R(out), R(in_), func, bias=bias))}, reads, writes, banks)

    def scan(out, d0, d1, op0, op1, n, reads, writes, banks=(), rate=1.0):
        add({"V": (vc(n, rate), lambda g: g.vector.tensor_tensor_scan(out, d0, d1, 0.0, op0, op1))}, reads, writes, banks)

    def iota(out, pat, base, cm, n, writes, isint=False):
        if isint:
            add({"G": (130 + 2 * n * CYC, lambda g: g.iota(out, pat, base, cm))}, [], writes)
        else:
            add({"G": (130 + 2 * n * CYC, lambda g: g.iota(out, pat, base, cm, allow_small_or_imprecise_dtypes=True))}, [], writes)

    def mset(ap, v, n, writes, rate=0.5, late=False):
        if late:
            iota(ap, [[0, n]], int(v), 0, n, writes)
        else:
            add({"V": (vc(n, rate), lambda g: g.vector.memset(ap, v))}, [], writes)

    def pick(out, in_, pat, op, fill, base, cm, n, reads, writes):
        add({"G": (170 + 2 * n * CYC, lambda g: g.affine_select(out, in_, pat, op, fill, base, cm))}, reads, writes)

    def dma(e, pairs, sem, lat, reads, writes):
        def run(g):
            for o, i in pairs:
                (g.sync if e == "S" else g.scalar).dma_start(o, i).then_inc(T.sem[sem], 16)
        add({e: (60.0 * len(pairs), run)}, reads, writes)
        ops[-1].update({"sem": sem, "val": 16 * len(pairs), "lat": lat})

    def remote(kind, items, sem, lat, reads, writes):
        add({"G": (200.0, lambda g: net[kind](items, T.sem[sem]))}, reads, writes)
        ops[-1].update({"sem": sem, "val": net["in"][kind] if net else 0, "lat": lat, "far": 1})

    pos = {"CB": 0, "CF": 0, "TB": 0, "C16": 0}
    C = {}

    def alloc(buf, name, n):
        C[name] = (T[buf], pos[buf], n)
        pos[buf] += (n + 15) // 16 * 16

    def c(name, a=0, b=None, p0=0, p1=128):
        t, o, n = C[name]
        return t[p0:p1, o + a:o + (n if b is None else b)]

    for nm, n in (("II", 256), ("nII", 128), ("IH", 128), ("I16", 128), ("I17", 128), ("PM", 256), ("PMh", 256), ("PT", 256), ("CK", 256), ("ONES", 128), ("Wv", 8),
                  ("MM", 128), ("BB", 256), ("B8", 16), ("nB8", 8), ("Wd", 8), ("Ww", 8), ("Wn", 16), ("W2", 16), ("LWa", 128), ("LWb", 128),
                  ("W4V", 8), ("CH", 256), ("THN", 128), ("WV", 128), ("W4", 256), ("nBD", 256),
                  ("MM16", 128), ("MK", 256), ("MK2", 128), ("MKp", 128), ("MKt", 128), ("hold", 256), ("rst", 160), ("rstr", 128),
                  ("HP", 128), ("CR", 128), ("CRC", 160), ("EX0", 256), ("EXb", 128), ("EXK", 128), ("TRT", 768), ("Z8", 240), ("Zq", 224),
                  ("LS", 128), ("CT", 384), ("NH", 128), ("C2", 16), ("SEL", 1024), ("nSEL", 512),
                  ("sI", 128), ("nsI", 128), ("THO0", 128), ("THO1", 128)):
        alloc("CB", nm, n)
    for nm, n in (("TR", 128), ("t4", 64), ("t5", 128), ("col", 32), ("sel", 8)):
        alloc("CF", nm, n)
    for nm, n in (("IIh", 128), ("I20", 256), ("BBh", 256), ("W21", 256), ("B8h", 8)):
        alloc("C16", nm, n)
    for nm, n in (("t0", 256), ("t1", 256), ("t2", 256), ("t3", 16), ("t6", 128), ("t7", 160), ("t8", 128), ("nONE", 64), ("zero", 512)):
        alloc("TB", nm, n)
    colnames = ["p", "pm", "pb", "p7", "h8", "w", "pw", "th", "nth", "thn", "w21", "p63", "p16", "w4", "m15", "wsel", "lwa", "lwb",
                "sp", "e0", "e1", "e2", "b0", "b1", "b2", "b3", "f0", "f1", "f2", "f3"]

    def col(nm, p0=0, p1=128):
        k = colnames.index(nm)
        return c("col", k, k + 1, p0, p1)

    CI = T.CI
    iota(CI[:, 0:1], [[0, 1]], 0, 1, 1, ["ci0"], True)
    iota(c("t0"), [[0, 2], [1, 128]], 0, 0, 256, ["t0"])
    iota(c("t2"), [[0, 16], [1, 16]], 0, 0, 256, ["t2"])
    iota(c("t3"), [[0, 2], [1, 8]], 0, 0, 16, ["t3"])
    iota(c("t1"), [[0, 2], [1, 8], [0, 16]], 0, 0, 256, ["t1"])
    for o in ops:
        o["early"] = 1
    iota(c("zero"), [[0, 512]], 0, 0, 512, ["zero"])

    def eye(dst, v, a=0):
        pick(c(dst, a, a + 128), c("zero", 0, 128), [[-1, 128]], OP.not_equal, v, 0, 1, 128, ["zero"], [dst])
    cp(col("p"), CI[:, 0:1], 1, ["ci0"], ["c.p"])
    for j, (nm, s1, s2) in enumerate((("pm", 0, 15), ("pb", 4, 7), ("p7", 0, 7), ("h8", 3, 1))):
        ts(CI[:, 1 + j:2 + j], CI[:, 0:1], s1, s2, OP.arith_shift_right, OP.bitwise_and, 1, ["ci0"], ["ci%d" % (1 + j)])
        cp(col(nm), CI[:, 1 + j:2 + j], 1, ["ci%d" % (1 + j)], ["c." + nm])

    def cts(nm, src, s1, s2, o0, o1):
        rd = ["c." + s for s in (src, s1, s2) if isinstance(s, str)]
        a, b = (col(s) if isinstance(s, str) else s for s in (s1, s2))
        alt = None
        if o0 == OP.mult and o1 in (None, OP.add):
            alt = (AF.Identity, 0.0 if o1 is None else b, a)
        if o0 == OP.add and o1 is None:
            alt = (AF.Identity, a, 1.0)
        ts(col(nm), col(src), a, b, o0, o1, 1, rd, ["c." + nm], act=alt)

    def eq(dst, src, cn, mul=None, n=None):
        n = n or C[dst][2]
        if mul is None:
            ts(c(dst, 0, n), c(src, 0, n), col(cn), None, OP.is_equal, None, n, [src, "c." + cn], [dst], rate=0.5)
        else:
            rd = [src, "c." + cn] + (["c." + mul] if isinstance(mul, str) else [])
            ts(c(dst, 0, n), c(src, 0, n), col(cn), col(mul) if isinstance(mul, str) else mul, OP.is_equal, OP.mult, n, rd, [dst], rate=0.5)

    def lin(dst, src, mul, off=0.0, a=0, n=None, rate=0.5, flex=True):
        n = n or C[dst][2]
        m = col(mul) if isinstance(mul, str) else mul
        o = col(off) if isinstance(off, str) else off
        rd = [src] + ["c." + s for s in (mul, off) if isinstance(s, str)]
        ts(c(dst, a, a + n), c(src, 0, n), m, o, OP.mult, OP.add, n, rd, [dst], rate=rate, act=(AF.Identity, o, m) if flex else None)

    eq("II", "t0", "p")
    eq("MM", "t2", "pm")
    eq("BB", "t1", "pb")
    eq("B8", "t3", "pb")
    lin("nII", "II", -1.0); lin("IH", "II", 0.5); lin("I16", "II", 65536.0); lin("I17", "II", 131072.0)
    for nm, v in (("PT", 8192.0), ("PMh", 81920.0), ("PM", 163840.0)):
        eye(nm, -v); eye(nm, v, 128)
    lin("I20", "II", 20.0, flex=False); lin("IIh", "II", 1.0, flex=False); lin("BBh", "BB", 1.0, flex=False); lin("B8h", "B8", 1.0, flex=False)
    mset(c("t4", 0, 16), 0.5, 16, ["t4"])
    mset(c("t4", 16, 32), 0.0, 16, ["t4"])
    add({"V": (vc(16), lambda g: g.vector.tensor_tensor_scan(c("t4", 32, 48), c("t4", 0, 16), c("t4", 16, 32), 65536.0, OP.mult, OP.add))}, ["t4"], ["t4b"])
    tt(c("t4", 48, 64), c("t4", 32, 48), c("MM", 0, 16), OP.mult, 16, ["t4b", "MM"], ["t4c"])
    add({"V": (vc(16), lambda g: g.vector.tensor_reduce(col("th"), c("t4", 48, 64), AxisListType.X, OP.add))}, ["t4c"], ["c.th"])
    cts("m15", "pm", 15.0, 0.5, OP.is_lt, OP.mult)
    cts("pw", "th", "m15", None, OP.mult, None)
    cts("e0", "pm", 15.0, -32768.0, OP.is_equal, OP.mult)
    cts("thn", "e0", "pw", None, OP.subtract, None)
    cts("nth", "th", -1.0, None, OP.mult, None)
    lin("nB8", "B8", -1.0); lin("Wd", "B8", -16.0); lin("Ww", "B8", "pw"); lin("Wv", "Ww", 0.5); lin("Wn", "B8", -U); lin("W2", "B8", 2 * U)
    lin("CH", "BB", "nth", a=128, n=128); lin("THN", "BB", "thn"); lin("nBD", "BB", -U)
    cts("b0", "pb", 0.0, None, OP.is_equal, None)
    cts("b1", "pb", 1.0, -16.0, OP.is_equal, OP.mult)
    cts("b2", "pb", 2.0, -65536.0, OP.is_equal, OP.mult)
    cts("b3", "b1", "b2", None, OP.add, None)
    lin("CH", "t2", "b0", "b3", n=128)
    cts("p16", "p", 16.0, None, OP.mult, None)
    lin("MM16", "MM", "p16")
    ts(c("hold"), c("t2"), 0.0, None, OP.not_equal, None, 256, ["t2"], ["hold"], rate=0.5)
    ts(c("rst"), c("t2", 0, 160), 0.0, 4.0, OP.is_equal, OP.mult, 160, ["t2"], ["rst"], rate=0.5)
    ts(c("rstr"), c("t2", 0, 128), 15.0, 4.0, OP.is_equal, OP.mult, 128, ["t2"], ["rstr"], rate=0.5)
    ts(c("t6"), c("t2", 0, 128), col("pm"), None, OP.is_le, None, 128, ["t2", "c.pm"], ["t6"], rate=0.5)
    tt(c("HP"), c("t6"), c("hold", 0, 128), OP.mult, 128, ["t6", "hold"], ["HP"])
    cts("w", "pm", 15.0, 7.0, OP.mult, OP.add)
    cts("w4", "w", 4.0, None, OP.mult, None)
    cts("w21", "w", 21.0, None, OP.mult, None)
    cts("e0", "w21", 2048.0, -4096.0, OP.is_ge, OP.mult)
    cts("w21", "w21", "e0", None, OP.add, None)
    lin("WV", "BB", "w"); lin("W4", "BB", "w4"); lin("W21", "BB", "w21", flex=False); lin("W4V", "B8", "w4")
    big = 16777216.0
    lin("MK", "MM", big, -big, n=128); lin("MK", "MM", 1.5 * big, -big, a=128, n=128); lin("MK2", "MM", big + 2048.0, -big, flex=False); lin("MKp", "MM", 8192.0 - big, big, flex=False)
    tt(c("MKt"), c("MK", 0, 128), c("t0", 0, 128), OP.add, 128, ["MK", "t0"], ["MKt"])
    mset(c("ONES"), 1.0, 128, ["ONES"])
    cts("f0", "p", 0.0, U / 32, OP.is_equal, OP.mult)
    cts("f1", "p", 1.0, -TH * U, OP.is_equal, OP.mult)
    lin("CR", "t2", "f0", "f1")
    cts("f0", "p", 8.0, U / 32, OP.is_equal, OP.mult)
    cts("f1", "p", 9.0, -TH * U, OP.is_equal, OP.mult)
    cts("f2", "p", 10.0, -U / 2, OP.is_equal, OP.mult)
    cts("f3", "f1", "f2", None, OP.add, None)
    lin("t7", "t2", "f0", "f3")
    ts(c("CRC"), c("t1", 96, 256), col("p"), -U, OP.is_equal, OP.mult, 160, ["t1", "c.p"], ["CRC"], rate=0.5)
    tt(c("CRC"), c("CRC"), c("t7"), OP.add, 160, ["CRC", "t7"], ["CRC"])
    cts("e1", "h8", -128.0, 256.0, OP.mult, OP.add)
    eq("EX0", "t1", "p7", "e1")
    cts("e2", "h8", -4096.75, -4096.25, OP.mult, OP.add)
    cts("b0", "p", 16.0, "e2", OP.is_lt, OP.mult)
    cts("b1", "h8", 0.75, 0.25, OP.mult, OP.add)
    cts("wsel", "b0", "b1", None, OP.add, None)
    eq("EXK", "t1", "p7", "wsel")
    ts(c("sel"), c("t3", 0, 8), col("p7"), col("wsel"), OP.is_equal, OP.mult, 8, ["t3", "c.p7", "c.wsel"], ["sel"])
    mset(c("nONE"), -1.0, 64, ["nONE"])
    for x, b in enumerate(BLK):
        for dst, src, n, o in (("SEL", "ONES", 128, 128 * b), ("nSEL", "nONE", 64, 64 * x)):
            ts(c(dst, o, o + n), c(src), c("sel", b, b + 1), None, OP.mult, None, n, [src, "sel"], ["%s%d" % (dst, b)], rate=0.5,
               act=(AF.Identity, 0.0, c("sel", b, b + 1)))
    sels = ["%s%d" % (s, b) for s in ("SEL", "nSEL") for b in range(8)]
    eq("EXb", "t1", "p")
    pick(c("TRT", 0, 512), c("zero"), [[0, 8], [-1, 64]], OP.is_gt, 0.25, 0, 1, 512, ["zero"], ["TRT"])
    for p0 in (0, 64):
        pick(c("TRT", 512, 768, p0, p0 + 64), c("zero", 0, 256, p0, p0 + 64), [[0, 4], [-1, 64]], OP.is_gt, 0.25, 0, 1, 256, ["zero"], ["TRT"])
    mset(c("Z8", 0, 464), 0.0, 464, ["Z8", "Zq"], late=True)
    mset(c("Z8", 112, 128), 8192.0, 16, ["Z8"], late=True)
    mset(c("Zq", 96, 112, 0, 64), 8192.0, 16, ["Zq"], late=True)
    mset(c("Zq", 112, 128, 64, 128), 8192.0, 16, ["Zq"], late=True)
    for h in range(2):
        if NE[h] < 4:
            ts(c("THO%d" % h), c("t2", 0, 128), 4.0 * NE[h], -128.0, OP.is_ge, OP.mult, 128, ["t2"], ["THO%d" % h], rate=0.5)
    if min(NE) < 4:
        lin("sI", "II", S97); lin("nsI", "II", -S97)
    mset(c("CK", 0, 128), 122880.0, 128, ["CK"], late=True); mset(c("CK", 128, 256), -40960.0, 128, ["CK"], late=True)
    cts("e0", "pm", 15.0, -16.0, OP.is_equal, OP.mult)
    cts("e1", "p", 1.0, "e0", OP.add, OP.add)
    eq("LS", "t0", "e1")
    for j, v in enumerate((2048.0, -6144.0, -8192.0)):
        mset(c("CT", 128 * j, 128 * j + 128), v, 128, ["CT"], late=True)
    mset(c("NH"), -0.5, 128, ["NH"])
    iota(c("C2"), [[16, 2], [0, 8]], 0, 0, 16, ["C2"])
    cts("sp", "pm", 5120.0, None, OP.add, None)
    ts(c("t5"), c("t0", 0, 128), col("sp"), 0.25, OP.add, OP.mult, 128, ["t0", "c.sp"], ["t5"])
    tt(c("TR"), c("t5"), c("rst", 0, 128), OP.mult, 128, ["t5", "rst"], ["TR"])

    lin("t8", "BB", "pm")
    for nm, sg, b0 in (("LWa", -1, 7), ("LWb", 1, -8)):
        pick(c(nm), c("t8"), [[0, 8], [sg, 16]], OP.is_ge, 0.0, b0, 0, 128, ["t8"], [nm])

    X, S, Ku, Kf, z, at, ai, AR = T.X, T.S, T.Ku, T.Kf, T.z, T.at, T.ai, T.AR
    mset(AR[0:32, :], 1.0, 128, ["AR"], late=True)
    mset(AR[0:8, :], 0.0, 128, ["AR"], late=True)
    iota(ai[0:8, 0:1], [[0, 1]], 0, 0, 1, ["ai0"], True)

    def zwin(h, rnd, j, n=1):
        o = 3072 + 384 * (rnd % 2) + 128 * (3 - n - j)
        return T["wb%d" % h][:, o:o + 128 * n]

    def lwin(h, rnd, j, n=1):
        o = 3840 + 384 * (rnd % 2) + 128 * (3 - n - j)
        return T["wb%d" % h][:, o:o + 128 * n]

    def kwin(h, rnd, j, n=1):
        o = 1408 + 384 * (rnd % 2) + 128 * (3 - n - j)
        return T["wf%d" % h][:, o:o + 128 * n]

    def skeys(h, rnd):
        return ["%s%d%d" % (s, rnd % 2, h) for s in ("zw", "lw", "kw")]

    for h in range(2):
        L = slice(128 * h, 128 * h + 128)
        zk, lk, kk_ = skeys(h, 0)
        mset(T["wb%d" % h][:, 1216:1520], 0.0, 304, ["kd%d" % h, "ks%d" % h])
        cp(Ku[:, L], T.Ki[:, L], 128, ["in0"], ["Ku%d" % h])
        ts(kwin(h, 0, 1), T.Ki[:, L], 20.0, None, OP.mult, None, 128, ["in0"], [kk_])
        cp(zwin(h, 0, 0), z[:, L], 128, ["in0", "z%d" % h], [zk], rate=0.5, flex=True)
        cp(T.Lb[0:8, L], T.Li[0:8, L], 128, ["in0"], ["Lb%d" % h])
        m = T["ps%d" % (6 + h)]
        pe([(m[:, 0:128], c("EXb", 0, 128, 0, 8), T.Lb[0:8, L], True, True, 128, 128, 0)], ["EXb", "Lb%d" % h], ["m0%d" % h], [6 + h])
        ts(lwin(h, 0, 0), m[:, 0:128], col("pm"), None, OP.is_equal, None, 128, ["m0%d" % h, "c.pm"], [lk], [6 + h])
        cp(lwin(h, 0, 1), lwin(h, 0, 0), 128, [lk], [lk + "b"], rate=0.5, flex=True)
    pick(S[:, W:W + A], T.Si[:, :], [[0, A]], OP.is_ge, 0.0, 0, 0, A, ["in2"], ["S"])
    xq = []
    for j in range(3):
        for cq in range(4):
            xq.append("X%d%d" % (j, cq))
            cp(X[rows((q - 1 - j) % N), 1024 * cq:1024 * cq + 1024], T.LX[rows(cq), 1024 * j:1024 * j + 1024], 1024, ["inx%d" % j], xq[-1:],
               rate=0.5, flex=True)

    ring = [0, 0]
    I = c("II", 0, 128)

    def names(h):
        return lambda s: "%s%d" % (s, h)

    def bufs(h):
        return T["wb%d" % h], T["wf%d" % h], T["wi%d" % h], T["wu%d" % h], T["wh%d" % h]

    def sub_chunk(h, src, skeys, base, ch, lx, lz, rz, zkeys):
        s = session(h)
        mms = []
        for kk in range(4):
            mms.append((sap(s, 128 * kk, 128 * kk + 128), lx, src[:, base + 4 * ch + kk:base + 2048:16], True, False, 128, 128, 0))
            mms.append((sap(s, 128 * kk, 128 * kk + 128), lz, rz, False, True, 128, 128, 0))
        pe(mms, ["II", "nII"] + skeys + zkeys, ["sl%d" % s["id"]], [s])
        return s, "sl%d" % s["id"]

    def ringbuf(h):
        r = ring[h]
        ring[h] = (r + 1) % NRING
        return r

    def gather(out, win, off, n, reads, writes, flex=True):
        cp(out, win.indirect(off), n, reads, writes, rate=GAM, flex=flex)
        ops[-1]["ng"] = n * CYC

    def perm(h, out, wide, src, back):
        mms = []
        for cl in range(3):
            o = (cl - 128 * h) % 3
            s = 32 * (cl + 1) if back else 128 - 32 * (cl + 1)
            mms.append((out(o), wide(s), src(o), 43, 0))
        return mms

    def singles(mms):
        return [mm for x in mms for mm in group([x])]

    def stage_a(h, rnd):
        bias[0] = BIAS[0] * (1 - h)
        k = names(h)
        wb, wf, wi, wu, wh = bufs(h)
        xg, acc, m = T["xg%d" % h], T["ps%d" % (4 + h)], T["ps%d" % (6 + h)]
        ab, mb = [4 + h], [6 + h]
        l0 = 128 * h
        for j in range(2):
            gather(xg[:, 1024 * j:1024 * j + 1024], X[:, 0:W], Ku[:, l0 + 64 * j:l0 + 64 * j + 64], 1024, ["X", "in1", k("Ku")] + xq, [k("xg%d" % j)])
        allm = [k("m0"), k("m1"), k("m2"), k("m3")]
        zk, lk, kk_ = skeys(h, rnd)
        zc, lc = zwin(h, rnd, 0), lwin(h, rnd, 0)
        pe([(m[:, 256:384], c("LS"), lc, True, True, 128, 128, 0)], [lk, "LS"], [k("m2")], mb)
        cp(lwin(h, rnd, 2), m[:, 256:384], 128, [k("m2")], [k("dL")], mb, flex=True)
        pe([(acc[:, 0:128], lc, c("CH", 0, 128), True, False, 128, 128, 0),
            (m[:, 0:128], lc, c("CH", 128, 256), True, False, 128, 128, 0)], [lk, "CH"], [k("acc")] + allm, ab + mb)
        for ch in range(4):
            s, sl = sub_chunk(h, xg, [k("xg0"), k("xg1")], 0, ch, I, c("nII", 0, 128), zc, [zk])
            r = ringbuf(h)
            u, v = T["ur%d" % h][:, 512 * r:512 * r + 512], T["vr%d" % h][:, 512 * r:512 * r + 512]
            act(u, sap(s), AF.Abs, 512, [sl], [k("u%d" % r)], [s])
            if ch in PAIR[h]:
                continue
            nc = 2 if ch - 1 in PAIR[h] else 1
            r0 = r + 1 - nc
            us, vs = [k("u%d" % j) for j in range(r0, r + 1)], [k("v%d" % j) for j in range(r0, r + 1)]
            u, v = T["ur%d" % h], T["vr%d" % h]
            wt = over(v[:, 512 * r0:512 * r + 512], u[:, 512 * r0:512 * r + 512], 48.5, 512 * nc, us, vs, (), 0.5, c("Ww"), c("Wv"))
            mu, mv = [], []
            for kk in range(4 * nc):
                kq = 4 * (ch + 1 - nc) + kk
                mu.append((acc[:, kq:128:16], u[:, 512 * r0 + 128 * kk:512 * r0 + 128 * kk + 128], c("Wd"), False, False, 8, 128, 0))
                mv.append((m[:, kq:128:16], v[:, 512 * r0 + 128 * kk:512 * r0 + 128 * kk + 128], wt, False, kq == 15, 8, 128, 0))
            pe(mu + mv, us + vs + ["Wd", "Ww", "Wv", k("acc")], [k("acc")] + allm, ab + mb)
        bias[0] = BIAS[1] * (1 - h) + BIAS[11]
        wt = over(wb[:, 0:128], m[:, 0:128], -16384.0, 128, [k("m0")], [k("sg")], mb, 1.0, c("I17"), c("I16"))
        pe([(acc[:, 0:128], wt, wb[:, 0:128], False, True, 128, 128, 0)], [k("sg"), "I16", "I17", k("acc")], [k("acc")], ab)
        scan(wi[:, 0:128], c("hold", 0, 128), acc[:, 0:128], OP.mult, OP.min, 128, [k("acc"), "hold"], [k("s0")], ab)
        ts(wi[:, 128:136], wi[:, 15:128:16], 15, None, OP.bitwise_and, None, 8, [k("s0")], [k("i0")])
        cp(wb[:, 1216:1344:16], wi[:, 128:136], 8, [k("i0")], [k("kd")])
        scan(wb[:, 1376:1504], c("HP"), wb[:, 1216:1344], OP.mult, OP.add, 128, [k("kd"), "HP"], [k("ks")], rate=0.5)
        b8 = c("B8", 0, 8)
        pe(group([(m[:, 0:8], c("MM16"), b8, 8, 0), (m[:, 0:8], wb[:, 1217:1345], b8, 8, 0),
                  (m[:, 0:8], wb[:, 1376:1504], b8, 8, 0), (m[:, 0:8], wb[:, 1377:1505], c("nB8"), 8, 0)]),
           [k("ks"), k("kd"), "B8", "nB8", "MM16"], [k("m0")], mb)
        cp(wu[:, 0:8], m[:, 0:8], 8, [k("m0")], [k("ou")], mb)
        tt(wb[:, 128:256], xg[:, 0:2048].indirect(wu[:, 0:8]), zc, OP.subtract, 128, [k("xg0"), k("xg1"), k("ou"), zk], [k("as")], rate=GAM)
        act(wb[:, 256:384], wb[:, 128:256], AF.Abs, 128, [k("as")], [k("D")])
        z0 = 3072 + 384 * (rnd % 2) + 256
        mms = [(m[:, 0:256], I, c("MK"), 256, 0)]
        for wt, o0, sh in (("W4", 0, 0), ("W21", 128, 96)):
            mms += perm(h, lambda o: m[:, o0 + o:o0 + 128:3], lambda s: c(wt, (s + sh) % 128, (s + sh) % 128 + 128),
                        lambda o: wb[:, 256 + o:384:3], False)
        pe(group(mms), ["II", "MK", "W4", "W21", k("D")], [k("m0"), k("m1")], mb)
        pe(singles(perm(h, lambda o: acc[:, 256 + o:384:3], lambda s: c("II", s, s + 128), lambda o: wb[:, z0 + o:z0 + 128:3], False)
                   + perm(h, lambda o: acc[:, 384 + o:512:3], lambda s: c("II", s, s + 128), lambda o: wb[:, 256 + o:384:3], False)),
           ["II", zk, k("D")], [k("acc")], ab)
        cp(wb[:, 384:640], acc[:, 256:512], 256, [k("acc")], [k("zD")], ab, flex=True)
        scan(wi[:, 640:896], c("hold"), m[:, 0:256], OP.mult, OP.max, 256, [k("m0"), k("m1"), "hold"], [k("r1")], mb)
        ts(wi[:, 136:152], wi[:, 655:896:16], 2, 1023, OP.arith_shift_right, OP.bitwise_and, 16, [k("r1")], [k("i3")])
        cp(wu[:, 8:24], wi[:, 136:152], 16, [k("i3")], [k("cu")])
        if rnd == 0:
            gather(wu[:, 64:320], T.Si[:, 0:A], wu[:, 8:24], 256, ["in2", k("cu")], [k("Pu")], flex=False)
        else:
            gather(wu[:, 64:320], S[:, W:W + A], wu[:, 8:24], 256, ["S", k("cu")], [k("Pu")], flex=False)
        ts(wh[:, 0:256], wu[:, 64:320], -2048.0, None, OP.add, None, 256, [k("Pu")], [k("Pc")], rate=0.5)
        pe(group([(m[:, 256:384], c("IH"), c("NH"), 128, 0), (m[:, 256:384], I, zc, 128, 0), (m[:, 256:384], c("IH"), wb[:, 128:256], 128, 0)])
           + group([(m[:, 384:512], c("WV"), wb[:, 256:384], 128, 0)]), ["IH", "NH", "II", "WV", zk, k("as"), k("D")], [k("m2"), k("m3")], mb)
        tt(wi[:, 256:384], m[:, 384:512], kwin(h, rnd, 1), OP.add, 128, [k("m3"), kk_], [k("k1")], mb)
        ts(wi[:, 384:512], wi[:, 256:384], 2, 4095, OP.arith_shift_right, OP.bitwise_and, 128, [k("k1")], [k("k2")])
        ts(kwin(h, rnd, 0), wi[:, 384:512], 20.0, None, OP.mult, None, 128, [k("k2")], [k("K5")])
        ts(zwin(h, rnd, 1), m[:, 256:384], MAGIC, -MAGIC, OP.add, OP.add, 128, [k("m2")], [k("zf")], mb)

    def stage_c(h, rnd):
        last = rnd == RO - 1
        bias[0] = BIAS[2] * (1 - h)
        k = names(h)
        wb, wf, wi, wu, wh = bufs(h)
        yg, acc, m = T["yg%d" % h], T["ps%d" % (4 + h)], T["ps%d" % (6 + h)]
        ab, mb = [4 + h], [6 + h]
        zB, DB = wb[:, 384:512], wb[:, 512:640]
        for j in range(4):
            gather(yg[:, 1024 * j:1024 * j + 1024], X[:, 0:W], wu[:, 64 + 64 * j:128 + 64 * j], 1024, ["X", k("Pu")], [k("yg%d" % j)])
        ro = C["rstr"][1]

        def best(role):
            a, n, wd = 128 * role, "BC"[role], 128 + 32 * role
            scan(wf[:, 3 * a:3 * a + wd], c("rst", 0, wd), acc[:, a:a + wd], OP.add, OP.min, wd, [k("acc"), "rst"], [k("s1" + n)], ab)
            src = wf[:, 127::-1] if role == 0 else wf[:, 511:383:-1]
            scan(wf[:, 255 + a:127 + a:-1], T.CB[:, ro + 127:ro - 1:-1], src, OP.add, OP.min, 128, [k("s1" + n), "rstr"], [k("s2" + n)])
            tt(wb[:, 640 + a:768 + a], acc[:, a:a + 128], wf[:, 128 + a:256 + a], OP.is_equal, 128, [k("acc"), k("s2" + n)], [k("oh" + n)], ab)

        def partner():
            best(0)
            pe(group([(m[:, 0:128], wb[:, 640:768], I, 128, 0)]), ["II", k("ohB")], [k("m0")], mb)
            tt(wh[:, 256:384], m[:, 0:128], wh[:, 0:128], OP.mult, 128, [k("m0"), k("Pc")], [k("pay")], mb)
            pe(group([(m[:, 256:384], I, c("MK2"), 128, 0), (m[:, 256:384], c("BBh", 0, 128), wh[:, 256:384], 128, 0)])
               + group([(m[:, 128:144], c("ONES"), c("C2"), 16, 0), (m[:, 128:136], DB, c("W4V"), 8, 0),
                        (m[:, 136:144], wh[:, 256:384], c("B8h"), 8, 0)]),
               ["II", "MK2", "BBh", "B8h", "ONES", "C2", "W4V", k("zD"), k("pay")], [k("m1"), k("m2")], mb)
            scan(wf[:, 640:768], c("hold", 0, 128), m[:, 256:384], OP.mult, OP.max, 128, [k("m2"), "hold"], [k("sc")], mb)
            cp(wu[:, 24:32], wf[:, 655:768:16], 8, [k("sc")], [k("ju")])
            gather(wb[:, 896:1024], X[:, 0:W], wu[:, 24:32], 128, ["X", k("ju")], [k("yj")])
            cp(wi[:, 152:168], m[:, 128:144], 16, [k("m1")], [k("i4")], mb)
            ts(wi[:, 168:184], wi[:, 152:168], 4032, None, OP.bitwise_and, None, 16, [k("i4")], [k("hi")])
            ts(wi[:, 184:200], wi[:, 152:168], 63, None, OP.bitwise_and, None, 16, [k("i4")], [k("lo")])
            mms = singles(perm(h, lambda o: m[:, 256 + o:384:3], lambda s: c("II", s, s + 128), lambda o: wb[:, 896 + o:1024:3], True))
            if last:
                mms += group([(m[:, 384:512], c("IH"), x, 128, 0) for x in (c("NH"), DB, wb[:, 896:1024])])
            else:
                mms += group([(m[:, 384:512], I, x, 128, 0) for x in (DB, wb[:, 896:1024])])
            pe(mms, ["II", "IH", "NH", k("yj"), k("zD")], [k("m2"), k("m3")], mb)
            cp(zwin(h, rnd, 2), m[:, 256:384], 128, [k("m2")], [k("yh")], mb, flex=True)
            if last:
                va, mv = T["VA%d" % h][:, :], T["mv%d" % h]
                ts(va, m[:, 384:512], MAGIC, -MAGIC, OP.add, OP.add, 128, [k("m3")], [k("nw")], mb)
                remote("all", [(va, mv)], k("bv"), 3000.0, [k("nw")], [k("mv")])
                dma("S", [(mv[q], va)], k("ov"), 2000.0, [k("nw")], [k("mvo")])
                dma("S", [(T["VL%d" % h][:, :], mv[:, rows(q), :])], k("vl"), 2200.0, [k("mv"), k("mvo")], [k("VL")])
            else:
                ts(wi[:, 512:640], m[:, 384:512], 0.5, -0.25, OP.mult, OP.add, 128, [k("m3")], [k("nw")], mb)

        for role in range(2):
            if role == 1:
                bias[0] = BIAS[12] * (1 - h) + BIAS[13]
                partner()
                bias[0] = BIAS[2] * (1 - h)
            wd = 128 + 32 * role
            o = acc[:, 128 * role:128 * role + wd]
            if role:
                mms = [(o, AR[0:11, :], c("CRC", 0, 160, 0, 11), True, False, wd, 128, 0)]
            else:
                mms = [(o, c("ONES"), c("CR"), True, False, wd, 128, 0)]
            mms.append((o, DB, c("nBD", 96 * role, 96 * role + wd), False, False, wd, 128, 0))
            pe(mms, ["ONES", "CR", "CRC", "nBD", k("zD")] + ["AR"] * role, [k("acc")], ab)
            if role == 0:
                sd = session(6 + h)
                pe(singles([(sap(sd, 128 * kk, 128 * kk + 128), I, DB, 128, 0) for kk in range(4)]), ["II", k("zD"), k("yg0")], [k("D4")], [sd])
            for ch in range(4):
                s, sl = sub_chunk(h, yg, [k("yg%d" % (2 * role)), k("yg%d" % (2 * role + 1))], 2048 * role, ch,
                                  c("II", 32 * role, 32 * role + 128), c("nII"), zB, [k("zD")])
                r = ringbuf(h)
                u, v = T["ur%d" % h][:, 512 * r:512 * r + 512], T["vr%d" % h][:, 512 * r:512 * r + 512]
                act(u, sap(s), AF.Abs, 512, [sl], [k("u%d" % r)], [s])
                tt(v, u, sap(sd), OP.max, 512, [k("u%d" % r), k("D4")], [k("v%d" % r)], [sd])
                mv = []
                for buf, wt in (("ur", "Wn"), ("vr", "W2")):
                    for kk in range(4):
                        kq = 4 * ch + kk
                        mv.append((acc[:, 128 * role + kq:128 * role + wd:16], T["%s%d" % (buf, h)][:, 512 * r + 128 * kk:512 * r + 128 * kk + 128],
                                   c(wt, 6 * role, 8 + 8 * role), False, kq == 15 and buf == "vr", 8, 128, 0))
                pe(mv, [k("u%d" % r), k("v%d" % r), "Wn", "W2", k("acc")], [k("acc")], ab)
        bias[0] = BIAS[3] * (1 - h) + BIAS[10]
        best(1)
        tt(wb[:, 1152:1160], wf[:, 431:544:16], wf[:, 15:128:16], OP.is_le, 8, [k("s1B"), k("s1C")], [k("hit")])
        tt(wb[:, 1160:1168], wb[:, 1152:1160], wf[:, 15:128:16], OP.is_le, 8, [k("s1B"), k("hit")], [k("nei")])
        tt(wb[:, 1168:1184], wi[:, 168:184], wb[:, 1152:1168], OP.mult, 16, [k("hit"), k("nei"), k("hi")], [k("kh")])
        tt(wb[:, 1184:1200], wi[:, 184:200], wb[:, 1152:1168], OP.mult, 16, [k("hit"), k("nei"), k("lo")], [k("kl")])
        bias[0] = BIAS[14]
        pe(group([(m[:, 384:512], wb[:, 768:896], I, 128, 0)]), ["II", k("ohC")], [k("m3")], mb)
        tt(wh[:, 384:512], m[:, 384:512], wh[:, 128:256], OP.mult, 128, [k("m3"), k("Pc")], [k("payC")], mb)
        pe(group([(m[:, 256:512], wb[:, 640:768], c("PT"), 256, 0)]
                 + [(m[:, 256:512], I, c("CT", 0, 256), 256, 0) if last else (m[:, 384:512], I, c("CT", 256, 384), 128, 0)]
                 + [(m[:, 256:384], c("IIh"), wh[:, 0:128], 128, 0), (m[:, 384:512], c("BBh", 32, 160), wh[:, 384:512], 128, 0)]),
           ["II", "CT", "PT", "IIh", "BBh", k("ohB"), k("Pc"), k("payC")], [k("m2"), k("m3")], mb)
        if last:
            cp(wf[:, 1024:1152], m[:, 256:384], 128, [k("m2")], [k("tu")], mb, flex=True)
            tt(T["MS%d" % h][:, 0:128], m[:, 384:512], wf[:, 1024:1152], OP.max, 128, [k("m3"), k("tu")], [k("nc")], mb)
        else:
            ts(wf[:, 1024:1280], m[:, 256:512], 2048.0, None, OP.add, None, 256, [k("m2"), k("m3")], [k("tu")], mb, act=(AF.Identity, 2048.0, 1.0))

    def stage_e(h, rnd):
        last = rnd == RO - 1
        zk, lk, kk_ = skeys(h, rnd)
        zn, ln, kn = skeys(h, rnd + 1)
        bias[0] = BIAS[5] * (1 - h) + BIAS[6]
        k = names(h)
        wb, wf, wi, wu, wh = bufs(h)
        xg, acc, m = T["xg%d" % h], T["ps%d" % (4 + h)], T["ps%d" % (6 + h)]
        ab, mb = [4 + h], [6 + h]
        L = slice(128 * h, 128 * h + 128)
        RT = wb[0:48, 1024:1152]
        pe([(m[0:48, 128:256], wb[:, 1152:1200], I, True, True, 128, 48, 0)], ["II", k("hit"), k("nei"), k("kh"), k("kl")], [k("m1")], mb)
        if last:
            cp(RT, m[0:48, 128:256], 128, [k("m1")], [k("RT")], mb, flex=True)
        else:
            add({"A": (vc(128) + 35, lambda g: g.scalar.activation(RT, m[0:48, 128:256], AF.Copy, accum_out=at[0:48, h:h + 1]))},
                [k("m1")], [k("RT"), k("cnt")], mb)
        pe(group([(m[:, 0:128], I, c("MKt"), 128, 0)]
                 + perm(h, lambda o: m[:, o:128:3], lambda s: c("EX0", s, s + 128, 0, 16), lambda o: wb[0:16, 1024 + o:1152:3], True)),
           ["II", "MKt", "EX0", k("RT")], [k("m0")], mb)
        scan(wf[:, 768:896], c("hold", 0, 128), m[:, 0:128], OP.mult, OP.max, 128, [k("m0"), "hold"], [k("sc2")], mb)
        cp(wu[:, 40:48], wf[:, 783:896:16], 8, [k("sc2")], [k("su")])
        su = wu[:, 40:48]
        gather(z[:, L] if last else zwin(h, rnd + 1, 0), zwin(h, rnd, 0, 3), su, 128, [k("su"), zk, k("zf"), k("yh")], [k("z") if last else zn])
        gather(lwin(h, rnd + 1, 0), lwin(h, rnd, 0, 3), su, 128, [k("su"), lk, lk + "b", k("dL")], [ln])
        if not last:
            cp(lwin(h, rnd + 1, 1), lwin(h, rnd + 1, 0), 128, [ln], [ln + "b"], rate=0.5, flex=True)
        bias[0] = BIAS[4] * (1 - h) + BIAS[9]
        blk = BLK
        lo, hi = wb[0:48, 1024:1088], wb[0:48, 1088:1152]
        sel = lambda b, n: c("SEL", 128 * b, 128 * b + n, 0, 48)
        s = session(2 + h)
        sl = "sl%d" % s["id"]
        pe(group([(sap(s), RT, c("nSEL", 0, 512, 0, 48), 512, 0)] + [(sap(s, 64 * x, 64 * x + 64), sel(blk[x], 128), lo, 64, 0) for x in range(8)]),
           sels + [k("RT")], [sl], [s])
        tt(wb[:, 2048:2560], sap(s), c("TRT", 0, 512), OP.is_equal, 512, [sl, "TRT"], [k("e0")], [s])
        s = session(2 + h)
        sl = "sl%d" % s["id"]
        pe([mm for j in range(2) for mm in group([(sap(s, 0, 256, 64 * j), hi, c("nSEL", 256 * j, 256 * j + 256, 0, 48), 256, 0)]
                                                 + [(sap(s, 64 * x, 64 * x + 64, 64 * j), sel(2 * x + j, 64), hi, 64, 0) for x in range(4)])],
           sels + [k("RT")], [sl], [s])
        tt(wb[:, 2560:2816], sap(s, 0, 256), c("TRT", 512, 768), OP.is_equal, 256, [sl, "TRT"], [k("e1")], [s])
        pe(group([(m[:, 128:256], I, c("MKp"), 128, 0), (m[:, 128:256], c("EXK", 0, 128, 0, 48), RT, 128, 0)]
                 + [(m[:, 192:256], c("Zq", 96 - 32 * x, 224 - 32 * x), wb[:, 2560 + 64 * x:2624 + 64 * x], 64, 0) for x in range(4)]
                 + [(m[:, 128:192], c("Z8", 112 - 16 * blk[x], 240 - 16 * blk[x]), wb[:, 2048 + 64 * x:2112 + 64 * x], 64, 0) for x in range(8)]),
           ["II", "MKp", "EXK", "Z8", "Zq", k("RT"), k("e0"), k("e1")], [k("m1")], mb)
        scan(wf[:, 640:768], c("TR"), m[:, 128:256], OP.max, OP.min, 128, [k("m1"), "TR"], [k("sc")], mb)
        cp(T["MS%d" % h][:, 128:136] if last else wu[:, 32:40], wf[:, 655:768:16], 8, [k("sc")], [k("ku")], flex=last)
        bias[0] = LASTB[h] if last else BIAS[7] * (1 - h) + BIAS[8]
        ov = T["ov%d" % h]
        c0 = 0
        for ch in range(4):
            o = ov[:, 512 * ch:512 * ch + 512]
            if ch < NE[h]:
                s, sl = sub_chunk(4 + h, xg, [k("xg0"), k("xg1")], 0, ch, I, c("nII", 0, 128), zwin(h, rnd, 2), [k("yh")])
                act(o, sap(s), AF.Abs, 512, [sl], [k("ov%d" % ch)], [s])
                if ch % 2 == 0 and ch + 1 < NE[h]:
                    continue
                o, ks = ov[:, 512 * c0:512 * ch + 512], [k("ov%d" % j) for j in range(c0, ch + 1)]
                wt = over(o, o, 48.5, 512 * (ch + 1 - c0), ks, ks, (), 0.5, c("Ww"), c("Wv"))
            else:
                s, sl = sub_chunk(4 + h, xg, [k("xg0"), k("xg1")], 0, ch, c("sI"), c("nsI"), zwin(h, rnd, 2), [k("yh"), "sI", "nsI"])
                ks, wt = [k("ov%d" % ch)], c("Ww")
                ts(o, sap(s), MAGIC, MAGIC, OP.add, OP.not_equal, 512, [sl], ks, [s])
            mv = [(acc[:, 0:128], lwin(h, rnd, 0), c("THN"), True, False, 128, 128, 0)] if c0 == 0 else []
            if c0 == 0 and NE[h] < 4:
                mv.append((acc[:, 0:128], c("ONES"), c(k("THO")), False, False, 128, 128, 0))
            for kq in range(4 * c0, 4 * ch + 4):
                mv.append((acc[:, kq:128:16], ov[:, 128 * kq:128 * kq + 128], wt, False, kq == 15, 8, 128, 0))
            pe(mv, ks + ["Ww", "Wv", "THN", "ONES", k("THO"), lk, k("acc")], [k("acc")], ab)
            c0 = ch + 1
        wt = over(wb[:, 1536:1664], acc[:, 0:128], -16384.25, 128, [k("acc")], [k("off")], ab, 1.0, c("PM"), c("PMh"))
        pe(group([(acc[:, 128:384], I, c("CK"), 256, 0), (acc[:, 128:384], wb[:, 1536:1664], wt, 256, 0)]
                 + [mm for a in (128, 256) for mm in perm(h, lambda o: acc[:, a + o:a + 128:3], lambda s: c("I20", s, s + 128), lambda o: wh[:, o:128:3], True)]),
           ["II", "I20", "CK", "PM", "PMh", k("off"), k("Pc")], [k("acc")], ab)
        tt(wf[:, 896:1024], acc[:, 128:256], kwin(h, rnd, 1), OP.min, 128, [k("acc"), kk_], [k("d2")], ab)
        tt(kwin(h, rnd, 2), acc[:, 256:384], wf[:, 896:1024], OP.max, 128, [k("acc"), k("d2")], [k("Kc")], ab)
        rd = [k("su"), kk_, k("K5"), k("Kc")]
        ts(Ku[:, L], kwin(h, rnd, 0, 3).indirect(su), 0.05, 0.25, OP.mult, OP.add, 128, rd, [k("Ku")], rate=GAM)
        ops[-1]["ng"] = 128 * CYC
        if last:
            cp(Kf[:, L], Ku[:, L], 128, [k("Ku")], [k("Kf")])
            remote("all", [(Kf[:, L], T["mk%d" % h])], k("bk"), 2800.0, [k("Kf")], [k("mk")])
            dma("S", [(T["mk%d" % h][q], Kf[:, L])], k("ok"), 2000.0, [k("Kf")], [k("mko")])
            dma("S", [(T.yk[:, L], T["mk%d" % h][:, rows(q), :])], k("yk"), 2200.0, [k("mk"), k("mko")], [k("yk")])
        else:
            gather(kwin(h, rnd + 1, 1), kwin(h, rnd, 0, 3), su, 128, rd, [kn])

    def writes(h):
        k = names(h)
        wb, wf, wi, wu, wh = bufs(h)
        cp(X[:, 0:WX].indirect(wu[:, 32:40]), wi[:, 512:640], 128, [k("ku"), k("nw"), "X"], ["X"], rate=SCA)
        tt(S[:, 0:WX].indirect(wu[:, 32:40]), wf[:, 1024:1152], wf[:, 1152:1280], OP.max, 128, [k("ku"), k("tu"), "S"], ["S"], rate=SCA)
        ops[-1]["ns"] = ops[-2]["ns"] = 128 * CYC

    def last_writes(h):
        k = names(h)
        ms, lm = T["MS%d" % h], T["LM%d" % h]
        remote("all", [(ms[:, 0:136], [lm[:, 136 * r:136 * r + 136] for r in range(N)])], k("bu"), 3000.0, [k("ku"), k("nc")], [k("LM")])
        for j, r in enumerate([q] + others):
            src = ms[rows(q), 0:136] if r == q else lm[rows(q), 136 * r:136 * r + 136]
            cp(ms[rows(r), 136:272], src, 136, [k("ku"), k("nc")] if r == q else [k("LM")], [k("MT%d" % j)], flex=True)
        rd = [k("MT%d" % j) for j in range(N)]
        ku = T.KU[:, 8 * h:8 * h + 8]
        cp(ku, ms[:, 264:272], 8, rd, [k("KU")])
        cp(T.NX[:, 0:WX].indirect(ku), T["VL%d" % h][:, :], 128, [k("KU"), k("VL"), "NX", "NXo"], ["NX"], rate=SCA)
        cp(T.NS[:, 0:WX].indirect(ku), ms[:, 136:264], 128, [k("KU"), "NS", "NSo"], ["NS"], rate=SCA)
        ops[-1]["ns"] = ops[-2]["ns"] = 128 * CYC

    SA = slice(W, W + A)
    for rnd in range(RO):
        last = rnd == RO - 1
        turn[0] = rnd
        for j, stage in enumerate((stage_a, stage_c, stage_e)):
            for h in range(2):
                base[0] = len(ops) - 100 * (2 * j + h) - 1000 * last
                stage(h, rnd)
        base[0] = len(ops) - 600
        bias[0] = 0.0
        if not last:
            writes(0); writes(1)
            ts(ai[0:8, 1:2], ai[0:8, 0:1], at[0:8, 0:1], at[0:8, 1:2], OP.add, OP.add, 1, ["ai0", "cnt0", "cnt1"], ["ai1"])
            ts(ai[0:8, 0:1], ai[0:8, 1:2], 31, None, OP.bitwise_and, None, 1, ["ai1"], ["ai0"])
            cp(at[0:8, 2:3], ai[0:8, 0:1], 1, ["ai0"], ["af"])
            ts(AR[0:8, :], c("ONES", 0, 128, 0, 8), at[0:8, 2:3], None, OP.mult, None, 128, ["ONES", "af"], ["AR"], rate=0.5)
        if rnd == RO - 2:
            base[0] = len(ops) - 620
            dma("S", [(T.ox[r], X[rows(r), 0:W]) for r in others], "ox", 6000.0, ["X"], ["ox"])
            dma("S", [(T.oa[r], S[rows(r), SA]) for r in others], "oa", 4000.0, ["S"], ["oa"])
            remote("turn", [(T.ox, T.mx)], "bx", 6000.0, ["ox"], ["mx"])
            remote("turn", [(T.oa, T.ma)], "ba", 4000.0, ["oa"], ["ma"])
            dma("S", [(T.NX[rows(q), 0:W], X[rows(q), 0:W])], "nxo", 3000.0, ["X", "ox"], ["NXo"])
            dma("S", [(T.NS[rows(q), SA], S[rows(q), SA])], "nso", 3000.0, ["S", "oa"], ["NSo"])
            dma("S", [(T.NX[rows(r), 0:W], T.mx[r]) for r in others], "nx", 5000.0, ["mx"], ["NX"])
            dma("S", [(T.NS[rows(r), SA], T.ma[r]) for r in others], "ns", 4000.0, ["ma"], ["NS"])
    base[0] = len(ops) - 640
    m = T.ps7
    pe(group([(m[:, 0:128], c("LWa"), lwin(0, RO, 0), 128, 0), (m[:, 0:128], c("LWb"), lwin(1, RO, 0), 128, 0)]),
       ["LWa", "LWb", skeys(0, RO)[1], skeys(1, RO)[1]], ["m01"], [7])
    cp(T.Lo[:, :], m[:, 0:128], 128, ["m01"], ["Lo"], [7], flex=True)
    remote("all", [(z[:, :], T.mz), (T.Lo[:, :], T.ml)], "zl", 2800.0, ["z0", "z1", "Lo"], ["mz"])
    dma("S", [(T.mz[q], z[:, :]), (T.ml[q], T.Lo[:, :])], "zlo", 2000.0, ["z0", "z1", "Lo"], ["mzo"])
    dma("S", [(T.yz[:, :], T.mz[:, rows(q), :])], "yz", 2200.0, ["mz", "mzo"], ["yz"])
    dma("S", [(T.yl[:, :], T.ml[:, 32 * q:32 * q + 32:8, :])], "yl", 2200.0, ["mz", "mzo"], ["yl"])
    last_writes(0); last_writes(1)
    dma("S", [(T.yx[:, :], T.NX[:, 0:W])], "yx", 6000.0, ["NX", "NXo"], ["yx"])
    dma("A", [(T.ya[:, :], T.NS[:, SA])], "ya", 5000.0, ["NS", "NSo"], ["ya"])
    return ops


READY = {"in0": 9000.0, "in1": 7000.0, "in2": 16000.0, "inx0": 7500.0, "inx1": 9000.0, "inx2": 10500.0}
ENG = ("P", "V", "A", "G", "S")


def links(ops):
    n = len(ops)
    deps = [set() for _ in range(n)]
    lastw, readers = {}, {}
    for i, o in enumerate(ops):
        for key in o["r"]:
            if key in lastw:
                deps[i].add(lastw[key])
        for key in o["w"]:
            if key in lastw:
                deps[i].add(lastw[key])
            deps[i].update(readers.get(key, ()))
        for key in o["r"]:
            readers.setdefault(key, []).append(i)
        for key in o["w"]:
            lastw[key] = i
            readers[key] = []
        deps[i].discard(i)
    first, seen = {}, set()
    for i, o in enumerate(ops):
        for b in o["b"]:
            if isinstance(b, dict) and b["id"] not in seen:
                seen.add(b["id"])
                if b["h"] in first:
                    deps[i].add(first[b["h"]])
                first[b["h"]] = i
    succ = [[] for _ in range(n)]
    for i in range(n):
        for d in deps[i]:
            succ[d].append(i)
    prio = [0.0] * n
    for i in range(n - 1, -1, -1):
        prio[i] = min(a[0] for a in ops[i]["alts"].values()) + ops[i].get("lat", LAT) + max([prio[s] for s in succ[i]], default=0.0)
    for o in ops:
        o["in"] = max([READY.get(key, 0.0) for key in o["r"]], default=0.0)
        if "G" in o["alts"] and "early" not in o:
            o["in"] = max(o["in"], 10000.0)
    return deps, succ, prio


def schedule(ops, lk):
    n = len(ops)
    deps, succ = [set(d) for d in lk[0]], lk[1]
    for o in ops:
        for b in o["b"]:
            if isinstance(b, dict):
                b["bank"], b["left"] = None, 0
    for o in ops:
        for b in o["b"]:
            if isinstance(b, dict):
                b["left"] += 1
    left = [len(deps[i]) for i in range(n)]
    ready = [i for i in range(n) if left[i] == 0]
    dready = [o["in"] for o in ops]
    efree = {e: 0.0 for e in ENG}
    bfree, blast = [0.0] * 8, [None] * 8
    eng, end, order = [None] * n, [0.0] * n, []
    held = [False] * 4
    prio = [lk[2][i] + ops[i]["bias"] + 500.0 * NUDGE.get(ops[i]["pos"], 0) for i in range(n)]
    while ready:
        best = None
        cand = []
        t0 = 1e18
        free = None
        for b in range(4):
            if not held[b] and (free is None or bfree[b] < bfree[free]):
                free = b
        for i in ready:
            dr = dready[i]
            if dr > t0 + WIN:
                continue
            o = ops[i]
            banks = []
            for b in o["b"]:
                if isinstance(b, dict):
                    b = b["bank"] if b["bank"] is not None else free
                banks.append(b)
            if None in banks:
                continue
            pick = None
            for e, (cost, _) in o["alts"].items():
                st = efree[e] if efree[e] > dr else dr
                for b in banks:
                    if blast[b] is not None:
                        t = bfree[b] + (LAT if eng[blast[b]] != e else 0.0)
                        if t > st:
                            st = t
                val = st + cost + (VPEN + 400.0 * LEAN.get(o["pos"], 0) if e == "V" else 0.0)
                if pick is None or val < pick[3]:
                    pick = (st, e, cost, val)
            if pick[0] < t0:
                t0 = pick[0]
            cand.append((pick[0], i, pick[1], pick[2], banks))
        for x in cand:
            if x[0] <= t0 + WIN and (best is None or prio[x[1]] > prio[best[1]]):
                best = x
        st, i, e, cost, banks = best
        ready.remove(i)
        eng[i], end[i] = e, st + cost
        ops[i]["e"] = e
        efree[e] = end[i]
        for b0, b in zip(ops[i]["b"], banks):
            if isinstance(b0, dict):
                b0["bank"] = b
                b0["left"] -= 1
                held[b] = b0["left"] > 0
            if blast[b] is not None:
                deps[i].add(blast[b])
            blast[b], bfree[b] = i, end[i]
        order.append(i)
        done = end[i] + ops[i].get("lat", LAT)
        for s in succ[i]:
            left[s] -= 1
            if done > dready[s]:
                dready[s] = done
            if left[s] == 0:
                ready.append(s)
    return order, eng, deps, end


SPREAD = [(1.5, 3.8, 170.0), (1.9, 5.0, 130.0)]
TUNED = []


def span(ops, lk):
    order, eng, deps, end = schedule(ops, lk)
    tot = 0.0
    for gam, sca, lat in SPREAD:
        fin, free, most = [0.0] * len(ops), {e: 0.0 for e in ENG}, 0.0
        for i in order:
            o, e = ops[i], eng[i]
            st = free[e]
            if o["in"] > st:
                st = o["in"]
            for d in deps[i]:
                t = fin[d] + (0.0 if e == "P" and eng[d] == "P" else lat)
                if t > st:
                    st = t
            free[e] = st + o["alts"][e][0] + o.get("ng", 0) * (gam - GAM) + o.get("ns", 0) * (sca - SCA)
            fin[i] = free[e] + o.get("lat", 0.0)
            if fin[i] > most:
                most = fin[i]
        tot += most
    return tot / len(SPREAD)


def tune(ops, lk, steps):
    rng = np.random.RandomState(7)
    poss = sorted({o["pos"] for o in ops if o["pos"] >= 0})
    flex = sorted({o["pos"] for o in ops if o["pos"] >= 0 and len(o["alts"]) > 1})
    best = span(ops, lk)
    for _ in range(steps):
        keep = (dict(NUDGE), dict(LEAN))
        if rng.rand() < 0.65:
            p, w, d = poss[rng.randint(len(poss))], (1, 1, 3, 6, 15)[rng.randint(5)], (-8, -4, -2, -1, 1, 2, 4, 8)[rng.randint(8)]
            for j in range(p, p + w):
                NUDGE[j] = NUDGE.get(j, 0) + d
        else:
            LEAN[flex[rng.randint(len(flex))]] = (-4, -2, 0, 2, 4)[rng.randint(5)]
        s = span(ops, lk)
        if s <= best:
            best = s
        else:
            NUDGE.clear(); NUDGE.update(keep[0]); LEAN.clear(); LEAN.update(keep[1])
    return best


def polish(ops, lk, steps):
    order, eng, _, _ = schedule(ops, lk)
    n = len(ops)
    banks = [[b["bank"] if isinstance(b, dict) else b for b in o["b"]] for o in ops]
    fixed = [set(d) for d in lk[0]]
    stay, members = {}, {}
    for i in order:
        for b in ops[i]["b"]:
            if isinstance(b, dict):
                if b["id"] not in members:
                    members[b["id"]] = []
                    if b["bank"] in stay:
                        fixed[i].update(members[stay[b["bank"]]])
                    stay[b["bank"]] = b["id"]
                members[b["id"]].append(i)
    fixed = [sorted(d) for d in fixed]
    latm = [[o.get("lat", 0.0) * x[3] for o in ops] for x in POLISH]
    inm = [[o["in"] * x[4] for o in ops] for x in POLISH]
    cost = [[{e: a[0] + o.get("ng", 0) * (x[0] - GAM) + o.get("ns", 0) * (x[1] - SCA) for e, a in o["alts"].items()} for o in ops]
            for x in POLISH]

    def walk(order, eng, m):
        lat, co, lats, ins = POLISH[m][2], cost[m], latm[m], inm[m]
        fin, why = [0.0] * n, [-1] * n
        free, elast, blast = {e: 0.0 for e in ENG}, {e: -1 for e in ENG}, [-1] * 8
        most, last = 0.0, -1
        for i in order:
            e = eng[i]
            st, w = free[e], elast[e]
            if ins[i] > st:
                st, w = ins[i], -1
            pe_ = e == "P"
            for d in fixed[i]:
                t = fin[d] if pe_ and eng[d] == "P" else fin[d] + lat
                if t > st:
                    st, w = t, d
            for b in banks[i]:
                d = blast[b]
                if d >= 0:
                    t = fin[d] if pe_ and eng[d] == "P" else fin[d] + lat
                    if t > st:
                        st, w = t, d
                blast[b] = i
            t = free[e] = st + co[i][e]
            elast[e] = i
            t += lats[i]
            fin[i], why[i] = t, w
            if t > most:
                most, last = t, i
        return most, why, last

    def lift(order, i, j):
        a, b = order.index(j), order.index(i)
        need, up, rest = set(fixed[i]), [i], []
        for x in order[b - 1:a - 1 if a else None:-1]:
            if x in need:
                up.append(x)
                need.update(fixed[x])
            else:
                rest.append(x)
        if j in up:
            return None
        return order[:a] + up[::-1] + rest[::-1] + order[b + 1:]

    place = {(o["pos"], o["rnd"]): i for i, o in enumerate(ops) if o["pos"] >= 0}

    def twin(i, s):
        return i if s == 0 else place.get((ops[i]["pos"], ops[i]["rnd"] + s))

    rng = np.random.RandomState(11)
    res = [walk(order, eng, m) for m in range(len(POLISH))]
    now = best = sum(r[0] for r in res)
    keep = (order, list(eng))
    for step in range(steps):
        _, why, i = res[rng.randint(len(res))]
        pairs = []
        while why[i] >= 0:
            if why[i] not in fixed[i] or len(ops[i]["alts"]) > 1:
                pairs.append((i, why[i]))
            i = why[i]
        i, j = pairs[rng.randint(len(pairs))]
        new, ne = order, eng
        shifts = range(1 - RO, RO) if rng.rand() < ALIKE else [0]
        flip = [x for x in (i, j) if len(ops[x]["alts"]) > 1]
        if flip and (j in fixed[i] or rng.rand() < 0.3):
            x = flip[rng.randint(len(flip))]
            ne = list(eng)
            for s in shifts:
                y = twin(x, s)
                if y is not None:
                    ne[y] = "V" if eng[x] == "A" else "A"
        else:
            for s in shifts:
                x, y = twin(i, s), twin(j, s)
                if x is not None and y is not None and new.index(y) < new.index(x):
                    new = lift(new, x, y) or new
            if new is order:
                continue
        r = [walk(new, ne, m) for m in range(len(POLISH))]
        s = sum(x[0] for x in r)
        if s <= now + HEAT * (1.0 - step / steps) * rng.exponential():
            order, eng, res, now = new, ne, r, s
            if s < best:
                best, keep = s, (order, list(eng))
    return keep[0], keep[1], banks, fixed, best / len(POLISH)


POLISH = [(1.5, 3.8, 170.0, 1.0, 0.9), (1.8, 5.0, 120.0, 1.5, 1.0)]
HEAT, ALIKE = 60.0, 0.7


def rank_program(g, core, T, topo):
    q = T.rank_of(core)
    if q is None:
        return
    sem = T.sem
    others = [(q + d) % N for d in (1, 2, 3)]
    rows = lambda r: slice(32 * r, 32 * r + 32)
    sent = [0]

    def dst(r):
        rid, pid, _ = topo.addr(T.cores[r])
        return DstId(rid=rid, pnc=pid)

    def shared(r):
        return [e for e in topo.engines(T.cores[r], T.cores[(r + 1) % N])
                if all(e in topo.engines(T.cores[r], T.cores[(r + d) % N]) for d in (2, 3))]

    def send(src, land, r, rsem):
        rid, pid, _ = topo.addr(T.cores[r])
        g.remote_dma(land, src, rsem, sem.snd, pid, rid, topo.mask(core, T.cores[r]))
        sent[0] += len(topo.engines(core, T.cores[r]))

    def each(items, rsem):
        (src, land), = items
        en = shared(q)
        w = len(en) // 4
        g.remote_dma_fused([RemoteDMATransfer(dst_ids=[dst(r)], dma_engine_mask=sum(1 << e for e in en[w * j:w * j + w]),
                                              remote_sem=rsem, src=src[r], dst=land[q]) for j, r in enumerate(others)], local_sem=sem.snd)
        sent[0] += 3 * w

    def spread(items, rsem):
        en = shared(q)
        w = len(en) // len(items)
        g.remote_dma_fused([RemoteDMATransfer(dst_ids=[dst(r) for r in others], dma_engine_mask=sum(1 << e for e in en[w * j:w * j + w]),
                                              remote_sem=rsem, srcs=[src], dsts=[land[q]] * 3) for j, (src, land) in enumerate(items)],
                           local_sem=sem.snd)
        sent[0] += w * len(items)

    quarters = sum(len(shared(r)) // 4 for r in others)
    whole = sum(len(shared(r)) for r in others)

    def turn(items, rsem):
        (src, land), = items
        for r in others:
            send(src[r], land[q], r, rsem)

    def full(r):
        return len(topo.engines(T.cores[r], core))

    net = {"turn": turn, "all": spread, "in": {"turn": sum(full(r) for r in others), "all": whole}}

    ops = build_ops(T, q, net)
    if not TUNED:
        lk = links(ops)
        tune(ops, lk, STEPS)
        TUNED.extend(polish(ops, lk, STEPS2))
    order, eng, banks, fixed = TUNED[:4]
    deps, end, blast = [set(d) for d in fixed], {}, {}
    for j, i in enumerate(order):
        ops[i]["e"], end[i] = eng[i], j
        for b0, b in zip(ops[i]["b"], banks[i]):
            if isinstance(b0, dict):
                b0["bank"] = b
            if b in blast:
                deps[i].add(blast[b])
            blast[b] = i
    Q = {"P": g.tensor, "V": g.vector, "A": g.scalar, "G": g, "S": g.sync}
    idx, cnt = {}, {"P": 0, "V": 0, "A": 0, "G": 0}
    for i in order:
        if "sem" not in ops[i]:
            cnt[eng[i]] += 1
            idx[i] = cnt[eng[i]]

    for j, r in enumerate(others):
        for cq in range(4):
            g.sync.dma_start(T.SX[rows(cq), 1024 * j:1024 * j + 1024], T.x0[rows(r), 1024 * cq:1024 * cq + 1024]).then_inc(sem["stx%d" % j], 16)
    g.scalar.dma_start(T.sk[:, :, :], T.kw[:]).then_inc(sem.stk, 16)
    g.scalar.dma_start(T.sl[:, :, :], T.l0[:]).then_inc(sem.stk, 16)
    g.scalar.dma_start(T.sz[:, :, :], T.z0[:]).then_inc(sem.stk, 16)
    g.scalar.dma_start(T.lz[q], T.z0[rows(q), :]).then_inc(sem.own, 16)
    g.scalar.dma_start(T.lk[q], T.kw[rows(q), :]).then_inc(sem.own, 16)
    g.scalar.dma_start(T.ll[q], T.l0[2 * q:2 * q + 2, :]).then_inc(sem.own, 16)
    g.sync.dma_start(T.X[rows(q), 0:W], T.x0[rows(q), :]).then_inc(sem.inx, 16)
    g.sync.wait_ge(sem.stx2, 64)
    for r in others:
        g.sync.dma_start(T.ss[r], T.asc[rows(r), :]).then_inc(sem.sts, 16)
    back = [(q - d) % N for d in (1, 2, 3)]
    landed = [("in0", sem.ink, 48), ("in1", sem.inx, 16), ("in2", sem.ins, 16 * N)]
    landed += [("inx%d" % j, sem["ax%d" % j], full(r)) for j, r in enumerate(back)]

    known = {e: {} for e in Q}
    clock = {}

    def emit(i):
        e = eng[i]
        kn = known[e]
        need = {}
        for d in deps[i]:
            if "sem" in ops[d]:
                need[ops[d]["sem"]] = (ops[d]["val"], d)
            elif not (e == "P" and eng[d] == "P") and idx[d] > need.get(eng[d], (0, None))[0]:
                need[eng[d]] = (idx[d], d)
        for f, (v, d) in sorted(need.items(), key=lambda x: -end[x[1][1]]):
            if v > kn.get(f, 0):
                Q[e].wait_ge(sem[f], v)
                kn[f] = v
                if "far" not in ops[d]:
                    for f2, v2 in clock[d].items():
                        kn[f2] = max(kn.get(f2, 0), v2)
        if e == "G" and i in idx and idx[i] - 1 > kn.get("G", 0):
            g.wait_ge(sem.G, idx[i] - 1)
            kn["G"] = idx[i] - 1
        for key, s, v in landed:
            if key in ops[i]["r"] and not kn.get(key, 0):
                Q[e].wait_ge(s, v)
                kn[key] = 1
        if "sem" in ops[i]:
            ops[i]["alts"][e][1](g)
        else:
            ops[i]["alts"][e][1](g).then_inc(sem[e], 1)
        clock[i] = dict(kn)

    gfirst = [i for i in order if "early" in ops[i]]
    for i in gfirst:
        emit(i)
    g.wait_ge(sem.stk, 48)
    each([(T.sl, T.ll)], sem.ak)
    each([(T.sk, T.lk)], sem.ak)
    each([(T.sz, T.lz)], sem.ak)
    for j, r in enumerate(others):
        g.wait_ge(sem["stx%d" % j], 64)
        send(T.SX[:, 1024 * j:1024 * j + 1024], T.LX[:, 1024 * j:1024 * j + 1024], r, sem["ax%d" % j])
    g.wait_ge(sem.sts, 48)
    turn([(T.ss, T.ls)], sem.as_)
    g.sync.wait_ge(sem.own, 48)
    g.sync.wait_ge(sem.ak, 3 * quarters)
    g.sync.dma_start(T.Ki[:, :], T.lk[:, :, :]).then_inc(sem.ink, 16)
    g.sync.dma_start(T.Li[0:8, :], T.ll[:, :, :]).then_inc(sem.ink, 16)
    g.sync.dma_start(T.z[:, :], T.lz[:, :, :]).then_inc(sem.ink, 16)
    g.sync.dma_start(T.Si[rows(q), :], T.asc[rows(q), :]).then_inc(sem.ins, 16)
    g.sync.wait_ge(sem.as_, net["in"]["turn"])
    for r in back:
        g.sync.dma_start(T.Si[rows(r), :], T.ls[r]).then_inc(sem.ins, 16)

    for i in order:
        if i not in gfirst:
            emit(i)

    for o in ops:
        if "sem" in o and o["w"][0][0] == "y":
            g.wait_ge(sem[o["sem"]], o["val"])
    g.wait_ge(sem.snd, sent[0])
    for f in cnt:
        g.wait_ge(sem[f], cnt[f])
